import numpy as np, ml_dtypes
CORES = [66,74,82,90,194,202,210,218]
N = 8
BF = ml_dtypes.bfloat16
def gentries(a):
    return np.ascontiguousarray(a.reshape(8, 16, -1).transpose(0, 2, 1)).reshape(8, -1)
def gtable(e):
    e = np.asarray(e); return np.ascontiguousarray(e.reshape(8, -1, 16).transpose(0, 2, 1)).reshape(128, -1).astype(np.int32)
W, R, NR, TV = 2048, 32, 128, 3
K = R * NR; NONE = W - 1; SH = (N, 8, R, NR)
def hsh(a, b):
    return (((a * b) >> 5) + 37 * a + b) & (W - 1)
def pack(x, y, g, a, b, t):
    o = {"xt": np.ascontiguousarray(x.reshape(N, 128, W)).astype(np.float32).astype(BF), "yv": np.ascontiguousarray(y.reshape(N, 128, TV * NR)).astype(np.float32).astype(BF)}
    for k, v in (("gl", g), ("al", a), ("bl", b), ("th", t)): o[k] = np.stack([gtable(w.reshape(8, -1)) for w in v])
    return o
def robots(rng, share, mem):
    g = np.where(rng.random(SH) < share, rng.integers(0, NONE, SH), NONE); keep = rng.random(SH) < mem
    return g, np.where(keep, rng.integers(0, NONE, SH), NONE), np.where(keep, rng.integers(0, NONE, SH), NONE)
def pool(rng, goals, m):
    a = rng.permutation(NONE)[:64]; a[0] = 64; a[1] = 128
    lut = np.zeros(W, bool); lut[goals] = True
    i, j = np.nonzero(lut[hsh(a[:, None], np.arange(NONE)[None, :])]); s = rng.integers(0, len(i), m)
    return a[i[s]], j[s]
def halves(rng, x, y, q, e):
    near = np.zeros(W, bool); near[rng.permutation(NONE)[:W // 2]] = True
    x[q, e] = np.where(near[None, :], rng.integers(0, 64, (16, W)), rng.integers(128, 256, (16, W)))
    y[q, e, :, 0] = rng.integers(0, 64, (16, NR))
    return near
def pairs(rng, near):
    far = rng.permutation(np.nonzero(~near[:NONE])[0]); a = far[:128]
    i, j = np.nonzero(near[hsh(a[:, None], far[None, :])]); s = rng.permutation(len(i))
    u, v = a[i[s]], far[j[s]]
    return u, v, hsh(u, v)
def setup_inputs(rng):
    x = rng.integers(0, 256, (N, 8, 16, W)); y = rng.integers(0, 256, (N, 8, 16, TV, NR))
    g, a, b = robots(rng, rng.choice(np.array([0.3, 0.6, 0.9, 1.0]), (N, 8, 1, NR)), 0.4)
    return pack(x, y, g, a, b, rng.integers(900, 1700, SH))
def setup_inputs_clash(rng):
    x = rng.integers(0, 256, (N, 8, 16, W)); y = rng.integers(0, 256, (N, 8, 16, TV, NR)); g, a, b = robots(rng, 1.0, 0.3)
    for q in range(N):
        for e in range(8):
            goals = np.concatenate([np.array([0, W - 2]), rng.integers(1, W - 2, 2)]); c = rng.integers(0, 256, 16)
            x[q, e][:, goals] = c[:, None]; y[q, e][:, 0, :] = c[:, None]
            u, v = pool(rng, goals, (R // 2) * NR)
            g[q, e, 0::2] = u.reshape(R // 2, NR); g[q, e, 1::2] = v.reshape(R // 2, NR)
    g = np.where((rng.random((N, 8, 1, NR)) < 0.3) | (rng.random(SH) < 0.1), NONE, g)
    for q in range(N):
        for s, e in enumerate(rng.permutation(8)[:2]):
            u, v, n = pairs(rng, halves(rng, x, y, q, e))
            if s == 0:
                w = np.nonzero(n == n[0])[0]; i = w[rng.integers(0, len(w), K // 2)]
            else:
                i = rng.integers(0, len(n), K // 2); i[:NR] = rng.permutation(np.unique(n, return_index=True)[1])[:NR]
            g[q, e, 0::2] = u[i].reshape(R // 2, NR); g[q, e, 1::2] = v[i].reshape(R // 2, NR)
    return pack(x, y, g, a, b, rng.integers(900, 1700, SH))
def setup_inputs_ties(rng):
    s = rng.integers(0, 2, (N, 8, 1, 1)) * 3 + 1
    x = 100 + s * rng.integers(0, 8, (N, 8, 16, W)); y = 100 + s[..., None] * rng.integers(0, 8, (N, 8, 16, TV, NR))
    g, a, b = robots(rng, rng.choice(np.array([0.4, 0.7, 1.0]), (N, 8, 1, NR)), 0.6)
    return pack(x, y, g, a, b, np.where(s == 1, rng.integers(0, 60, SH), rng.integers(60, 200, SH)))
def setup_inputs_corners(rng):
    x = rng.integers(0, 256, (N, 8, 16, W)); y = rng.integers(0, 256, (N, 8, 16, TV, NR)); g, a, b = robots(rng, 1.0, 1.0)
    kd = rng.integers(0, 11, (N, 8, 1, NR)); k = np.arange(R)[None, None, :, None]
    none = g.copy()
    for q in range(N):
        for e in range(8):
            u, v = pool(rng, np.array([NONE]), (R // 2) * NR)
            none[q, e, 0::2] = u.reshape(R // 2, NR); none[q, e, 1::2] = v.reshape(R // 2, NR)
    g = np.where(kd == 6, g[:, :, :1], np.where(kd == 8, none, np.where((kd == 10) & (k % 2 == 0), 0, g)))
    full = (kd == 1) | ((kd == 2) & (k % 2 == 0)) | ((kd == 3) & (k % 2 == 1)) | ((kd == 4) & (k == R - 1)) | ((kd == 5) & (k == 0)) | (kd == 6) | ((kd == 7) & (k % 4 < 2)) | (kd == 8) | ((kd == 9) & (rng.random(SH) < 0.5)) | (kd == 10)
    g = np.where(full, g, NONE)
    a = np.where((kd == 9) | ((kd == 10) & (rng.random(SH) < 0.5)), NONE, a); b = np.where(kd == 7, NONE, b)
    a = np.where(rng.random(SH) < 0.05, rng.choice(np.array([0, W - 2]), SH), a)
    t = rng.choice(np.array([0, 4080, 1300, 1400]), SH, p=[0.3, 0.2, 0.25, 0.25])
    for q in range(N):
        for s, e in enumerate(rng.permutation(8)[:2]):
            near = halves(rng, x, y, q, e); far = np.nonzero(~near[:NONE])[0]
            second = (np.arange(R)[:, None] + rng.integers(0, 2, NR)[None, :]) % 2 == 0
            if s == 0:
                a[q, e] = rng.integers(0, NONE, (R, NR)); t[q, e] = rng.integers(0, 1000, (R, NR))
            else:
                far = far[near[hsh(NONE, far)]]; w = rng.random((R, NR)) < 0.5
                a[q, e] = np.where(w, NONE, a[q, e]); t[q, e] = np.where(w, t[q, e], 4080)
            g[q, e] = np.where(second, far[rng.integers(0, len(far), (R, NR))], NONE)
    return pack(x, y, g, a, b, t)
def setup_inputs_ends(rng):
    v = 255 * rng.integers(0, 2, (N, 1, 1, 1)); e = rng.integers(0, 4, (N, 8, 1, W))
    x = np.where(e == 0, 0, np.where(e == 1, 255, 255 * rng.integers(0, 2, (N, 8, 16, W))))
    near = (rng.random((N, 8, 1, W)) < 0.25) & (np.arange(16)[None, None, :, None] == rng.integers(0, 16, (N, 8, 1, W)))
    x = np.where(near, np.abs(x - 1), x)
    x[..., 0] = v[..., 0]; x[..., W - 2] = v[..., 0]; x[..., W - 74] = 255 - v[..., 0]
    e = rng.integers(0, 3, (N, 8, 1, TV, NR)); y = np.where(e == 0, 0, np.where(e == 1, 255, 255 * rng.integers(0, 2, (N, 8, 16, TV, NR))))
    S = np.array([0, 1, int(rng.integers(2, NR - 2)), NR - 2, NR - 1])
    k = np.arange(R)[None, None, :, None]
    ty = rng.choice(np.array([0, 1, 2]), (N, 8, 1, NR), p=[0.6, 0.3, 0.1])
    ty[..., S] = 1
    g = np.where(ty == 0, rng.choice(np.array([0, NONE]), SH), np.where(ty == 1, np.where(k % 2 == 0, W - 2, 0), np.where(rng.random(SH) < 0.3, NONE, rng.integers(0, NONE, SH))))
    a = rng.choice(np.array([0, NONE, W - 2]), SH, p=[0.45, 0.45, 0.1]); b = rng.choice(np.array([0, NONE, W - 2]), SH, p=[0.45, 0.45, 0.1])
    t = rng.choice(np.array([0, 4080, 4079, 1]), SH, p=[0.4, 0.4, 0.1, 0.1])
    far = np.roll(v, -1, axis=0)
    for i in S:
        y[:, :, :, 0, i] = 255 - v[..., 0]; y[:, :, :, 1, i] = 255 - far[..., 0]
        t[:, :, :, i] = 4080 - 4 * R - (np.arange(R)[None, None, :] // 2) % 2
    return pack(x, y, g, a, b, t)
def setup_inputs_spread(rng):
    x = np.minimum((np.exp2(8 * rng.random((N, 8, 1, W))) * rng.random((N, 8, 16, W))).astype(np.int64), 255)
    y = np.minimum((np.exp2(8 * rng.random((N, 8, 1, TV, NR))) * rng.random((N, 8, 16, TV, NR))).astype(np.int64), 255)
    g, a, b = robots(rng, rng.random((N, 8, 1, NR)), rng.random((N, 8, 1, NR)))
    few = rng.random((N, 8, 1, NR)) < 0.5
    g = np.where(few & (g != NONE), np.minimum((NONE * rng.random(SH) ** 6).astype(np.int64), NONE - 1), g)
    t = np.minimum(np.exp2(12 * rng.random(SH)).astype(np.int64) - 1, 4080)
    return pack(x, y, g, a, b, t)
def check_inputs(d):
    bad = []
    for k, hi in (("xt", 255), ("yv", 255), ("gl", NONE), ("al", NONE), ("bl", NONE), ("th", 4080)):
        v = np.asarray(d[k]).astype(np.float64)
        if not (np.all(v >= 0) and np.all(v <= hi)): bad.append("range of " + k)
        elif np.any(v != np.floor(v)): bad.append("whole numbers of " + k)
    return bad
def reference(xt, yv, gl, al, bl, th):
    x = xt.astype(np.float32).astype(np.int32).reshape(N, 8, 16, W); y = yv.astype(np.float32).astype(np.int32).reshape(N, 8, 16, TV, NR)
    g, a, b, h = [np.stack([gentries(v) for v in w]).astype(np.int32).reshape(N, 8, R, NR) for w in (gl, al, bl, th)]
    c = np.zeros((N, NR), np.int32); row = np.arange(R)[None, :, None]; rob = np.arange(NR)[None, :]
    for t in range(TV):
        for r in range(N):
            q = (r + t) % N; G, A, B = g[r].copy(), a[r].copy(), b[r].copy()
            G1 = np.roll(G, -1, axis=1); n = hsh(G, G1); view = y[r][:, :, t][:, :, None, :]
            xg = np.take_along_axis(x[q], G.reshape(8, 1, K), 2); xn = np.take_along_axis(x[q], n.reshape(8, 1, K), 2)
            dg = np.add.reduce(np.abs(xg.reshape(8, 16, R, NR) - view), axis=1); dn = np.add.reduce(np.abs(xn.reshape(8, 16, R, NR) - view), axis=1)
            dg1 = np.roll(dg, -1, axis=1); full = G != NONE; full1 = np.roll(full, -1, axis=1)
            opens = full & (A != NONE) & ~full1 & (dg > h[r] + c[r][None, None, :])
            opened = np.roll(opens, 1, axis=1)
            merge = full & full1 & ~np.roll(opens, -1, axis=1) & ((row + t) % 2 == 0) & (n != NONE) & (dn < np.minimum(dg, dg1))
            gone = np.roll(merge, 1, axis=1)
            take = ~full & ~opened & full1 & (n != NONE) & (dn < dg1)
            some = np.any(merge, axis=1); low = np.argmax(merge, axis=1)
            i0 = low * NR + rob; i1 = ((low + 1) % R) * NR + rob
            val = (np.take_along_axis(xg, i0[:, None, :], 2) + np.take_along_axis(xg, i1[:, None, :], 2)) >> 1
            goal = np.take_along_axis(n.reshape(8, K), i0, 1)
            for e in range(8):
                w = np.nonzero(some[e])[0]; u, first = np.unique(goal[e][w], return_index=True)
                x[q, e][:, u] = val[e][:, w[first]]
            clear = opens | opened | gone | take
            g[r] = np.where(opens, A, np.where(opened, np.roll(B, 1, axis=1), np.where(merge | take, n, np.where(gone, NONE, G))))
            na = np.where(merge, G, np.where(clear, NONE, A)); nb = np.where(merge, G1, np.where(clear, NONE, B))
            a[r] = na; b[r] = nb; c[r] = np.add.reduce(merge.astype(np.int32), axis=(0, 1))
    o = [np.stack([gtable(v.reshape(8, -1)) for v in w]).astype(np.float32) for w in (g, a, b)]
    return {"og": o[0], "oa": o[1], "ob": o[2], "ox": x.reshape(N, 128, W).astype(np.float32).astype(BF)}

@@ -1,0 +1,440 @@
+from concourse.mybir import AluOpType as A
+from concourse.mybir import ActivationFunctionType as F
+
+U = 128
+NONE = 2047
+WT = 2048 + 128
+BIG = 32768.0
+FAR = 1024.0
+CH = [(0, 0, 64), (0, 64, 128), (1, 0, 64), (1, 64, 128), (2, 0, 64), (2, 64, 96), (2, 96, 128)]
+
+SCRATCH = {}
+
+
+def _add(where, dtype, **kw):
+    for k, v in kw.items():
+        SCRATCH[k] = (where, [128] + (v if isinstance(v, list) else [v]), dtype)
+
+
+_add("sbuf", "bfloat16", tab0=WT, tab1=WT, tab2=WT, xsav=16, yvs=384, vx0=1024, vx1=1024, vx2=1024,
+     bo=128, lall=2048, ib=128, eq=1024, sc=1024, rst=1024, cs=128,
+     val0=128, val1=128, val2=128, a1v=128, a2v=128, b2v=128, b0v=128, c0v=128)
+for _k in range(len(CH)):
+    _add("sbuf", "bfloat16", **{"df%d" % _k: (CH[_k][2] - CH[_k][1]) * 16})
+_add("sbuf", "int32", gli=[32, 8], ali=[32, 8], bli=[32, 8], thi=[32, 8], pidx=8, p15=8, p4=8,
+     hb=128, pp=128, ny=128, sh=128, tt_=128, nxi=128, ki=24, gi=24, vi=128)
+_add("sbuf", "uint16", off=384, goff=24, lw0=8, lw1=8, lw2=8, a1l=8, a2l=8, b2l=8, b0l=8, c0l=8)
+_add("sbuf", "float16", gx0=136, gx1=136, gy0=128, gy1=128, abx0=256, abx1=256, aby0=256, aby1=256, ab2=256,
+     ex=136, ey=128, ax=128, ay=128, qy=128, nx=128, rr=128, ids=896,
+     ones=128, jc=128, oxf=128, oyp=136, mm=256, tx=128, ty=128, prod=1024)
+_add("sbuf", "float32", tha=128, thb=128, id32=128, ca=128, cb=128, cj=128, prow=8, pgrp=8, cc=8, dum=8, fb=[3, 8],
+     maskd=128, iw=WT, sgx=136, sqy=128, mn=128, mnm=128, mt=128, kn=384, k0=[3, 128], k1=[3, 64], k2=[3, 32],
+     k3=[3, 16], k4=[3, 8], k5=[3, 8], gf=8, bf=128, bd=128, xv=256, lm=8, lf=8,
+     ogs=[32, 8], oas=[32, 8], obs=[32, 8])
+_add("psum", "float32", **{"b%d" % k: 512 for k in range(8)})
+SEMAPHORES = ["pv", "pa", "pt", "pg", "dg", "dy", "dx", "da", "db", "dt", "og_", "oa_", "ob_", "ox_", "tl", "ls",
+              "t1", "t2"] + [s + k + "_" for s in ("a1", "a2", "b2", "b0", "c0") for k in "vl"]
+PART = {k: ("prod", U * j) for j, k in enumerate(("p1", "p2", "p3", "p4_", "p5", "p6", "p7", "p8"))}
+PART.update({k: ("ids", U * j) for j, k in enumerate(("id1", "idm", "id37", "id2047", "idn2047", "idbig", "idnbig"))})
+BANKS = ["b%d" % k for k in range(8)]
+
+
+def rank_program(g, core, T, topo):
+    rank = T.rank_of(core)
+    if rank is None:
+        return
+    n = len(T.cores)
+    Q = {"V": g.vector, "S": g.scalar, "P": g.tensor, "G": g, "Y": g.sync}
+    PS = {"V": "pv", "S": "pa", "P": "pt", "G": "pg"}
+    cnt = {"V": 0, "S": 0, "P": 0, "G": 0}
+    known = {e: {} for e in Q}
+    wr, rd, bank = {}, {}, {}
+
+    def wait(e, toks):
+        for eng, sem, val, snap in toks:
+            if known[e].get(sem, 0) >= val:
+                continue
+            Q[e].wait_ge(T.sem[sem], val)
+            for s, v in snap.items():
+                if known[e].get(s, 0) < v:
+                    known[e][s] = v
+            known[e][sem] = val
+
+    def hit(recs, lo, hi):
+        return [r[2] for r in recs if r[0] < hi and lo < r[1]]
+
+    def before(e, reads, writes):
+        toks = []
+        for b, lo, hi in reads:
+            toks += hit(wr.get(b, []), lo, hi)
+        for b, lo, hi in writes:
+            w = hit(wr.get(b, []), lo, hi)
+            toks += [t for t in w if not (e == "P" and t[0] == "P")]
+            toks += hit(rd.get(b, []), lo, hi)
+        for b, lo, hi in reads + writes:
+            if b in bank:
+                toks += [t for f, t in bank[b].items() if f != e]
+        toks.sort(key=lambda t: -t[2])
+        wait(e, toks)
+
+    def after(e, reads, writes, tok):
+        for b, lo, hi in writes:
+            wr[b] = [r for r in wr.get(b, []) if not (lo <= r[0] and r[1] <= hi)] + [(lo, hi, tok)]
+            rd[b] = [r for r in rd.get(b, []) if not (lo <= r[0] and r[1] <= hi)]
+        for b, lo, hi in reads:
+            rd[b] = [r for r in rd.get(b, []) if not (lo <= r[0] and r[1] <= hi and r[2][0] == e)] + [(lo, hi, tok)]
+        for b, lo, hi in reads + writes:
+            if b in BANKS:
+                bank.setdefault(b, {})[e] = tok
+
+    def landed(b, sem, val, e="D"):
+        after(e, [], [(b, 0, 10 ** 6)], (e, sem, val, {}))
+
+    def do(e, outs, ins, call):
+        reads = [r for v in ins for r in v[1]]
+        writes = [r for v in outs for r in v[1]]
+        before(e, reads, writes)
+        i = call(Q[e])
+        cnt[e] += 1
+        i.then_inc(T.sem[PS[e]], 1)
+        snap = dict(known[e])
+        after(e, reads, writes, (e, PS[e], cnt[e], snap))
+
+    def B(b, lo=0, hi=U):
+        if b in PART:
+            b, o = PART[b]
+            lo, hi = lo + o, hi + o
+        return (T[b][:, lo:hi], [(b, lo, hi)])
+
+    def X3(b, *ix):
+        return (T[b][(slice(None),) + ix], [(b, 0, 10 ** 6)])
+
+    ALL = slice(None)
+    EV, OD = slice(0, 32, 2), slice(1, 32, 2)
+
+    def ST(b, lo, hi, step):
+        return (T[b][:, lo:hi:step], [(b, lo, hi)])
+
+    def ind(w, o):
+        return (w[0].indirect(o[0]), w[1] + o[1])
+
+    def tt(o, a, b, op):
+        do("V", [o], [a, b], lambda q: q.tensor_tensor(out=o[0], in0=a[0], in1=b[0], op=op))
+
+    def ts(o, a, s1, op0, s2=None, op1=None):
+        col = [s1] if isinstance(s1, tuple) else []
+        x = s1[0] if col else s1
+        if op1 is None:
+            do("V", [o], [a] + col, lambda q: q.tensor_scalar(out=o[0], in0=a[0], scalar1=x, scalar2=None, op0=op0))
+        else:
+            do("V", [o], [a] + col, lambda q: q.tensor_scalar(out=o[0], in0=a[0], scalar1=x, scalar2=s2, op0=op0, op1=op1))
+
+    def cp(o, a):
+        do("V", [o], [a], lambda q: q.tensor_copy(out=o[0], in_=a[0]))
+
+    def fill(o, x):
+        do("V", [o], [], lambda q: q.memset(o[0], x))
+
+    def act(o, a, func, scale=1.0, bias=0.0):
+        do("S", [o], [a], lambda q: q.activation(out=o[0], in_=a[0], func=func, bias=bias, scale=scale))
+
+    def mm(o, l, r, start, stop):
+        do("P", [o], [l, r], lambda q: q.matmul(out=o[0], lhsT=l[0], rhs=r[0], start=start, stop=stop))
+
+    def psum(bk, lo, terms):
+        rots = [t[3] for t in terms]
+        cuts = [(0, U)]
+        if 1 in rots:
+            cuts = [(0, 120), (120, U)]
+        if -1 in rots:
+            cuts = [(0, 8), (8, U)]
+        for a, b in cuts:
+            for k, (l, buf, c0, rot) in enumerate(terms):
+                s = (a + 8 * rot) % U
+                mm(B(bk, lo + a, lo + b), B(l), B(buf, c0 + s, c0 + s + b - a), k == 0, k == len(terms) - 1)
+
+    def load(sem, b, src):
+        g.sync.dma_start(out=T[b][(ALL,) * len(T[b].shape)] if b != "tab0" else T[b][:, 0:2048], in_=src).then_inc(T.sem[sem], 16)
+        landed(b, sem, 16)
+
+    load("dg", "gli", T.gl[:, :])
+    load("dy", "yvs", T.yv[:, :])
+    load("dx", "tab0", T.xt[:, :])
+    load("da", "ali", T.al[:, :])
+    load("db", "bli", T.bl[:, :])
+    load("dt", "thi", T.th[:, :])
+
+    def iota(o, pattern, base, cm, flag=True):
+        if flag:
+            do("G", [o], [], lambda q: q.iota(o[0], pattern, base, cm, allow_small_or_imprecise_dtypes=True))
+        else:
+            do("G", [o], [], lambda q: q.iota(o[0], pattern, base, cm))
+
+    iota(B("pidx", 0, 8), [[16, 8]], 0, 1, False)
+    iota(B("cb"), [[0, 8], [1, 16]], 0, 0)
+    iota(B("ca"), [[1, 8], [0, 16]], 0, 0)
+    iota(B("cj"), [[4096, 16], [0, 8]], 0, 0)
+    iota(B("cc", 0, 8), [[16, 8]], 2048, 0)
+
+    fill(B("lall", 0, 2048), 0.0)
+    fill(B("eq", 0, 1024), 0.0)
+    fill(B("rst", 0, 1024), 1.0)
+    fill(ST("rst", 0, 1024, 128), 0.0)
+    fill(X3("fb", slice(1, 3), ALL), 0.25)
+    ts(B("p15", 0, 8), B("pidx", 0, 8), 15, A.bitwise_and)
+    ts(B("p4", 0, 8), B("pidx", 0, 8), 4, A.arith_shift_right)
+    cp(B("prow", 0, 8), B("p15", 0, 8))
+    cp(B("pgrp", 0, 8), B("p4", 0, 8))
+    ts(B("rr"), B("cb"), B("prow", 0, 1), A.is_equal)
+    ts(B("bo"), B("ca"), B("pgrp", 0, 1), A.is_equal)
+    tt(B("id1"), B("bo"), B("rr"), A.mult)
+    for b, x in (("id37", 37.0), ("idm", -1.0), ("id2047", 2047.0), ("idn2047", -2047.0), ("idbig", BIG), ("idnbig", -BIG)):
+        ts(B(b), B("id1"), x, A.mult)
+    ts(B("ones"), B("rr"), 0.0, A.mult, 1.0, A.add)
+
+    def late_consts():
+        for a in range(8):
+            cp((T.lall[:, 16 * a:16 * a + 129 * 15 + 1:129], [("lall", 0, 2048)]), B("bo", 16 * a, 16 * a + 16))
+        cp(B("jc"), B("cj"))
+        cp(B("id32"), B("id1"))
+        cp(B("ib"), B("id1"))
+        ts(B("maskd"), B("cb"), B("prow", 0, 1), A.is_ge, 4096.0, A.mult)
+        tt(B("dum", 0, 8), B("prow", 0, 8), B("cc", 0, 8), A.add)
+        ts(X3("fb", 0, ALL), B("dum", 0, 8), 65536.0, A.add, 2.0 ** -18, A.mult)
+
+    def views(t):
+        v = "vx%d" % t
+        act(B(v, 0, 128), B("yvs", t * 128, t * 128 + 128), F.Copy)
+        for w in (128, 256, 512):
+            act(B(v, w, 2 * w), B(v, 0, w), F.Copy)
+
+    def lists(t, ysrc):
+        gx, gy = "gx%d" % (t % 2), "gy%d" % (t % 2)
+        ts(B("ey"), B(gy), 2047.0, A.is_equal)
+        cp(B("off", 0, 128), B(gx))
+        psum("b1", 0, [("id37", gx, 0, 0), ("id1", gy, 0, 0)])
+        psum("b1", 128, [("id2047", "ones", 0, 0), ("idn2047", "ey", 0, 0)])
+        tt(B("pp"), B(gx), ysrc, A.mult)
+        ts(B("hb"), B(gx, 8, 136), 64.96875, A.mult, 75738.515625, A.add)
+        ts(B("sh"), B("pp"), 5, A.arith_shift_right)
+        ts(B("ny"), B("hb"), 2047, A.bitwise_and)
+        tt(B("tt_"), B("sh"), B("b1"), A.add)
+        tt(B("b7"), B("ny"), B("b1", 128, 256), A.max)
+        ts(B("nxi"), B("tt_"), 2047, A.bitwise_and)
+        tt(B("qy"), B("b7"), B(gy), A.min)
+        cp(B("nx"), B("nxi"))
+        cp(B("off", 128, 256), B("qy"))
+        cp(B("off", 256, 384), B("nx"))
+        ts(B("ex", 0, 136), B(gx, 0, 136), 2047.0, A.is_equal)
+
+    def prepare(t):
+        s = t % 2
+        gx, gy, abx, aby = "gx%d" % s, "gy%d" % s, "abx%d" % s, "aby%d" % s
+        ts(B("ax"), B(abx), 2047.0, A.is_equal)
+        ts(B("ay"), B(aby), 2047.0, A.is_equal)
+        for k, (src, gb) in enumerate((("nx", 0), (gx, 0), (gy, 0))):
+            psum("b2", 128 * k, [("id1", src, 0, 0), ("id1", "jc", 0, 0)])
+        act(B("kn", 0, 384), B("b2", 0, 384), F.Copy, scale=2.0 ** -18)
+        c = [("ib", "cs", 0, 0)] if t else []
+        hx, hy, rot = ("thb", "tha", 1) if t == 1 else ("tha", "thb", 0)
+        psum("b3", 0, [("id32", hx, 0, 0), ("idbig", "ax", 0, 0), ("idbig", "ex", 0, 0), ("idnbig", "ey", 0, 0), ("idbig", "ones", 0, 0)] + c)
+        psum("b3", 128, [("id32", hy, 0, rot), ("idbig", "ay", 0, 0), ("idbig", "ey", 0, 0), ("idnbig", "ex", 8, 0), ("idbig", "ones", 0, 0)] + c)
+        psum("b5", 0, [("id1", abx, 0, 0), ("idm", gx, 0, 0)])
+        psum("b5", 128, [("id1", aby, 128, -1), ("idn2047", "ones", 0, 0)])
+        psum("b5", 256, [("id1", "nx", 0, 0), ("idm", gx, 0, 0)])
+        psum("b5", 384, [("id1", abx, 128, 0), ("idn2047", "ones", 0, 0)])
+        psum("b6", 0, [("id1", aby, 0, 0), ("idm", gy, 0, 0)])
+        psum("b6", 128, [("id1", "qy", 0, 0), ("idn2047", "ones", 0, 0)])
+        psum("b6", 256, [("id2047", "ones", 0, 0), ("idm", gy, 0, 0)])
+
+    def contract(k):
+        l, lo, hi = CH[k]
+        d, w = "df%d" % k, (hi - lo) * 16
+        for r in range(16):
+            mm(B("b%d" % l, lo, hi), B("lall", 128 * r, 128 * r + 128),
+               (T[d][:, r:w:16], [(d, 0, w)]), r == 0, r == 15)
+
+    def scatter(tab, lst, val):
+        w = B(tab, 0, WT)
+        do("V", [w], [B(lst, 0, 8), B(val)],
+           lambda q: q.tensor_copy(out=w[0].indirect(T[lst][:, 0:8]), in_=T[val][:, :]))
+
+    ncall = [0]
+
+    def send(dst, dbuf, dsem, sbuf, width, lsem="ls"):
+        rid, pid = topo.addr(dst, core)
+        before("G", [(sbuf, 0, width)], [])
+        g.remote_dma(out_ap=T[dbuf][:, 0:width], in_ap=T[sbuf][:, 0:width], remote_sem=T.sem[dsem], local_sem=T.sem[lsem],
+                     pid=pid, routing_id=rid, dma_engine_mask=topo.mask(core, dst))
+        if lsem == "ls":
+            ncall[0] += len(topo.engines(core, dst))
+
+    NE = {d: len(topo.engines(T.cores[(rank + d) % n], core)) for d in (1, 2, -1, -2)}
+    peer = {d: T.cores[(rank + d) % n] for d in (1, 2, -1, -2)}
+    SLOT = {"a1": 1, "a2": 2, "b2": 1, "b0": -1, "c0": -2}
+    for s, d in SLOT.items():
+        landed(s + "v", s + "v_", NE[d])
+        landed(s + "l", s + "l_", NE[d])
+    landed("tab1", "t1", NE[1])
+    landed("tab2", "t2", NE[2])
+
+    cp(B("gx0"), X3("gli", EV, ALL))
+    cp(B("gy0"), X3("gli", OD, ALL))
+    cp(B("gx0", 128, 136), B("gx0", 0, 8))
+    views(0)
+    lists(0, B("gy0"))
+    late_consts()
+    cp(B("xsav", 0, 1), B("tab0", 2047, 2048))
+    fill(B("tab0", 2047, 2048), FAR)
+    send(peer[-1], "tab1", "t1", "tab0", 2048, "tl")
+    send(peer[-2], "tab2", "t2", "tab0", 2048, "tl")
+    tabtok = ("D", "tl", len(topo.engines(core, peer[-1])) + len(topo.engines(core, peer[-2])), {})
+    after("D", [("tab0", 0, WT)], [], tabtok)
+    iota(B("iw", 0, WT), [[1, WT]], 0, 0)
+
+    def visit(t):
+        s = t % 2
+        gx, gy, abx, aby = "gx%d" % s, "gy%d" % s, "abx%d" % s, "aby%d" % s
+        tab = "tab%d" % t
+        for k in range(7):
+            l, lo, hi = CH[k]
+            w = (hi - lo) * 16
+            d = "df%d" % k
+            tt(B(d, 0, w), ind(B(tab, 0, 2048), B("off", l * 128 + lo, l * 128 + hi)), B("vx%d" % t, 0, w), A.subtract)
+            if k == 3 and t == 0:
+                cp(B("abx0", 0, 128), X3("ali", EV, ALL))
+                cp(B("aby0", 0, 128), X3("ali", OD, ALL))
+                cp(B("abx0", 128, 256), X3("bli", EV, ALL))
+                cp(B("aby0", 128, 256), X3("bli", OD, ALL))
+                cp(B("tha"), X3("thi", EV, ALL))
+                cp(B("thb"), X3("thi", OD, ALL))
+            act(B(d, 0, w), B(d, 0, w), F.Abs)
+            if k == 3:
+                act(B("sgx", 0, 128), B("b0"), F.Copy)
+                act(B("sgx", 128, 136), B("b0", 0, 8), F.Copy)
+                contract(3)
+                if t == 0:
+                    prepare(0)
+            elif k == 5:
+                act(B("sqy"), B("b1"), F.Copy)
+                contract(5)
+            elif k < 6:
+                contract(k)
+        tt(B("oyp", 8, 136), B("sqy"), B("b3", 128, 256), A.is_gt)
+        tt(B("oxf"), B("sgx"), B("b3"), A.is_gt)
+        psum("b4", 0, [("idbig", "ex", 0, 0), ("idbig", "ey", 0, 0), ("idbig", "oyp", 8, 0)])
+        tt(B("mn"), B("b1"), B("sgx"), A.min)
+        cp(B("oyp", 0, 8), B("oyp", 128, 136))
+        if t == 1:
+            scatter("tab0", "lw0", "val0")
+            scatter("tab2", "a2l", "a2v")
+        if t == 2:
+            scatter("tab0", "b0l", "b0v")
+            cp(B("tab0", 2047, 2048), B("xsav", 0, 1))
+        contract(6)
+        tt(B("mnm"), B("mn"), B("b4"), A.subtract)
+        tt(B("b7"), B("b2"), B("mnm"), A.is_ge)
+        tt(B("mm"), B("b2"), B("mnm"), A.is_lt)
+        for k in range(3):
+            tt(X3("k0", k, ALL), B("b7"), B("kn", 128 * k, 128 * k + 128), A.add)
+        for a, b, w in (("k0", "k1", 64), ("k1", "k2", 32), ("k2", "k3", 16), ("k3", "k4", 8)):
+            tt(X3(b, ALL, ALL), X3(a, ALL, slice(0, w)), X3(a, ALL, slice(w, 2 * w)), A.min)
+        tt(X3("k5", ALL, ALL), X3("k4", ALL, ALL), X3("fb", ALL, ALL), A.min)
+        ts(B("ki", 0, 24), X3("k5", ALL, ALL), 2.0 ** 18, A.mult)
+        ts(B("gi", 0, 24), B("ki", 0, 24), 4095, A.bitwise_and)
+        cp(B("goff", 0, 24), B("gi", 0, 24))
+        cp(B("gf", 0, 8), B("gi", 0, 8))
+        act(B("xv", 0, 256), ind(B(tab, 0, 2048), B("goff", 8, 24)), F.Copy, scale=0.5, bias=-0.125)
+        cp(B("bf"), ind(B("iw", 0, WT), B("goff", 0, 8)))
+        tt(B("bd"), B("bf"), B("maskd"), A.max)
+        for c in range(1, 8):
+            ts(B("eq", 128 * c, 128 * c + 16 * c), B("bf", 0, 16 * c), B("gf", c, c + 1), A.is_equal)
+        val, lw = "val%d" % t, "lw%d" % t
+        tt(B("vi"), B("xv", 0, 128), B("xv", 128, 256), A.add)
+        for c in range(8):
+            ts(B("eq", 144 * c, 144 * c + 16), B("bd", 16 * c, 16 * c + 16), B("gf", c, c + 1), A.is_equal)
+        cp(B(val), B("vi"))
+        e, z, r = B("eq", 0, 1024), B("sc", 0, 1024), B("rst", 0, 1024)
+        do("V", [z], [e, r], lambda q: q.tensor_tensor_scan(out=z[0], data0=r[0], data1=e[0], initial=0.0, op0=A.mult, op1=A.max))
+        tt(B("lm", 0, 8), ST("sc", 127, 1024, 128), B("dum", 0, 8), A.mult)
+        tt(B("lf", 0, 8), B("lm", 0, 8), B("gf", 0, 8), A.max)
+        cp(B(lw, 0, 8), B("lf", 0, 8))
+        for slot, d in ((("a1", -1), ("a2", -2)), (("b2", -1), ("b0", 1)), (("c0", 2),))[t]:
+            send(peer[d], slot + "v", slot + "v_", val, 128)
+            send(peer[d], slot + "l", slot + "l_", lw, 8)
+        psum("b4", 128, [("idbig", "ey", 0, 0), ("idbig", "ones", 0, 0), ("idnbig", "ex", 0, 0), ("idbig", "oyp", 0, 0)])
+        psum("b4", 256, [("idbig", "ones", 0, 0), ("idnbig", "ey", 0, 0), ("idbig", "oxf", 0, 0), ("idbig", "ex", 8, 0)])
+        tt(B("mt"), B("sqy"), B("b4", 128, 256), A.subtract)
+        tt(B("b7", 128, 256), B("sgx", 8, 136), B("b4", 256, 384), A.subtract)
+        tt(B("tx"), B("b2"), B("mt"), A.is_lt)
+        tt(B("ty"), B("sqy"), B("b7", 128, 256), A.is_lt)
+        tt(B("p1"), B("b5"), B("oxf"), A.mult)
+        tt(B("p2"), B("b5", 128, 256), B("oyp", 0, 128), A.mult)
+        tt(B("p3"), B("b5", 256, 384), B("mm"), A.mult)
+        tt(B("p4_"), B("b6"), B("oyp", 8, 136), A.mult)
+        tt(B("p5"), B("b5", 384, 512), B("oxf"), A.mult)
+        tt(B("p6"), B("b6", 256, 384), B("mm"), A.mult)
+        tt(B("p7"), B("b6", 128, 256), B("ty"), A.mult)
+        tt(B("p8"), B("b5", 256, 384), B("tx"), A.mult)
+        ry, rx = ((0, 1), (-1, 0), (0, 0))[t]
+        ny = [("id1", b, 0, ry) for b in (gy, "p4_", "p5", "p6", "p7")]
+        nx = [("id1", b, 0, rx) for b in (gx, "p1", "p2", "p3", "p8")]
+        psum("b0", 0, ny)
+        psum("b0", 128, nx)
+        psum("b3", 0, [("id2047", "oxf", 0, 0), ("id2047", "oyp", 0, 0), ("id2047", "tx", 0, 0), ("id2047", "mm", 0, 0)])
+        psum("b3", 128, [("id2047", "ones", 0, 0), ("idn2047", "mm", 0, 0)])
+        psum("b3", 256, [("id2047", "oyp", 8, 0), ("id2047", "oxf", 0, 0), ("id2047", "ty", 0, 0), ("id2047", "mm", 0, 0)])
+        if t < 2:
+            u = 1 - s
+            hx, hy = "gx%d" % u, "gy%d" % u
+            cp(B(hx), B("b0"))
+            cp(B(hy), B("b0", 128, 256))
+            cp(B(hx, 128, 136), B(hx, 0, 8))
+            lists(t + 1, B("b0", 128, 256))
+            cp(B("mm", 128, 256), B("mm"))
+            for k in range(16):
+                mm(B("b2", 384, 512), B("rr"), B("mm", 8 * k, 8 * k + 128), k == 0, k == 15)
+            act(B("cs"), B("b2", 384, 512), F.Copy)
+            views(t + 1)
+        else:
+            act(X3("ogs", OD, ALL), B("b0"), F.Copy)
+            act(X3("ogs", EV, ALL), B("b0", 128, 256), F.Copy)
+            before("Y", [("ogs", 0, 9)], [])
+            g.sync.dma_start(out=T.og[:, :], in_=T.ogs[:, :, :]).then_inc(T.sem.og_, 16)
+        tt(B("b7", 256, 384), B("b3", 128, 256), B(gx), A.max)
+        tt(B("b7", 384, 512), B("b3", 128, 256), B(gy), A.max)
+        tt(B("ab2", 0, 128), B("b3"), B(abx), A.max)
+        tt(B("ab2", 128, 256), B("b3"), B(abx, 128, 256), A.max)
+        if t < 2:
+            nax, nay = "abx%d" % u, "aby%d" % u
+            for o in (0, 128):
+                for a, b in ((0, 120), (120, 128)) if t == 0 else ((0, 128),):
+                    d = (a - 8 * rx) % U
+                    d, a2, b2 = (o + a, o + (a + 8) % U, 0) if t == 0 else (o, o, 0)
+                    w = b - a
+                    tt(B(nay, d, d + w), B("b7", 256 + a2, 256 + a2 + w), B("ab2", a2, a2 + w), A.min)
+                for a, b in ((0, 8), (8, 128)) if t == 1 else ((0, 128),):
+                    w = b - a
+                    sr = (a - 8) % U if t == 1 else a
+                    tt(B(nax, o + a, o + b), B("b3", 256 + sr, 256 + sr + w), B(aby, o + sr, o + sr + w), A.max)
+            prepare(t + 1)
+        else:
+            for o, b, q, sm in ((0, "oas", T.oa, "oa_"), (128, "obs", T.ob, "ob_")):
+                tt(X3(b, EV, ALL), B("b7", 256 + o, 384 + o), B("ab2", o, o + 128), A.min)
+                tt(X3(b, OD, ALL), B("b3", 256, 384), B(aby, o, o + 128), A.max)
+                before("Y", [(b, 0, 9)], [])
+                g.sync.dma_start(out=q[:, :], in_=T[b][:, :, :]).then_inc(T.sem[sm], 16)
+
+    visit(0)
+    scatter("tab1", "a1l", "a1v")
+    visit(1)
+    scatter("tab2", "b2l", "b2v")
+    visit(2)
+    scatter("tab0", "c0l", "c0v")
+    before("Y", [("tab0", 0, 2048)], [])
+    g.sync.dma_start(out=T.ox[:, :], in_=T.tab0[:, 0:2048]).then_inc(T.sem.ox_, 16)
+    for sm in ("og_", "oa_", "ob_", "ox_"):
+        g.sync.wait_ge(T.sem[sm], 16)
+    for e in ("V", "S", "P", "G"):
+        g.wait_ge(T.sem[PS[e]], cnt[e])
+    g.wait_ge(T.sem.ls, ncall[0])

@@ -1,12 +1,20 @@
+from concourse.bass import DstId, RemoteDMATransfer
 from concourse.mybir import AluOpType as A
 from concourse.mybir import ActivationFunctionType as F
 
-U = 128
+L = 136
+S = 17
+E = 16 * S
 NONE = 2047
-WT = 2048 + 128
+WT = 2048 + 256
 BIG = 32768.0
+MID = 6144.0
 FAR = 1024.0
-CH = [(0, 0, 64), (0, 64, 128), (1, 0, 64), (1, 64, 128), (2, 0, 64), (2, 64, 96), (2, 96, 128)]
+EQ = 584
+GATHERS = [(0, 0, 4), (0, 4, 8), (1, 0, 4), (1, 4, 8), (2, 0, 4), (2, 4, 6), (2, 6, 8)]
+IDS = {"id1": 1.0, "id1184": 1184.0, "id32": 32.0, "id65": 65.0, "idf": -1.0 / 32, "id4058": 4058.0, "id515": 33.0 / 64,
+       "idbig": BIG, "idm": -1.0, "idnbig": -BIG, "id4096": 4096.0, "idn4096": -4096.0, "idnmid": -MID, "id2047": 2047.0,
+       "idn2047": -2047.0, "id2048": 2048.0, "idn8": -8.0}
 
 SCRATCH = {}
 
@@ -16,32 +24,62 @@ def _add(where, dtype, **kw):
         SCRATCH[k] = (where, [128] + (v if isinstance(v, list) else [v]), dtype)
 
 
-_add("sbuf", "bfloat16", tab0=WT, tab1=WT, tab2=WT, xsav=16, yvs=384, vx0=1024, vx1=1024, vx2=1024,
-     bo=128, lall=2048, ib=128, eq=1024, sc=1024, rst=1024, cs=128,
-     val0=128, val1=128, val2=128, a1v=128, a2v=128, b2v=128, b0v=128, c0v=128)
-for _k in range(len(CH)):
-    _add("sbuf", "bfloat16", **{"df%d" % _k: (CH[_k][2] - CH[_k][1]) * 16})
-_add("sbuf", "int32", gli=[32, 8], ali=[32, 8], bli=[32, 8], thi=[32, 8], pidx=8, p15=8, p4=8,
-     hb=128, pp=128, ny=128, sh=128, tt_=128, nxi=128, ki=24, gi=24, vi=128)
-_add("sbuf", "uint16", off=384, goff=24, lw0=8, lw1=8, lw2=8, a1l=8, a2l=8, b2l=8, b0l=8, c0l=8)
-_add("sbuf", "float16", gx0=136, gx1=136, gy0=128, gy1=128, abx0=256, abx1=256, aby0=256, aby1=256, ab2=256,
-     ex=136, ey=128, ax=128, ay=128, qy=128, nx=128, rr=128, ids=896,
-     ones=128, jc=128, oxf=128, oyp=136, mm=256, tx=128, ty=128, prod=1024)
-_add("sbuf", "float32", tha=128, thb=128, id32=128, ca=128, cb=128, cj=128, prow=8, pgrp=8, cc=8, dum=8, fb=[3, 8],
-     maskd=128, iw=WT, sgx=136, sqy=128, mn=128, mnm=128, mt=128, kn=384, k0=[3, 128], k1=[3, 64], k2=[3, 32],
-     k3=[3, 16], k4=[3, 8], k5=[3, 8], gf=8, bf=128, bd=128, xv=256, lm=8, lf=8,
-     ogs=[32, 8], oas=[32, 8], obs=[32, 8])
+_add("sbuf", "bfloat16", tab0=WT, tab1=WT, tab2=WT, hand=512, xsav=16, yvs=384, vexp=[8, 4, 16], z1=128, z2=144, zm=144,
+     xg=24 * E)
+_add("sbuf", "bfloat16", mx=[24, E])
+_add("sbuf", "int32", gli=256, ali=256, bli=256, thi=256, pidx=8, p15=8, p4=8, p7=8, p8=8, qi=24, qj=24,
+     nxi=[8, S], qyi=[8, S], ki=24, gi=24, val0=128, val1=128, val2=128, a1v=128, a2v=128, b2v=128, b0v=128, c0v=128)
+_add("sbuf", "uint16", offx=L, offy=L, offn=L, goff=24, pin=24, pout=16,
+     lw0=8, lw1=8, lw2=8, a1l=8, a2l=8, b2l=8, b0l=8, c0l=8)
+_add("sbuf", "float16", g0=2 * L, g1=2 * L, aa0=2 * L, aa1=2 * L, bb0=2 * L, bb1=2 * L, ab2=2 * L, f8=2 * L, an=2 * L,
+     qy=[8, S], nx=[8, S], rr=128, bo=128, ids=128 * len(IDS), ones=L, onesp=L, pa_=L, pb_=L, rs=L, jc=L,
+     ox_=L, oy_=L, ty=L, nm=L, u=L, p1=L, p2=L, p4_=L, p5=L, p7_=L, pu=L, q6=L, bf=128, eq=EQ, w=EQ, sc=EQ)
+_add("sbuf", "float32", th2=2 * L, id32f=128, ca=128, cb=128, cz=144, cj=L, c16=24, c32=8, cn=16, col=16,
+     dum=8, sp4=8, iw=WT, sgx=L, sqy=L, mnu=L, mnm=L, tex=L, pp=L, s3=3 * L, gf=8, xv=256,
+     wg=2 * L, wa=2 * L, wb=2 * L, ogs=256, oas=256, obs=256)
 _add("psum", "float32", **{"b%d" % k: 512 for k in range(8)})
-SEMAPHORES = ["pv", "pa", "pt", "pg", "dg", "dy", "dx", "da", "db", "dt", "og_", "oa_", "ob_", "ox_", "tl", "ls",
+SEMAPHORES = ["pv", "pa", "pt", "pg", "dg", "dy", "dx", "ds", "da", "db", "dt", "sog", "soa", "sob", "sox", "tl", "ls", "hd",
               "t1", "t2"] + [s + k + "_" for s in ("a1", "a2", "b2", "b0", "c0") for k in "vl"]
-PART = {k: ("prod", U * j) for j, k in enumerate(("p1", "p2", "p3", "p4_", "p5", "p6", "p7", "p8"))}
-PART.update({k: ("ids", U * j) for j, k in enumerate(("id1", "idm", "id37", "id2047", "idn2047", "idbig", "idnbig"))})
+PART = {k: ("ids", 128 * j) for j, k in enumerate(IDS)}
+PART.update(id32f=("id32f", 0), z1=("z1", 0))
 BANKS = ["b%d" % k for k in range(8)]
+
+
+def carriers(rank, T, topo):
+    n, own = len(T.cores), T.cores[rank]
+    to = [T.cores[(rank - d) % n] for d in (1, 2)]
+    return [own] + [c for c in topo.cores_of(own) if c != own and all(topo.may_write(c, d) for d in to)]
+
+
+def helper_program(g, core, T, topo):
+    n = len(T.cores)
+    for rank in range(n):
+        cs = carriers(rank, T, topo)
+        if core in cs[1:]:
+            k, w = cs.index(core), 2048 // len(cs)
+            g.wait_ge(T.sem.hd, hand_engines(rank, T, topo)[k - 1][1])
+            sent = 0
+            for d in (1, 2):
+                dst = T.cores[(rank - d) % n]
+                rid, pid = topo.addr(dst, core)
+                g.remote_dma(out_ap=T["tab%d" % d][:, k * w:k * w + w], in_ap=T.hand[:, 0:w], remote_sem=T.sem["t%d" % d],
+                             local_sem=T.sem.ls, pid=pid, routing_id=rid, dma_engine_mask=topo.mask(core, dst))
+                sent += len(topo.engines(core, dst))
+            g.wait_ge(T.sem.ls, sent)
+
+
+def hand_engines(rank, T, topo):
+    own = T.cores[rank]
+    out = topo.engines(own, T.cores[(rank - 1) % len(T.cores)])
+    e = [x for x in topo.engines(own, carriers(rank, T, topo)[1]) if x not in out]
+    h = len(e) // 2
+    return [(sum(1 << x for x in p), len(p)) for p in (e[:h], e[h:], e)]
 
 
 def rank_program(g, core, T, topo):
     rank = T.rank_of(core)
     if rank is None:
+        helper_program(g, core, T, topo)
         return
     n = len(T.cores)
     Q = {"V": g.vector, "S": g.scalar, "P": g.tensor, "G": g, "Y": g.sync}
@@ -68,8 +106,7 @@ def rank_program(g, core, T, topo):
         for b, lo, hi in reads:
             toks += hit(wr.get(b, []), lo, hi)
         for b, lo, hi in writes:
-            w = hit(wr.get(b, []), lo, hi)
-            toks += [t for t in w if not (e == "P" and t[0] == "P")]
+            toks += [t for t in hit(wr.get(b, []), lo, hi) if not (e == "P" and t[0] == "P")]
             toks += hit(rd.get(b, []), lo, hi)
         for b, lo, hi in reads + writes:
             if b in bank:
@@ -77,92 +114,102 @@ def rank_program(g, core, T, topo):
         toks.sort(key=lambda t: -t[2])
         wait(e, toks)
 
-    def after(e, reads, writes, tok):
+    def after(e, reads, writes, tok, whole=True):
         for b, lo, hi in writes:
-            wr[b] = [r for r in wr.get(b, []) if not (lo <= r[0] and r[1] <= hi)] + [(lo, hi, tok)]
-            rd[b] = [r for r in rd.get(b, []) if not (lo <= r[0] and r[1] <= hi)]
+            if whole:
+                wr[b] = [r for r in wr.get(b, []) if not (lo <= r[0] and r[1] <= hi)]
+                rd[b] = [r for r in rd.get(b, []) if not (lo <= r[0] and r[1] <= hi)]
+            wr[b] = wr.get(b, []) + [(lo, hi, tok)]
         for b, lo, hi in reads:
             rd[b] = [r for r in rd.get(b, []) if not (lo <= r[0] and r[1] <= hi and r[2][0] == e)] + [(lo, hi, tok)]
         for b, lo, hi in reads + writes:
             if b in BANKS:
                 bank.setdefault(b, {})[e] = tok
 
-    def landed(b, sem, val, e="D"):
-        after(e, [], [(b, 0, 10 ** 6)], (e, sem, val, {}))
+    def landed(b, sem, val, lo=0, hi=10 ** 6):
+        after("D", [], [(b, lo, hi)], ("D", sem, val, {}))
 
-    def do(e, outs, ins, call):
+    def do(e, outs, ins, call, apart=False):
         reads = [r for v in ins for r in v[1]]
         writes = [r for v in outs for r in v[1]]
-        before(e, reads, writes)
+        before(e, reads, [] if apart else writes)
         i = call(Q[e])
         cnt[e] += 1
         i.then_inc(T.sem[PS[e]], 1)
-        snap = dict(known[e])
-        after(e, reads, writes, (e, PS[e], cnt[e], snap))
+        after(e, reads, writes, (e, PS[e], cnt[e], dict(known[e])), not apart)
 
-    def B(b, lo=0, hi=U):
+    ALL = slice(None)
+
+    def B(b, lo=0, hi=L):
         if b in PART:
             b, o = PART[b]
-            lo, hi = lo + o, hi + o
+            lo, hi = o, o + 128
         return (T[b][:, lo:hi], [(b, lo, hi)])
 
     def X3(b, *ix):
-        return (T[b][(slice(None),) + ix], [(b, 0, 10 ** 6)])
-
-    ALL = slice(None)
-    EV, OD = slice(0, 32, 2), slice(1, 32, 2)
+        return (T[b][(ALL,) + (ix or (ALL, ALL))], [(b, 0, 10 ** 6)])
 
     def ST(b, lo, hi, step):
-        return (T[b][:, lo:hi:step], [(b, lo, hi)])
+        return (T[b][:, lo:hi:step], [(b, min(lo, hi), max(lo, hi) + 1)])
+
+    def SEG(b, c0, c1, *ix):
+        return (T[b][(ALL, slice(c0, c1)) + ix], [(b, c0, c1)])
 
     def ind(w, o):
         return (w[0].indirect(o[0]), w[1] + o[1])
 
-    def tt(o, a, b, op):
-        do("V", [o], [a, b], lambda q: q.tensor_tensor(out=o[0], in0=a[0], in1=b[0], op=op))
+    def tt(o, a, b, op, apart=False):
+        do("V", [o], [a, b], lambda q: q.tensor_tensor(out=o[0], in0=a[0], in1=b[0], op=op), apart)
 
-    def ts(o, a, s1, op0, s2=None, op1=None):
-        col = [s1] if isinstance(s1, tuple) else []
-        x = s1[0] if col else s1
+    def ts(o, a, s1, op0, s2=None, op1=None, apart=False):
+        cols = [s for s in (s1, s2) if isinstance(s, tuple)]
+        x, y = [s[0] if isinstance(s, tuple) else s for s in (s1, s2)]
         if op1 is None:
-            do("V", [o], [a] + col, lambda q: q.tensor_scalar(out=o[0], in0=a[0], scalar1=x, scalar2=None, op0=op0))
+            do("V", [o], [a] + cols, lambda q: q.tensor_scalar(out=o[0], in0=a[0], scalar1=x, scalar2=None, op0=op0), apart)
         else:
-            do("V", [o], [a] + col, lambda q: q.tensor_scalar(out=o[0], in0=a[0], scalar1=x, scalar2=s2, op0=op0, op1=op1))
+            do("V", [o], [a] + cols, lambda q: q.tensor_scalar(out=o[0], in0=a[0], scalar1=x, scalar2=y, op0=op0, op1=op1), apart)
 
-    def cp(o, a):
-        do("V", [o], [a], lambda q: q.tensor_copy(out=o[0], in_=a[0]))
+    def cp(o, a, apart=False):
+        do("V", [o], [a], lambda q: q.tensor_copy(out=o[0], in_=a[0]), apart)
 
-    def fill(o, x):
-        do("V", [o], [], lambda q: q.memset(o[0], x))
+    def fill(o, x, apart=False):
+        do("V", [o], [], lambda q: q.memset(o[0], x), apart)
 
-    def act(o, a, func, scale=1.0, bias=0.0):
-        do("S", [o], [a], lambda q: q.activation(out=o[0], in_=a[0], func=func, bias=bias, scale=scale))
+    def scan(o, d0, d1, op0, op1):
+        do("V", [o], [d0, d1], lambda q: q.tensor_tensor_scan(out=o[0], data0=d0[0], data1=d1[0], initial=0.0, op0=op0, op1=op1))
 
-    def mm(o, l, r, start, stop):
-        do("P", [o], [l, r], lambda q: q.matmul(out=o[0], lhsT=l[0], rhs=r[0], start=start, stop=stop))
+    def act(o, a, scale=1.0, bias=0.0, apart=False):
+        do("S", [o], [a], lambda q: q.activation(out=o[0], in_=a[0], func=F.Copy, bias=bias, scale=scale), apart)
 
-    def psum(bk, lo, terms):
-        rots = [t[3] for t in terms]
-        cuts = [(0, U)]
-        if 1 in rots:
-            cuts = [(0, 120), (120, U)]
-        if -1 in rots:
-            cuts = [(0, 8), (8, U)]
-        for a, b in cuts:
-            for k, (l, buf, c0, rot) in enumerate(terms):
-                s = (a + 8 * rot) % U
-                mm(B(bk, lo + a, lo + b), B(l), B(buf, c0 + s, c0 + s + b - a), k == 0, k == len(terms) - 1)
+    def group(mats):
+        for k, (o, l, r) in enumerate(mats):
+            do("P", [o], [l, r], lambda q: q.matmul(out=o[0], lhsT=l[0], rhs=r[0], start=k == 0, stop=k == len(mats) - 1))
 
-    def load(sem, b, src):
-        g.sync.dma_start(out=T[b][(ALL,) * len(T[b].shape)] if b != "tab0" else T[b][:, 0:2048], in_=src).then_inc(T.sem[sem], 16)
-        landed(b, sem, 16)
+    def terms(bk, lo, ts_):
+        out = []
+        for l, buf, c, turn in ts_:
+            l = B(l)
+            if buf in ("nx", "qy"):
+                out.append((B(bk, lo, lo + L), l, X3(buf)))
+                continue
+            if turn in ("", "0"):
+                out.append((B(bk, lo, lo + L), l, B(buf, c, c + L)))
+            if turn in ("n", "N"):
+                out.append((B(bk, lo + 1, lo + L), l, B(buf, c, c + L - 1)))
+            if turn in ("p", "P"):
+                out.append((B(bk, lo, lo + L - 1), l, B(buf, c + 1, c + L)))
+            a, b = {"0": (0, 16), "N": (1, 16), "P": (16, 1)}.get(turn, (None, None))
+            if a is not None:
+                out.append((ST(bk, lo + a, lo + L, S), l, ST(buf, c + b, c + L, S)))
+        return out
 
-    load("dg", "gli", T.gl[:, :])
-    load("dy", "yvs", T.yv[:, :])
-    load("dx", "tab0", T.xt[:, :])
-    load("da", "ali", T.al[:, :])
-    load("db", "bli", T.bl[:, :])
-    load("dt", "thi", T.th[:, :])
+    def psum(bk, lo, ts_):
+        group(terms(bk, lo, ts_))
+
+    def load(q, sem, dst, src):
+        before(q, [], dst[1])
+        Q[q].dma_start(out=dst[0], in_=src).then_inc(T.sem[sem], 16)
+        landed(dst[1][0][0], sem, 16, dst[1][0][1], dst[1][0][2])
 
     def iota(o, pattern, base, cm, flag=True):
         if flag:
@@ -170,270 +217,343 @@ def rank_program(g, core, T, topo):
         else:
             do("G", [o], [], lambda q: q.iota(o[0], pattern, base, cm))
 
-    iota(B("pidx", 0, 8), [[16, 8]], 0, 1, False)
-    iota(B("cb"), [[0, 8], [1, 16]], 0, 0)
-    iota(B("ca"), [[1, 8], [0, 16]], 0, 0)
-    iota(B("cj"), [[4096, 16], [0, 8]], 0, 0)
-    iota(B("cc", 0, 8), [[16, 8]], 2048, 0)
+    fill(B("tab0", 2032, 2048), FAR)
+    load("Y", "dg", B("gli", 0, 256), T.gl[:, :])
+    load("S", "dx", (T.tab0[:, 0:NONE], [("tab0", 0, 2048)]), T.xt[:, 0:NONE])
+    load("Y", "dy", B("yvs", 0, 384), T.yv[:, :])
+    load("Y", "da", B("ali", 0, 256), T.al[:, :])
+    load("Y", "db", B("bli", 0, 256), T.bl[:, :])
+    load("Y", "dt", B("thi", 0, 256), T.th[:, :])
+    load("Y", "ds", B("xsav", 0, 2), T.xt[:, NONE - 1:NONE + 1])
 
-    fill(B("lall", 0, 2048), 0.0)
-    fill(B("eq", 0, 1024), 0.0)
-    fill(B("rst", 0, 1024), 1.0)
-    fill(ST("rst", 0, 1024, 128), 0.0)
-    fill(X3("fb", slice(1, 3), ALL), 0.25)
-    ts(B("p15", 0, 8), B("pidx", 0, 8), 15, A.bitwise_and)
-    ts(B("p4", 0, 8), B("pidx", 0, 8), 4, A.arith_shift_right)
-    cp(B("prow", 0, 8), B("p15", 0, 8))
-    cp(B("pgrp", 0, 8), B("p4", 0, 8))
-    ts(B("rr"), B("cb"), B("prow", 0, 1), A.is_equal)
-    ts(B("bo"), B("ca"), B("pgrp", 0, 1), A.is_equal)
-    tt(B("id1"), B("bo"), B("rr"), A.mult)
-    for b, x in (("id37", 37.0), ("idm", -1.0), ("id2047", 2047.0), ("idn2047", -2047.0), ("idbig", BIG), ("idnbig", -BIG)):
-        ts(B(b), B("id1"), x, A.mult)
-    ts(B("ones"), B("rr"), 0.0, A.mult, 1.0, A.add)
+    def C(k):
+        return B("col", k, k + 1)
 
-    def late_consts():
-        for a in range(8):
-            cp((T.lall[:, 16 * a:16 * a + 129 * 15 + 1:129], [("lall", 0, 2048)]), B("bo", 16 * a, 16 * a + 16))
-        cp(B("jc"), B("cj"))
-        cp(B("id32"), B("id1"))
-        cp(B("ib"), B("id1"))
-        ts(B("maskd"), B("cb"), B("prow", 0, 1), A.is_ge, 4096.0, A.mult)
-        tt(B("dum", 0, 8), B("prow", 0, 8), B("cc", 0, 8), A.add)
-        ts(X3("fb", 0, ALL), B("dum", 0, 8), 65536.0, A.add, 2.0 ** -18, A.mult)
+    iota(B("pidx", 0, 2), [[0, 2]], 0, 1, False)
+    iota(B("c16", 0, S), [[16, S]], 0, 0)
+    iota(B("cb", 0, 128), [[0, 8], [1, 16]], 0, 0)
+    iota(B("ca", 0, 128), [[1, 8], [0, 16]], 0, 0)
+    iota(B("cj"), [[0, 8], [-2, S]], 32, 0)
+    iota(B("cz", 0, 144), [[1, 144]], -15, 0)
+    iota(B("c32", 0, 8), [[32, 8]], 2048, 0)
+    iota(B("cn", 0, 16), [[-1, 16]], 16, 0)
+
+    fill((T.mx[:, :, 0:16], [("mx", 0, 24 * E)]), 0.0)
+    ts(B("p15", 0, 1), B("pidx", 0, 1), 15, A.bitwise_and)
+    ts(B("p4", 0, 1), B("pidx", 0, 1), 4, A.arith_shift_right)
+    fill(B("ones"), 1.0)
+    ts(C(0), B("p15", 0, 1), -8.0, A.add)
+    ts(C(1), B("p15", 0, 1), -16.0, A.mult, 256.0, A.add)
+    cp(C(2), B("p15", 0, 1))
+    cp(C(3), B("p4", 0, 1))
+    ts(B("qi", 0, S), B("c16", 0, S), C(0), A.add, 1.0 / S, A.mult)
+    ts(B("rr", 0, 128), B("cb", 0, 128), C(2), A.is_equal)
+    ts(B("qj", 0, S), B("qi", 0, S), float(S), A.mult, C(1), A.add)
+    ts(B("bo", 0, 128), B("ca", 0, 128), C(3), A.is_equal)
+    ts(B("qi", 0, S), B("qj", 0, S), 255, A.bitwise_and)
+    tt(B("id1"), B("bo", 0, 128), B("rr", 0, 128), A.mult)
+    cp(B("pin", 0, S), B("qi", 0, S))
+
+    def ids(*names):
+        for b in names:
+            ts(B(b), B("id1"), IDS[b], A.mult)
+
+    def turn_in(o, src):
+        cp(o, ind(B(src, 0, 256), B("pin", 0, S)))
 
     def views(t):
-        v = "vx%d" % t
-        act(B(v, 0, 128), B("yvs", t * 128, t * 128 + 128), F.Copy)
-        for w in (128, 256, 512):
-            act(B(v, w, 2 * w), B(v, 0, w), F.Copy)
+        for k in (0, 1):
+            act(X3("vexp", ALL, k, ALL), B("yvs", t * 128, t * 128 + 128), apart=k == 1)
+        act(X3("vexp", ALL, slice(2, 4), ALL), X3("vexp", ALL, slice(0, 2), ALL), apart=True)
+        group([(B("b0", 0, 512), B("z1"), X3("vexp", ALL, ALL, ALL))])
 
-    def lists(t, ysrc):
-        gx, gy = "gx%d" % (t % 2), "gy%d" % (t % 2)
-        ts(B("ey"), B(gy), 2047.0, A.is_equal)
-        cp(B("off", 0, 128), B(gx))
-        psum("b1", 0, [("id37", gx, 0, 0), ("id1", gy, 0, 0)])
-        psum("b1", 128, [("id2047", "ones", 0, 0), ("idn2047", "ey", 0, 0)])
-        tt(B("pp"), B(gx), ysrc, A.mult)
-        ts(B("hb"), B(gx, 8, 136), 64.96875, A.mult, 75738.515625, A.add)
-        ts(B("sh"), B("pp"), 5, A.arith_shift_right)
-        ts(B("ny"), B("hb"), 2047, A.bitwise_and)
-        tt(B("tt_"), B("sh"), B("b1"), A.add)
-        tt(B("b7"), B("ny"), B("b1", 128, 256), A.max)
-        ts(B("nxi"), B("tt_"), 2047, A.bitwise_and)
-        tt(B("qy"), B("b7"), B(gy), A.min)
-        cp(B("nx"), B("nxi"))
-        cp(B("off", 128, 256), B("qy"))
-        cp(B("off", 256, 384), B("nx"))
-        ts(B("ex", 0, 136), B(gx, 0, 136), 2047.0, A.is_equal)
+    def lists_a(t, ysrc):
+        gg = "g%d" % (t % 2)
+        cp(B("offx"), B(gg))
+        ts(B("f8", 0, 2 * L), B(gg, 0, 2 * L), 2047.0, A.not_equal, -8.0, A.mult)
+        tt(B("pp"), B(gg), ysrc, A.mult)
+        psum("b3", 0, [("id1184", gg, 0, ""), ("id32", gg, L, "")])
+        psum("b3", L, [("idbig", "f8", L, ""), ("id4058", "ones", 0, ""), ("id515", "ones", 0, ""), ("id65", gg, 0, "n"),
+                       ("idf", gg, 0, "n")])
+
+    def lists_b(t):
+        gg = "g%d" % (t % 2)
+        tt(X3("qyi"), B("b3", L, 2 * L), B(gg, L, 2 * L), A.max)
+        tt(X3("nxi"), B("b3"), B("pp"), A.add)
+        ts(X3("qyi"), X3("qyi"), 2047, A.bitwise_and)
+        ts(X3("nxi"), X3("nxi"), 5, A.arith_shift_right, 2047, A.bitwise_and)
+        cp(X3("qy"), X3("qyi"))
+        cp(X3("nx", ALL, slice(1, S)), X3("nxi", ALL, slice(1, S)))
+        cp(B("offy"), X3("qy"))
+        cp(B("offn"), X3("nxi"))
+
+    def extra(t):
+        first = terms("b5", L, [("idn8", "pb_", 0, "")] if t else [("id1", "pb_", 0, ""), ("idm", "pb_", 0, "")])
+        pads = ST("b5", L, 2 * L, S)
+        group(first + [(pads, B("zm", 15 - r, 143 - r), ST("yvs", 128 * t + r, 128 * t + 128, 16)) for r in range(16)]
+              + [(pads, B("rr", 0, 128), ST("nm", s, L, S)) for s in range(1, S) if t])
+        scan(B("tex"), B("rs"), B("b5", L, 2 * L), A.mult, A.subtract)
 
     def prepare(t):
-        s = t % 2
-        gx, gy, abx, aby = "gx%d" % s, "gy%d" % s, "abx%d" % s, "aby%d" % s
-        ts(B("ax"), B(abx), 2047.0, A.is_equal)
-        ts(B("ay"), B(aby), 2047.0, A.is_equal)
-        for k, (src, gb) in enumerate((("nx", 0), (gx, 0), (gy, 0))):
-            psum("b2", 128 * k, [("id1", src, 0, 0), ("id1", "jc", 0, 0)])
-        act(B("kn", 0, 384), B("b2", 0, 384), F.Copy, scale=2.0 ** -18)
-        c = [("ib", "cs", 0, 0)] if t else []
-        hx, hy, rot = ("thb", "tha", 1) if t == 1 else ("tha", "thb", 0)
-        psum("b3", 0, [("id32", hx, 0, 0), ("idbig", "ax", 0, 0), ("idbig", "ex", 0, 0), ("idnbig", "ey", 0, 0), ("idbig", "ones", 0, 0)] + c)
-        psum("b3", 128, [("id32", hy, 0, rot), ("idbig", "ay", 0, 0), ("idbig", "ey", 0, 0), ("idnbig", "ex", 8, 0), ("idbig", "ones", 0, 0)] + c)
-        psum("b5", 0, [("id1", abx, 0, 0), ("idm", gx, 0, 0)])
-        psum("b5", 128, [("id1", aby, 128, -1), ("idn2047", "ones", 0, 0)])
-        psum("b5", 256, [("id1", "nx", 0, 0), ("idm", gx, 0, 0)])
-        psum("b5", 384, [("id1", abx, 128, 0), ("idn2047", "ones", 0, 0)])
-        psum("b6", 0, [("id1", aby, 0, 0), ("idm", gy, 0, 0)])
-        psum("b6", 128, [("id1", "qy", 0, 0), ("idn2047", "ones", 0, 0)])
-        psum("b6", 256, [("id2047", "ones", 0, 0), ("idm", gy, 0, 0)])
+        ts(B("an", 0, 2 * L), B("aa%d" % (t % 2), 0, 2 * L), 2047.0, A.is_equal)
+        hx, hy, turn = (L, 0, "n") if t == 1 else (0, L, "")
+        psum("b4", L, [("idbig", "onesp", 0, ""), ("idbig", "an", L, ""), ("id4096", "f8", L, ""), ("idn4096", "f8", 0, "n"),
+                       ("id32f", "th2", hy, turn), ("id32f", "tex", 0, "")])
+        psum("b4", 0, [("idbig", "onesp", 0, ""), ("idbig", "an", 0, ""), ("id4096", "f8", 0, ""), ("idn4096", "f8", L, ""),
+                       ("id32f", "th2", hx, ""), ("id32f", "tex", 0, "")])
 
-    def contract(k):
-        l, lo, hi = CH[k]
-        d, w = "df%d" % k, (hi - lo) * 16
-        for r in range(16):
-            mm(B("b%d" % l, lo, hi), B("lall", 128 * r, 128 * r + 128),
-               (T[d][:, r:w:16], [(d, 0, w)]), r == 0, r == 15)
+    def differences(t):
+        s = t % 2
+        gg, aa, bb = "g%d" % s, "aa%d" % s, "bb%d" % s
+        psum("b4", 2 * L, [("id1", "qy", 0, ""), ("idn2047", "ones", 0, "")])
+        psum("b6", 0, [("id1", aa, 0, ""), ("idm", gg, 0, "")])
+        psum("b6", L, [("id1", bb, 0, ""), ("idn2047", "ones", 0, "")])
+        psum("b6", 2 * L, [("id1", "nx", 0, ""), ("idm", gg, 0, "")])
+        psum("b7", 0, [("id1", bb, L, ""), ("idn2047", "ones", 0, "")])
+        psum("b7", L, [("id1", aa, L, ""), ("idm", gg, L, "")])
+        psum("b7", 2 * L, [("id2047", "ones", 0, ""), ("idm", gg, L, "")])
+        for k, (src, c) in enumerate((("nx", 0), (gg, 0), (gg, L))):
+            psum("b5", L * k, [("id1", src, c, ""), ("id2048", "jc", 0, "")])
+
+    def memory_masks(t):
+        gg = "g%d" % (t % 2)
+        psum("b4", 0, [("id1", gg, 0, ""), ("id4096", "nm", 0, "")])
+        psum("b4", L, [("id1", gg, L, ""), ("id4096", "nm", 0, "")])
+        psum("b4", 2 * L, [("id2047", "ox_", 0, ""), ("id2047", "u", 0, ""), ("id2047", "oy_", 0, "P")])
+        psum("b5", 0, [("id2047", b, 0, "") for b in ("oy_", "ox_", "ty", "ones")] + [("idn2047", "nm", 0, "")])
+
+    def memories(t):
+        old = ["%s%d" % (m, t % 2) for m in ("aa", "bb")]
+        new = ["%s%d" % (m, 1 - t % 2) for m in ("aa", "bb")] if t < 2 else ["wa", "wb"]
+        both = list(zip(old, new, (0, L)))
+        for m, w, o in both:
+            tt(B("ab2", o, o + L), B("b4", 2 * L, 3 * L), B(m), A.max)
+        for m, w, o in both:
+            if t == 1:
+                tt(B(w, 0, L - 1), B("b5", 1, L), B(m, L + 1, 2 * L), A.max)
+            else:
+                tt(B(w, (0, 0, L)[t], (L, L, 2 * L)[t]), B("b5"), B(m, L, 2 * L), A.max)
+        for m, w, o in both:
+            if t == 0:
+                tt(B(w, L + 1, 2 * L), B("b4", o, o + L - 1), B("ab2", o, o + L - 1), A.min)
+            else:
+                tt(B(w, (0, L, 0)[t], (0, 2 * L, L)[t]), B("b4", o, o + L), B("ab2", o, o + L), A.min)
+        for m, w, o in both:
+            if t == 0:
+                tt(ST(w, L + 1, 2 * L, S), ST("b4", o + 16, o + L, S), ST("ab2", o + 16, o + L, S), A.min)
+            if t == 1:
+                tt(ST(w, 16, L, S), ST("b5", 1, L, S), ST(m, L + 1, 2 * L, S), A.max)
+
+    def gather(t, k):
+        l, c0, c1 = GATHERS[k]
+        act(B("xg", E * (8 * l + c0), E * (8 * l + c1)),
+            ind(B("tab%d" % t, 0, 2048), B(("offx", "offy", "offn")[l], S * c0, S * c1)))
+
+    def larger(k):
+        l, c0, c1 = GATHERS[k]
+        for c in range(c0, c1):
+            for q in range(4):
+                a = 16 + 64 * q
+                o = E * (8 * l + c) + a
+                tt((T.mx[:, 8 * l + c, a:a + 64], [("mx", o, o + 64)]), B("xg", o, o + 64), B("b0", 64 * c, 64 * c + 64), A.max)
+
+    def half(l, c0):
+        c = 8 * l + c0
+        o, a = B("b%d" % (l + 1), S * c0, S * c0 + 4 * S), E * c
+        return ([(o, B("zm", 15 - r, 143 - r), (T.xg[:, a + r:a + 4 * E:16], [("xg", a, a + 4 * E)])) for r in range(16)]
+                + [(o, B("z2", 15 - r, 143 - r), (T.mx[:, c:c + 4, r:E:16], [("mx", a, a + 4 * E)])) for r in range(16)])
+
+    def contract(l, c0):
+        group(half(l, c0))
 
     def scatter(tab, lst, val):
         w = B(tab, 0, WT)
-        do("V", [w], [B(lst, 0, 8), B(val)],
+        do("V", [w], [B(lst, 0, 8), B(val, 0, 128)],
            lambda q: q.tensor_copy(out=w[0].indirect(T[lst][:, 0:8]), in_=T[val][:, :]))
 
     ncall = [0]
 
-    def send(dst, dbuf, dsem, sbuf, width, lsem="ls"):
+    def send(dst, dbuf, sbuf, width):
         rid, pid = topo.addr(dst, core)
         before("G", [(sbuf, 0, width)], [])
-        g.remote_dma(out_ap=T[dbuf][:, 0:width], in_ap=T[sbuf][:, 0:width], remote_sem=T.sem[dsem], local_sem=T.sem[lsem],
+        g.remote_dma(out_ap=T[dbuf][:, 0:width], in_ap=T[sbuf][:, 0:width], remote_sem=T.sem[dbuf + "_"], local_sem=T.sem.ls,
                      pid=pid, routing_id=rid, dma_engine_mask=topo.mask(core, dst))
-        if lsem == "ls":
-            ncall[0] += len(topo.engines(core, dst))
+        ncall[0] += len(topo.engines(core, dst))
 
-    NE = {d: len(topo.engines(T.cores[(rank + d) % n], core)) for d in (1, 2, -1, -2)}
     peer = {d: T.cores[(rank + d) % n] for d in (1, 2, -1, -2)}
-    SLOT = {"a1": 1, "a2": 2, "b2": 1, "b0": -1, "c0": -2}
-    for s, d in SLOT.items():
-        landed(s + "v", s + "v_", NE[d])
-        landed(s + "l", s + "l_", NE[d])
-    landed("tab1", "t1", NE[1])
-    landed("tab2", "t2", NE[2])
+    for s, d in {"a1": 1, "a2": 2, "b2": 1, "b0": -1, "c0": -2}.items():
+        for k in "vl":
+            landed(s + k, s + k + "_", len(topo.engines(peer[d], core)))
+    for d in (1, 2):
+        landed("tab%d" % d, "t%d" % d, sum(len(topo.engines(c, core)) for c in carriers((rank + d) % n, T, topo)))
 
-    cp(B("gx0"), X3("gli", EV, ALL))
-    cp(B("gy0"), X3("gli", OD, ALL))
-    cp(B("gx0", 128, 136), B("gx0", 0, 8))
+    def send_table():
+        cs, he = carriers(rank, T, topo), hand_engines(rank, T, topo)
+        w = 2048 // len(cs)
+
+        def tr(dst, mask, sem, dbuf, k, at):
+            return RemoteDMATransfer(dst_ids=[DstId(rid=topo.addr(dst, core)[0], pnc=topo.addr(dst, core)[1])], dma_engine_mask=mask,
+                                     remote_sem=T.sem[sem], src=T.tab0[:, k * w:k * w + w], dst=T[dbuf][:, at:at + w])
+        before("G", [("tab0", 0, 2048)], [])
+        hands = [tr(cs[k], he[k - 1][0], "hd", "hand", k, 0) for k in range(1, len(cs))]
+        g.remote_dma_fused(hands[:2] + [tr(peer[-1], topo.mask(core, peer[-1]), "t1", "tab1", 0, 0)], local_sem=T.sem.tl)
+        g.remote_dma_fused(hands[2:] + [tr(peer[-2], topo.mask(core, peer[-2]), "t2", "tab2", 0, 0)], local_sem=T.sem.tl)
+        gone = sum(h[1] for h in he) + len(topo.engines(core, peer[-1])) + len(topo.engines(core, peer[-2]))
+        after("D", [("tab0", 0, WT)], [], ("D", "tl", gone, {}))
+
+    def start_of(c):
+        return 146 * c if c < 4 else 162 * (7 - c) + S
+
+    def late_constants():
+        fill(B("w", 0, EQ), 1.0)
+        ts(B("p7", 0, 1), B("pidx", 0, 1), 7, A.bitwise_and)
+        ts(B("p8", 0, 1), B("pidx", 0, 1), 8, A.bitwise_and)
+        ts(B("sp4", 0, 8), B("dum", 0, 8), 4.0, A.mult, -1.0, A.add)
+        ts(C(5), B("p7", 0, 1), float(S), A.mult)
+        ts(C(6), B("p8", 0, 1), float(S), A.mult)
+        for c in range(8):
+            o = start_of(c) + 16 * c
+            ts(B("w", o, o + 16), B("rr", 0, 16), B("sp4", c, c + 1), A.mult, 1.0, A.add)
+        ts(B("pout", 0, 16), B("cn", 0, 16), C(5), A.add, C(6), A.add)
+        fill(ST("w", 0, EQ, 146), 0.0)
+        fill(ST("w", S, EQ, 162), 0.0)
+        fill(B("aa1", L, L + 1), 0.0)
+        fill(B("bb1", L, L + 1), 0.0)
+
+    turn_in(B("g0", 0, 2 * L), "gli")
+    ts(C(4), C(3), 16.0, A.mult)
+    ids("id1184", "id32", "id65", "idf", "id4058", "id515", "idbig")
+    cp(B("z1", 0, 128), B("id1"))
+    ts(B("zm", 0, 144), B("cz", 0, 144), C(4), A.is_equal, -1.0, A.mult)
+    lists_a(0, B("g0", L, 2 * L))
     views(0)
-    lists(0, B("gy0"))
-    late_consts()
-    cp(B("xsav", 0, 1), B("tab0", 2047, 2048))
-    fill(B("tab0", 2047, 2048), FAR)
-    send(peer[-1], "tab1", "t1", "tab0", 2048, "tl")
-    send(peer[-2], "tab2", "t2", "tab0", 2048, "tl")
-    tabtok = ("D", "tl", len(topo.engines(core, peer[-1])) + len(topo.engines(core, peer[-2])), {})
-    after("D", [("tab0", 0, WT)], [], tabtok)
+    send_table()
     iota(B("iw", 0, WT), [[1, WT]], 0, 0)
+    ts(B("z2", 0, 144), B("zm", 0, 144), -2.0, A.mult)
+    ts(B("onesp"), B("cj"), 30.0, A.max, -29.0, A.add)
+    cp(B("jc"), B("cj"))
+    ts(B("dum", 0, 8), B("c32", 0, 8), C(2), A.add, C(2), A.add)
+    cp(X3("nx", ALL, 0), B("dum", 0, 8))
+    lists_b(0)
+    ts(B("pa_"), B("onesp"), -4.0, A.mult, 5.0, A.add)
+    ts(B("pb_"), B("onesp"), 8.0, A.mult, -8.0, A.add)
+    ts(B("rs"), B("onesp"), -0.5, A.mult, 1.5, A.add)
+    ids("idm", "id4096", "idn4096", "idn2047", "id2047", "id2048", "idnbig", "idnmid", "idn8")
+    cp(B("id32f", 0, 128), B("id1"))
 
     def visit(t):
         s = t % 2
-        gx, gy, abx, aby = "gx%d" % s, "gy%d" % s, "abx%d" % s, "aby%d" % s
-        tab = "tab%d" % t
-        for k in range(7):
-            l, lo, hi = CH[k]
-            w = (hi - lo) * 16
-            d = "df%d" % k
-            tt(B(d, 0, w), ind(B(tab, 0, 2048), B("off", l * 128 + lo, l * 128 + hi)), B("vx%d" % t, 0, w), A.subtract)
-            if k == 3 and t == 0:
-                cp(B("abx0", 0, 128), X3("ali", EV, ALL))
-                cp(B("aby0", 0, 128), X3("ali", OD, ALL))
-                cp(B("abx0", 128, 256), X3("bli", EV, ALL))
-                cp(B("aby0", 128, 256), X3("bli", OD, ALL))
-                cp(B("tha"), X3("thi", EV, ALL))
-                cp(B("thb"), X3("thi", OD, ALL))
-            act(B(d, 0, w), B(d, 0, w), F.Abs)
-            if k == 3:
-                act(B("sgx", 0, 128), B("b0"), F.Copy)
-                act(B("sgx", 128, 136), B("b0", 0, 8), F.Copy)
-                contract(3)
-                if t == 0:
-                    prepare(0)
-            elif k == 5:
-                act(B("sqy"), B("b1"), F.Copy)
-                contract(5)
-            elif k < 6:
-                contract(k)
-        tt(B("oyp", 8, 136), B("sqy"), B("b3", 128, 256), A.is_gt)
-        tt(B("oxf"), B("sgx"), B("b3"), A.is_gt)
-        psum("b4", 0, [("idbig", "ex", 0, 0), ("idbig", "ey", 0, 0), ("idbig", "oyp", 8, 0)])
-        tt(B("mn"), B("b1"), B("sgx"), A.min)
-        cp(B("oyp", 0, 8), B("oyp", 128, 136))
+        gg, tab = "g%d" % s, "tab%d" % t
+        for k in range(len(GATHERS)):
+            gather(t, k)
+        if t:
+            memories(t - 1)
+            extra(t)
+        else:
+            extra(0)
+            turn_in(B("aa0", 0, 2 * L), "ali")
+        larger(0)
+        contract(0, 0)
+        if t == 0:
+            turn_in(B("bb0", 0, 2 * L), "bli")
+            turn_in(B("th2", 0, 2 * L), "thi")
+        prepare(t)
+        larger(1)
+        contract(0, 4)
+        differences(t)
+        if t == 0:
+            late_constants()
         if t == 1:
             scatter("tab0", "lw0", "val0")
-            scatter("tab2", "a2l", "a2v")
         if t == 2:
             scatter("tab0", "b0l", "b0v")
-            cp(B("tab0", 2047, 2048), B("xsav", 0, 1))
-        contract(6)
-        tt(B("mnm"), B("mn"), B("b4"), A.subtract)
-        tt(B("b7"), B("b2"), B("mnm"), A.is_ge)
-        tt(B("mm"), B("b2"), B("mnm"), A.is_lt)
+        larger(2)
+        contract(1, 0)
+        cp(B("sgx"), B("b1"))
+        if t == 1:
+            scatter("tab2", "a2l", "a2v")
+        if t == 2:
+            cp(B("tab0", NONE, NONE + 1), B("xsav", 1, 2))
+        tt(B("ox_"), B("sgx"), B("b4"), A.is_gt)
+        larger(3)
+        contract(1, 4)
+        cp(ST("sgx", 0, L, S), ST("b1", 16, L, S))
+        tt(B("p1"), B("b6"), B("ox_"), A.mult)
+        tt(B("p5"), B("b6", L, 2 * L), B("ox_"), A.mult)
+        psum("b1", 2 * L, [("idnbig", "onesp", 0, ""), ("id4096", "f8", L, ""), ("idnbig", "ox_", 0, ""), ("idn4096", "f8", 0, "n"),
+                           ("id32f", "sgx", 0, "n")])
+        cp(B("sqy"), B("b2"))
+        tt(B("oy_"), B("sqy"), B("b4", L, 2 * L), A.is_gt)
+        larger(4)
+        mask = terms("b3", 0, [("idbig", "pa_", 0, ""), ("id4096", "f8", L, ""), ("idbig", "oy_", 0, "P")])
+        psum("b1", 0, [("id32f", "sgx", 0, ""), ("idnbig", "pb_", 0, ""), ("idnmid", "oy_", 0, "")])
+        psum("b1", L, [("id32f", "sgx", 0, ""), ("idn4096", "f8", 0, ""), ("idnbig", "ones", 0, ""), ("idnmid", "oy_", 0, "")])
+        tt(B("ty"), B("sqy"), B("b1", 2 * L, 3 * L), A.is_lt)
+        tt(B("p2"), B("b7"), B("oy_"), A.mult)
+        tt(B("p4_"), B("b7", L, 2 * L), B("oy_"), A.mult)
+        larger(5)
+        tt(B("mnm"), B("b1", L, 2 * L), B("sqy"), A.min)
+        tt(B("mnu"), B("b1"), B("sqy"), A.min)
+        tt(B("p7_"), B("b4", 2 * L, 3 * L), B("ty"), A.mult)
+        larger(6)
+        group(mask + half(2, 0) + half(2, 4))
+        tt(B("nm"), B("b3"), B("mnm"), A.is_ge)
+        tt(B("u"), B("b3"), B("mnu"), A.is_lt)
         for k in range(3):
-            tt(X3("k0", k, ALL), B("b7"), B("kn", 128 * k, 128 * k + 128), A.add)
-        for a, b, w in (("k0", "k1", 64), ("k1", "k2", 32), ("k2", "k3", 16), ("k3", "k4", 8)):
-            tt(X3(b, ALL, ALL), X3(a, ALL, slice(0, w)), X3(a, ALL, slice(w, 2 * w)), A.min)
-        tt(X3("k5", ALL, ALL), X3("k4", ALL, ALL), X3("fb", ALL, ALL), A.min)
-        ts(B("ki", 0, 24), X3("k5", ALL, ALL), 2.0 ** 18, A.mult)
+            scan(B("s3", L * k, L * k + L), B("nm"), B("b5", L * k, L * k + L), A.mult, A.max)
+        cp(B("ki", 0, 24), ST("s3", 16, 3 * L, S))
+        tt(B("q6"), B("b7", 2 * L, 3 * L), B("nm"), A.mult)
         ts(B("gi", 0, 24), B("ki", 0, 24), 4095, A.bitwise_and)
+        tt(B("pu"), B("b6", 2 * L, 3 * L), B("u"), A.mult)
         cp(B("goff", 0, 24), B("gi", 0, 24))
         cp(B("gf", 0, 8), B("gi", 0, 8))
-        act(B("xv", 0, 256), ind(B(tab, 0, 2048), B("goff", 8, 24)), F.Copy, scale=0.5, bias=-0.125)
-        cp(B("bf"), ind(B("iw", 0, WT), B("goff", 0, 8)))
-        tt(B("bd"), B("bf"), B("maskd"), A.max)
-        for c in range(1, 8):
-            ts(B("eq", 128 * c, 128 * c + 16 * c), B("bf", 0, 16 * c), B("gf", c, c + 1), A.is_equal)
-        val, lw = "val%d" % t, "lw%d" % t
-        tt(B("vi"), B("xv", 0, 128), B("xv", 128, 256), A.add)
-        for c in range(8):
-            ts(B("eq", 144 * c, 144 * c + 16), B("bd", 16 * c, 16 * c + 16), B("gf", c, c + 1), A.is_equal)
-        cp(B(val), B("vi"))
-        e, z, r = B("eq", 0, 1024), B("sc", 0, 1024), B("rst", 0, 1024)
-        do("V", [z], [e, r], lambda q: q.tensor_tensor_scan(out=z[0], data0=r[0], data1=e[0], initial=0.0, op0=A.mult, op1=A.max))
-        tt(B("lm", 0, 8), ST("sc", 127, 1024, 128), B("dum", 0, 8), A.mult)
-        tt(B("lf", 0, 8), B("lm", 0, 8), B("gf", 0, 8), A.max)
-        cp(B(lw, 0, 8), B("lf", 0, 8))
-        for slot, d in ((("a1", -1), ("a2", -2)), (("b2", -1), ("b0", 1)), (("c0", 2),))[t]:
-            send(peer[d], slot + "v", slot + "v_", val, 128)
-            send(peer[d], slot + "l", slot + "l_", lw, 8)
-        psum("b4", 128, [("idbig", "ey", 0, 0), ("idbig", "ones", 0, 0), ("idnbig", "ex", 0, 0), ("idbig", "oyp", 0, 0)])
-        psum("b4", 256, [("idbig", "ones", 0, 0), ("idnbig", "ey", 0, 0), ("idbig", "oxf", 0, 0), ("idbig", "ex", 8, 0)])
-        tt(B("mt"), B("sqy"), B("b4", 128, 256), A.subtract)
-        tt(B("b7", 128, 256), B("sgx", 8, 136), B("b4", 256, 384), A.subtract)
-        tt(B("tx"), B("b2"), B("mt"), A.is_lt)
-        tt(B("ty"), B("sqy"), B("b7", 128, 256), A.is_lt)
-        tt(B("p1"), B("b5"), B("oxf"), A.mult)
-        tt(B("p2"), B("b5", 128, 256), B("oyp", 0, 128), A.mult)
-        tt(B("p3"), B("b5", 256, 384), B("mm"), A.mult)
-        tt(B("p4_"), B("b6"), B("oyp", 8, 136), A.mult)
-        tt(B("p5"), B("b5", 384, 512), B("oxf"), A.mult)
-        tt(B("p6"), B("b6", 256, 384), B("mm"), A.mult)
-        tt(B("p7"), B("b6", 128, 256), B("ty"), A.mult)
-        tt(B("p8"), B("b5", 256, 384), B("tx"), A.mult)
-        ry, rx = ((0, 1), (-1, 0), (0, 0))[t]
-        ny = [("id1", b, 0, ry) for b in (gy, "p4_", "p5", "p6", "p7")]
-        nx = [("id1", b, 0, rx) for b in (gx, "p1", "p2", "p3", "p8")]
-        psum("b0", 0, ny)
-        psum("b0", 128, nx)
-        psum("b3", 0, [("id2047", "oxf", 0, 0), ("id2047", "oyp", 0, 0), ("id2047", "tx", 0, 0), ("id2047", "mm", 0, 0)])
-        psum("b3", 128, [("id2047", "ones", 0, 0), ("idn2047", "mm", 0, 0)])
-        psum("b3", 256, [("id2047", "oyp", 8, 0), ("id2047", "oxf", 0, 0), ("id2047", "ty", 0, 0), ("id2047", "mm", 0, 0)])
+        ty_, tx_ = (("0", "N"), ("P", ""), ("", ""))[t]
+        psum("b2", 0, [("id2047", "ones", 0, "")] + [("id1", b, 0, ty_) for b in ("p4_", "p5", "p7_")] + [("idm", "q6", 0, ty_)])
+        psum("b1", 0, [("id1", "p2", 0, "")] * (t == 0) + [("id1", gg, 0, tx_.lower())] + [("id1", "p2", 0, "P")] * (t > 0)
+             + [("id1", b, 0, tx_) for b in ("p1", "pu")])
+        act(B("xv", 0, 256), ind(B(tab, 0, 2048), B("goff", 8, 24)), scale=0.5, bias=-0.125)
         if t < 2:
-            u = 1 - s
-            hx, hy = "gx%d" % u, "gy%d" % u
-            cp(B(hx), B("b0"))
-            cp(B(hy), B("b0", 128, 256))
-            cp(B(hx, 128, 136), B(hx, 0, 8))
-            lists(t + 1, B("b0", 128, 256))
-            cp(B("mm", 128, 256), B("mm"))
-            for k in range(16):
-                mm(B("b2", 384, 512), B("rr"), B("mm", 8 * k, 8 * k + 128), k == 0, k == 15)
-            act(B("cs"), B("b2", 384, 512), F.Copy)
             views(t + 1)
-        else:
-            act(X3("ogs", OD, ALL), B("b0"), F.Copy)
-            act(X3("ogs", EV, ALL), B("b0", 128, 256), F.Copy)
-            before("Y", [("ogs", 0, 9)], [])
-            g.sync.dma_start(out=T.og[:, :], in_=T.ogs[:, :, :]).then_inc(T.sem.og_, 16)
-        tt(B("b7", 256, 384), B("b3", 128, 256), B(gx), A.max)
-        tt(B("b7", 384, 512), B("b3", 128, 256), B(gy), A.max)
-        tt(B("ab2", 0, 128), B("b3"), B(abx), A.max)
-        tt(B("ab2", 128, 256), B("b3"), B(abx, 128, 256), A.max)
+        cp(B("bf", 0, 128), ind(B("iw", 0, WT), B("goff", 0, 8)))
+        cp(ST("eq", 16, 503, 162), B("gi", 0, 4))
+        cp(ST("eq", 583, 144, -146), B("gi", 4, 8), apart=True)
+        for c in range(8):
+            o = start_of(c)
+            ts(B("eq", o, o + 16 * c + 16), B("bf", 0, 16 * c + 16), B("gf", c, c + 1), A.is_equal, 0.25, A.mult, apart=True)
+        val, lw = "val%d" % t, "lw%d" % t
+        tt(B(val, 0, 128), B("xv", 0, 128), B("xv", 128, 256), A.add)
+        scan(B("sc", 0, EQ), B("w", 0, EQ), B("eq", 0, EQ), A.mult, A.max)
+        hh = "g%d" % (1 - s)
         if t < 2:
-            nax, nay = "abx%d" % u, "aby%d" % u
-            for o in (0, 128):
-                for a, b in ((0, 120), (120, 128)) if t == 0 else ((0, 128),):
-                    d = (a - 8 * rx) % U
-                    d, a2, b2 = (o + a, o + (a + 8) % U, 0) if t == 0 else (o, o, 0)
-                    w = b - a
-                    tt(B(nay, d, d + w), B("b7", 256 + a2, 256 + a2 + w), B("ab2", a2, a2 + w), A.min)
-                for a, b in ((0, 8), (8, 128)) if t == 1 else ((0, 128),):
-                    w = b - a
-                    sr = (a - 8) % U if t == 1 else a
-                    tt(B(nax, o + a, o + b), B("b3", 256 + sr, 256 + sr + w), B(aby, o + sr, o + sr + w), A.max)
-            prepare(t + 1)
+            cp(B(hh), B("b2"))
+        cp(B(lw, 0, 4), ST("sc", 16, 503, 162))
+        cp(B(lw, 4, 8), ST("sc", 583, 144, -146))
+        slots = ((("a1", -1), ("a2", -2)), (("b2", -1), ("b0", 1)), (("c0", 2),))[t]
+        for slot, d in slots:
+            send(peer[d], slot + "v", val, 128)
+            send(peer[d], slot + "l", lw, 8)
+        if t < 2:
+            cp(B(hh, L, 2 * L), B("b1"))
+            lists_a(t + 1, B("b1"))
+            memory_masks(t)
+            lists_b(t + 1)
+            scatter("tab%d" % (t + 1), slots[0][0] + "l", slots[0][0] + "v")
         else:
-            for o, b, q, sm in ((0, "oas", T.oa, "oa_"), (128, "obs", T.ob, "ob_")):
-                tt(X3(b, EV, ALL), B("b7", 256 + o, 384 + o), B("ab2", o, o + 128), A.min)
-                tt(X3(b, OD, ALL), B("b3", 256, 384), B(aby, o, o + 128), A.max)
-                before("Y", [(b, 0, 9)], [])
-                g.sync.dma_start(out=q[:, :], in_=T[b][:, :, :]).then_inc(T.sem[sm], 16)
+            memory_masks(t)
+            act(B("wg"), B("b1"))
+            act(B("wg", L, 2 * L), B("b2"))
+            memories(t)
+            scatter("tab0", "c0l", "c0v")
+            before("Y", [("tab0", 0, 2048)], [])
+            g.sync.dma_start(out=T.ox[:, :], in_=T.tab0[:, 0:2048]).then_inc(T.sem.sox, 16)
+            for w, b, q, sm in (("wg", "ogs", T.og, "sog"), ("wa", "oas", T.oa, "soa"), ("wb", "obs", T.ob, "sob")):
+                act(B(b, 0, 256), ind(B(w, 0, 2 * L), B("pout", 0, 16)))
+                before("S", [(b, 0, 256)], [])
+                g.scalar.dma_start(out=q[:, :], in_=T[b][:, :]).then_inc(T.sem[sm], 16)
 
-    visit(0)
-    scatter("tab1", "a1l", "a1v")
-    visit(1)
-    scatter("tab2", "b2l", "b2v")
-    visit(2)
-    scatter("tab0", "c0l", "c0v")
-    before("Y", [("tab0", 0, 2048)], [])
-    g.sync.dma_start(out=T.ox[:, :], in_=T.tab0[:, 0:2048]).then_inc(T.sem.ox_, 16)
-    for sm in ("og_", "oa_", "ob_", "ox_"):
+    for t in range(3):
+        visit(t)
+    for sm in ("sog", "soa", "sob", "sox"):
         g.sync.wait_ge(T.sem[sm], 16)
     for e in ("V", "S", "P", "G"):
         g.wait_ge(T.sem[PS[e]], cnt[e])

@@ -1,3 +1,4 @@
+import numpy as np
 from concourse.bass import DstId, RemoteDMATransfer
 from concourse.mybir import AluOpType as A
 from concourse.mybir import ActivationFunctionType as F
@@ -11,10 +12,12 @@ BIG = 32768.0
 MID = 6144.0
 FAR = 1024.0
 EQ = 584
-GATHERS = [(0, 0, 4), (0, 4, 8), (1, 0, 4), (1, 4, 8), (2, 0, 4), (2, 4, 6), (2, 6, 8)]
+GATHERS = [("V", 0, 0, 34), ("V", 0, 34, 68), ("S", 0, 68, 136), ("S", 1, 0, 68), ("S", 1, 68, 136), ("S", 2, 0, 68),
+           ("S", 2, 68, 102), ("S", 2, 102, 128), ("S", 2, 128, 136)]
 IDS = {"id1": 1.0, "id1184": 1184.0, "id32": 32.0, "id65": 65.0, "idf": -1.0 / 32, "id4058": 4058.0, "id515": 33.0 / 64,
        "idbig": BIG, "idm": -1.0, "idnbig": -BIG, "id4096": 4096.0, "idn4096": -4096.0, "idnmid": -MID, "id2047": 2047.0,
-       "idn2047": -2047.0, "id2048": 2048.0, "idn8": -8.0}
+       "id2048": 2048.0, "idn2047": -2047.0, "idq": -0.25}
+CYC, PCYC, WAKE, ISSUE, WAY, LOAD, COPY, STORE = 0.00083, 0.00045, 0.15, 0.3, 2.0, 4.5, 8.0, 3.0
 
 SCRATCH = {}
 
@@ -25,30 +28,40 @@ def _add(where, dtype, **kw):
 
 
 _add("sbuf", "bfloat16", tab0=WT, tab1=WT, tab2=WT, hand=512, xsav=16, yvs=384, vexp=[8, 4, 16], z1=128, z2=144, zm=144,
-     xg=24 * E)
-_add("sbuf", "bfloat16", mx=[24, E])
-_add("sbuf", "int32", gli=256, ali=256, bli=256, thi=256, pidx=8, p15=8, p4=8, p7=8, p8=8, qi=24, qj=24,
-     nxi=[8, S], qyi=[8, S], ki=24, gi=24, val0=128, val1=128, val2=128, a1v=128, a2v=128, b2v=128, b0v=128, c0v=128)
-_add("sbuf", "uint16", offx=L, offy=L, offn=L, goff=24, pin=24, pout=16,
-     lw0=8, lw1=8, lw2=8, a1l=8, a2l=8, b2l=8, b0l=8, c0l=8)
+     zh=128, xv=256, xg=24 * E, mx=[24, E])
+_add("sbuf", "int32", gli=256, ali=256, bli=256, thi=256, pidx=8, p15=8, p4=8, p7=8, p8=8, qi=24, qj=24, qk=24,
+     nxi=[8, S], nxj=[8, S], qyi=[8, S], qyj=[8, S], gi=24, s3=3 * L)
+_add("sbuf", "uint16", offx=L, offy=L, offn=L, goff=24, pin=24, pout=16, m0=L, m1=L, m2=L, a1=L, a2=L, e2=L, e0=L, c0=L)
 _add("sbuf", "float16", g0=2 * L, g1=2 * L, aa0=2 * L, aa1=2 * L, bb0=2 * L, bb1=2 * L, ab2=2 * L, f8=2 * L, an=2 * L,
-     qy=[8, S], nx=[8, S], rr=128, bo=128, ids=128 * len(IDS), ones=L, onesp=L, pa_=L, pb_=L, rs=L, jc=L,
-     ox_=L, oy_=L, ty=L, nm=L, u=L, p1=L, p2=L, p4_=L, p5=L, p7_=L, pu=L, q6=L, bf=128, eq=EQ, w=EQ, sc=EQ)
+     qy=[8, S], nx=[8, S], rr=128, bo=128, ids=128 * len(IDS), ones=L, onesp=L, pa_=L, pb_=L, jc=L,
+     ox_=L, oy_=L, ty=L, nm=L, u=L, rl=8 * L, bf=128, eq=EQ, w=EQ, sc=EQ)
 _add("sbuf", "float32", th2=2 * L, id32f=128, ca=128, cb=128, cz=144, cj=L, c16=24, c32=8, cn=16, col=16,
-     dum=8, sp4=8, iw=WT, sgx=L, sqy=L, mnu=L, mnm=L, tex=L, pp=L, s3=3 * L, gf=8, xv=256,
+     dum=8, sp4=8, iw=WT, sgx=L, sqy=L, mnu=L, mnm=L, tex=8, svn=24, tha=[16, S], thb=[16, S], tht=[16, S], pp=L, gf=8,
      wg=2 * L, wa=2 * L, wb=2 * L, ogs=256, oas=256, obs=256)
 _add("psum", "float32", **{"b%d" % k: 512 for k in range(8)})
 SEMAPHORES = ["pv", "pa", "pt", "pg", "dg", "dy", "dx", "ds", "da", "db", "dt", "sog", "soa", "sob", "sox", "tl", "ls", "hd",
-              "t1", "t2"] + [s + k + "_" for s in ("a1", "a2", "b2", "b0", "c0") for k in "vl"]
+              "t1", "t2"] + [s + "_" for s in ("a1", "a2", "e2", "e0", "c0")]
 PART = {k: ("ids", 128 * j) for j, k in enumerate(IDS)}
-PART.update(id32f=("id32f", 0), z1=("z1", 0))
-BANKS = ["b%d" % k for k in range(8)]
+PART.update(id32f=("id32f", 0), z1=("z1", 0), zh=("zh", 0))
+COLS = {k: np.arange(int(np.prod(v[1][1:]))).reshape(v[1][1:]) for k, v in SCRATCH.items()}
+WIDE = {k: v[2] in ("float32", "int32") for k, v in SCRATCH.items()}
+COUNTER = {"V": "pv", "S": "pa", "P": "pt", "G": "pg"}
+ROUNDS = 4
+ORDER = []
 
 
 def carriers(rank, T, topo):
     n, own = len(T.cores), T.cores[rank]
     to = [T.cores[(rank - d) % n] for d in (1, 2)]
     return [own] + [c for c in topo.cores_of(own) if c != own and all(topo.may_write(c, d) for d in to)]
+
+
+def hand_engines(rank, T, topo):
+    own = T.cores[rank]
+    out = topo.engines(own, T.cores[(rank - 1) % len(T.cores)])
+    e = [x for x in topo.engines(own, carriers(rank, T, topo)[1]) if x not in out]
+    h = len(e) // 2
+    return [(sum(1 << x for x in p), len(p)) for p in (e[:h], e[h:], e)]
 
 
 def helper_program(g, core, T, topo):
@@ -68,12 +81,48 @@ def helper_program(g, core, T, topo):
             g.wait_ge(T.sem.ls, sent)
 
 
-def hand_engines(rank, T, topo):
-    own = T.cores[rank]
-    out = topo.engines(own, T.cores[(rank - 1) % len(T.cores)])
-    e = [x for x in topo.engines(own, carriers(rank, T, topo)[1]) if x not in out]
-    h = len(e) // 2
-    return [(sum(1 << x for x in p), len(p)) for p in (e[:h], e[h:], e)]
+def issue_order(ops):
+    lag = [{d: ops[d]["tail"] + (0.0 if ops[d]["e"] == o["e"] == "P" or o["e"] == "D" else WAKE) for d in o["deps"]} for o in ops]
+    back = [{} for _ in ops]
+    for k, l in enumerate(lag):
+        for d, x in l.items():
+            back[d][k] = x
+
+    def place(before, after, key, first):
+        left, at, start = [len(b) for b in before], list(first), [0.0] * len(ops)
+        busy = {e: [] for e in "VSPGY"}
+        ready = sorted((key[k], k) for k in range(len(ops)) if not left[k])
+        while ready:
+            k = ready.pop(0)[1]
+            t0, c = at[k], ops[k]["cost"]
+            if ops[k]["e"] != "D":
+                q = busy[ops[k]["e"]]
+                i = len(q)
+                while i and q[i - 1][1] > t0:
+                    i -= 1
+                while i < len(q) and q[i][0] < t0 + c - 1e-9:
+                    t0 = max(t0, q[i][1])
+                    i += 1
+                q.insert(i, (t0, t0 + c))
+            start[k] = t0
+            for x, l in after[k].items():
+                at[x] = max(at[x], t0 + c + l)
+                left[x] -= 1
+                if not left[x]:
+                    ready.append((key[x], x))
+            ready.sort()
+        return start
+
+    tails = [o["tail"] for o in ops]
+    key, best = [-k for k in range(len(ops))], None
+    for _ in range(ROUNDS):
+        rev = place(back, lag, key, tails)
+        fwd = place(lag, back, [-rev[k] - ops[k]["cost"] for k in range(len(ops))], [0.0] * len(ops))
+        end = max(fwd[k] + ops[k]["cost"] + tails[k] for k in range(len(ops)))
+        if best is None or end < best[0]:
+            best = (end, fwd)
+        key = [-fwd[k] - ops[k]["cost"] for k in range(len(ops))]
+    return sorted(range(len(ops)), key=lambda k: (best[1][k], k))
 
 
 def rank_program(g, core, T, topo):
@@ -83,120 +132,137 @@ def rank_program(g, core, T, topo):
         return
     n = len(T.cores)
     Q = {"V": g.vector, "S": g.scalar, "P": g.tensor, "G": g, "Y": g.sync}
-    PS = {"V": "pv", "S": "pa", "P": "pt", "G": "pg"}
-    cnt = {"V": 0, "S": 0, "P": 0, "G": 0}
-    known = {e: {} for e in Q}
-    wr, rd, bank = {}, {}, {}
 
-    def wait(e, toks):
-        for eng, sem, val, snap in toks:
-            if known[e].get(sem, 0) >= val:
+    ops, writer, readers, bank = [], {}, {}, {}
+
+    def note(e, outs, ins, call, cost, tail=0.0, sem=None, deps=()):
+        k, deps = len(ops), set(deps)
+        for ap, parts in ins:
+            for b, cols in parts:
+                deps.update(np.unique(writer[b][cols]).tolist() if b in writer else [])
+        for ap, parts in outs:
+            for b, cols in parts:
+                w = writer.setdefault(b, np.full(COLS[b].size, -1))
+                deps.update(np.unique(w[cols]).tolist())
+                for r, m in list(readers.get(b, {}).items()):
+                    if m[cols].any():
+                        deps.add(r)
+                        m[cols] = False
+                        if not m.any():
+                            del readers[b][r]
+                w[cols] = k
+        for ap, parts in ins:
+            for b, cols in parts:
+                if b not in ("ids", "zm", "z2"):
+                    readers.setdefault(b, {}).setdefault(k, np.zeros(COLS[b].size, bool))[cols] = True
+        for b in {b for ap, parts in list(ins) + list(outs) for b, cols in parts if SCRATCH[b][0] == "psum"}:
+            rec = bank.setdefault(b, [e, [], []])
+            if rec[0] != e:
+                rec[:] = [e, [], rec[1]]
+            deps.update(rec[2] + (rec[1][-1:] if e == "P" else []))
+            rec[1].append(k)
+        ops.append({"e": e, "deps": sorted(deps - {-1, k}), "call": call, "cost": cost, "tail": tail, "sem": sem})
+        return k
+
+    def issue():
+        if not ORDER:
+            ORDER.extend(issue_order(ops))
+        cnt, known, token = {e: 0 for e in COUNTER}, {e: {} for e in Q}, {}
+        for k in ORDER:
+            o = ops[k]
+            e = o["e"]
+            if e == "D":
+                token[k] = o["sem"] + ({},)
                 continue
-            Q[e].wait_ge(T.sem[sem], val)
-            for s, v in snap.items():
-                if known[e].get(s, 0) < v:
-                    known[e][s] = v
-            known[e][sem] = val
-
-    def hit(recs, lo, hi):
-        return [r[2] for r in recs if r[0] < hi and lo < r[1]]
-
-    def before(e, reads, writes):
-        toks = []
-        for b, lo, hi in reads:
-            toks += hit(wr.get(b, []), lo, hi)
-        for b, lo, hi in writes:
-            toks += [t for t in hit(wr.get(b, []), lo, hi) if not (e == "P" and t[0] == "P")]
-            toks += hit(rd.get(b, []), lo, hi)
-        for b, lo, hi in reads + writes:
-            if b in bank:
-                toks += [t for f, t in bank[b].items() if f != e]
-        toks.sort(key=lambda t: -t[2])
-        wait(e, toks)
-
-    def after(e, reads, writes, tok, whole=True):
-        for b, lo, hi in writes:
-            if whole:
-                wr[b] = [r for r in wr.get(b, []) if not (lo <= r[0] and r[1] <= hi)]
-                rd[b] = [r for r in rd.get(b, []) if not (lo <= r[0] and r[1] <= hi)]
-            wr[b] = wr.get(b, []) + [(lo, hi, tok)]
-        for b, lo, hi in reads:
-            rd[b] = [r for r in rd.get(b, []) if not (lo <= r[0] and r[1] <= hi and r[2][0] == e)] + [(lo, hi, tok)]
-        for b, lo, hi in reads + writes:
-            if b in BANKS:
-                bank.setdefault(b, {})[e] = tok
-
-    def landed(b, sem, val, lo=0, hi=10 ** 6):
-        after("D", [], [(b, lo, hi)], ("D", sem, val, {}))
-
-    def do(e, outs, ins, call, apart=False):
-        reads = [r for v in ins for r in v[1]]
-        writes = [r for v in outs for r in v[1]]
-        before(e, reads, [] if apart else writes)
-        i = call(Q[e])
-        cnt[e] += 1
-        i.then_inc(T.sem[PS[e]], 1)
-        after(e, reads, writes, (e, PS[e], cnt[e], dict(known[e])), not apart)
+            toks = [token[d] for d in o["deps"] if d in token and not ops[d]["e"] == e == "P"]
+            for sem, val, snap in sorted(toks, key=lambda x: -x[1]):
+                if known[e].get(sem, 0) < val:
+                    Q[e].wait_ge(T.sem[sem], val)
+                    for s, v in list(snap.items()) + [(sem, val)]:
+                        known[e][s] = max(known[e].get(s, 0), v)
+            i = o["call"](Q[e])
+            if o["sem"]:
+                i.then_inc(T.sem[o["sem"][0]], 16)
+                token[k] = o["sem"] + (dict(known[e]),)
+            elif i is not None:
+                cnt[e] += 1
+                i.then_inc(T.sem[COUNTER[e]], 1)
+                token[k] = (COUNTER[e], cnt[e], dict(known[e]))
+        return cnt
 
     ALL = slice(None)
+
+    def X(b, *ix):
+        ix = ix or (ALL,) * COLS[b].ndim
+        return (T[b][(ALL,) + ix], [(b, COLS[b][ix].reshape(-1))])
 
     def B(b, lo=0, hi=L):
         if b in PART:
             b, o = PART[b]
             lo, hi = o, o + 128
-        return (T[b][:, lo:hi], [(b, lo, hi)])
-
-    def X3(b, *ix):
-        return (T[b][(ALL,) + (ix or (ALL, ALL))], [(b, 0, 10 ** 6)])
+        return X(b, slice(lo, hi))
 
     def ST(b, lo, hi, step):
-        return (T[b][:, lo:hi:step], [(b, min(lo, hi), max(lo, hi) + 1)])
-
-    def SEG(b, c0, c1, *ix):
-        return (T[b][(ALL, slice(c0, c1)) + ix], [(b, c0, c1)])
+        return X(b, slice(lo, hi, step))
 
     def ind(w, o):
         return (w[0].indirect(o[0]), w[1] + o[1])
 
-    def tt(o, a, b, op, apart=False):
-        do("V", [o], [a, b], lambda q: q.tensor_tensor(out=o[0], in0=a[0], in1=b[0], op=op), apart)
+    def cycles(o, ins, two=False):
+        k = len(o[1][0][1])
+        if len(ins[0][1]) > 1:
+            return 60 + 1.56 * k
+        if two:
+            return max(64, k * (1 if any(SCRATCH[v[1][0][0]][0] == "psum" for v in ins) else 2))
+        return max(64, k * (1 if any(WIDE[v[1][0][0]] for v in [o] + ins) else 0.5))
 
-    def ts(o, a, s1, op0, s2=None, op1=None, apart=False):
+    def tt(o, a, b, op):
+        note("V", [o], [a, b], lambda q: q.tensor_tensor(out=o[0], in0=a[0], in1=b[0], op=op), CYC * cycles(o, [a, b], True))
+
+    def ts(o, a, s1, op0, s2=None, op1=None):
         cols = [s for s in (s1, s2) if isinstance(s, tuple)]
         x, y = [s[0] if isinstance(s, tuple) else s for s in (s1, s2)]
-        if op1 is None:
-            do("V", [o], [a] + cols, lambda q: q.tensor_scalar(out=o[0], in0=a[0], scalar1=x, scalar2=None, op0=op0), apart)
-        else:
-            do("V", [o], [a] + cols, lambda q: q.tensor_scalar(out=o[0], in0=a[0], scalar1=x, scalar2=y, op0=op0, op1=op1), apart)
+        more = {} if op1 is None else {"op1": op1}
+        note("V", [o], [a] + cols, lambda q: q.tensor_scalar(out=o[0], in0=a[0], scalar1=x, scalar2=y, op0=op0, **more),
+             CYC * cycles(o, [a]))
 
-    def cp(o, a, apart=False):
-        do("V", [o], [a], lambda q: q.tensor_copy(out=o[0], in_=a[0]), apart)
+    def cp(o, a):
+        note("V", [o], [a], lambda q: q.tensor_copy(out=o[0], in_=a[0]), CYC * cycles(o, [a]))
 
-    def fill(o, x, apart=False):
-        do("V", [o], [], lambda q: q.memset(o[0], x), apart)
+    def fill(o, x):
+        note("V", [o], [], lambda q: q.memset(o[0], x), CYC * cycles(o, [o]))
 
     def scan(o, d0, d1, op0, op1):
-        do("V", [o], [d0, d1], lambda q: q.tensor_tensor_scan(out=o[0], data0=d0[0], data1=d1[0], initial=0.0, op0=op0, op1=op1))
+        note("V", [o], [d0, d1], lambda q: q.tensor_tensor_scan(out=o[0], data0=d0[0], data1=d1[0], initial=0.0, op0=op0, op1=op1),
+             CYC * cycles(o, [d0, d1]))
 
-    def act(o, a, scale=1.0, bias=0.0, apart=False):
-        do("S", [o], [a], lambda q: q.activation(out=o[0], in_=a[0], func=F.Copy, bias=bias, scale=scale), apart)
+    def act(o, a, scale=1.0, bias=0.0, func=F.Copy):
+        cols = [s for s in (scale, bias) if isinstance(s, tuple)]
+        x, y = [s[0] if isinstance(s, tuple) else s for s in (scale, bias)]
+        k = len(o[1][0][1])
+        note("S", [o], [a] + cols, lambda q: q.activation(out=o[0], in_=a[0], func=func, bias=y, scale=x),
+             CYC * (80 + 1.56 * k if len(a[1]) > 1 else max(64, k)))
 
-    def group(mats):
+    def matmul(o, l, r, start, stop):
+        note("P", [o], [l, r], lambda q: q.matmul(out=o[0], lhsT=l[0], rhs=r[0], start=start, stop=stop),
+             PCYC * max(64, len(o[1][0][1])) * (4 if WIDE[r[1][0][0]] else 1))
+
+    def group(mats, start=True, stop=True):
         for k, (o, l, r) in enumerate(mats):
-            do("P", [o], [l, r], lambda q: q.matmul(out=o[0], lhsT=l[0], rhs=r[0], start=k == 0, stop=k == len(mats) - 1))
+            matmul(o, l, r, start and k == 0, stop and k == len(mats) - 1)
 
     def terms(bk, lo, ts_):
         out = []
         for l, buf, c, turn in ts_:
             l = B(l)
-            if buf in ("nx", "qy"):
-                out.append((B(bk, lo, lo + L), l, X3(buf)))
+            if COLS[buf].ndim == 2:
+                out.append((B(bk, lo, lo + L), l, X(buf, slice(c, c + 8), ALL)))
                 continue
             if turn in ("", "0"):
                 out.append((B(bk, lo, lo + L), l, B(buf, c, c + L)))
             if turn in ("n", "N"):
                 out.append((B(bk, lo + 1, lo + L), l, B(buf, c, c + L - 1)))
-            if turn in ("p", "P"):
+            if turn == "P":
                 out.append((B(bk, lo, lo + L - 1), l, B(buf, c + 1, c + L)))
             a, b = {"0": (0, 16), "N": (1, 16), "P": (16, 1)}.get(turn, (None, None))
             if a is not None:
@@ -206,30 +272,36 @@ def rank_program(g, core, T, topo):
     def psum(bk, lo, ts_):
         group(terms(bk, lo, ts_))
 
-    def load(q, sem, dst, src):
-        before(q, [], dst[1])
-        Q[q].dma_start(out=dst[0], in_=src).then_inc(T.sem[sem], 16)
-        landed(dst[1][0][0], sem, 16, dst[1][0][1], dst[1][0][2])
+    def dma(q, sem, outs, ins, out, in_, time):
+        note(q, outs, ins, lambda e: e.dma_start(out=out, in_=in_), 0.05, time, (sem, 16))
 
-    def iota(o, pattern, base, cm, flag=True):
-        if flag:
-            do("G", [o], [], lambda q: q.iota(o[0], pattern, base, cm, allow_small_or_imprecise_dtypes=True))
-        else:
-            do("G", [o], [], lambda q: q.iota(o[0], pattern, base, cm))
+    def iota(o, pattern, base, cm):
+        more = {"allow_small_or_imprecise_dtypes": True} if SCRATCH[o[1][0][0]][2] == "float32" else {}
+        note("G", [o], [], lambda q: q.iota(o[0], pattern, base, cm, **more), 0.13 + 2 * CYC * len(o[1][0][1]))
+
+    def remote(ins, call):
+        def run(q):
+            call(q)
+        return note("G", [], ins, run, ISSUE)
+
+    def arrives(outs, ins, sem, val, since, time):
+        note("D", outs, ins, None, 0.0, time, (sem, val), [since])
 
     fill(B("tab0", 2032, 2048), FAR)
-    load("Y", "dg", B("gli", 0, 256), T.gl[:, :])
-    load("S", "dx", (T.tab0[:, 0:NONE], [("tab0", 0, 2048)]), T.xt[:, 0:NONE])
-    load("Y", "dy", B("yvs", 0, 384), T.yv[:, :])
-    load("Y", "da", B("ali", 0, 256), T.al[:, :])
-    load("Y", "db", B("bli", 0, 256), T.bl[:, :])
-    load("Y", "dt", B("thi", 0, 256), T.th[:, :])
-    load("Y", "ds", B("xsav", 0, 2), T.xt[:, NONE - 1:NONE + 1])
+    dma("Y", "dg", [B("gli", 0, 256)], [], T.gli[:, :], T.gl[:, :], LOAD / 2)
+    dma("S", "dx", [B("tab0", 0, 2048)], [], T.tab0[:, 0:NONE], T.xt[:, 0:NONE], LOAD)
+    dma("Y", "dy", [B("yvs", 0, 384)], [], T.yvs[:, :], T.yv[:, :], LOAD / 2)
+    for sem, b, src in (("dt", "thi", T.th), ("da", "ali", T.al), ("db", "bli", T.bl)):
+        dma("Y", sem, [B(b, 0, 256)], [], T[b][:, :], src[:, :], LOAD)
+    dma("Y", "ds", [B("xsav", 0, 2)], [], T.xsav[:, 0:2], T.xt[:, NONE - 1:NONE + 1], LOAD)
 
     def C(k):
         return B("col", k, k + 1)
 
-    iota(B("pidx", 0, 2), [[0, 2]], 0, 1, False)
+    def start_of(c):
+        return 146 * c if c < 4 else 162 * (7 - c) + S
+
+    iota(B("pidx", 0, 2), [[0, 2]], 0, 1)
     iota(B("c16", 0, S), [[16, S]], 0, 0)
     iota(B("cb", 0, 128), [[0, 8], [1, 16]], 0, 0)
     iota(B("ca", 0, 128), [[1, 8], [0, 16]], 0, 0)
@@ -237,92 +309,114 @@ def rank_program(g, core, T, topo):
     iota(B("cz", 0, 144), [[1, 144]], -15, 0)
     iota(B("c32", 0, 8), [[32, 8]], 2048, 0)
     iota(B("cn", 0, 16), [[-1, 16]], 16, 0)
-
-    fill((T.mx[:, :, 0:16], [("mx", 0, 24 * E)]), 0.0)
-    ts(B("p15", 0, 1), B("pidx", 0, 1), 15, A.bitwise_and)
-    ts(B("p4", 0, 1), B("pidx", 0, 1), 4, A.arith_shift_right)
+    iota(B("iw", 0, WT), [[1, WT]], 0, 0)
+    fill(X("mx", ALL, slice(0, 16)), 0.0)
     fill(B("ones"), 1.0)
+    for b, x, op in (("p15", 15, A.bitwise_and), ("p4", 4, A.arith_shift_right), ("p7", 7, A.bitwise_and), ("p8", 8, A.bitwise_and)):
+        ts(B(b, 0, 1), B("pidx", 0, 1), x, op)
     ts(C(0), B("p15", 0, 1), -8.0, A.add)
     ts(C(1), B("p15", 0, 1), -16.0, A.mult, 256.0, A.add)
     cp(C(2), B("p15", 0, 1))
     cp(C(3), B("p4", 0, 1))
+    ts(C(4), B("p4", 0, 1), 16.0, A.mult)
+    ts(C(5), B("p7", 0, 1), float(S), A.mult)
+    ts(C(6), B("p8", 0, 1), float(S), A.mult)
     ts(B("qi", 0, S), B("c16", 0, S), C(0), A.add, 1.0 / S, A.mult)
-    ts(B("rr", 0, 128), B("cb", 0, 128), C(2), A.is_equal)
     ts(B("qj", 0, S), B("qi", 0, S), float(S), A.mult, C(1), A.add)
+    ts(B("qk", 0, S), B("qj", 0, S), 255, A.bitwise_and)
+    cp(B("pin", 0, S), B("qk", 0, S))
+    ts(B("pout", 0, 16), B("cn", 0, 16), C(5), A.add, C(6), A.add)
+    ts(B("rr", 0, 128), B("cb", 0, 128), C(2), A.is_equal)
     ts(B("bo", 0, 128), B("ca", 0, 128), C(3), A.is_equal)
-    ts(B("qi", 0, S), B("qj", 0, S), 255, A.bitwise_and)
     tt(B("id1"), B("bo", 0, 128), B("rr", 0, 128), A.mult)
-    cp(B("pin", 0, S), B("qi", 0, S))
-
-    def ids(*names):
-        for b in names:
-            ts(B(b), B("id1"), IDS[b], A.mult)
+    for b in ("id1184", "id32", "id65", "idf", "id4058", "id515", "idbig"):
+        ts(B(b), B("id1"), IDS[b], A.mult)
+    for b in ("z1", "idm", "id4096", "idn4096", "idnbig", "id2048", "id32f", "idnmid", "idn2047", "id2047", "idq", "zh"):
+        act(B(b), B("id1"), scale={"z1": 1.0, "zh": 0.5, "id32f": 1.0}.get(b) or IDS[b])
+    ts(B("zm", 0, 144), B("cz", 0, 144), C(4), A.is_equal, -1.0, A.mult)
+    ts(B("z2", 0, 144), B("zm", 0, 144), -2.0, A.mult)
+    ts(B("onesp"), B("cj"), 30.0, A.max, -29.0, A.add)
+    ts(B("pa_"), B("onesp"), -4.0, A.mult, 5.0, A.add)
+    ts(B("pb_"), B("onesp"), 8.0, A.mult, -8.0, A.add)
+    cp(B("jc"), B("cj"))
+    ts(B("dum", 0, 8), B("c32", 0, 8), C(2), A.add, C(2), A.add)
+    cp(X("nx", ALL, 0), B("dum", 0, 8))
+    ts(B("sp4", 0, 8), B("dum", 0, 8), 4.0, A.mult, -1.0, A.add)
+    fill(B("w", 0, EQ), 1.0)
+    for c in range(8):
+        o = start_of(c) + 16 * c
+        ts(B("w", o, o + 16), B("rr", 0, 16), B("sp4", c, c + 1), A.mult, 1.0, A.add)
+    fill(ST("w", 0, EQ, 146), 0.0)
+    fill(ST("w", S, EQ, 162), 0.0)
+    fill(B("aa1", L, L + 1), 0.0)
+    fill(B("bb1", L, L + 1), 0.0)
 
     def turn_in(o, src):
         cp(o, ind(B(src, 0, 256), B("pin", 0, S)))
 
     def views(t):
         for k in (0, 1):
-            act(X3("vexp", ALL, k, ALL), B("yvs", t * 128, t * 128 + 128), apart=k == 1)
-        act(X3("vexp", ALL, slice(2, 4), ALL), X3("vexp", ALL, slice(0, 2), ALL), apart=True)
-        group([(B("b0", 0, 512), B("z1"), X3("vexp", ALL, ALL, ALL))])
+            act(X("vexp", ALL, k, ALL), B("yvs", t * 128, t * 128 + 128))
+        act(X("vexp", ALL, slice(2, 4), ALL), X("vexp", ALL, slice(0, 2), ALL))
+        group([(B("b0", 0, 512), B("z1"), X("vexp"))])
 
-    def lists_a(t, ysrc):
+    def lists(t, ysrc):
         gg = "g%d" % (t % 2)
         cp(B("offx"), B(gg))
         ts(B("f8", 0, 2 * L), B(gg, 0, 2 * L), 2047.0, A.not_equal, -8.0, A.mult)
         tt(B("pp"), B(gg), ysrc, A.mult)
-        psum("b3", 0, [("id1184", gg, 0, ""), ("id32", gg, L, "")])
         psum("b3", L, [("idbig", "f8", L, ""), ("id4058", "ones", 0, ""), ("id515", "ones", 0, ""), ("id65", gg, 0, "n"),
                        ("idf", gg, 0, "n")])
+        psum("b3", 0, [("id1184", gg, 0, ""), ("id32", gg, L, "")])
+        tt(X("qyi"), B("b3", L, 2 * L), B(gg, L, 2 * L), A.max)
+        tt(X("nxi"), B("b3"), B("pp"), A.add)
+        ts(X("qyj"), X("qyi"), 2047, A.bitwise_and)
+        ts(X("nxj"), X("nxi"), 5, A.arith_shift_right, 2047, A.bitwise_and)
+        cp(X("qy"), X("qyj"))
+        cp(B("offy"), X("qy"))
+        cp(B("offn"), X("nxj"))
+        cp(X("nx", ALL, slice(1, S)), X("nxj", ALL, slice(1, S)))
 
-    def lists_b(t):
-        gg = "g%d" % (t % 2)
-        tt(X3("qyi"), B("b3", L, 2 * L), B(gg, L, 2 * L), A.max)
-        tt(X3("nxi"), B("b3"), B("pp"), A.add)
-        ts(X3("qyi"), X3("qyi"), 2047, A.bitwise_and)
-        ts(X3("nxi"), X3("nxi"), 5, A.arith_shift_right, 2047, A.bitwise_and)
-        cp(X3("qy"), X3("qyi"))
-        cp(X3("nx", ALL, slice(1, S)), X3("nxi", ALL, slice(1, S)))
-        cp(B("offy"), X3("qy"))
-        cp(B("offn"), X3("nxi"))
+    def count(t):
+        o = B("b2", L, L + 8)
+        group([(o, B("id32f"), B("svn", 8 * t, 8 * t + 8))] + [(o, B("rr", 0, 128), ST("nm", s, L, S)) for s in range(1, S)])
+        act(B("tex", 0, 8), o, scale=-1.0, bias=128.0)
 
-    def extra(t):
-        first = terms("b5", L, [("idn8", "pb_", 0, "")] if t else [("id1", "pb_", 0, ""), ("idm", "pb_", 0, "")])
-        pads = ST("b5", L, 2 * L, S)
-        group(first + [(pads, B("zm", 15 - r, 143 - r), ST("yvs", 128 * t + r, 128 * t + 128, 16)) for r in range(16)]
-              + [(pads, B("rr", 0, 128), ST("nm", s, L, S)) for s in range(1, S) if t])
-        scan(B("tex"), B("rs"), B("b5", L, 2 * L), A.mult, A.subtract)
-
-    def prepare(t):
+    def thresholds(t):
+        for c in range(8):
+            seg = slice(c, 16, 8)
+            act(X("tht", seg, ALL), X(("tha", "thb")[t % 2], seg, ALL), bias=B("tex", c, c + 1), func=F.Identity)
         ts(B("an", 0, 2 * L), B("aa%d" % (t % 2), 0, 2 * L), 2047.0, A.is_equal)
-        hx, hy, turn = (L, 0, "n") if t == 1 else (0, L, "")
-        psum("b4", L, [("idbig", "onesp", 0, ""), ("idbig", "an", L, ""), ("id4096", "f8", L, ""), ("idn4096", "f8", 0, "n"),
-                       ("id32f", "th2", hy, turn), ("id32f", "tex", 0, "")])
-        psum("b4", 0, [("idbig", "onesp", 0, ""), ("idbig", "an", 0, ""), ("id4096", "f8", 0, ""), ("idn4096", "f8", L, ""),
-                       ("id32f", "th2", hx, ""), ("id32f", "tex", 0, "")])
+        psum("b4", 0, [("idbig", "onesp", 0, ""), ("id4096", "f8", 0, ""), ("idn4096", "f8", L, ""), ("id32f", "tht", 0, ""),
+                       ("idbig", "an", 0, "")])
+        psum("b4", L, [("idbig", "onesp", 0, ""), ("id4096", "f8", L, ""), ("idn4096", "f8", 0, "n"), ("id32f", "tht", 8, ""),
+                       ("idbig", "an", L, "")])
 
-    def differences(t):
-        s = t % 2
-        gg, aa, bb = "g%d" % s, "aa%d" % s, "bb%d" % s
-        psum("b4", 2 * L, [("id1", "qy", 0, ""), ("idn2047", "ones", 0, "")])
-        psum("b6", 0, [("id1", aa, 0, ""), ("idm", gg, 0, "")])
-        psum("b6", L, [("id1", bb, 0, ""), ("idn2047", "ones", 0, "")])
-        psum("b6", 2 * L, [("id1", "nx", 0, ""), ("idm", gg, 0, "")])
-        psum("b7", 0, [("id1", bb, L, ""), ("idn2047", "ones", 0, "")])
-        psum("b7", L, [("id1", aa, L, ""), ("idm", gg, L, "")])
-        psum("b7", 2 * L, [("id2047", "ones", 0, ""), ("idm", gg, L, "")])
-        for k, (src, c) in enumerate((("nx", 0), (gg, 0), (gg, L))):
-            psum("b5", L * k, [("id1", src, c, ""), ("id2048", "jc", 0, "")])
+    def sources_early(t):
+        aa, bb = "aa%d" % (t % 2), "bb%d" % (t % 2)
+        for k, (src, c, flag) in enumerate(((aa, L, "oy_"), (bb, 0, "ox_"), (aa, 0, "ox_"), (bb, L, "oy_"), ("qy", 0, "ty"))):
+            psum(("b7", "b6")[k // 3], L * (k % 3), [("idm", src, c, ""), ("id4096", flag, 0, "")])
+        act(B("rl", 0, 3 * L), B("b7", 0, 3 * L), bias=-2049.0, func=F.Relu)
+        act(B("rl", 3 * L, 5 * L), B("b6", 0, 2 * L), bias=-2049.0, func=F.Relu)
 
-    def memory_masks(t):
+    def new_places(t):
         gg = "g%d" % (t % 2)
-        psum("b4", 0, [("id1", gg, 0, ""), ("id4096", "nm", 0, "")])
-        psum("b4", L, [("id1", gg, L, ""), ("id4096", "nm", 0, "")])
-        psum("b4", 2 * L, [("id2047", "ox_", 0, ""), ("id2047", "u", 0, ""), ("id2047", "oy_", 0, "P")])
-        psum("b5", 0, [("id2047", b, 0, "") for b in ("oy_", "ox_", "ty", "ones")] + [("idn2047", "nm", 0, "")])
+        psum("b7", 0, [("idm", gg, L, ""), ("idn4096", "oy_", 0, ""), ("id4096", "nm", 0, "")])
+        psum("b7", L, [("idm", "nx", 0, ""), ("id4096", "u", 0, "")])
+        psum("b7", 2 * L, [("idm", gg, 0, ""), ("idn4096", "ox_", 0, "")] + [("idn4096", "pb_", 0, "")] * (t == 0)
+             + [("idn4096", "u", 0, "")])
+        act(B("rl", 5 * L, 7 * L), B("b7", 0, 2 * L), bias=-2049.0, func=F.Relu)
+        act(B("rl", 7 * L, 8 * L), B("b7", 2 * L, 3 * L), bias=2047.0, func=F.Relu)
+        ty_, tx_, tb_ = (("0", "N", ""), ("P", "", "P"), ("", "", "P"))[t]
+        psum("b6", 0, [("id2047", "ones", 0, "")] + [("idm", "rl", L * k, ty_) for k in (0, 1, 4, 5)])
+        psum("b1", 0, [("id2047", "ones", 0, ""), ("idm", "rl", 3 * L, tb_)] + [("idm", "rl", L * k, tx_) for k in (2, 6, 7)])
 
     def memories(t):
+        gg = "g%d" % (t % 2)
+        psum("b4", 2 * L, [("id2047", "ox_", 0, ""), ("id2047", "oy_", 0, "P"), ("id2047", "u", 0, "")])
+        psum("b4", 0, [("id1", gg, 0, ""), ("id4096", "nm", 0, "")])
+        psum("b4", L, [("id1", gg, L, ""), ("id4096", "nm", 0, "")])
+        psum("b5", 0, [("id2047", b, 0, "") for b in ("oy_", "ox_", "ty", "ones")] + [("idn2047", "nm", 0, "")])
         old = ["%s%d" % (m, t % 2) for m in ("aa", "bb")]
         new = ["%s%d" % (m, 1 - t % 2) for m in ("aa", "bb")] if t < 2 else ["wa", "wb"]
         both = list(zip(old, new, (0, L)))
@@ -344,48 +438,39 @@ def rank_program(g, core, T, topo):
             if t == 1:
                 tt(ST(w, 16, L, S), ST("b5", 1, L, S), ST(m, L + 1, 2 * L, S), A.max)
 
-    def gather(t, k):
-        l, c0, c1 = GATHERS[k]
-        act(B("xg", E * (8 * l + c0), E * (8 * l + c1)),
-            ind(B("tab%d" % t, 0, 2048), B(("offx", "offy", "offn")[l], S * c0, S * c1)))
-
-    def larger(k):
-        l, c0, c1 = GATHERS[k]
-        for c in range(c0, c1):
+    def gather(t, l):
+        for e, k, c0, c1 in GATHERS:
+            if k == l:
+                (cp if e == "V" and t else act)(B("xg", 16 * (L * l + c0), 16 * (L * l + c1)),
+                                                ind(B("tab%d" % t, 0, 2048), B(("offx", "offy", "offn")[l], c0, c1)))
+        for c in range(8):
             for q in range(4):
                 a = 16 + 64 * q
                 o = E * (8 * l + c) + a
-                tt((T.mx[:, 8 * l + c, a:a + 64], [("mx", o, o + 64)]), B("xg", o, o + 64), B("b0", 64 * c, 64 * c + 64), A.max)
+                tt(X("mx", 8 * l + c, slice(a, a + 64)), B("xg", o, o + 64), B("b0", 64 * c, 64 * c + 64), A.max)
 
     def half(l, c0):
         c = 8 * l + c0
         o, a = B("b%d" % (l + 1), S * c0, S * c0 + 4 * S), E * c
-        return ([(o, B("zm", 15 - r, 143 - r), (T.xg[:, a + r:a + 4 * E:16], [("xg", a, a + 4 * E)])) for r in range(16)]
-                + [(o, B("z2", 15 - r, 143 - r), (T.mx[:, c:c + 4, r:E:16], [("mx", a, a + 4 * E)])) for r in range(16)])
+        return ([(o, B("zm", 15 - r, 143 - r), ST("xg", a + r, a + 4 * E, 16)) for r in range(16)]
+                + [(o, B("z2", 15 - r, 143 - r), X("mx", slice(c, c + 4), slice(r, E, 16))) for r in range(16)])
 
-    def contract(l, c0):
-        group(half(l, c0))
-
-    def scatter(tab, lst, val):
+    def scatter(tab, msg):
         w = B(tab, 0, WT)
-        do("V", [w], [B(lst, 0, 8), B(val, 0, 128)],
-           lambda q: q.tensor_copy(out=w[0].indirect(T[lst][:, 0:8]), in_=T[val][:, :]))
-
-    ncall = [0]
-
-    def send(dst, dbuf, sbuf, width):
-        rid, pid = topo.addr(dst, core)
-        before("G", [(sbuf, 0, width)], [])
-        g.remote_dma(out_ap=T[dbuf][:, 0:width], in_ap=T[sbuf][:, 0:width], remote_sem=T.sem[dbuf + "_"], local_sem=T.sem.ls,
-                     pid=pid, routing_id=rid, dma_engine_mask=topo.mask(core, dst))
-        ncall[0] += len(topo.engines(core, dst))
+        note("V", [w], [B(msg)], lambda q: q.tensor_copy(out=w[0].indirect(T[msg][:, 128:L]), in_=T[msg][:, 0:128]),
+             CYC * (60 + 3.8 * 128))
 
     peer = {d: T.cores[(rank + d) % n] for d in (1, 2, -1, -2)}
-    for s, d in {"a1": 1, "a2": 2, "b2": 1, "b0": -1, "c0": -2}.items():
-        for k in "vl":
-            landed(s + k, s + k + "_", len(topo.engines(peer[d], core)))
-    for d in (1, 2):
-        landed("tab%d" % d, "t%d" % d, sum(len(topo.engines(c, core)) for c in carriers((rank + d) % n, T, topo)))
+    sent = [0]
+
+    def send(d, slot, msg):
+        dst = peer[d]
+        rid, pid = topo.addr(dst, core)
+        k = remote([B(msg)], lambda q: q.remote_dma(out_ap=T[slot][:, :], in_ap=T[msg][:, :], remote_sem=T.sem[slot + "_"],
+                                                    local_sem=T.sem.ls, pid=pid, routing_id=rid,
+                                                    dma_engine_mask=topo.mask(core, dst)))
+        sent[0] += len(topo.engines(core, dst))
+        arrives([B(slot)], [], slot + "_", len(topo.engines(peer[-d], core)), k, WAY)
 
     def send_table():
         cs, he = carriers(rank, T, topo), hand_engines(rank, T, topo)
@@ -394,167 +479,110 @@ def rank_program(g, core, T, topo):
         def tr(dst, mask, sem, dbuf, k, at):
             return RemoteDMATransfer(dst_ids=[DstId(rid=topo.addr(dst, core)[0], pnc=topo.addr(dst, core)[1])], dma_engine_mask=mask,
                                      remote_sem=T.sem[sem], src=T.tab0[:, k * w:k * w + w], dst=T[dbuf][:, at:at + w])
-        before("G", [("tab0", 0, 2048)], [])
         hands = [tr(cs[k], he[k - 1][0], "hd", "hand", k, 0) for k in range(1, len(cs))]
-        g.remote_dma_fused(hands[:2] + [tr(peer[-1], topo.mask(core, peer[-1]), "t1", "tab1", 0, 0)], local_sem=T.sem.tl)
-        g.remote_dma_fused(hands[2:] + [tr(peer[-2], topo.mask(core, peer[-2]), "t2", "tab2", 0, 0)], local_sem=T.sem.tl)
+        own = [tr(peer[-d], topo.mask(core, peer[-d]), "t%d" % d, "tab%d" % d, 0, 0) for d in (1, 2)]
+        tab = B("tab0", 0, 2048)
+        remote([tab], lambda q: q.remote_dma_fused(hands[:2] + own[:1], local_sem=T.sem.tl))
+        k = remote([tab], lambda q: q.remote_dma_fused(hands[2:] + own[1:], local_sem=T.sem.tl))
         gone = sum(h[1] for h in he) + len(topo.engines(core, peer[-1])) + len(topo.engines(core, peer[-2]))
-        after("D", [("tab0", 0, WT)], [], ("D", "tl", gone, {}))
-
-    def start_of(c):
-        return 146 * c if c < 4 else 162 * (7 - c) + S
-
-    def late_constants():
-        fill(B("w", 0, EQ), 1.0)
-        ts(B("p7", 0, 1), B("pidx", 0, 1), 7, A.bitwise_and)
-        ts(B("p8", 0, 1), B("pidx", 0, 1), 8, A.bitwise_and)
-        ts(B("sp4", 0, 8), B("dum", 0, 8), 4.0, A.mult, -1.0, A.add)
-        ts(C(5), B("p7", 0, 1), float(S), A.mult)
-        ts(C(6), B("p8", 0, 1), float(S), A.mult)
-        for c in range(8):
-            o = start_of(c) + 16 * c
-            ts(B("w", o, o + 16), B("rr", 0, 16), B("sp4", c, c + 1), A.mult, 1.0, A.add)
-        ts(B("pout", 0, 16), B("cn", 0, 16), C(5), A.add, C(6), A.add)
-        fill(ST("w", 0, EQ, 146), 0.0)
-        fill(ST("w", S, EQ, 162), 0.0)
-        fill(B("aa1", L, L + 1), 0.0)
-        fill(B("bb1", L, L + 1), 0.0)
+        arrives([], [tab], "tl", gone, k, COPY)
+        for d in (1, 2):
+            arrives([B("tab%d" % d, 0, WT)], [], "t%d" % d,
+                    sum(len(topo.engines(c, core)) for c in carriers((rank + d) % n, T, topo)), k, COPY * d)
 
     turn_in(B("g0", 0, 2 * L), "gli")
-    ts(C(4), C(3), 16.0, A.mult)
-    ids("id1184", "id32", "id65", "idf", "id4058", "id515", "idbig")
-    cp(B("z1", 0, 128), B("id1"))
-    ts(B("zm", 0, 144), B("cz", 0, 144), C(4), A.is_equal, -1.0, A.mult)
-    lists_a(0, B("g0", L, 2 * L))
+    lists(0, B("g0", L, 2 * L))
     views(0)
     send_table()
-    iota(B("iw", 0, WT), [[1, WT]], 0, 0)
-    ts(B("z2", 0, 144), B("zm", 0, 144), -2.0, A.mult)
-    ts(B("onesp"), B("cj"), 30.0, A.max, -29.0, A.add)
-    cp(B("jc"), B("cj"))
-    ts(B("dum", 0, 8), B("c32", 0, 8), C(2), A.add, C(2), A.add)
-    cp(X3("nx", ALL, 0), B("dum", 0, 8))
-    lists_b(0)
-    ts(B("pa_"), B("onesp"), -4.0, A.mult, 5.0, A.add)
-    ts(B("pb_"), B("onesp"), 8.0, A.mult, -8.0, A.add)
-    ts(B("rs"), B("onesp"), -0.5, A.mult, 1.5, A.add)
-    ids("idm", "id4096", "idn4096", "idn2047", "id2047", "id2048", "idnbig", "idnmid", "idn8")
-    cp(B("id32f", 0, 128), B("id1"))
+    group([(B("b2", L, L + 24), B("zm", 15 - r, 143 - r), ST("yvs", r, 384, 16)) for r in range(16)])
+    act(B("svn", 0, 24), B("b2", L, L + 24))
+    act(B("tex", 0, 8), B("svn", 0, 8), scale=-1.0)
+    turn_in(B("th2", 0, 2 * L), "thi")
+    act(X("tha"), B("th2", 0, 2 * L))
+    act(X("thb", slice(0, 8), ALL), X("tha", slice(8, 16), ALL))
+    act(X("thb", slice(8, 16), slice(1, S)), X("tha", slice(0, 8), slice(0, 16)))
+    act(X("thb", slice(8, 16), 0), X("tha", slice(0, 8), 0))
+    turn_in(B("aa0", 0, 2 * L), "ali")
+    turn_in(B("bb0", 0, 2 * L), "bli")
 
     def visit(t):
         s = t % 2
-        gg, tab = "g%d" % s, "tab%d" % t
-        for k in range(len(GATHERS)):
-            gather(t, k)
-        if t:
-            memories(t - 1)
-            extra(t)
-        else:
-            extra(0)
-            turn_in(B("aa0", 0, 2 * L), "ali")
-        larger(0)
-        contract(0, 0)
-        if t == 0:
-            turn_in(B("bb0", 0, 2 * L), "bli")
-            turn_in(B("th2", 0, 2 * L), "thi")
-        prepare(t)
-        larger(1)
-        contract(0, 4)
-        differences(t)
-        if t == 0:
-            late_constants()
-        if t == 1:
-            scatter("tab0", "lw0", "val0")
-        if t == 2:
-            scatter("tab0", "b0l", "b0v")
-        larger(2)
-        contract(1, 0)
+        gg, tab, msg = "g%d" % s, "tab%d" % t, "m%d" % t
+        thresholds(t)
+        for k, (src, c) in enumerate((("nx", 0), (gg, 0), (gg, L))):
+            psum("b5", L * k, [("id1", src, c, ""), ("id2048", "jc", 0, "")])
+        psum("b1", L, [("idbig", "ones", 0, ""), ("id4096", "f8", 0, ""), ("idnbig", "pb_", 0, "")])
+        gather(t, 0)
+        group(half(0, 0))
+        group(half(0, 4))
         cp(B("sgx"), B("b1"))
-        if t == 1:
-            scatter("tab2", "a2l", "a2v")
-        if t == 2:
-            cp(B("tab0", NONE, NONE + 1), B("xsav", 1, 2))
-        tt(B("ox_"), B("sgx"), B("b4"), A.is_gt)
-        larger(3)
-        contract(1, 4)
         cp(ST("sgx", 0, L, S), ST("b1", 16, L, S))
-        tt(B("p1"), B("b6"), B("ox_"), A.mult)
-        tt(B("p5"), B("b6", L, 2 * L), B("ox_"), A.mult)
-        psum("b1", 2 * L, [("idnbig", "onesp", 0, ""), ("id4096", "f8", L, ""), ("idnbig", "ox_", 0, ""), ("idn4096", "f8", 0, "n"),
-                           ("id32f", "sgx", 0, "n")])
+        tt(B("ox_"), B("sgx"), B("b4"), A.is_gt)
+        psum("b6", 2 * L, [("idnbig", "onesp", 0, ""), ("id4096", "f8", L, ""), ("idn4096", "f8", 0, "n"), ("id32f", "sgx", 0, "n"),
+                           ("idnbig", "ox_", 0, "")])
+        gather(t, 1)
+        group(half(1, 0))
+        group(half(1, 4))
         cp(B("sqy"), B("b2"))
         tt(B("oy_"), B("sqy"), B("b4", L, 2 * L), A.is_gt)
-        larger(4)
-        mask = terms("b3", 0, [("idbig", "pa_", 0, ""), ("id4096", "f8", L, ""), ("idbig", "oy_", 0, "P")])
+        tt(B("ty"), B("sqy"), B("b6", 2 * L, 3 * L), A.is_lt)
         psum("b1", 0, [("id32f", "sgx", 0, ""), ("idnbig", "pb_", 0, ""), ("idnmid", "oy_", 0, "")])
-        psum("b1", L, [("id32f", "sgx", 0, ""), ("idn4096", "f8", 0, ""), ("idnbig", "ones", 0, ""), ("idnmid", "oy_", 0, "")])
-        tt(B("ty"), B("sqy"), B("b1", 2 * L, 3 * L), A.is_lt)
-        tt(B("p2"), B("b7"), B("oy_"), A.mult)
-        tt(B("p4_"), B("b7", L, 2 * L), B("oy_"), A.mult)
-        larger(5)
-        tt(B("mnm"), B("b1", L, 2 * L), B("sqy"), A.min)
         tt(B("mnu"), B("b1"), B("sqy"), A.min)
-        tt(B("p7_"), B("b4", 2 * L, 3 * L), B("ty"), A.mult)
-        larger(6)
-        group(mask + half(2, 0) + half(2, 4))
+        tt(B("mnm"), B("mnu"), B("b1", L, 2 * L), A.subtract)
+        sources_early(t)
+        gather(t, 2)
+        group(terms("b3", 0, [("idbig", "pa_", 0, ""), ("id4096", "f8", L, "")]) + half(2, 0)
+              + terms("b3", 0, [("idbig", "oy_", 0, "P")]) + half(2, 4))
         tt(B("nm"), B("b3"), B("mnm"), A.is_ge)
         tt(B("u"), B("b3"), B("mnu"), A.is_lt)
         for k in range(3):
             scan(B("s3", L * k, L * k + L), B("nm"), B("b5", L * k, L * k + L), A.mult, A.max)
-        cp(B("ki", 0, 24), ST("s3", 16, 3 * L, S))
-        tt(B("q6"), B("b7", 2 * L, 3 * L), B("nm"), A.mult)
-        ts(B("gi", 0, 24), B("ki", 0, 24), 4095, A.bitwise_and)
-        tt(B("pu"), B("b6", 2 * L, 3 * L), B("u"), A.mult)
-        cp(B("goff", 0, 24), B("gi", 0, 24))
+        for lo, hi in ((0, 8), (8, 24)):
+            ts(B("gi", lo, hi), ST("s3", S * lo + 16, S * hi, S), 4095, A.bitwise_and)
+            cp(B("goff", lo, hi), B("gi", lo, hi))
         cp(B("gf", 0, 8), B("gi", 0, 8))
-        ty_, tx_ = (("0", "N"), ("P", ""), ("", ""))[t]
-        psum("b2", 0, [("id2047", "ones", 0, "")] + [("id1", b, 0, ty_) for b in ("p4_", "p5", "p7_")] + [("idm", "q6", 0, ty_)])
-        psum("b1", 0, [("id1", "p2", 0, "")] * (t == 0) + [("id1", gg, 0, tx_.lower())] + [("id1", "p2", 0, "P")] * (t > 0)
-             + [("id1", b, 0, tx_) for b in ("p1", "pu")])
-        act(B("xv", 0, 256), ind(B(tab, 0, 2048), B("goff", 8, 24)), scale=0.5, bias=-0.125)
-        if t < 2:
-            views(t + 1)
+        act(B("xv", 0, 256), ind(B(tab, 0, 2048), B("goff", 8, 24)))
+        group([(B("b3", 2 * L, 2 * L + 128), B("idq"), B("ones", 0, 128))]
+              + [(B("b3", 2 * L, 2 * L + 128), B("zh"), B("xv", o, o + 128)) for o in (0, 128)])
+        cp(B(msg, 0, 128), B("b3", 2 * L, 2 * L + 128))
         cp(B("bf", 0, 128), ind(B("iw", 0, WT), B("goff", 0, 8)))
         cp(ST("eq", 16, 503, 162), B("gi", 0, 4))
-        cp(ST("eq", 583, 144, -146), B("gi", 4, 8), apart=True)
+        cp(ST("eq", 583, 144, -146), B("gi", 4, 8))
         for c in range(8):
             o = start_of(c)
-            ts(B("eq", o, o + 16 * c + 16), B("bf", 0, 16 * c + 16), B("gf", c, c + 1), A.is_equal, 0.25, A.mult, apart=True)
-        val, lw = "val%d" % t, "lw%d" % t
-        tt(B(val, 0, 128), B("xv", 0, 128), B("xv", 128, 256), A.add)
+            ts(B("eq", o, o + 16 * c + 16), B("bf", 0, 16 * c + 16), B("gf", c, c + 1), A.is_equal, 0.25, A.mult)
         scan(B("sc", 0, EQ), B("w", 0, EQ), B("eq", 0, EQ), A.mult, A.max)
-        hh = "g%d" % (1 - s)
-        if t < 2:
-            cp(B(hh), B("b2"))
-        cp(B(lw, 0, 4), ST("sc", 16, 503, 162))
-        cp(B(lw, 4, 8), ST("sc", 583, 144, -146))
-        slots = ((("a1", -1), ("a2", -2)), (("b2", -1), ("b0", 1)), (("c0", 2),))[t]
+        cp(B(msg, 128, 132), ST("sc", 16, 503, 162))
+        cp(B(msg, 132, 136), ST("sc", 583, 144, -146))
+        slots = ((("a1", -1), ("a2", -2)), (("e2", -1), ("e0", 1)), (("c0", 2),))[t]
         for slot, d in slots:
-            send(peer[d], slot + "v", val, 128)
-            send(peer[d], slot + "l", lw, 8)
+            send(d, slot, msg)
+        new_places(t)
+        memories(t)
         if t < 2:
-            cp(B(hh, L, 2 * L), B("b1"))
-            lists_a(t + 1, B("b1"))
-            memory_masks(t)
-            lists_b(t + 1)
-            scatter("tab%d" % (t + 1), slots[0][0] + "l", slots[0][0] + "v")
-        else:
-            memory_masks(t)
-            act(B("wg"), B("b1"))
-            act(B("wg", L, 2 * L), B("b2"))
-            memories(t)
-            scatter("tab0", "c0l", "c0v")
-            before("Y", [("tab0", 0, 2048)], [])
-            g.sync.dma_start(out=T.ox[:, :], in_=T.tab0[:, 0:2048]).then_inc(T.sem.sox, 16)
-            for w, b, q, sm in (("wg", "ogs", T.og, "sog"), ("wa", "oas", T.oa, "soa"), ("wb", "obs", T.ob, "sob")):
-                act(B(b, 0, 256), ind(B(w, 0, 2 * L), B("pout", 0, 16)))
-                before("S", [(b, 0, 256)], [])
-                g.scalar.dma_start(out=q[:, :], in_=T[b][:, :]).then_inc(T.sem[sm], 16)
+            hh = "g%d" % (1 - s)
+            views(t + 1)
+            count(t + 1)
+            act(B(hh), B("b6"))
+            act(B(hh, L, 2 * L), B("b1"))
+            lists(t + 1, B("b1"))
+        for into, m in ((("tab1", "a1"), ("tab0", "m0"), ("tab2", "a2")), (("tab2", "e2"), ("tab0", "e0")), (("tab0", "c0"),))[t]:
+            scatter(into, m)
+        if t == 1:
+            cp(B("tab0", NONE, NONE + 1), B("xsav", 1, 2))
 
     for t in range(3):
         visit(t)
+    dma("Y", "sox", [], [B("tab0", 0, 2048)], T.ox[:, :], T.tab0[:, 0:2048], STORE)
+    act(B("wg"), B("b1"))
+    act(B("wg", L, 2 * L), B("b6"))
+    for w, b, q, sm in (("wg", "ogs", T.og, "sog"), ("wa", "oas", T.oa, "soa"), ("wb", "obs", T.ob, "sob")):
+        act(B(b, 0, 256), ind(B(w, 0, 2 * L), B("pout", 0, 16)))
+        dma("S", sm, [], [B(b, 0, 256)], q[:, :], T[b][:, :], STORE)
+
+    cnt = issue()
     for sm in ("sog", "soa", "sob", "sox"):
         g.sync.wait_ge(T.sem[sm], 16)
-    for e in ("V", "S", "P", "G"):
-        g.wait_ge(T.sem[PS[e]], cnt[e])
-    g.wait_ge(T.sem.ls, ncall[0])
+    for e in COUNTER:
+        g.wait_ge(T.sem[COUNTER[e]], cnt[e])
+    g.wait_ge(T.sem.ls, sent[0])

@@ -3,21 +3,21 @@ from concourse.bass import DstId, RemoteDMATransfer
 from concourse.mybir import AluOpType as A
 from concourse.mybir import ActivationFunctionType as F
 
-L = 136
+U = 128
 S = 17
-E = 16 * S
+M = 136
 NONE = 2047
 WT = 2048 + 256
 BIG = 32768.0
 MID = 6144.0
 FAR = 1024.0
 EQ = 584
-GATHERS = [("V", 0, 0, 34), ("V", 0, 34, 68), ("S", 0, 68, 136), ("S", 1, 0, 68), ("S", 1, 68, 136), ("S", 2, 0, 68),
-           ("S", 2, 68, 102), ("S", 2, 102, 128), ("S", 2, 128, 136)]
+CUTS = ((0, 32, 64, 128), (0, 64, 128), (0, 64, 96, 120, 128))
+ON_VECTOR = (((0, 0),), ((0, 0), (0, 32)), ((0, 0), (0, 32)))
 IDS = {"id1": 1.0, "id1184": 1184.0, "id32": 32.0, "id65": 65.0, "idf": -1.0 / 32, "id4058": 4058.0, "id515": 33.0 / 64,
        "idbig": BIG, "idm": -1.0, "idnbig": -BIG, "id4096": 4096.0, "idn4096": -4096.0, "idnmid": -MID, "id2047": 2047.0,
        "id2048": 2048.0, "idn2047": -2047.0, "idq": -0.25}
-CYC, PCYC, WAKE, ISSUE, WAY, LOAD, COPY, STORE = 0.00083, 0.00045, 0.15, 0.3, 2.0, 4.5, 8.0, 3.0
+CYC, PCYC, WAKE, ISSUE, WAY, LOAD, COPY, STORE = 0.00083, 0.00045, 0.15, 0.3, 2.0, 3.2, 8.0, 3.0
 
 SCRATCH = {}
 
@@ -27,18 +27,18 @@ def _add(where, dtype, **kw):
         SCRATCH[k] = (where, [128] + (v if isinstance(v, list) else [v]), dtype)
 
 
+L1, L2 = [8, S], [16, S]
 _add("sbuf", "bfloat16", tab0=WT, tab1=WT, tab2=WT, hand=512, xsav=16, yvs=384, vexp=[8, 4, 16], z1=128, z2=144, zm=144,
-     zh=128, xv=256, xg=24 * E, mx=[24, E])
-_add("sbuf", "int32", gli=256, ali=256, bli=256, thi=256, pidx=8, p15=8, p4=8, p7=8, p8=8, qi=24, qj=24, qk=24,
-     nxi=[8, S], nxj=[8, S], qyi=[8, S], qyj=[8, S], gi=24, s3=3 * L)
-_add("sbuf", "uint16", offx=L, offy=L, offn=L, goff=24, pin=24, pout=16, m0=L, m1=L, m2=L, a1=L, a2=L, e2=L, e0=L, c0=L)
-_add("sbuf", "float16", g0=2 * L, g1=2 * L, aa0=2 * L, aa1=2 * L, bb0=2 * L, bb1=2 * L, ab2=2 * L, f8=2 * L, an=2 * L,
-     qy=[8, S], nx=[8, S], rr=128, bo=128, ids=128 * len(IDS), ones=L, onesp=L, pa_=L, pb_=L, jc=L,
-     ox_=L, oy_=L, ty=L, nm=L, u=L, rl=8 * L, bf=128, eq=EQ, w=EQ, sc=EQ)
-_add("sbuf", "float32", th2=2 * L, id32f=128, ca=128, cb=128, cz=144, cj=L, c16=24, c32=8, cn=16, col=16,
-     dum=8, sp4=8, iw=WT, sgx=L, sqy=L, mnu=L, mnm=L, tex=8, svn=24, tha=[16, S], thb=[16, S], tht=[16, S], pp=L, gf=8,
-     wg=2 * L, wa=2 * L, wb=2 * L, ogs=256, oas=256, obs=256)
-_add("psum", "float32", **{"b%d" % k: 512 for k in range(8)})
+     zh=128, xv=256, xg=48 * U, mx=48 * U)
+_add("sbuf", "int32", gli=256, ali=256, bli=256, thi=256, pidx=8, p15=8, p4=8, nxi=U, nxj=U, qyi=U, qyj=U, gi=24, s3=24 * S)
+_add("sbuf", "uint16", offx=U, offy=U, offn=U, goff=24, pin=16, pout=16, m0=M, m1=M, m2=M, a1=M, a2=M, e2=M, e0=M, c0=M)
+_add("sbuf", "float16", g0=L2, g1=L2, aa0=L2, aa1=L2, bb0=L2, bb1=L2, ab2=L2, f8=L2, an=L2, qy=L1, nx=L1, ones=L1, jc=L1,
+     ox_=L1, oy_=L1, ty=L1, nm=8 * S, u=L1, rl=[64, S], ing=256, ina=256, inb=256, rr=128, bo=128, ids=128 * len(IDS), bf=128,
+     eq=EQ, w=EQ, sc=EQ)
+_add("sbuf", "float32", th2=256, id32f=128, ca=128, cb=128, cz=144, cj=8 * S, c16=16, c32=8, cn=16, col=16,
+     dum=8, sp4=8, iw=WT, sgx=L1, sqy=U, mnu=U, mnm=L1, tex=8, svn=24, tha=L2, thb=L2, tht=L2, pp=U, gf=8,
+     wg=256, wa=256, wb=256, ogs=256, oas=256, obs=256)
+_add("psum", "float32", b0=512, b5=512, **{"b%d" % k: [30, S] for k in (1, 2, 3, 4, 6, 7)})
 SEMAPHORES = ["pv", "pa", "pt", "pg", "dg", "dy", "dx", "ds", "da", "db", "dt", "sog", "soa", "sob", "sox", "tl", "ls", "hd",
               "t1", "t2"] + [s + "_" for s in ("a1", "a2", "e2", "e0", "c0")]
 PART = {k: ("ids", 128 * j) for j, k in enumerate(IDS)}
@@ -48,6 +48,9 @@ WIDE = {k: v[2] in ("float32", "int32") for k, v in SCRATCH.items()}
 COUNTER = {"V": "pv", "S": "pa", "P": "pt", "G": "pg"}
 ROUNDS = 4
 ORDER = []
+PAIRS, WHOLE = slice(1, S), slice(0, S)
+TURNS = {"": [(PAIRS, PAIRS)], "f": [(WHOLE, WHOLE)], "n": [(PAIRS, slice(0, 16))], "N": [(slice(2, S), slice(1, 16)), (1, 16)],
+         "P": [(slice(1, 16), slice(2, S)), (16, 1)], "P0": [(slice(0, 16), PAIRS), (16, 1)], "0": [(PAIRS, PAIRS), (0, 16)]}
 
 
 def carriers(rank, T, topo):
@@ -82,7 +85,9 @@ def helper_program(g, core, T, topo):
 
 
 def issue_order(ops):
-    lag = [{d: ops[d]["tail"] + (0.0 if ops[d]["e"] == o["e"] == "P" or o["e"] == "D" else WAKE) for d in o["deps"]} for o in ops]
+    lag = [{d: ops[d]["tail"] + (0.0 if ops[d]["e"] == o["e"] in "PYG" or o["e"] == "D" else WAKE) for d in o["deps"]} for o in ops]
+    for o, l in zip(ops, lag):
+        l.update({d: 0.0 for d in o["behind"]})
     back = [{} for _ in ops]
     for k, l in enumerate(lag):
         for d, x in l.items():
@@ -135,7 +140,7 @@ def rank_program(g, core, T, topo):
 
     ops, writer, readers, bank = [], {}, {}, {}
 
-    def note(e, outs, ins, call, cost, tail=0.0, sem=None, deps=()):
+    def note(e, outs, ins, call, cost, tail=0.0, sem=None, deps=(), behind=()):
         k, deps = len(ops), set(deps)
         for ap, parts in ins:
             for b, cols in parts:
@@ -161,7 +166,7 @@ def rank_program(g, core, T, topo):
                 rec[:] = [e, [], rec[1]]
             deps.update(rec[2] + (rec[1][-1:] if e == "P" else []))
             rec[1].append(k)
-        ops.append({"e": e, "deps": sorted(deps - {-1, k}), "call": call, "cost": cost, "tail": tail, "sem": sem})
+        ops.append({"e": e, "deps": sorted(deps - {-1, k}), "call": call, "cost": cost, "tail": tail, "sem": sem, "behind": behind})
         return k
 
     def issue():
@@ -196,7 +201,7 @@ def rank_program(g, core, T, topo):
         ix = ix or (ALL,) * COLS[b].ndim
         return (T[b][(ALL,) + ix], [(b, COLS[b][ix].reshape(-1))])
 
-    def B(b, lo=0, hi=L):
+    def B(b, lo=0, hi=U):
         if b in PART:
             b, o = PART[b]
             lo, hi = o, o + 128
@@ -204,6 +209,9 @@ def rank_program(g, core, T, topo):
 
     def ST(b, lo, hi, step):
         return X(b, slice(lo, hi, step))
+
+    def P(b, k=0, cols=PAIRS, lists=1):
+        return X(b, slice(8 * k, 8 * (k + lists)), cols)
 
     def ind(w, o):
         return (w[0].indirect(o[0]), w[1] + o[1])
@@ -247,53 +255,38 @@ def rank_program(g, core, T, topo):
         note("P", [o], [l, r], lambda q: q.matmul(out=o[0], lhsT=l[0], rhs=r[0], start=start, stop=stop),
              PCYC * max(64, len(o[1][0][1])) * (4 if WIDE[r[1][0][0]] else 1))
 
-    def group(mats, start=True, stop=True):
+    def group(mats):
         for k, (o, l, r) in enumerate(mats):
-            matmul(o, l, r, start and k == 0, stop and k == len(mats) - 1)
+            matmul(o, l, r, k == 0, k == len(mats) - 1)
 
-    def terms(bk, lo, ts_):
-        out = []
-        for l, buf, c, turn in ts_:
-            l = B(l)
-            if COLS[buf].ndim == 2:
-                out.append((B(bk, lo, lo + L), l, X(buf, slice(c, c + 8), ALL)))
-                continue
-            if turn in ("", "0"):
-                out.append((B(bk, lo, lo + L), l, B(buf, c, c + L)))
-            if turn in ("n", "N"):
-                out.append((B(bk, lo + 1, lo + L), l, B(buf, c, c + L - 1)))
-            if turn == "P":
-                out.append((B(bk, lo, lo + L - 1), l, B(buf, c + 1, c + L)))
-            a, b = {"0": (0, 16), "N": (1, 16), "P": (16, 1)}.get(turn, (None, None))
-            if a is not None:
-                out.append((ST(bk, lo + a, lo + L, S), l, ST(buf, c + b, c + L, S)))
-        return out
+    def terms(bk, k, ts_):
+        return [(P(bk, k, a), B(l), X(buf) if buf == "nm" else P(buf, c, b)) for l, buf, c, turn in ts_ for a, b in TURNS[turn]]
 
-    def psum(bk, lo, ts_):
-        group(terms(bk, lo, ts_))
+    def psum(bk, k, ts_):
+        group(terms(bk, k, ts_))
 
-    def dma(q, sem, outs, ins, out, in_, time):
-        note(q, outs, ins, lambda e: e.dma_start(out=out, in_=in_), 0.05, time, (sem, 16))
+    def dma(q, sem, outs, ins, out, in_, time, behind=()):
+        return note(q, outs, ins, lambda e: e.dma_start(out=out, in_=in_), 0.05, time, (sem, 16), behind=behind)
 
     def iota(o, pattern, base, cm):
         more = {"allow_small_or_imprecise_dtypes": True} if SCRATCH[o[1][0][0]][2] == "float32" else {}
         note("G", [o], [], lambda q: q.iota(o[0], pattern, base, cm, **more), 0.13 + 2 * CYC * len(o[1][0][1]))
 
-    def remote(ins, call):
+    def remote(ins, call, behind=()):
         def run(q):
             call(q)
-        return note("G", [], ins, run, ISSUE)
+        return note("G", [], ins, run, ISSUE, behind=behind)
 
     def arrives(outs, ins, sem, val, since, time):
         note("D", outs, ins, None, 0.0, time, (sem, val), [since])
 
     fill(B("tab0", 2032, 2048), FAR)
-    dma("Y", "dg", [B("gli", 0, 256)], [], T.gli[:, :], T.gl[:, :], LOAD / 2)
+    k = dma("Y", "dg", [B("gli", 0, 256)], [], T.gli[:, :], T.gl[:, :], LOAD - 1.2)
     dma("S", "dx", [B("tab0", 0, 2048)], [], T.tab0[:, 0:NONE], T.xt[:, 0:NONE], LOAD)
-    dma("Y", "dy", [B("yvs", 0, 384)], [], T.yvs[:, :], T.yv[:, :], LOAD / 2)
+    k = dma("Y", "dy", [B("yvs", 0, 384)], [], T.yvs[:, :], T.yv[:, :], LOAD - 1.0, [k])
     for sem, b, src in (("dt", "thi", T.th), ("da", "ali", T.al), ("db", "bli", T.bl)):
-        dma("Y", sem, [B(b, 0, 256)], [], T[b][:, :], src[:, :], LOAD)
-    dma("Y", "ds", [B("xsav", 0, 2)], [], T.xsav[:, 0:2], T.xt[:, NONE - 1:NONE + 1], LOAD)
+        k = dma("Y", sem, [B(b, 0, 256)], [], T[b][:, :], src[:, :], LOAD + 0.8, [k])
+    dma("Y", "ds", [B("xsav", 0, 2)], [], T.xsav[:, 0:2], T.xt[:, NONE - 1:NONE + 1], LOAD + 0.8, [k])
 
     def C(k):
         return B("col", k, k + 1)
@@ -302,45 +295,38 @@ def rank_program(g, core, T, topo):
         return 146 * c if c < 4 else 162 * (7 - c) + S
 
     iota(B("pidx", 0, 2), [[0, 2]], 0, 1)
-    iota(B("c16", 0, S), [[16, S]], 0, 0)
+    iota(B("c16", 0, 16), [[1, 16]], 240, 0)
     iota(B("cb", 0, 128), [[0, 8], [1, 16]], 0, 0)
     iota(B("ca", 0, 128), [[1, 8], [0, 16]], 0, 0)
-    iota(B("cj"), [[0, 8], [-2, S]], 32, 0)
+    iota(X("cj"), [[0, 8], [-2, S]], 32, 0)
     iota(B("cz", 0, 144), [[1, 144]], -15, 0)
     iota(B("c32", 0, 8), [[32, 8]], 2048, 0)
-    iota(B("cn", 0, 16), [[-1, 16]], 16, 0)
+    iota(B("cn", 0, 16), [[-1, 16]], 15, 0)
     iota(B("iw", 0, WT), [[1, WT]], 0, 0)
-    fill(X("mx", ALL, slice(0, 16)), 0.0)
-    fill(B("ones"), 1.0)
-    for b, x, op in (("p15", 15, A.bitwise_and), ("p4", 4, A.arith_shift_right), ("p7", 7, A.bitwise_and), ("p8", 8, A.bitwise_and)):
-        ts(B(b, 0, 1), B("pidx", 0, 1), x, op)
-    ts(C(0), B("p15", 0, 1), -8.0, A.add)
-    ts(C(1), B("p15", 0, 1), -16.0, A.mult, 256.0, A.add)
+    fill(X("ones"), 1.0)
+    fill(P("mnm", 0, 0), 4 * BIG)
+    for b in ("g0", "g1"):
+        fill(P(b, 1, 0), 0.0)
+    ts(B("p15", 0, 1), B("pidx", 0, 1), 15, A.bitwise_and)
+    ts(B("p4", 0, 1), B("pidx", 0, 1), 4, A.arith_shift_right)
+    ts(C(0), B("p15", 0, 1), 16.0, A.mult)
     cp(C(2), B("p15", 0, 1))
     cp(C(3), B("p4", 0, 1))
     ts(C(4), B("p4", 0, 1), 16.0, A.mult)
-    ts(C(5), B("p7", 0, 1), float(S), A.mult)
-    ts(C(6), B("p8", 0, 1), float(S), A.mult)
-    ts(B("qi", 0, S), B("c16", 0, S), C(0), A.add, 1.0 / S, A.mult)
-    ts(B("qj", 0, S), B("qi", 0, S), float(S), A.mult, C(1), A.add)
-    ts(B("qk", 0, S), B("qj", 0, S), 255, A.bitwise_and)
-    cp(B("pin", 0, S), B("qk", 0, S))
-    ts(B("pout", 0, 16), B("cn", 0, 16), C(5), A.add, C(6), A.add)
+    ts(B("pin", 0, 16), B("c16", 0, 16), C(0), A.subtract)
+    ts(B("pout", 0, 16), B("cn", 0, 16), C(0), A.add)
     ts(B("rr", 0, 128), B("cb", 0, 128), C(2), A.is_equal)
     ts(B("bo", 0, 128), B("ca", 0, 128), C(3), A.is_equal)
     tt(B("id1"), B("bo", 0, 128), B("rr", 0, 128), A.mult)
-    for b in ("id1184", "id32", "id65", "idf", "id4058", "id515", "idbig"):
+    for b in ("id1184", "id32", "id65", "idf", "id4058", "id515", "idbig", "idm", "id4096", "idn4096"):
         ts(B(b), B("id1"), IDS[b], A.mult)
-    for b in ("z1", "idm", "id4096", "idn4096", "idnbig", "id2048", "id32f", "idnmid", "idn2047", "id2047", "idq", "zh"):
+    for b in ("z1", "idnbig", "id2048", "id32f", "idnmid", "idn2047", "id2047", "idq", "zh"):
         act(B(b), B("id1"), scale={"z1": 1.0, "zh": 0.5, "id32f": 1.0}.get(b) or IDS[b])
     ts(B("zm", 0, 144), B("cz", 0, 144), C(4), A.is_equal, -1.0, A.mult)
     ts(B("z2", 0, 144), B("zm", 0, 144), -2.0, A.mult)
-    ts(B("onesp"), B("cj"), 30.0, A.max, -29.0, A.add)
-    ts(B("pa_"), B("onesp"), -4.0, A.mult, 5.0, A.add)
-    ts(B("pb_"), B("onesp"), 8.0, A.mult, -8.0, A.add)
-    cp(B("jc"), B("cj"))
+    cp(X("jc"), X("cj"))
     ts(B("dum", 0, 8), B("c32", 0, 8), C(2), A.add, C(2), A.add)
-    cp(X("nx", ALL, 0), B("dum", 0, 8))
+    cp(P("nx", 0, 0), B("dum", 0, 8))
     ts(B("sp4", 0, 8), B("dum", 0, 8), 4.0, A.mult, -1.0, A.add)
     fill(B("w", 0, EQ), 1.0)
     for c in range(8):
@@ -348,11 +334,9 @@ def rank_program(g, core, T, topo):
         ts(B("w", o, o + 16), B("rr", 0, 16), B("sp4", c, c + 1), A.mult, 1.0, A.add)
     fill(ST("w", 0, EQ, 146), 0.0)
     fill(ST("w", S, EQ, 162), 0.0)
-    fill(B("aa1", L, L + 1), 0.0)
-    fill(B("bb1", L, L + 1), 0.0)
 
     def turn_in(o, src):
-        cp(o, ind(B(src, 0, 256), B("pin", 0, S)))
+        cp(B(o, 0, 256), ind(B(src, 0, 256), B("pin", 0, 16)))
 
     def views(t):
         for k in (0, 1):
@@ -360,104 +344,86 @@ def rank_program(g, core, T, topo):
         act(X("vexp", ALL, slice(2, 4), ALL), X("vexp", ALL, slice(0, 2), ALL))
         group([(B("b0", 0, 512), B("z1"), X("vexp"))])
 
-    def lists(t, ysrc):
+    def lists(t, xsrc, ysrc):
         gg = "g%d" % (t % 2)
-        cp(B("offx"), B(gg))
-        ts(B("f8", 0, 2 * L), B(gg, 0, 2 * L), 2047.0, A.not_equal, -8.0, A.mult)
-        tt(B("pp"), B(gg), ysrc, A.mult)
-        psum("b3", L, [("idbig", "f8", L, ""), ("id4058", "ones", 0, ""), ("id515", "ones", 0, ""), ("id65", gg, 0, "n"),
+        cp(B("offx"), xsrc)
+        ts(P("f8", 0, WHOLE), P(gg, 0, WHOLE), 2047.0, A.not_equal, -8.0, A.mult)
+        ts(P("f8", 1), P(gg, 1), 2047.0, A.not_equal, -8.0, A.mult)
+        tt(B("pp"), P(gg), ysrc, A.mult)
+        psum("b3", 1, [("idbig", "f8", 1, ""), ("id4058", "ones", 0, ""), ("id515", "ones", 0, ""), ("id65", gg, 0, "n"),
                        ("idf", gg, 0, "n")])
-        psum("b3", 0, [("id1184", gg, 0, ""), ("id32", gg, L, "")])
-        tt(X("qyi"), B("b3", L, 2 * L), B(gg, L, 2 * L), A.max)
-        tt(X("nxi"), B("b3"), B("pp"), A.add)
-        ts(X("qyj"), X("qyi"), 2047, A.bitwise_and)
-        ts(X("nxj"), X("nxi"), 5, A.arith_shift_right, 2047, A.bitwise_and)
-        cp(X("qy"), X("qyj"))
-        cp(B("offy"), X("qy"))
-        cp(B("offn"), X("nxj"))
-        cp(X("nx", ALL, slice(1, S)), X("nxj", ALL, slice(1, S)))
+        psum("b3", 0, [("id1184", gg, 0, ""), ("id32", gg, 1, "")])
+        tt(B("qyi"), P("b3", 1), P(gg, 1), A.max)
+        tt(B("nxi"), P("b3"), B("pp"), A.add)
+        ts(B("qyj"), B("qyi"), 2047, A.bitwise_and)
+        ts(B("nxj"), B("nxi"), 5, A.arith_shift_right, 2047, A.bitwise_and)
+        cp(B("offy"), B("qyj"))
+        cp(B("offn"), B("nxj"))
+        cp(P("qy"), B("offy"))
+        cp(P("nx"), B("offn"))
 
     def count(t):
-        o = B("b2", L, L + 8)
-        group([(o, B("id32f"), B("svn", 8 * t, 8 * t + 8))] + [(o, B("rr", 0, 128), ST("nm", s, L, S)) for s in range(1, S)])
+        o = P("b2", 1, 0)
+        group([(o, B("id32f"), B("svn", 8 * t, 8 * t + 8))] + [(o, B("rr", 0, 128), ST("nm", s, 8 * S, S)) for s in range(1, S)])
         act(B("tex", 0, 8), o, scale=-1.0, bias=128.0)
 
     def thresholds(t):
         for c in range(8):
             seg = slice(c, 16, 8)
-            act(X("tht", seg, ALL), X(("tha", "thb")[t % 2], seg, ALL), bias=B("tex", c, c + 1), func=F.Identity)
-        ts(B("an", 0, 2 * L), B("aa%d" % (t % 2), 0, 2 * L), 2047.0, A.is_equal)
-        psum("b4", 0, [("idbig", "onesp", 0, ""), ("id4096", "f8", 0, ""), ("idn4096", "f8", L, ""), ("id32f", "tht", 0, ""),
+            act(X("tht", seg, PAIRS), X(("tha", "thb")[t % 2], seg, PAIRS), bias=B("tex", c, c + 1), func=F.Identity)
+        ts(P("an", 0, PAIRS, 2), P("aa%d" % (t % 2), 0, PAIRS, 2), 2047.0, A.is_equal)
+        psum("b4", 0, [("idbig", "ones", 0, ""), ("id4096", "f8", 0, ""), ("idn4096", "f8", 1, ""), ("id32f", "tht", 0, ""),
                        ("idbig", "an", 0, "")])
-        psum("b4", L, [("idbig", "onesp", 0, ""), ("id4096", "f8", L, ""), ("idn4096", "f8", 0, "n"), ("id32f", "tht", 8, ""),
-                       ("idbig", "an", L, "")])
+        psum("b4", 1, [("idbig", "ones", 0, ""), ("id4096", "f8", 1, ""), ("idn4096", "f8", 0, "n"), ("id32f", "tht", 1, ""),
+                       ("idbig", "an", 1, "")])
 
     def sources_early(t):
         aa, bb = "aa%d" % (t % 2), "bb%d" % (t % 2)
-        for k, (src, c, flag) in enumerate(((aa, L, "oy_"), (bb, 0, "ox_"), (aa, 0, "ox_"), (bb, L, "oy_"), ("qy", 0, "ty"))):
-            psum(("b7", "b6")[k // 3], L * (k % 3), [("idm", src, c, ""), ("id4096", flag, 0, "")])
-        act(B("rl", 0, 3 * L), B("b7", 0, 3 * L), bias=-2049.0, func=F.Relu)
-        act(B("rl", 3 * L, 5 * L), B("b6", 0, 2 * L), bias=-2049.0, func=F.Relu)
+        for k, (src, c, flag) in enumerate(((aa, 1, "oy_"), (bb, 0, "ox_"), (aa, 0, "ox_"), (bb, 1, "oy_"), ("qy", 0, "ty"))):
+            psum(("b7", "b6")[k // 3], k % 3, [("idm", src, c, ""), ("id4096", flag, 0, "")])
+        act(P("rl", 0, PAIRS, 3), P("b7", 0, PAIRS, 3), bias=-2049.0, func=F.Relu)
+        act(P("rl", 3, PAIRS, 2), P("b6", 0, PAIRS, 2), bias=-2049.0, func=F.Relu)
 
     def new_places(t):
         gg = "g%d" % (t % 2)
-        psum("b7", 0, [("idm", gg, L, ""), ("idn4096", "oy_", 0, ""), ("id4096", "nm", 0, "")])
-        psum("b7", L, [("idm", "nx", 0, ""), ("id4096", "u", 0, "")])
-        psum("b7", 2 * L, [("idm", gg, 0, ""), ("idn4096", "ox_", 0, "")] + [("idn4096", "pb_", 0, "")] * (t == 0)
-             + [("idn4096", "u", 0, "")])
-        act(B("rl", 5 * L, 7 * L), B("b7", 0, 2 * L), bias=-2049.0, func=F.Relu)
-        act(B("rl", 7 * L, 8 * L), B("b7", 2 * L, 3 * L), bias=2047.0, func=F.Relu)
-        ty_, tx_, tb_ = (("0", "N", ""), ("P", "", "P"), ("", "", "P"))[t]
-        psum("b6", 0, [("id2047", "ones", 0, "")] + [("idm", "rl", L * k, ty_) for k in (0, 1, 4, 5)])
-        psum("b1", 0, [("id2047", "ones", 0, ""), ("idm", "rl", 3 * L, tb_)] + [("idm", "rl", L * k, tx_) for k in (2, 6, 7)])
+        psum("b7", 0, [("id4096", "nm", 0, "f"), ("idm", gg, 1, ""), ("idn4096", "oy_", 0, "")])
+        psum("b7", 1, [("idm", "nx", 0, ""), ("id4096", "u", 0, "")])
+        psum("b7", 2, [("idm", gg, 0, ""), ("idn4096", "ox_", 0, ""), ("idn4096", "u", 0, "")])
+        act(P("rl", 5, PAIRS, 2), P("b7", 0, PAIRS, 2), bias=-2049.0, func=F.Relu)
+        act(P("rl", 7), P("b7", 2), bias=2047.0, func=F.Relu)
+        ty_, tx_, tb_ = (("0", "N", ""), ("P0", "", "P"), ("", "", "P"))[t]
+        psum("b6", 0, [("id2047", "ones", 0, "f")] + [("idm", "rl", k, ty_) for k in (0, 1, 4, 5)])
+        psum("b1", 0, [("id2047", "ones", 0, ""), ("idm", "rl", 3, tb_)] + [("idm", "rl", k, tx_) for k in (2, 6, 7)])
 
     def memories(t):
         gg = "g%d" % (t % 2)
-        psum("b4", 2 * L, [("id2047", "ox_", 0, ""), ("id2047", "oy_", 0, "P"), ("id2047", "u", 0, "")])
-        psum("b4", 0, [("id1", gg, 0, ""), ("id4096", "nm", 0, "")])
-        psum("b4", L, [("id1", gg, L, ""), ("id4096", "nm", 0, "")])
-        psum("b5", 0, [("id2047", b, 0, "") for b in ("oy_", "ox_", "ty", "ones")] + [("idn2047", "nm", 0, "")])
-        old = ["%s%d" % (m, t % 2) for m in ("aa", "bb")]
-        new = ["%s%d" % (m, 1 - t % 2) for m in ("aa", "bb")] if t < 2 else ["wa", "wb"]
-        both = list(zip(old, new, (0, L)))
-        for m, w, o in both:
-            tt(B("ab2", o, o + L), B("b4", 2 * L, 3 * L), B(m), A.max)
-        for m, w, o in both:
-            if t == 1:
-                tt(B(w, 0, L - 1), B("b5", 1, L), B(m, L + 1, 2 * L), A.max)
-            else:
-                tt(B(w, (0, 0, L)[t], (L, L, 2 * L)[t]), B("b5"), B(m, L, 2 * L), A.max)
-        for m, w, o in both:
-            if t == 0:
-                tt(B(w, L + 1, 2 * L), B("b4", o, o + L - 1), B("ab2", o, o + L - 1), A.min)
-            else:
-                tt(B(w, (0, L, 0)[t], (0, 2 * L, L)[t]), B("b4", o, o + L), B("ab2", o, o + L), A.min)
-        for m, w, o in both:
-            if t == 0:
-                tt(ST(w, L + 1, 2 * L, S), ST("b4", o + 16, o + L, S), ST("ab2", o + 16, o + L, S), A.min)
-            if t == 1:
-                tt(ST(w, 16, L, S), ST("b5", 1, L, S), ST(m, L + 1, 2 * L, S), A.max)
+        psum("b4", 2, [("id2047", "ox_", 0, ""), ("id2047", "oy_", 0, "P"), ("id2047", "u", 0, "")])
+        psum("b4", 0, [("id4096", "nm", 0, "f"), ("id1", gg, 0, "")])
+        psum("b4", 1, [("id4096", "nm", 0, "f"), ("id1", gg, 1, "")])
+        psum("b2", 2, [("idn2047", "nm", 0, "f")] + [("id2047", b, 0, "") for b in ("oy_", "ox_", "ty", "ones")])
+        for k, m in enumerate(("aa", "bb")):
+            old, new = "%s%d" % (m, t % 2), "%s%d" % (m, 1 - t % 2)
+            tt(P("ab2", k), P("b4", 2), P(old), A.max)
+            for a, b in TURNS[("", "P", "")[t]]:
+                tt(P(new, 0, a) if t < 2 else B("w" + m[0], U, 2 * U), P("b2", 2, b), P(old, 1, b), A.max)
+            for a, b in TURNS[("N", "", "")[t]]:
+                tt(P(new, 1, a) if t < 2 else B("w" + m[0]), P("b4", k, b), P("ab2", k, b), A.min)
 
     def gather(t, l):
-        for e, k, c0, c1 in GATHERS:
-            if k == l:
-                (cp if e == "V" and t else act)(B("xg", 16 * (L * l + c0), 16 * (L * l + c1)),
-                                                ind(B("tab%d" % t, 0, 2048), B(("offx", "offy", "offn")[l], c0, c1)))
-        for c in range(8):
-            for q in range(4):
-                a = 16 + 64 * q
-                o = E * (8 * l + c) + a
-                tt(X("mx", 8 * l + c, slice(a, a + 64)), B("xg", o, o + 64), B("b0", 64 * c, 64 * c + 64), A.max)
+        for c0, c1 in zip(CUTS[l], CUTS[l][1:]):
+            (cp if (l, c0) in ON_VECTOR[t] else act)(B("xg", 16 * (U * l + c0), 16 * (U * l + c1)),
+                                                     ind(B("tab%d" % t, 0, 2048), B(("offx", "offy", "offn")[l], c0, c1)))
+        for o in range(0, 16 * U, 64):
+            a, c = 16 * U * l + o, o // 256
+            tt(B("mx", a, a + 64), B("xg", a, a + 64), B("b0", 64 * c, 64 * c + 64), A.max)
 
     def half(l, c0):
-        c = 8 * l + c0
-        o, a = B("b%d" % (l + 1), S * c0, S * c0 + 4 * S), E * c
-        return ([(o, B("zm", 15 - r, 143 - r), ST("xg", a + r, a + 4 * E, 16)) for r in range(16)]
-                + [(o, B("z2", 15 - r, 143 - r), X("mx", slice(c, c + 4), slice(r, E, 16))) for r in range(16)])
+        o, a = X("b%d" % (l + 1), slice(c0, c0 + 4), PAIRS), 256 * (8 * l + c0)
+        return [(o, B(z, 15 - r, 143 - r), ST(x, a + r, a + 1024, 16)) for z, x in (("zm", "xg"), ("z2", "mx")) for r in range(16)]
 
     def scatter(tab, msg):
         w = B(tab, 0, WT)
-        note("V", [w], [B(msg)], lambda q: q.tensor_copy(out=w[0].indirect(T[msg][:, 128:L]), in_=T[msg][:, 0:128]),
+        note("V", [w], [B(msg, 0, M)], lambda q: q.tensor_copy(out=w[0].indirect(T[msg][:, 128:M]), in_=T[msg][:, 0:128]),
              CYC * (60 + 3.8 * 128))
 
     peer = {d: T.cores[(rank + d) % n] for d in (1, 2, -1, -2)}
@@ -466,11 +432,11 @@ def rank_program(g, core, T, topo):
     def send(d, slot, msg):
         dst = peer[d]
         rid, pid = topo.addr(dst, core)
-        k = remote([B(msg)], lambda q: q.remote_dma(out_ap=T[slot][:, :], in_ap=T[msg][:, :], remote_sem=T.sem[slot + "_"],
-                                                    local_sem=T.sem.ls, pid=pid, routing_id=rid,
-                                                    dma_engine_mask=topo.mask(core, dst)))
+        k = remote([B(msg, 0, M)], lambda q: q.remote_dma(out_ap=T[slot][:, :], in_ap=T[msg][:, :], remote_sem=T.sem[slot + "_"],
+                                                          local_sem=T.sem.ls, pid=pid, routing_id=rid,
+                                                          dma_engine_mask=topo.mask(core, dst)))
         sent[0] += len(topo.engines(core, dst))
-        arrives([B(slot)], [], slot + "_", len(topo.engines(peer[-d], core)), k, WAY)
+        arrives([B(slot, 0, M)], [], slot + "_", len(topo.engines(peer[-d], core)), k, WAY)
 
     def send_table():
         cs, he = carriers(rank, T, topo), hand_engines(rank, T, topo)
@@ -482,69 +448,74 @@ def rank_program(g, core, T, topo):
         hands = [tr(cs[k], he[k - 1][0], "hd", "hand", k, 0) for k in range(1, len(cs))]
         own = [tr(peer[-d], topo.mask(core, peer[-d]), "t%d" % d, "tab%d" % d, 0, 0) for d in (1, 2)]
         tab = B("tab0", 0, 2048)
-        remote([tab], lambda q: q.remote_dma_fused(hands[:2] + own[:1], local_sem=T.sem.tl))
-        k = remote([tab], lambda q: q.remote_dma_fused(hands[2:] + own[1:], local_sem=T.sem.tl))
+        k = remote([tab], lambda q: q.remote_dma_fused(hands[:2] + own[:1], local_sem=T.sem.tl))
+        k = remote([tab], lambda q: q.remote_dma_fused(hands[2:] + own[1:], local_sem=T.sem.tl), [k])
         gone = sum(h[1] for h in he) + len(topo.engines(core, peer[-1])) + len(topo.engines(core, peer[-2]))
         arrives([], [tab], "tl", gone, k, COPY)
         for d in (1, 2):
             arrives([B("tab%d" % d, 0, WT)], [], "t%d" % d,
-                    sum(len(topo.engines(c, core)) for c in carriers((rank + d) % n, T, topo)), k, COPY * d)
+                    sum(len(topo.engines(c, core)) for c in carriers((rank + d) % n, T, topo)), k, COPY + 6 * d)
 
-    turn_in(B("g0", 0, 2 * L), "gli")
-    lists(0, B("g0", L, 2 * L))
+    turn_in("ing", "gli")
+    cp(P("g0", 0, PAIRS, 2), B("ing", 0, 256))
+    cp(P("g0", 0, 0), ST("ing", 15, U, 16))
+    lists(0, B("ing"), P("g0", 1))
     views(0)
     send_table()
-    group([(B("b2", L, L + 24), B("zm", 15 - r, 143 - r), ST("yvs", r, 384, 16)) for r in range(16)])
-    act(B("svn", 0, 24), B("b2", L, L + 24))
+    sums = X("b4", slice(0, 24), 0)
+    group([(sums, B("zm", 15 - r, 143 - r), ST("yvs", r, 384, 16)) for r in range(16)])
+    act(B("svn", 0, 24), sums)
     act(B("tex", 0, 8), B("svn", 0, 8), scale=-1.0)
-    turn_in(B("th2", 0, 2 * L), "thi")
-    act(X("tha"), B("th2", 0, 2 * L))
-    act(X("thb", slice(0, 8), ALL), X("tha", slice(8, 16), ALL))
-    act(X("thb", slice(8, 16), slice(1, S)), X("tha", slice(0, 8), slice(0, 16)))
-    act(X("thb", slice(8, 16), 0), X("tha", slice(0, 8), 0))
-    turn_in(B("aa0", 0, 2 * L), "ali")
-    turn_in(B("bb0", 0, 2 * L), "bli")
+    turn_in("th2", "thi")
+    cp(P("tha", 0, PAIRS, 2), B("th2", 0, 256))
+    act(P("thb"), P("tha", 1))
+    for a, b in TURNS["N"]:
+        act(P("thb", 1, a), P("tha", 0, b))
+    for m in "ab":
+        turn_in("in" + m, m + "li")
+        cp(P(m + m + "0", 0, PAIRS, 2), B("in" + m, 0, 256))
 
     def visit(t):
         s = t % 2
         gg, tab, msg = "g%d" % s, "tab%d" % t, "m%d" % t
         thresholds(t)
-        for k, (src, c) in enumerate((("nx", 0), (gg, 0), (gg, L))):
-            psum("b5", L * k, [("id1", src, c, ""), ("id2048", "jc", 0, "")])
-        psum("b1", L, [("idbig", "ones", 0, ""), ("id4096", "f8", 0, ""), ("idnbig", "pb_", 0, "")])
+        keys = [B("b5", 8 * S * k, 8 * S * (k + 1)) for k in range(3)]
+        for o, src in zip(keys, (X("nx"), P(gg, 0, WHOLE), P(gg, 1, WHOLE))):
+            group([(o, B("id2048"), X("jc")), (o, B("id1"), src)])
+        psum("b1", 1, [("idbig", "ones", 0, ""), ("id4096", "f8", 0, "")])
         gather(t, 0)
         group(half(0, 0))
         group(half(0, 4))
-        cp(B("sgx"), B("b1"))
-        cp(ST("sgx", 0, L, S), ST("b1", 16, L, S))
-        tt(B("ox_"), B("sgx"), B("b4"), A.is_gt)
-        psum("b6", 2 * L, [("idnbig", "onesp", 0, ""), ("id4096", "f8", L, ""), ("idn4096", "f8", 0, "n"), ("id32f", "sgx", 0, "n"),
-                           ("idnbig", "ox_", 0, "")])
+        cp(P("sgx"), P("b1"))
+        cp(P("sgx", 0, 0), P("b1", 0, 16))
+        tt(P("ox_"), P("sgx"), P("b4"), A.is_gt)
+        psum("b6", 2, [("idnbig", "ones", 0, ""), ("id4096", "f8", 1, ""), ("idn4096", "f8", 0, "n"), ("id32f", "sgx", 0, "n"),
+                       ("idnbig", "ox_", 0, "")])
         gather(t, 1)
         group(half(1, 0))
         group(half(1, 4))
-        cp(B("sqy"), B("b2"))
-        tt(B("oy_"), B("sqy"), B("b4", L, 2 * L), A.is_gt)
-        tt(B("ty"), B("sqy"), B("b6", 2 * L, 3 * L), A.is_lt)
-        psum("b1", 0, [("id32f", "sgx", 0, ""), ("idnbig", "pb_", 0, ""), ("idnmid", "oy_", 0, "")])
-        tt(B("mnu"), B("b1"), B("sqy"), A.min)
-        tt(B("mnm"), B("mnu"), B("b1", L, 2 * L), A.subtract)
+        cp(B("sqy"), P("b2"))
+        tt(P("oy_"), B("sqy"), P("b4", 1), A.is_gt)
+        tt(P("ty"), B("sqy"), P("b6", 2), A.is_lt)
+        psum("b1", 0, [("id32f", "sgx", 0, ""), ("idnmid", "oy_", 0, "")])
+        tt(B("mnu"), P("b1"), B("sqy"), A.min)
+        tt(P("mnm"), B("mnu"), P("b1", 1), A.subtract)
         sources_early(t)
         gather(t, 2)
-        group(terms("b3", 0, [("idbig", "pa_", 0, ""), ("id4096", "f8", L, "")]) + half(2, 0)
+        group(terms("b3", 0, [("idbig", "ones", 0, "f"), ("id4096", "f8", 1, "")]) + half(2, 0)
               + terms("b3", 0, [("idbig", "oy_", 0, "P")]) + half(2, 4))
-        tt(B("nm"), B("b3"), B("mnm"), A.is_ge)
-        tt(B("u"), B("b3"), B("mnu"), A.is_lt)
+        tt(X("nm"), P("b3", 0, WHOLE), X("mnm"), A.is_ge)
+        tt(P("u"), P("b3"), B("mnu"), A.is_lt)
         for k in range(3):
-            scan(B("s3", L * k, L * k + L), B("nm"), B("b5", L * k, L * k + L), A.mult, A.max)
+            scan(B("s3", 8 * S * k, 8 * S * (k + 1)), X("nm"), keys[k], A.mult, A.max)
         for lo, hi in ((0, 8), (8, 24)):
             ts(B("gi", lo, hi), ST("s3", S * lo + 16, S * hi, S), 4095, A.bitwise_and)
             cp(B("goff", lo, hi), B("gi", lo, hi))
         cp(B("gf", 0, 8), B("gi", 0, 8))
+        halves = P("b3", 2)
         act(B("xv", 0, 256), ind(B(tab, 0, 2048), B("goff", 8, 24)))
-        group([(B("b3", 2 * L, 2 * L + 128), B("idq"), B("ones", 0, 128))]
-              + [(B("b3", 2 * L, 2 * L + 128), B("zh"), B("xv", o, o + 128)) for o in (0, 128)])
-        cp(B(msg, 0, 128), B("b3", 2 * L, 2 * L + 128))
+        group([(halves, B("idq"), P("ones"))] + [(halves, B("zh"), B("xv", o, o + 128)) for o in (0, 128)])
+        cp(B(msg), halves)
         cp(B("bf", 0, 128), ind(B("iw", 0, WT), B("goff", 0, 8)))
         cp(ST("eq", 16, 503, 162), B("gi", 0, 4))
         cp(ST("eq", 583, 144, -146), B("gi", 4, 8))
@@ -563,9 +534,9 @@ def rank_program(g, core, T, topo):
             hh = "g%d" % (1 - s)
             views(t + 1)
             count(t + 1)
-            act(B(hh), B("b6"))
-            act(B(hh, L, 2 * L), B("b1"))
-            lists(t + 1, B("b1"))
+            act(P(hh, 0, WHOLE), P("b6", 0, WHOLE))
+            act(P(hh, 1), P("b1"))
+            lists(t + 1, P(hh), P("b1"))
         for into, m in ((("tab1", "a1"), ("tab0", "m0"), ("tab2", "a2")), (("tab2", "e2"), ("tab0", "e0")), (("tab0", "c0"),))[t]:
             scatter(into, m)
         if t == 1:
@@ -574,10 +545,10 @@ def rank_program(g, core, T, topo):
     for t in range(3):
         visit(t)
     dma("Y", "sox", [], [B("tab0", 0, 2048)], T.ox[:, :], T.tab0[:, 0:2048], STORE)
-    act(B("wg"), B("b1"))
-    act(B("wg", L, 2 * L), B("b6"))
+    act(B("wg"), P("b1"))
+    act(B("wg", U, 2 * U), P("b6"))
     for w, b, q, sm in (("wg", "ogs", T.og, "sog"), ("wa", "oas", T.oa, "soa"), ("wb", "obs", T.ob, "sob")):
-        act(B(b, 0, 256), ind(B(w, 0, 2 * L), B("pout", 0, 16)))
+        act(B(b, 0, 256), ind(B(w, 0, 256), B("pout", 0, 16)))
         dma("S", sm, [], [B(b, 0, 256)], q[:, :], T[b][:, :], STORE)
 
     cnt = issue()

@@ -9,15 +9,14 @@ M = 136
 NONE = 2047
 WT = 2048 + 256
 BIG = 32768.0
-MID = 6144.0
 FAR = 1024.0
 EQ = 584
-CUTS = ((0, 32, 64, 128), (0, 64, 128), (0, 64, 96, 120, 128))
-ON_VECTOR = (((0, 0),), ((0, 0), (0, 32)), ((0, 0), (0, 32)))
-IDS = {"id1": 1.0, "id1184": 1184.0, "id32": 32.0, "id65": 65.0, "idf": -1.0 / 32, "id4058": 4058.0, "id515": 33.0 / 64,
-       "idbig": BIG, "idm": -1.0, "idnbig": -BIG, "id4096": 4096.0, "idn4096": -4096.0, "idnmid": -MID, "id2047": 2047.0,
-       "id2048": 2048.0, "idn2047": -2047.0, "idq": -0.25}
-CYC, PCYC, WAKE, ISSUE, WAY, LOAD, COPY, STORE = 0.00083, 0.00045, 0.15, 0.3, 2.0, 3.2, 8.0, 3.0
+CUTS = ((0, 32, 64, 128), (0, 64, 128), (0, 32, 64, 96, 112, 128))
+ON_VECTOR = ((), ((0, 0), (0, 32), (2, 112)), ((0, 0), (0, 32), (2, 112)))
+IDS = {"id1": 1.0, "id1184": 1184.0, "id32": 32.0, "id65": 65.0, "idf": -1.0 / 32, "id217": 217.0,
+       "idbig": BIG, "idm": -1.0, "idnbig": -BIG, "id4096": 4096.0, "idn4096": -4096.0, "idn512": -512.0, "id2047": 2047.0,
+       "id2048": 2048.0, "idn2047": -2047.0}
+CYC, PCYC, WAKE, ISSUE, WAY, LOAD, COPY, STORE = 0.00083, 0.00053, 0.18, 0.3, 2.3, 2.6, 8.0, 3.0
 
 SCRATCH = {}
 
@@ -28,19 +27,19 @@ def _add(where, dtype, **kw):
 
 
 L1, L2 = [8, S], [16, S]
-_add("sbuf", "bfloat16", tab0=WT, tab1=WT, tab2=WT, hand=512, xsav=16, yvs=384, vexp=[8, 4, 16], z1=128, z2=144, zm=144,
+_add("sbuf", "bfloat16", tab0=WT, tab1=WT, tab2=WT, hand1=512, hand2=512, xsav=16, yvs=384, vexp=[8, 64], z1=128, z2=144, zm=144,
      zh=128, xv=256, xg=48 * U, mx=48 * U)
 _add("sbuf", "int32", gli=256, ali=256, bli=256, thi=256, pidx=8, p15=8, p4=8, nxi=U, nxj=U, qyi=U, qyj=U, gi=24, s3=24 * S)
-_add("sbuf", "uint16", offx=U, offy=U, offn=U, goff=24, pin=16, pout=16, m0=M, m1=M, m2=M, a1=M, a2=M, e2=M, e0=M, c0=M)
+_add("sbuf", "uint16", offx=U, offy=U, offn=U, goff=24, pin=16, pout=16, m0=M, m1=M, m2=M, a1=M, e2=M, e0=M, c0=M)
 _add("sbuf", "float16", g0=L2, g1=L2, aa0=L2, aa1=L2, bb0=L2, bb1=L2, ab2=L2, f8=L2, an=L2, qy=L1, nx=L1, ones=L1, jc=L1,
-     ox_=L1, oy_=L1, ty=L1, nm=8 * S, u=L1, rl=[64, S], ing=256, ina=256, inb=256, rr=128, bo=128, ids=128 * len(IDS), bf=128,
+     kq=U, op=L2, ty=L1, near=L1, oyf=L1, nm=8 * S, cnt=8 * S, cnb=8 * S, rs=8 * S, rm=128, u=L1, rl=[64, S], ing=256, ina=256, inb=256, rr=128, bo=128, ids=128 * len(IDS), bf=128,
      eq=EQ, w=EQ, sc=EQ)
 _add("sbuf", "float32", th2=256, id32f=128, ca=128, cb=128, cz=144, cj=8 * S, c16=16, c32=8, cn=16, col=16,
-     dum=8, sp4=8, iw=WT, sgx=L1, sqy=U, mnu=U, mnm=L1, tex=8, svn=24, tha=L2, thb=L2, tht=L2, pp=U, gf=8,
+     dum=8, sp4=8, iw=WT, sgx=L1, mnu=U, mnm=L1, tex=24, thr=2 * U, tha=L2, thb=L2, tht=L2, pp=U, gf=8,
      wg=256, wa=256, wb=256, ogs=256, oas=256, obs=256)
-_add("psum", "float32", b0=512, b5=512, **{"b%d" % k: [30, S] for k in (1, 2, 3, 4, 6, 7)})
-SEMAPHORES = ["pv", "pa", "pt", "pg", "dg", "dy", "dx", "ds", "da", "db", "dt", "sog", "soa", "sob", "sox", "tl", "ls", "hd",
-              "t1", "t2"] + [s + "_" for s in ("a1", "a2", "e2", "e0", "c0")]
+_add("psum", "float32", b0=512, b5=512, b7=512, **{"b%d" % k: [30, S] for k in (1, 2, 3, 4, 6)})
+SEMAPHORES = ["pv", "pa", "pt", "pg", "dg", "dy", "dx", "ds", "da", "db", "dt", "sog", "soa", "sob", "sox", "tl", "ls", "h1",
+              "h2", "t1", "t2"] + [s + "_" for s in ("a1", "e2", "e0", "c0")]
 PART = {k: ("ids", 128 * j) for j, k in enumerate(IDS)}
 PART.update(id32f=("id32f", 0), z1=("z1", 0), zh=("zh", 0))
 COLS = {k: np.arange(int(np.prod(v[1][1:]))).reshape(v[1][1:]) for k, v in SCRATCH.items()}
@@ -60,11 +59,11 @@ def carriers(rank, T, topo):
 
 
 def hand_engines(rank, T, topo):
-    own = T.cores[rank]
+    own, cs = T.cores[rank], carriers(rank, T, topo)
     out = topo.engines(own, T.cores[(rank - 1) % len(T.cores)])
-    e = [x for x in topo.engines(own, carriers(rank, T, topo)[1]) if x not in out]
-    h = len(e) // 2
-    return [(sum(1 << x for x in p), len(p)) for p in (e[:h], e[h:], e)]
+    e = out + [x for x in topo.engines(own, cs[1]) if x not in out]
+    h = len(e) // len(cs)
+    return [(sum(1 << x for x in e[k * h:k * h + h]), h) for k in range(len(cs))]
 
 
 def helper_program(g, core, T, topo):
@@ -73,12 +72,12 @@ def helper_program(g, core, T, topo):
         cs = carriers(rank, T, topo)
         if core in cs[1:]:
             k, w = cs.index(core), 2048 // len(cs)
-            g.wait_ge(T.sem.hd, hand_engines(rank, T, topo)[k - 1][1])
             sent = 0
             for d in (1, 2):
                 dst = T.cores[(rank - d) % n]
                 rid, pid = topo.addr(dst, core)
-                g.remote_dma(out_ap=T["tab%d" % d][:, k * w:k * w + w], in_ap=T.hand[:, 0:w], remote_sem=T.sem["t%d" % d],
+                g.wait_ge(T.sem["h%d" % d], hand_engines(rank, T, topo)[k][1])
+                g.remote_dma(out_ap=T["tab%d" % d][:, k * w:k * w + w], in_ap=T["hand%d" % d][:, 0:w], remote_sem=T.sem["t%d" % d],
                              local_sem=T.sem.ls, pid=pid, routing_id=rid, dma_engine_mask=topo.mask(core, dst))
                 sent += len(topo.engines(core, dst))
             g.wait_ge(T.sem.ls, sent)
@@ -138,7 +137,7 @@ def rank_program(g, core, T, topo):
     n = len(T.cores)
     Q = {"V": g.vector, "S": g.scalar, "P": g.tensor, "G": g, "Y": g.sync}
 
-    ops, writer, readers, bank = [], {}, {}, {}
+    ops, writer, readers, bank, gathered, first, hold = [], {}, {}, {}, [], [], []
 
     def note(e, outs, ins, call, cost, tail=0.0, sem=None, deps=(), behind=()):
         k, deps = len(ops), set(deps)
@@ -166,7 +165,8 @@ def rank_program(g, core, T, topo):
                 rec[:] = [e, [], rec[1]]
             deps.update(rec[2] + (rec[1][-1:] if e == "P" else []))
             rec[1].append(k)
-        ops.append({"e": e, "deps": sorted(deps - {-1, k}), "call": call, "cost": cost, "tail": tail, "sem": sem, "behind": behind})
+        ops.append({"e": e, "deps": sorted(deps - {-1, k}), "call": call, "cost": cost, "tail": tail, "sem": sem,
+                    "behind": list(behind) + hold})
         return k
 
     def issue():
@@ -211,7 +211,12 @@ def rank_program(g, core, T, topo):
         return X(b, slice(lo, hi, step))
 
     def P(b, k=0, cols=PAIRS, lists=1):
+        if COLS[b].ndim == 1:
+            return B(b, U * k, U * (k + lists))
         return X(b, slice(8 * k, 8 * (k + lists)), cols)
+
+    def memory(t, m):
+        return "in" + m if t == 0 else "%s%s%d" % (m, m, t % 2)
 
     def ind(w, o):
         return (w[0].indirect(o[0]), w[1] + o[1])
@@ -224,8 +229,9 @@ def rank_program(g, core, T, topo):
             return max(64, k * (1 if any(SCRATCH[v[1][0][0]][0] == "psum" for v in ins) else 2))
         return max(64, k * (1 if any(WIDE[v[1][0][0]] for v in [o] + ins) else 0.5))
 
-    def tt(o, a, b, op):
-        note("V", [o], [a, b], lambda q: q.tensor_tensor(out=o[0], in0=a[0], in1=b[0], op=op), CYC * cycles(o, [a, b], True))
+    def tt(o, a, b, op, behind=()):
+        return note("V", [o], [a, b], lambda q: q.tensor_tensor(out=o[0], in0=a[0], in1=b[0], op=op),
+                    CYC * cycles(o, [a, b], True), behind=behind)
 
     def ts(o, a, s1, op0, s2=None, op1=None):
         cols = [s for s in (s1, s2) if isinstance(s, tuple)]
@@ -244,12 +250,12 @@ def rank_program(g, core, T, topo):
         note("V", [o], [d0, d1], lambda q: q.tensor_tensor_scan(out=o[0], data0=d0[0], data1=d1[0], initial=0.0, op0=op0, op1=op1),
              CYC * cycles(o, [d0, d1]))
 
-    def act(o, a, scale=1.0, bias=0.0, func=F.Copy):
+    def act(o, a, scale=1.0, bias=0.0, func=F.Copy, behind=()):
         cols = [s for s in (scale, bias) if isinstance(s, tuple)]
         x, y = [s[0] if isinstance(s, tuple) else s for s in (scale, bias)]
         k = len(o[1][0][1])
         note("S", [o], [a] + cols, lambda q: q.activation(out=o[0], in_=a[0], func=func, bias=y, scale=x),
-             CYC * (80 + 1.56 * k if len(a[1]) > 1 else max(64, k)))
+             CYC * (80 + 1.56 * k if len(a[1]) > 1 else 80 + max(64, k)), behind=behind)
 
     def matmul(o, l, r, start, stop):
         note("P", [o], [l, r], lambda q: q.matmul(out=o[0], lhsT=l[0], rhs=r[0], start=start, stop=stop),
@@ -268,9 +274,9 @@ def rank_program(g, core, T, topo):
     def dma(q, sem, outs, ins, out, in_, time, behind=()):
         return note(q, outs, ins, lambda e: e.dma_start(out=out, in_=in_), 0.05, time, (sem, 16), behind=behind)
 
-    def iota(o, pattern, base, cm):
+    def iota(o, pattern, base, cm, behind=()):
         more = {"allow_small_or_imprecise_dtypes": True} if SCRATCH[o[1][0][0]][2] == "float32" else {}
-        note("G", [o], [], lambda q: q.iota(o[0], pattern, base, cm, **more), 0.13 + 2 * CYC * len(o[1][0][1]))
+        note("G", [o], [], lambda q: q.iota(o[0], pattern, base, cm, **more), 0.13 + 2 * CYC * len(o[1][0][1]), behind=behind)
 
     def remote(ins, call, behind=()):
         def run(q):
@@ -281,9 +287,9 @@ def rank_program(g, core, T, topo):
         note("D", outs, ins, None, 0.0, time, (sem, val), [since])
 
     fill(B("tab0", 2032, 2048), FAR)
-    k = dma("Y", "dg", [B("gli", 0, 256)], [], T.gli[:, :], T.gl[:, :], LOAD - 1.2)
-    dma("S", "dx", [B("tab0", 0, 2048)], [], T.tab0[:, 0:NONE], T.xt[:, 0:NONE], LOAD)
-    k = dma("Y", "dy", [B("yvs", 0, 384)], [], T.yvs[:, :], T.yv[:, :], LOAD - 1.0, [k])
+    k = dma("Y", "dg", [B("gli", 0, 256)], [], T.gli[:, :], T.gl[:, :], LOAD - 0.9)
+    k = dma("Y", "dy", [B("yvs", 0, 384)], [], T.yvs[:, :], T.yv[:, :], LOAD - 0.7, [k])
+    k = dma("Y", "dx", [B("tab0", 0, 2048)], [], T.tab0[:, 0:NONE], T.xt[:, 0:NONE], LOAD, [k])
     for sem, b, src in (("dt", "thi", T.th), ("da", "ali", T.al), ("db", "bli", T.bl)):
         k = dma("Y", sem, [B(b, 0, 256)], [], T[b][:, :], src[:, :], LOAD + 0.8, [k])
     dma("Y", "ds", [B("xsav", 0, 2)], [], T.xsav[:, 0:2], T.xt[:, NONE - 1:NONE + 1], LOAD + 0.8, [k])
@@ -302,8 +308,8 @@ def rank_program(g, core, T, topo):
     iota(B("cz", 0, 144), [[1, 144]], -15, 0)
     iota(B("c32", 0, 8), [[32, 8]], 2048, 0)
     iota(B("cn", 0, 16), [[-1, 16]], 15, 0)
-    iota(B("iw", 0, WT), [[1, WT]], 0, 0)
     fill(X("ones"), 1.0)
+    fill(X("kq"), 1801.0 / 64)
     fill(P("mnm", 0, 0), 4 * BIG)
     for b in ("g0", "g1"):
         fill(P(b, 1, 0), 0.0)
@@ -318,10 +324,12 @@ def rank_program(g, core, T, topo):
     ts(B("rr", 0, 128), B("cb", 0, 128), C(2), A.is_equal)
     ts(B("bo", 0, 128), B("ca", 0, 128), C(3), A.is_equal)
     tt(B("id1"), B("bo", 0, 128), B("rr", 0, 128), A.mult)
-    for b in ("id1184", "id32", "id65", "idf", "id4058", "id515", "idbig", "idm", "id4096", "idn4096"):
+    for b in ("id1184", "id32", "id65", "idf", "id217", "idbig", "idm", "id4096", "idn4096"):
         ts(B(b), B("id1"), IDS[b], A.mult)
-    for b in ("z1", "idnbig", "id2048", "id32f", "idnmid", "idn2047", "id2047", "idq", "zh"):
+    for b in ("z1", "idnbig", "id2048", "idn512", "idn2047", "id2047", "zh"):
         act(B(b), B("id1"), scale={"z1": 1.0, "zh": 0.5, "id32f": 1.0}.get(b) or IDS[b])
+    ts(B("rm"), B("rr"), -1.0, A.mult)
+    ts(X("rs"), X("cj"), 32.0, A.not_equal)
     ts(B("zm", 0, 144), B("cz", 0, 144), C(4), A.is_equal, -1.0, A.mult)
     ts(B("z2", 0, 144), B("zm", 0, 144), -2.0, A.mult)
     cp(X("jc"), X("cj"))
@@ -329,29 +337,31 @@ def rank_program(g, core, T, topo):
     cp(P("nx", 0, 0), B("dum", 0, 8))
     ts(B("sp4", 0, 8), B("dum", 0, 8), 4.0, A.mult, -1.0, A.add)
     fill(B("w", 0, EQ), 1.0)
-    for c in range(8):
-        o = start_of(c) + 16 * c
-        ts(B("w", o, o + 16), B("rr", 0, 16), B("sp4", c, c + 1), A.mult, 1.0, A.add)
-    fill(ST("w", 0, EQ, 146), 0.0)
-    fill(ST("w", S, EQ, 162), 0.0)
+
+    def weights():
+        for c in range(8):
+            o = start_of(c) + 16 * c
+            ts(B("w", o, o + 16), B("rr", 0, 16), B("sp4", c, c + 1), A.mult, 1.0, A.add)
+        fill(ST("w", 0, EQ, 146), 0.0)
+        fill(ST("w", S, EQ, 162), 0.0)
 
     def turn_in(o, src):
         cp(B(o, 0, 256), ind(B(src, 0, 256), B("pin", 0, 16)))
 
     def views(t):
-        for k in (0, 1):
-            act(X("vexp", ALL, k, ALL), B("yvs", t * 128, t * 128 + 128))
-        act(X("vexp", ALL, slice(2, 4), ALL), X("vexp", ALL, slice(0, 2), ALL))
+        for k in (0, 16):
+            act(X("vexp", ALL, slice(k, k + 16)), B("yvs", t * 128, t * 128 + 128), behind=gathered[-1:])
+        act(X("vexp", ALL, slice(32, 64)), X("vexp", ALL, slice(0, 32)))
         group([(B("b0", 0, 512), B("z1"), X("vexp"))])
 
     def lists(t, xsrc, ysrc):
         gg = "g%d" % (t % 2)
-        cp(B("offx"), xsrc)
+        if t:
+            cp(B("offx"), xsrc)
         ts(P("f8", 0, WHOLE), P(gg, 0, WHOLE), 2047.0, A.not_equal, -8.0, A.mult)
         ts(P("f8", 1), P(gg, 1), 2047.0, A.not_equal, -8.0, A.mult)
         tt(B("pp"), P(gg), ysrc, A.mult)
-        psum("b3", 1, [("idbig", "f8", 1, ""), ("id4058", "ones", 0, ""), ("id515", "ones", 0, ""), ("id65", gg, 0, "n"),
-                       ("idf", gg, 0, "n")])
+        psum("b3", 1, [("idbig", "f8", 1, ""), ("id217", "kq", 0, ""), ("id65", gg, 0, "n"), ("idf", gg, 0, "n")])
         psum("b3", 0, [("id1184", gg, 0, ""), ("id32", gg, 1, "")])
         tt(B("qyi"), P("b3", 1), P(gg, 1), A.max)
         tt(B("nxi"), P("b3"), B("pp"), A.add)
@@ -363,71 +373,80 @@ def rank_program(g, core, T, topo):
         cp(P("nx"), B("offn"))
 
     def count(t):
-        o = P("b2", 1, 0)
-        group([(o, B("id32f"), B("svn", 8 * t, 8 * t + 8))] + [(o, B("rr", 0, 128), ST("nm", s, 8 * S, S)) for s in range(1, S)])
-        act(B("tex", 0, 8), o, scale=-1.0, bias=128.0)
+        back = slice(8 * S - 1, None, -1)
+        scan(X("cnt"), X("rs"), X("nm"), A.mult, A.add)
+        scan(X("cnb", back), X("rs"), X("cnt", back), A.mult, A.max)
 
     def thresholds(t):
         for c in range(8):
             seg = slice(c, 16, 8)
-            act(X("tht", seg, PAIRS), X(("tha", "thb")[t % 2], seg, PAIRS), bias=B("tex", c, c + 1), func=F.Identity)
-        ts(P("an", 0, PAIRS, 2), P("aa%d" % (t % 2), 0, PAIRS, 2), 2047.0, A.is_equal)
-        psum("b4", 0, [("idbig", "ones", 0, ""), ("id4096", "f8", 0, ""), ("idn4096", "f8", 1, ""), ("id32f", "tht", 0, ""),
-                       ("idbig", "an", 0, "")])
-        psum("b4", 1, [("idbig", "ones", 0, ""), ("id4096", "f8", 1, ""), ("idn4096", "f8", 0, "n"), ("id32f", "tht", 1, ""),
-                       ("idbig", "an", 1, "")])
+            o, a, x = X("tht", seg, PAIRS), X(("tha", "thb")[t % 2], seg, PAIRS), B("tex", 8 * t + c, 8 * t + c + 1)
+            if t:
+                act(o, a, bias=x, func=F.Identity, behind=first[-1:])
+            else:
+                ts(o, a, x, A.add)
+        ts(P("an", 0, PAIRS, 2), P(memory(t, "a"), 0, PAIRS, 2), 2047.0, A.is_equal)
+        for k, turn in enumerate(("", "n")):
+            group([(P("b4", k, WHOLE), B("rm"), X("cnb"))] * (t > 0)
+                  + terms("b4", k, [("idbig", "an", k, ""), ("id4096", "f8", k, ""), ("idn4096", "f8", 1 - k, turn)]))
+        tt(B("thr", 0, 2 * U), P("b4", 0, PAIRS, 2), P("tht", 0, PAIRS, 2), A.add)
 
     def sources_early(t):
-        aa, bb = "aa%d" % (t % 2), "bb%d" % (t % 2)
-        for k, (src, c, flag) in enumerate(((aa, 1, "oy_"), (bb, 0, "ox_"), (aa, 0, "ox_"), (bb, 1, "oy_"), ("qy", 0, "ty"))):
-            psum(("b7", "b6")[k // 3], k % 3, [("idm", src, c, ""), ("id4096", flag, 0, "")])
-        act(P("rl", 0, PAIRS, 3), P("b7", 0, PAIRS, 3), bias=-2049.0, func=F.Relu)
-        act(P("rl", 3, PAIRS, 2), P("b6", 0, PAIRS, 2), bias=-2049.0, func=F.Relu)
+        for k, (bk, m) in enumerate((("b4", "a"), ("b6", "b"))):
+            both = P(bk, 0, PAIRS, 2)
+            group([(both, B("idm"), P(memory(t, m), 0, PAIRS, 2)), (both, B("id4096"), P("op", 0, PAIRS, 2))])
+            act(P("rl", 2 * k, PAIRS, 2), both, bias=-2049.0, func=F.Relu)
+        psum("b6", 2, [("idm", "qy", 0, ""), ("id4096", "f8", 1, ""), ("idn512", "f8", 0, "n"), ("idn4096", "op", 0, ""),
+                       ("id4096", "near", 0, "")])
+        act(P("rl", 4), P("b6", 2), bias=-2049.0 - 4096.0, func=F.Relu)
+        act(P("ty"), P("rl", 4), func=F.Sign)
 
     def new_places(t):
         gg = "g%d" % (t % 2)
-        psum("b7", 0, [("id4096", "nm", 0, "f"), ("idm", gg, 1, ""), ("idn4096", "oy_", 0, "")])
-        psum("b7", 1, [("idm", "nx", 0, ""), ("id4096", "u", 0, "")])
-        psum("b7", 2, [("idm", gg, 0, ""), ("idn4096", "ox_", 0, ""), ("idn4096", "u", 0, "")])
-        act(P("rl", 5, PAIRS, 2), P("b7", 0, PAIRS, 2), bias=-2049.0, func=F.Relu)
-        act(P("rl", 7), P("b7", 2), bias=2047.0, func=F.Relu)
+        psum("b2", 0, [("id4096", "nm", 0, "f"), ("idm", gg, 1, ""), ("idn4096", "op", 1, "")])
+        psum("b2", 1, [("idm", "nx", 0, ""), ("id4096", "u", 0, "")])
+        psum("b1", 2, [("idm", gg, 0, ""), ("idn4096", "op", 0, ""), ("idn4096", "u", 0, "")])
+        act(P("rl", 5, PAIRS, 2), P("b2", 0, PAIRS, 2), bias=-2049.0, func=F.Relu)
+        act(P("rl", 7), P("b1", 2), bias=2047.0, func=F.Relu)
         ty_, tx_, tb_ = (("0", "N", ""), ("P0", "", "P"), ("", "", "P"))[t]
-        psum("b6", 0, [("id2047", "ones", 0, "f")] + [("idm", "rl", k, ty_) for k in (0, 1, 4, 5)])
-        psum("b1", 0, [("id2047", "ones", 0, ""), ("idm", "rl", 3, tb_)] + [("idm", "rl", k, tx_) for k in (2, 6, 7)])
+        psum("b6", 0, [("id2047", "ones", 0, "f")] + [("idm", "rl", k, ty_) for k in (1, 2, 4, 5)])
+        psum("b1", 0, [("id2047", "ones", 0, ""), ("idm", "rl", 3, tb_)] + [("idm", "rl", k, tx_) for k in (0, 6, 7)])
 
     def memories(t):
         gg = "g%d" % (t % 2)
-        psum("b4", 2, [("id2047", "ox_", 0, ""), ("id2047", "oy_", 0, "P"), ("id2047", "u", 0, "")])
+        psum("b4", 2, [("id2047", "op", 0, ""), ("id2047", "op", 1, "P"), ("id2047", "u", 0, "")])
         psum("b4", 0, [("id4096", "nm", 0, "f"), ("id1", gg, 0, "")])
         psum("b4", 1, [("id4096", "nm", 0, "f"), ("id1", gg, 1, "")])
-        psum("b2", 2, [("idn2047", "nm", 0, "f")] + [("id2047", b, 0, "") for b in ("oy_", "ox_", "ty", "ones")])
-        for k, m in enumerate(("aa", "bb")):
-            old, new = "%s%d" % (m, t % 2), "%s%d" % (m, 1 - t % 2)
+        psum("b2", 2, [("idn2047", "nm", 0, "f"), ("id2047", "op", 0, ""), ("id2047", "op", 1, ""), ("id2047", "ones", 0, ""),
+                       ("id2047", "ty", 0, "")])
+        for k, m in enumerate("ab"):
+            old, new = memory(t, m), memory(t + 1, m)
             tt(P("ab2", k), P("b4", 2), P(old), A.max)
             for a, b in TURNS[("", "P", "")[t]]:
-                tt(P(new, 0, a) if t < 2 else B("w" + m[0], U, 2 * U), P("b2", 2, b), P(old, 1, b), A.max)
+                tt(P(new, 0, a) if t < 2 else B("w" + m, U, 2 * U), P("b2", 2, b), P(old, 1, b), A.max)
             for a, b in TURNS[("N", "", "")[t]]:
-                tt(P(new, 1, a) if t < 2 else B("w" + m[0]), P("b4", k, b), P("ab2", k, b), A.min)
+                tt(P(new, 1, a) if t < 2 else B("w" + m), P("b4", k, b), P("ab2", k, b), A.min)
 
     def gather(t, l):
         for c0, c1 in zip(CUTS[l], CUTS[l][1:]):
             (cp if (l, c0) in ON_VECTOR[t] else act)(B("xg", 16 * (U * l + c0), 16 * (U * l + c1)),
                                                      ind(B("tab%d" % t, 0, 2048), B(("offx", "offy", "offn")[l], c0, c1)))
+        gathered.append(len(ops) - 1)
         for o in range(0, 16 * U, 64):
             a, c = 16 * U * l + o, o // 256
             tt(B("mx", a, a + 64), B("xg", a, a + 64), B("b0", 64 * c, 64 * c + 64), A.max)
 
-    def half(l, c0):
-        o, a = X("b%d" % (l + 1), slice(c0, c0 + 4), PAIRS), 256 * (8 * l + c0)
-        return [(o, B(z, 15 - r, 143 - r), ST(x, a + r, a + 1024, 16)) for z, x in (("zm", "xg"), ("z2", "mx")) for r in range(16)]
+    def sums_of(l, c0, c1):
+        o, a, b = X("b%d" % (l + 1), slice(c0, c1), PAIRS), 256 * (8 * l + c0), 256 * (8 * l + c1)
+        return [(o, B(z, 15 - r, 143 - r), ST(x, a + r, b, 16)) for z, x in (("zm", "xg"), ("z2", "mx")) for r in range(16)]
 
-    def scatter(tab, msg):
+    def scatter(tab, msg, behind):
         w = B(tab, 0, WT)
         note("V", [w], [B(msg, 0, M)], lambda q: q.tensor_copy(out=w[0].indirect(T[msg][:, 128:M]), in_=T[msg][:, 0:128]),
-             CYC * (60 + 3.8 * 128))
+             CYC * (60 + 3.8 * 128), behind=behind)
 
     peer = {d: T.cores[(rank + d) % n] for d in (1, 2, -1, -2)}
-    sent = [0]
+    sent, last = [0], [None]
 
     def send(d, slot, msg):
         dst = peer[d]
@@ -436,44 +455,41 @@ def rank_program(g, core, T, topo):
                                                           local_sem=T.sem.ls, pid=pid, routing_id=rid,
                                                           dma_engine_mask=topo.mask(core, dst)))
         sent[0] += len(topo.engines(core, dst))
+        last[0] = k
         arrives([B(slot, 0, M)], [], slot + "_", len(topo.engines(peer[-d], core)), k, WAY)
 
-    def send_table():
+    def send_table(d):
         cs, he = carriers(rank, T, topo), hand_engines(rank, T, topo)
         w = 2048 // len(cs)
 
-        def tr(dst, mask, sem, dbuf, k, at):
-            return RemoteDMATransfer(dst_ids=[DstId(rid=topo.addr(dst, core)[0], pnc=topo.addr(dst, core)[1])], dma_engine_mask=mask,
-                                     remote_sem=T.sem[sem], src=T.tab0[:, k * w:k * w + w], dst=T[dbuf][:, at:at + w])
-        hands = [tr(cs[k], he[k - 1][0], "hd", "hand", k, 0) for k in range(1, len(cs))]
-        own = [tr(peer[-d], topo.mask(core, peer[-d]), "t%d" % d, "tab%d" % d, 0, 0) for d in (1, 2)]
+        def tr(dst, k, sem, dbuf):
+            return RemoteDMATransfer(dst_ids=[DstId(rid=topo.addr(dst, core)[0], pnc=topo.addr(dst, core)[1])],
+                                     dma_engine_mask=he[k][0], remote_sem=T.sem[sem], src=T.tab0[:, k * w:k * w + w],
+                                     dst=T[dbuf][:, 0:w])
+        pieces = [tr(peer[-d], 0, "t%d" % d, "tab%d" % d)] + [tr(cs[k], k, "h%d" % d, "hand%d" % d) for k in range(1, len(cs))]
         tab = B("tab0", 0, 2048)
-        k = remote([tab], lambda q: q.remote_dma_fused(hands[:2] + own[:1], local_sem=T.sem.tl))
-        k = remote([tab], lambda q: q.remote_dma_fused(hands[2:] + own[1:], local_sem=T.sem.tl), [k])
-        gone = sum(h[1] for h in he) + len(topo.engines(core, peer[-1])) + len(topo.engines(core, peer[-2]))
-        arrives([], [tab], "tl", gone, k, COPY)
-        for d in (1, 2):
-            arrives([B("tab%d" % d, 0, WT)], [], "t%d" % d,
-                    sum(len(topo.engines(c, core)) for c in carriers((rank + d) % n, T, topo)), k, COPY + 6 * d)
+        k = remote([tab], lambda q: q.remote_dma_fused(pieces, local_sem=T.sem.tl))
+        arrives([], [tab], "tl", d * sum(h[1] for h in he), k, COPY / 2)
+        far = [len(topo.engines(c, core)) for c in carriers((rank + d) % n, T, topo)[1:]]
+        arrives([B("tab%d" % d, 0, WT)], [], "t%d" % d, hand_engines((rank + d) % n, T, topo)[0][1] + sum(far), k, COPY)
+        return k
 
     turn_in("ing", "gli")
+    cp(B("offx"), B("ing"))
+    hold.append(len(ops) - 1)
     cp(P("g0", 0, PAIRS, 2), B("ing", 0, 256))
+    hold.pop()
     cp(P("g0", 0, 0), ST("ing", 15, U, 16))
     lists(0, B("ing"), P("g0", 1))
-    views(0)
-    send_table()
     sums = X("b4", slice(0, 24), 0)
     group([(sums, B("zm", 15 - r, 143 - r), ST("yvs", r, 384, 16)) for r in range(16)])
-    act(B("svn", 0, 24), sums)
-    act(B("tex", 0, 8), B("svn", 0, 8), scale=-1.0)
+    act(B("tex", 0, 8), X("b4", slice(0, 8), 0), scale=-1.0, bias=BIG)
+    act(B("tex", 8, 24), X("b4", slice(8, 24), 0), scale=-1.0, bias=BIG + 128.0)
+    views(0)
+    iota(B("iw", 0, WT), [[1, WT]], 0, 0, [send_table(1)])
     turn_in("th2", "thi")
     cp(P("tha", 0, PAIRS, 2), B("th2", 0, 256))
-    act(P("thb"), P("tha", 1))
-    for a, b in TURNS["N"]:
-        act(P("thb", 1, a), P("tha", 0, b))
-    for m in "ab":
-        turn_in("in" + m, m + "li")
-        cp(P(m + m + "0", 0, PAIRS, 2), B("in" + m, 0, 256))
+    turn_in("ina", "ali")
 
     def visit(t):
         s = t % 2
@@ -484,26 +500,28 @@ def rank_program(g, core, T, topo):
             group([(o, B("id2048"), X("jc")), (o, B("id1"), src)])
         psum("b1", 1, [("idbig", "ones", 0, ""), ("id4096", "f8", 0, "")])
         gather(t, 0)
-        group(half(0, 0))
-        group(half(0, 4))
+        for c in (0, 4):
+            group(sums_of(0, c, c + 4))
         cp(P("sgx"), P("b1"))
         cp(P("sgx", 0, 0), P("b1", 0, 16))
-        tt(P("ox_"), P("sgx"), P("b4"), A.is_gt)
-        psum("b6", 2, [("idnbig", "ones", 0, ""), ("id4096", "f8", 1, ""), ("idn4096", "f8", 0, "n"), ("id32f", "sgx", 0, "n"),
-                       ("idnbig", "ox_", 0, "")])
+        tt(P("op"), P("b1"), P("thr"), A.is_gt)
         gather(t, 1)
-        group(half(1, 0))
-        group(half(1, 4))
-        cp(B("sqy"), P("b2"))
-        tt(P("oy_"), B("sqy"), P("b4", 1), A.is_gt)
-        tt(P("ty"), B("sqy"), P("b6", 2), A.is_lt)
-        psum("b1", 0, [("id32f", "sgx", 0, ""), ("idnmid", "oy_", 0, "")])
-        tt(B("mnu"), P("b1"), B("sqy"), A.min)
+        for c in (0, 4):
+            group(sums_of(1, c, c + 4))
+        tt(P("op", 1), P("b2"), P("thr", 1), A.is_gt)
+        tt(B("mnu"), P("b2"), P("sgx"), A.min)
+        tt(P("near"), P("b2"), P("sgx", 0, slice(0, 16)), A.is_lt)
+        tt(P("oyf"), P("op", 1), P("b1", 1), A.is_gt)
         tt(P("mnm"), B("mnu"), P("b1", 1), A.subtract)
-        sources_early(t)
         gather(t, 2)
-        group(terms("b3", 0, [("idbig", "ones", 0, "f"), ("id4096", "f8", 1, "")]) + half(2, 0)
-              + terms("b3", 0, [("idbig", "oy_", 0, "P")]) + half(2, 4))
+        if t == 0:
+            hold.append(len(ops) - 1)
+            turn_in("inb", "bli")
+            weights()
+            hold.pop()
+        sources_early(t)
+        group(terms("b3", 0, [("idbig", "ones", 0, "f"), ("id4096", "f8", 1, "")]) + sums_of(2, 0, 4)
+              + terms("b3", 0, [("idbig", "op", 1, "P"), ("idbig", "oyf", 0, "")]) + sums_of(2, 4, 8))
         tt(X("nm"), P("b3", 0, WHOLE), X("mnm"), A.is_ge)
         tt(P("u"), P("b3"), B("mnu"), A.is_lt)
         for k in range(3):
@@ -514,8 +532,9 @@ def rank_program(g, core, T, topo):
         cp(B("gf", 0, 8), B("gi", 0, 8))
         halves = P("b3", 2)
         act(B("xv", 0, 256), ind(B(tab, 0, 2048), B("goff", 8, 24)))
-        group([(halves, B("idq"), P("ones"))] + [(halves, B("zh"), B("xv", o, o + 128)) for o in (0, 128)])
-        cp(B(msg), halves)
+        group([(halves, B("zh"), B("xv", o, o + 128)) for o in (0, 128)])
+        act(B(msg), halves, bias=-0.25)
+        first.append(len(ops) - 1)
         cp(B("bf", 0, 128), ind(B("iw", 0, WT), B("goff", 0, 8)))
         cp(ST("eq", 16, 503, 162), B("gi", 0, 4))
         cp(ST("eq", 583, 144, -146), B("gi", 4, 8))
@@ -525,31 +544,41 @@ def rank_program(g, core, T, topo):
         scan(B("sc", 0, EQ), B("w", 0, EQ), B("eq", 0, EQ), A.mult, A.max)
         cp(B(msg, 128, 132), ST("sc", 16, 503, 162))
         cp(B(msg, 132, 136), ST("sc", 583, 144, -146))
-        slots = ((("a1", -1), ("a2", -2)), (("e2", -1), ("e0", 1)), (("c0", 2),))[t]
+        slots = ((("a1", -1),), (("e2", -1), ("e0", 1)), (("c0", 2),))[t]
         for slot, d in slots:
             send(d, slot, msg)
         new_places(t)
         memories(t)
         if t < 2:
             hh = "g%d" % (1 - s)
+            if t == 0:
+                act(P("thb"), P("th2", 1), behind=gathered[-1:])
+                for a, b in TURNS["N"]:
+                    act(P("thb", 1, a), P("tha", 0, b), behind=gathered[-1:])
             views(t + 1)
             count(t + 1)
             act(P(hh, 0, WHOLE), P("b6", 0, WHOLE))
             act(P(hh, 1), P("b1"))
             lists(t + 1, P(hh), P("b1"))
-        for into, m in ((("tab1", "a1"), ("tab0", "m0"), ("tab2", "a2")), (("tab2", "e2"), ("tab0", "e0")), (("tab0", "c0"),))[t]:
-            scatter(into, m)
-        if t == 1:
+        if t == 2:
             cp(B("tab0", NONE, NONE + 1), B("xsav", 1, 2))
+        for into, m in ((("tab0", "m0"), ("tab1", "a1")), (("tab2", "e2"),), ())[t]:
+            scatter(into, m, [last[0]])
+            last[0] = len(ops) - 1
+        if t == 0:
+            send_table(2)
 
     for t in range(3):
         visit(t)
-    dma("Y", "sox", [], [B("tab0", 0, 2048)], T.ox[:, :], T.tab0[:, 0:2048], STORE)
     act(B("wg"), P("b1"))
     act(B("wg", U, 2 * U), P("b6"))
     for w, b, q, sm in (("wg", "ogs", T.og, "sog"), ("wa", "oas", T.oa, "soa"), ("wb", "obs", T.ob, "sob")):
-        act(B(b, 0, 256), ind(B(w, 0, 256), B("pout", 0, 16)))
-        dma("S", sm, [], [B(b, 0, 256)], q[:, :], T[b][:, :], STORE)
+        (act if w == "wg" else cp)(B(b, 0, 256), ind(B(w, 0, 256), B("pout", 0, 16)))
+        k = len(ops) - 1
+        dma("S" if w == "wg" else "Y", sm, [], [B(b, 0, 256)], q[:, :], T[b][:, :], STORE)
+    for m in ("e0", "c0"):
+        scatter("tab0", m, [k])
+    dma("Y", "sox", [], [B("tab0", 0, 2048)], T.ox[:, :], T.tab0[:, 0:2048], STORE)
 
     cnt = issue()
     for sm in ("sog", "soa", "sob", "sox"):

@@ -1,3 +1,4 @@
+import math
 import numpy as np
 from concourse.bass import DstId, RemoteDMATransfer
 from concourse.mybir import AluOpType as A
@@ -5,18 +6,30 @@ from concourse.mybir import ActivationFunctionType as F
 
 U = 128
 S = 17
-M = 136
+PARTS = ((4, 8), (0, 4))
+M = 68
+GAP = 72
+L = 65
 NONE = 2047
 WT = 2048 + 256
 BIG = 32768.0
+FUSE = 128
+MID = 2047.0
 FAR = 1024.0
-EQ = 584
-CUTS = ((0, 32, 64, 128), (0, 64, 128), (0, 32, 64, 96, 112, 128))
-ON_VECTOR = ((), ((0, 0), (0, 32), (2, 112)), ((0, 0), (0, 32), (2, 112)))
-IDS = {"id1": 1.0, "id1184": 1184.0, "id32": 32.0, "id65": 65.0, "idf": -1.0 / 32, "id217": 217.0,
-       "idbig": BIG, "idm": -1.0, "idnbig": -BIG, "id4096": 4096.0, "idn4096": -4096.0, "idn512": -512.0, "id2047": 2047.0,
-       "id2048": 2048.0, "idn2047": -2047.0}
-CYC, PCYC, WAKE, ISSUE, WAY, LOAD, COPY, STORE = 0.00083, 0.00053, 0.18, 0.3, 2.3, 2.6, 8.0, 3.0
+CUTS = {(0, 0): (64, 96, 128), (1, 0): (64, 112, 128), (2, 0): (64, 128), (0, 1): (0, 48, 64), (1, 1): (0, 48, 64),
+        (2, 1): (0, 32, 64)}
+ON_VECTOR = (((0, 96), (1, 112), (1, 48)), ((0, 96), (1, 112), (0, 48), (1, 48)), ((0, 96), (1, 112), (0, 48), (1, 48)))
+IDS = {"id1184": 1184.0, "id32": 32.0, "id65": 65.0, "idf": -1.0 / 32, "id217": 217.0,
+       "idbig": BIG, "idm": -1.0, "idnbig": -BIG, "id4096": 4096.0, "idn4096": -4096.0, "id2047": 2047.0, "idn2047": -2047.0}
+ON_SCALAR = ("id4096", "idn4096", "idn2047", "id2047", "idm")
+OPT = {"split": (1, 1, 1), "offx": "S", "off": ("VV", "SS", "SS"), "bf": "SV", "mo": "SV", "soff": "SV", "oas": "V", "pad": "V", "an": "VSS", "fl": "SS", "obs": "S", "inb": "S", "ina": "V", "f0": "V"}
+SLOTS = ("a1", "e2", "e0", "c0")
+EARLY = 512
+CYC, ISSUE, STORE = 0.00083, 0.3, 3.0
+CLOCKS = ((1.0, 1.56, 3.8, 0.000525, 0.11, 1.9, 3.2, 8.0, 1.5), (1.35, 1.15, 3.0, 0.000525, 0.18, 2.0, 2.8, 8.0, 1.0),
+          (1.1, 1.95, 5.0, 0.000525, 0.15, 1.5, 3.2, 10.0, 1.5), (1.05, 1.25, 2.5, 0.000525, 0.06, 2.4, 3.6, 11.0, 2.0))
+PLANS = [(1.0, g, 3.8, 0.000525, wake, way, 2.8, 8.0, 1.0) for g in (1.4, 1.7) for wake in (0.08, 0.13, 0.18)
+         for way in (1.4, 1.9, 2.4)]
 
 SCRATCH = {}
 
@@ -27,25 +40,24 @@ def _add(where, dtype, **kw):
 
 
 L1, L2 = [8, S], [16, S]
-_add("sbuf", "bfloat16", tab0=WT, tab1=WT, tab2=WT, hand1=512, hand2=512, xsav=16, yvs=384, vexp=[8, 64], z1=128, z2=144, zm=144,
-     zh=128, xv=256, xg=48 * U, mx=48 * U)
-_add("sbuf", "int32", gli=256, ali=256, bli=256, thi=256, pidx=8, p15=8, p4=8, nxi=U, nxj=U, qyi=U, qyj=U, gi=24, s3=24 * S)
-_add("sbuf", "uint16", offx=U, offy=U, offn=U, goff=24, pin=16, pout=16, m0=M, m1=M, m2=M, a1=M, e2=M, e0=M, c0=M)
-_add("sbuf", "float16", g0=L2, g1=L2, aa0=L2, aa1=L2, bb0=L2, bb1=L2, ab2=L2, f8=L2, an=L2, qy=L1, nx=L1, ones=L1, jc=L1,
-     kq=U, op=L2, ty=L1, near=L1, oyf=L1, nm=8 * S, cnt=8 * S, cnb=8 * S, rs=8 * S, rm=128, u=L1, rl=[64, S], ing=256, ina=256, inb=256, rr=128, bo=128, ids=128 * len(IDS), bf=128,
-     eq=EQ, w=EQ, sc=EQ)
-_add("sbuf", "float32", th2=256, id32f=128, ca=128, cb=128, cz=144, cj=8 * S, c16=16, c32=8, cn=16, col=16,
-     dum=8, sp4=8, iw=WT, sgx=L1, mnu=U, mnm=L1, tex=24, thr=2 * U, tha=L2, thb=L2, tht=L2, pp=U, gf=8,
-     wg=256, wa=256, wb=256, ogs=256, oas=256, obs=256)
-_add("psum", "float32", b0=512, b5=512, b7=512, **{"b%d" % k: [30, S] for k in (1, 2, 3, 4, 6)})
+_add("sbuf", "bfloat16", tab0=WT, tab1=WT, tab2=WT, hand1=512, hand2=512, xsav=16, yvs=384, id1=128, idn18=128, z2=144, zm=144,
+     one=128, cb=128, jc=L1, kb=8 * S, xv=256, vx=1024, xg=48 * U, mx=48 * U)
+_add("sbuf", "int32", gli=256, ali=256, bli=256, thi=256, pidx=8, p15=8, p4=8, nxi=U, nxj=U, qyi=U, qyj=U, gi=8, s3=8 * S)
+_add("sbuf", "uint16", offx=U, offy=U, offn=U, goff=8, soff=8, same=8, pin=16, pout=16, seg=24, mo=6 * M, mi=8 * GAP)
+_add("sbuf", "float16", g0=L2, g1=L2, mem0=[32, S], mem1=[32, S], ab2=L2, em=L2, an=L2, qy=L1, nx=L1, ones=L1,
+     kq=U, op=L2, ty=L1, u=L1, oyf=L1, near=L1, nm=8 * S, cnt=8 * S, cnb=8 * S, rs=8 * S, rm=128, rl=[64, S], ing=256, ina=256,
+     inb=256, ids=128 * len(IDS), bf=128, eq=8 * L, w=8 * L, sc=8 * L, spr=3 * U, ky=8 * S, s2=8 * S)
+_add("sbuf", "float32", c16=24, c32=8, cn=16, col=16, dum=8, sp4=8, iw=WT, sgx=L1, mnu=U, mnm=L1, tex=24,
+     thr=2 * U, tht=[8, 34], pp=U, gf=8, wg=256, wm=[2, 256], ogs=256, oas=256, obs=256)
+_add("psum", "float32", b0=[8, 64], b5=512, **{"b%d" % k: [30, S] for k in (1, 2, 3, 4, 6, 7)})
 SEMAPHORES = ["pv", "pa", "pt", "pg", "dg", "dy", "dx", "ds", "da", "db", "dt", "sog", "soa", "sob", "sox", "tl", "ls", "h1",
-              "h2", "t1", "t2"] + [s + "_" for s in ("a1", "e2", "e0", "c0")]
+              "h2", "t1", "t2"] + [s + h for s in SLOTS for h in "ab" if s + h != "e0b"]
 PART = {k: ("ids", 128 * j) for j, k in enumerate(IDS)}
-PART.update(id32f=("id32f", 0), z1=("z1", 0), zh=("zh", 0))
+PART.update(id1=("id1", 0), idn18=("idn18", 0))
 COLS = {k: np.arange(int(np.prod(v[1][1:]))).reshape(v[1][1:]) for k, v in SCRATCH.items()}
 WIDE = {k: v[2] in ("float32", "int32") for k, v in SCRATCH.items()}
 COUNTER = {"V": "pv", "S": "pa", "P": "pt", "G": "pg"}
-ROUNDS = 4
+ROUNDS, MOVES, SLACK, SEED = 3, 40000, 0.001, 1
 ORDER = []
 PAIRS, WHOLE = slice(1, S), slice(0, S)
 TURNS = {"": [(PAIRS, PAIRS)], "f": [(WHOLE, WHOLE)], "n": [(PAIRS, slice(0, 16))], "N": [(slice(2, S), slice(1, 16)), (1, 16)],
@@ -83,10 +95,134 @@ def helper_program(g, core, T, topo):
             g.wait_ge(T.sem.ls, sent)
 
 
+def timing(ops, clock):
+    f, gather, scatter, tensor, wake, way, load, copy, first = clock
+    cost, tail = [], []
+    for o in ops:
+        fix, more, kind = o["cost"]
+        per = {"g": gather * CYC * f, "s": scatter * CYC * f, "p": tensor * f, "c": CYC * f, "r": 0.0}[kind]
+        cost.append((fix * CYC * f if o["e"] in "VS" else fix) + more * per)
+        if kind == "r" and more:
+            cost[-1], first = cost[-1] + first, 0.0
+        what, share = o["tail"]
+        tail.append({"": 1.0, "way": way, "load": load, "copy": copy}[what] * share)
+    lags = [[(d, tail[d] + (0.0 if ops[d]["e"] == o["e"] in "PY" or o["e"] == "D" else wake)) for d in o["deps"]] for o in ops]
+    return cost, tail, lags
+
+
+def replay(order, queue, times, lo=0, hi=0, old=None, reach=None):
+    cost, tail, lags = times
+    b = lo >> 5
+    done, marks = (old[1][:], old[2][:b + 1]) if old else ([0.0] * len(order), [(0.0,) * 7])
+    free = list(marks[b])
+    for i in range(b << 5, len(order)):
+        if not i & 31 and i >> 5 > b:
+            if old and i > hi and old[2][i >> 5][:6] == tuple(free[:6]):
+                return max(old[0], free[6]), done, marks + old[2][i >> 5:]
+            marks.append(tuple(free))
+        k = order[i]
+        e = queue[k]
+        t = free[e]
+        for d, l in lags[k]:
+            if done[d] + l > t:
+                t = done[d] + l
+        t += cost[k]
+        if old and t != done[k] and reach[k] > hi:
+            hi = reach[k]
+        done[k] = t
+        if e:
+            free[e] = t
+        if t + tail[k] > free[6]:
+            free[6] = t + tail[k]
+    return free[6], done, marks
+
+
+def runs(order, before, times, done):
+    cost, tail, lags = times
+    k = max(order[-32:], key=lambda x: done[x] + tail[x])
+    out, run = [], [k]
+    while True:
+        start, q = done[k] - cost[k], before[k]
+        if q >= 0 and abs(done[q] - start) < 1e-9:
+            k = q
+            run.append(k)
+            continue
+        if len(run) > 1:
+            out.append(run[::-1])
+        by = [d for d, l in lags[k] if abs(done[d] + l - start) < 1e-9]
+        if not by:
+            return out
+        k = by[0]
+        run = [k]
+
+
 def issue_order(ops):
-    lag = [{d: ops[d]["tail"] + (0.0 if ops[d]["e"] == o["e"] in "PYG" or o["e"] == "D" else WAKE) for d in o["deps"]} for o in ops]
-    for o, l in zip(ops, lag):
-        l.update({d: 0.0 for d in o["behind"]})
+    queue = ["DVSPGY".index(o["e"]) for o in ops]
+    above, near = [], []
+    for o in ops:
+        far = 0
+        for d in o["deps"]:
+            far |= above[d]
+        near.append([d for d in o["deps"] if not far >> d & 1])
+        above.append(far | sum(1 << d for d in o["deps"]))
+    ops = [dict(o, deps=d) for o, d in zip(ops, near)]
+    clocks = [timing(ops, c) for c in CLOCKS]
+    order = min((list_schedule(ops, timing(ops, c)) for c in PLANS), key=lambda o: sum(replay(o, queue, c)[0] for c in clocks))
+    deps = [set(o["deps"]) | {d for d in o["behind"] if o["firm"]} for o in ops]
+    state = [replay(order, queue, c) for c in clocks]
+    scale = [len(clocks) * s[0] for s in state]
+    now, best, found, seed = 0.0, (0.0, order), None, [SEED]
+
+    def draw():
+        seed[0] = (seed[0] * 6364136223846793005 + 1442695040888963407) % 2 ** 64
+        return (seed[0] >> 11) / 2.0 ** 53
+
+    for step in range(MOVES):
+        if found is None:
+            place, before, reach, last = [0] * len(ops), [-1] * len(ops), [0] * len(ops), [-1] * 6
+            for i, k in enumerate(order):
+                place[k] = i
+                if queue[k]:
+                    before[k], last[queue[k]] = last[queue[k]], k
+                for d in near[k]:
+                    reach[d] = i
+            found = [r for c, s in zip(clocks, state) for r in runs(order, before, c, s[1]) for _ in range(int(len(r) ** 0.5))]
+        run, m = found[int(draw() * len(found))], draw()
+        i = int(draw() * (len(run) - 1))
+        j = len(run) - 1 if m < 0.25 else min(len(run) - 1, i + (1, 1, 2, 3, 5, 8, 16, 40)[int(draw() * 8)])
+        u, v = run[0 if m > 0.85 else i], run[j]
+        part = order[place[u]:place[v] + 1]
+        if draw() < 0.5:
+            moved, need = {v}, set(deps[v])
+            for x in part[-2::-1]:
+                if x in need:
+                    moved.add(x)
+                    need |= deps[x]
+        else:
+            stay = {u}
+            for x in part[1:]:
+                if deps[x] & stay:
+                    stay.add(x)
+            moved = set(part) - stay
+        if u in moved or v not in moved:
+            continue
+        new = order[:place[u]] + [x for x in part if x in moved] + [x for x in part if x not in moved] + order[place[v] + 1:]
+        limit, tried, change = -SLACK * (1 - step / MOVES) * math.log(draw() + 1e-12), [], 0.0
+        for c, s, z in zip(clocks, state, scale):
+            tried.append(replay(new, queue, c, place[u], place[v], s, reach))
+            change += (tried[-1][0] - s[0]) / z
+            if change > limit + 0.002:
+                break
+        if change <= limit:
+            order, state, now, found = new, tried, now + change, None
+            if now < best[0]:
+                best = (now, order)
+    return best[1]
+
+
+def list_schedule(ops, times):
+    cost, tails, lags = times
+    lag = [dict([(d, 0.0) for d in o["behind"]] + l) for o, l in zip(ops, lags)]
     back = [{} for _ in ops]
     for k, l in enumerate(lag):
         for d, x in l.items():
@@ -98,7 +234,7 @@ def issue_order(ops):
         ready = sorted((key[k], k) for k in range(len(ops)) if not left[k])
         while ready:
             k = ready.pop(0)[1]
-            t0, c = at[k], ops[k]["cost"]
+            t0, c = at[k], cost[k]
             if ops[k]["e"] != "D":
                 q = busy[ops[k]["e"]]
                 i = len(q)
@@ -117,15 +253,14 @@ def issue_order(ops):
             ready.sort()
         return start
 
-    tails = [o["tail"] for o in ops]
     key, best = [-k for k in range(len(ops))], None
     for _ in range(ROUNDS):
         rev = place(back, lag, key, tails)
-        fwd = place(lag, back, [-rev[k] - ops[k]["cost"] for k in range(len(ops))], [0.0] * len(ops))
-        end = max(fwd[k] + ops[k]["cost"] + tails[k] for k in range(len(ops)))
+        fwd = place(lag, back, [-rev[k] - cost[k] for k in range(len(ops))], [0.0] * len(ops))
+        end = max(fwd[k] + cost[k] + tails[k] for k in range(len(ops)))
         if best is None or end < best[0]:
             best = (end, fwd)
-        key = [-fwd[k] - ops[k]["cost"] for k in range(len(ops))]
+        key = [-fwd[k] - cost[k] for k in range(len(ops))]
     return sorted(range(len(ops)), key=lambda k: (best[1][k], k))
 
 
@@ -137,9 +272,9 @@ def rank_program(g, core, T, topo):
     n = len(T.cores)
     Q = {"V": g.vector, "S": g.scalar, "P": g.tensor, "G": g, "Y": g.sync}
 
-    ops, writer, readers, bank, gathered, first, hold = [], {}, {}, {}, [], [], []
+    ops, writer, readers, bank, gathered, hold, made, fused = [], {}, {}, {}, [], [], [], {}
 
-    def note(e, outs, ins, call, cost, tail=0.0, sem=None, deps=(), behind=()):
+    def note(e, outs, ins, call, cost, tail=("", 0.0), sem=None, deps=(), behind=(), firm=False):
         k, deps = len(ops), set(deps)
         for ap, parts in ins:
             for b, cols in parts:
@@ -166,7 +301,7 @@ def rank_program(g, core, T, topo):
             deps.update(rec[2] + (rec[1][-1:] if e == "P" else []))
             rec[1].append(k)
         ops.append({"e": e, "deps": sorted(deps - {-1, k}), "call": call, "cost": cost, "tail": tail, "sem": sem,
-                    "behind": list(behind) + hold})
+                    "behind": list(behind) + hold, "firm": firm or e in "GY", "name": outs[0][1][0][0] if outs else ""})
         return k
 
     def issue():
@@ -190,8 +325,9 @@ def rank_program(g, core, T, topo):
                 i.then_inc(T.sem[o["sem"][0]], 16)
                 token[k] = o["sem"] + (dict(known[e]),)
             elif i is not None:
-                cnt[e] += 1
-                i.then_inc(T.sem[COUNTER[e]], 1)
+                for j in i if isinstance(i, list) else [i]:
+                    cnt[e] += 1
+                    j.then_inc(T.sem[COUNTER[e]], 1)
                 token[k] = (COUNTER[e], cnt[e], dict(known[e]))
         return cnt
 
@@ -210,13 +346,15 @@ def rank_program(g, core, T, topo):
     def ST(b, lo, hi, step):
         return X(b, slice(lo, hi, step))
 
-    def P(b, k=0, cols=PAIRS, lists=1):
+    def P(b, k=0, cols=PAIRS, lists=1, h=(0, 8)):
+        if b == "nm":
+            return B(b, S * h[0], S * h[1])
         if COLS[b].ndim == 1:
-            return B(b, U * k, U * (k + lists))
-        return X(b, slice(8 * k, 8 * (k + lists)), cols)
+            return B(b, U * k + 16 * h[0], U * (k + lists - 1) + 16 * h[1])
+        return X(b, slice(8 * k + h[0], 8 * (k + lists - 1) + h[1]), cols)
 
-    def memory(t, m):
-        return "in" + m if t == 0 else "%s%s%d" % (m, m, t % 2)
+    def memory(t, m, k):
+        return ("in" + m, k) if t == 0 else ("mem%d" % (t % 2), {"b0": 0, "a0": 1, "a1": 2, "b1": 3}[m + str(k)])
 
     def ind(w, o):
         return (w[0].indirect(o[0]), w[1] + o[1])
@@ -224,151 +362,164 @@ def rank_program(g, core, T, topo):
     def cycles(o, ins, two=False):
         k = len(o[1][0][1])
         if len(ins[0][1]) > 1:
-            return 60 + 1.56 * k
+            return (60, k, "g")
         if two:
-            return max(64, k * (1 if any(SCRATCH[v[1][0][0]][0] == "psum" for v in ins) else 2))
-        return max(64, k * (1 if any(WIDE[v[1][0][0]] for v in [o] + ins) else 0.5))
+            return (max(64, k * (1 if any(SCRATCH[v[1][0][0]][0] == "psum" for v in ins) else 2)), 0, "c")
+        return (max(64, k * (1 if any(WIDE[v[1][0][0]] for v in [o] + ins) else 0.5)), 0, "c")
 
     def tt(o, a, b, op, behind=()):
         return note("V", [o], [a, b], lambda q: q.tensor_tensor(out=o[0], in0=a[0], in1=b[0], op=op),
-                    CYC * cycles(o, [a, b], True), behind=behind)
+                    cycles(o, [a, b], True), behind=behind)
 
     def ts(o, a, s1, op0, s2=None, op1=None):
         cols = [s for s in (s1, s2) if isinstance(s, tuple)]
         x, y = [s[0] if isinstance(s, tuple) else s for s in (s1, s2)]
         more = {} if op1 is None else {"op1": op1}
         note("V", [o], [a] + cols, lambda q: q.tensor_scalar(out=o[0], in0=a[0], scalar1=x, scalar2=y, op0=op0, **more),
-             CYC * cycles(o, [a]))
+             cycles(o, [a]))
 
     def cp(o, a):
-        note("V", [o], [a], lambda q: q.tensor_copy(out=o[0], in_=a[0]), CYC * cycles(o, [a]))
+        note("V", [o], [a], lambda q: q.tensor_copy(out=o[0], in_=a[0]), cycles(o, [a]))
 
     def fill(o, x):
-        note("V", [o], [], lambda q: q.memset(o[0], x), CYC * cycles(o, [o]))
+        note("V", [o], [], lambda q: q.memset(o[0], x), cycles(o, [o]))
 
     def scan(o, d0, d1, op0, op1):
         note("V", [o], [d0, d1], lambda q: q.tensor_tensor_scan(out=o[0], data0=d0[0], data1=d1[0], initial=0.0, op0=op0, op1=op1),
-             CYC * cycles(o, [d0, d1]))
+             cycles(o, [d0, d1]))
 
     def act(o, a, scale=1.0, bias=0.0, func=F.Copy, behind=()):
         cols = [s for s in (scale, bias) if isinstance(s, tuple)]
         x, y = [s[0] if isinstance(s, tuple) else s for s in (scale, bias)]
         k = len(o[1][0][1])
         note("S", [o], [a] + cols, lambda q: q.activation(out=o[0], in_=a[0], func=func, bias=y, scale=x),
-             CYC * (80 + 1.56 * k if len(a[1]) > 1 else 80 + max(64, k)), behind=behind)
+             (80, k, "g") if len(a[1]) > 1 else (80 + max(64, k), 0, "c"), behind=behind)
 
     def matmul(o, l, r, start, stop):
         note("P", [o], [l, r], lambda q: q.matmul(out=o[0], lhsT=l[0], rhs=r[0], start=start, stop=stop),
-             PCYC * max(64, len(o[1][0][1])) * (4 if WIDE[r[1][0][0]] else 1))
+             (0.0, max(64, len(o[1][0][1])), "p"))
 
-    def group(mats):
-        for k, (o, l, r) in enumerate(mats):
-            matmul(o, l, r, k == 0, k == len(mats) - 1)
+    def block(mats, start, stop):
+        last = len(mats) - 1
+        note("P", [mats[0][0]], [x for o, l, r in mats for x in (l, r)],
+             lambda q: [q.matmul(out=o[0], lhsT=l[0], rhs=r[0], start=start and k == 0, stop=stop and k == last)
+                        for k, (o, l, r) in enumerate(mats)], (0.0, 64 * len(mats), "p"))
 
-    def terms(bk, k, ts_):
-        return [(P(bk, k, a), B(l), X(buf) if buf == "nm" else P(buf, c, b)) for l, buf, c, turn in ts_ for a, b in TURNS[turn]]
+    def group(mats, start=True):
+        for k, m in enumerate(mats):
+            if isinstance(m, list):
+                block(m, start and k == 0, k == len(mats) - 1)
+            else:
+                matmul(*m, start and k == 0, k == len(mats) - 1)
+
+    def terms(bk, k, ts_, h=(0, 8)):
+        return [(P(bk, k, a, h=h), B(l), P(buf, c, b, h=h)) for l, buf, c, turn in ts_ for a, b in TURNS[turn]]
 
     def psum(bk, k, ts_):
         group(terms(bk, k, ts_))
 
     def dma(q, sem, outs, ins, out, in_, time, behind=()):
-        return note(q, outs, ins, lambda e: e.dma_start(out=out, in_=in_), 0.05, time, (sem, 16), behind=behind)
+        return note(q, outs, ins, lambda e: e.dma_start(out=out, in_=in_), (0.05, 0, "r"), time, (sem, 16), behind=behind)
 
     def iota(o, pattern, base, cm, behind=()):
-        more = {"allow_small_or_imprecise_dtypes": True} if SCRATCH[o[1][0][0]][2] == "float32" else {}
-        note("G", [o], [], lambda q: q.iota(o[0], pattern, base, cm, **more), 0.13 + 2 * CYC * len(o[1][0][1]), behind=behind)
+        more = {"allow_small_or_imprecise_dtypes": True} if SCRATCH[o[1][0][0]][2] != "int32" else {}
+        return note("G", [o], [], lambda q: q.iota(o[0], pattern, base, cm, **more), (0.13, 2 * len(o[1][0][1]), "c"),
+                    behind=behind)
 
     def remote(ins, call, behind=()):
         def run(q):
             call(q)
-        return note("G", [], ins, run, ISSUE, behind=behind)
+        return note("G", [], ins, run, (ISSUE, 1, "r"), behind=behind)
 
     def arrives(outs, ins, sem, val, since, time):
-        note("D", outs, ins, None, 0.0, time, (sem, val), [since])
+        note("D", outs, ins, None, (0.0, 0, "r"), time, (sem, val), [since])
 
     fill(B("tab0", 2032, 2048), FAR)
-    k = dma("Y", "dg", [B("gli", 0, 256)], [], T.gli[:, :], T.gl[:, :], LOAD - 0.9)
-    k = dma("Y", "dy", [B("yvs", 0, 384)], [], T.yvs[:, :], T.yv[:, :], LOAD - 0.7, [k])
-    k = dma("Y", "dx", [B("tab0", 0, 2048)], [], T.tab0[:, 0:NONE], T.xt[:, 0:NONE], LOAD, [k])
-    for sem, b, src in (("dt", "thi", T.th), ("da", "ali", T.al), ("db", "bli", T.bl)):
-        k = dma("Y", sem, [B(b, 0, 256)], [], T[b][:, :], src[:, :], LOAD + 0.8, [k])
-    dma("Y", "ds", [B("xsav", 0, 2)], [], T.xsav[:, 0:2], T.xt[:, NONE - 1:NONE + 1], LOAD + 0.8, [k])
+    k = dma("Y", "dy", [B("yvs", 0, 384)], [], T.yvs[:, :], T.yv[:, :], ("load", 0.55))
+    k = dma("Y", "dg", [B("gli", 0, 256)], [], T.gli[:, :], T.gl[:, :], ("load", 0.65), [k])
+    k = dma("Y", "dx", [B("tab0", 0, 2048)], [], T.tab0[:, 0:NONE], T.xt[:, 0:NONE], ("load", 1.0), [k])
+    for j, (sem, b, src) in enumerate((("da", "ali", T.al), ("dt", "thi", T.th), ("db", "bli", T.bl))):
+        k = dma("Y", sem, [B(b, 0, 256)], [], T[b][:, :], src[:, :], ("load", 1.12 + 0.1 * j), [k])
+    dma("Y", "ds", [B("xsav", 0, 2)], [], T.xsav[:, 0:2], T.xt[:, NONE - 1:NONE + 1], ("load", 1.4), [k])
 
     def C(k):
         return B("col", k, k + 1)
 
-    def start_of(c):
-        return 146 * c if c < 4 else 162 * (7 - c) + S
-
     iota(B("pidx", 0, 2), [[0, 2]], 0, 1)
-    iota(B("c16", 0, 16), [[1, 16]], 240, 0)
-    iota(B("cb", 0, 128), [[0, 8], [1, 16]], 0, 0)
-    iota(B("ca", 0, 128), [[1, 8], [0, 16]], 0, 0)
-    iota(X("cj"), [[0, 8], [-2, S]], 32, 0)
-    iota(B("cz", 0, 144), [[1, 144]], -15, 0)
+    fill(B("one"), 1.0)
+    note("G", [B("id1")], [B("one")], lambda q: q.affine_select(T.id1[:, :], T.one[:, :], [[-1, 128]], A.is_equal, 0.0, 0, 1),
+         (0.17, 256, "c"))
+    iota(B("c16", 0, 24), [[1, 24]], 240, 0)
     iota(B("c32", 0, 8), [[32, 8]], 2048, 0)
-    iota(B("cn", 0, 16), [[-1, 16]], 15, 0)
+    iota(B("cb", 0, 128), [[0, 8], [1, 16]], 0, 0)
+    iota(X("jc"), [[0, 8], [-128, S]], 2048, 0)
+    iota(B("kb", 0, 8 * S), [[-256, 8], [-16, S]], 2064, 0)
+    k = iota(B("cn", 0, 16), [[-1, 16]], 15, 0)
+    iota(B("iw", 0, EARLY), [[1, EARLY]], 0, 0, [k])
     fill(X("ones"), 1.0)
     fill(X("kq"), 1801.0 / 64)
     fill(P("mnm", 0, 0), 4 * BIG)
-    for b in ("g0", "g1"):
-        fill(P(b, 1, 0), 0.0)
+    fill(P("em", 1, 0), 0.0)
     ts(B("p15", 0, 1), B("pidx", 0, 1), 15, A.bitwise_and)
     ts(B("p4", 0, 1), B("pidx", 0, 1), 4, A.arith_shift_right)
     ts(C(0), B("p15", 0, 1), 16.0, A.mult)
     cp(C(2), B("p15", 0, 1))
-    cp(C(3), B("p4", 0, 1))
-    ts(C(4), B("p4", 0, 1), 16.0, A.mult)
+    ts(C(3), B("p4", 0, 1), 32.0, A.mult, 2048.0, A.add)
     ts(B("pin", 0, 16), B("c16", 0, 16), C(0), A.subtract)
     ts(B("pout", 0, 16), B("cn", 0, 16), C(0), A.add)
-    ts(B("rr", 0, 128), B("cb", 0, 128), C(2), A.is_equal)
-    ts(B("bo", 0, 128), B("ca", 0, 128), C(3), A.is_equal)
-    tt(B("id1"), B("bo", 0, 128), B("rr", 0, 128), A.mult)
-    for b in ("id1184", "id32", "id65", "idf", "id217", "idbig", "idm", "id4096", "idn4096"):
-        ts(B(b), B("id1"), IDS[b], A.mult)
-    for b in ("z1", "idnbig", "id2048", "idn512", "idn2047", "id2047", "zh"):
-        act(B(b), B("id1"), scale={"z1": 1.0, "zh": 0.5, "id32f": 1.0}.get(b) or IDS[b])
-    ts(B("rm"), B("rr"), -1.0, A.mult)
-    ts(X("rs"), X("cj"), 32.0, A.not_equal)
-    ts(B("zm", 0, 144), B("cz", 0, 144), C(4), A.is_equal, -1.0, A.mult)
+    ts(B("rm", 0, 128), B("cb", 0, 128), C(2), A.is_equal)
+    for b in IDS:
+        if b in ON_SCALAR:
+            act(B(b), B("id1"), scale=IDS[b])
+        else:
+            ts(B(b), B("id1"), IDS[b], A.mult)
+    ts(B("idn18"), B("id1"), -8 * BIG, A.mult)
+    fill(X("cnb"), 16.0)
+    ts(B("seg", 0, 24), B("c16", 0, 24), 240.0, A.subtract)
+    ts(X("rs"), X("jc"), 2048.0, A.not_equal)
+    ts(X("ky"), X("kb"), C(2), A.subtract)
+    fill(B("zm", 0, 144), 0.0)
+    ts(ST("zm", 15, 143, 16), B("c32", 0, 8), C(3), A.is_equal, -1.0, A.mult)
     ts(B("z2", 0, 144), B("zm", 0, 144), -2.0, A.mult)
-    cp(X("jc"), X("cj"))
     ts(B("dum", 0, 8), B("c32", 0, 8), C(2), A.add, C(2), A.add)
     cp(P("nx", 0, 0), B("dum", 0, 8))
+    ts(B("same", 0, 8), B("dum", 0, 8), 0.5, A.mult, -1024.0, A.add)
     ts(B("sp4", 0, 8), B("dum", 0, 8), 4.0, A.mult, -1.0, A.add)
-    fill(B("w", 0, EQ), 1.0)
+    fill(B("w", 0, 8 * L), 1.0)
+    for c in range(8):
+        o = L * c + 16 * (c % 4)
+        act(B("w", o, o + 16), B("rm", 0, 16), scale=B("sp4", c, c + 1), bias=1.0, func=F.Identity)
+    fill(ST("w", 0, 8 * L, L), 0.0)
 
-    def weights():
-        for c in range(8):
-            o = start_of(c) + 16 * c
-            ts(B("w", o, o + 16), B("rr", 0, 16), B("sp4", c, c + 1), A.mult, 1.0, A.add)
-        fill(ST("w", 0, EQ, 146), 0.0)
-        fill(ST("w", S, EQ, 162), 0.0)
+    def less(e, o, a):
+        act(o, a, scale=-1.0, bias=2047.0)
 
-    def turn_in(o, src):
-        cp(B(o, 0, 256), ind(B(src, 0, 256), B("pin", 0, 16)))
+    def none(e, o, a):
+        if e == "V":
+            ts(o, a, 2047.0, A.is_equal)
+        else:
+            act(o, a, bias=-2046.0, func=F.Relu)
 
     def views(t):
-        for k in (0, 16):
-            act(X("vexp", ALL, slice(k, k + 16)), B("yvs", t * 128, t * 128 + 128), behind=gathered[-1:])
-        act(X("vexp", ALL, slice(32, 64)), X("vexp", ALL, slice(0, 32)))
-        group([(B("b0", 0, 512), B("z1"), X("vexp"))])
+        group([(X("b0", ALL, slice(k, k + 16)), B("id1"), B("yvs", t * 128, t * 128 + 128)) for k in range(0, 64, 16)])
 
     def lists(t, xsrc, ysrc):
         gg = "g%d" % (t % 2)
         if t:
-            cp(B("offx"), xsrc)
-        ts(P("f8", 0, WHOLE), P(gg, 0, WHOLE), 2047.0, A.not_equal, -8.0, A.mult)
-        ts(P("f8", 1), P(gg, 1), 2047.0, A.not_equal, -8.0, A.mult)
+            {"V": cp, "S": act}[OPT["offx"]](B("offx"), xsrc)
         tt(B("pp"), P(gg), ysrc, A.mult)
-        psum("b3", 1, [("idbig", "f8", 1, ""), ("id217", "kq", 0, ""), ("id65", gg, 0, "n"), ("idf", gg, 0, "n")])
+        psum("b3", 1, [("id217", "kq", 0, ""), ("id65", gg, 0, "n"), ("idf", gg, 0, "n"), ("idn18", "em", 1, "")])
         psum("b3", 0, [("id1184", gg, 0, ""), ("id32", gg, 1, "")])
-        tt(B("qyi"), P("b3", 1), P(gg, 1), A.max)
+        tt(B("qyi"), P("b3", 1), P(gg, 1), A.min)
         tt(B("nxi"), P("b3"), B("pp"), A.add)
         ts(B("qyj"), B("qyi"), 2047, A.bitwise_and)
         ts(B("nxj"), B("nxi"), 5, A.arith_shift_right, 2047, A.bitwise_and)
-        cp(B("offy"), B("qyj"))
-        cp(B("offn"), B("nxj"))
+        for k, (o, a) in enumerate((("offy", "qyj"), ("offn", "nxj"))):
+            if OPT["off"][t][k] == "V":
+                cp(B(o), B(a))
+            else:
+                act(B(o), ind(B(a), B("same", 0, 8)))
+        made[:] = [len(ops) - 2, len(ops) - 1]
         cp(P("qy"), B("offy"))
         cp(P("nx"), B("offn"))
 
@@ -378,85 +529,104 @@ def rank_program(g, core, T, topo):
         scan(X("cnb", back), X("rs"), X("cnt", back), A.mult, A.max)
 
     def thresholds(t):
-        for c in range(8):
-            seg = slice(c, 16, 8)
-            o, a, x = X("tht", seg, PAIRS), X(("tha", "thb")[t % 2], seg, PAIRS), B("tex", 8 * t + c, 8 * t + c + 1)
-            if t:
-                act(o, a, bias=x, func=F.Identity, behind=first[-1:])
-            else:
-                ts(o, a, x, A.add)
-        ts(P("an", 0, PAIRS, 2), P(memory(t, "a"), 0, PAIRS, 2), 2047.0, A.is_equal)
-        for k, turn in enumerate(("", "n")):
-            group([(P("b4", k, WHOLE), B("rm"), X("cnb"))] * (t > 0)
-                  + terms("b4", k, [("idbig", "an", k, ""), ("id4096", "f8", k, ""), ("idn4096", "f8", 1 - k, turn)]))
-        tt(B("thr", 0, 2 * U), P("b4", 0, PAIRS, 2), P("tht", 0, PAIRS, 2), A.add)
+        if t == 0:
+            for c in range(8):
+                ts(X("tht", c, slice(1, 33)), X("thi", slice(248 + c, None, -8)), BIG + MID + 128.0, A.add)
+        none(OPT["an"][t], P("an", 0, PAIRS, 2), P(*memory(t, "a", 0), PAIRS, 2))
+        for k in (1, 0):
+            group([(P("b7", k, WHOLE), B("rm"), X("cnb"))]
+                  + terms("b7", k, [("id1", "spr", t, ""), ("idnbig", "em", k, ""), ("idbig", "em", 1 - k, ("", "n")[k]),
+                                    ("idnbig", "an", k, "")]))
+        for k in (1, 0):
+            a = ((2, 1), (1, 0))[t % 2][k]
+            tt(P("thr", k), X("tht", ALL, slice(a, a + 31, 2)), P("b7", k), A.subtract)
 
     def sources_early(t):
         for k, (bk, m) in enumerate((("b4", "a"), ("b6", "b"))):
-            both = P(bk, 0, PAIRS, 2)
-            group([(both, B("idm"), P(memory(t, m), 0, PAIRS, 2)), (both, B("id4096"), P("op", 0, PAIRS, 2))])
-            act(P("rl", 2 * k, PAIRS, 2), both, bias=-2049.0, func=F.Relu)
-        psum("b6", 2, [("idm", "qy", 0, ""), ("id4096", "f8", 1, ""), ("idn512", "f8", 0, "n"), ("idn4096", "op", 0, ""),
+            group([(P(bk, l), B("idm"), P(*memory(t, m, l))) for l in range(2)]
+                  + [(P(bk, 0, PAIRS, 2), B("id4096"), P("op", 0, PAIRS, 2))])
+        psum("b6", 2, [("idm", "qy", 0, ""), ("idbig", "em", 1, ""), ("idnbig", "em", 0, "n"), ("idn4096", "op", 0, ""),
                        ("id4096", "near", 0, "")])
-        act(P("rl", 4), P("b6", 2), bias=-2049.0 - 4096.0, func=F.Relu)
+        for k, bk in enumerate(("b4", "b6")):
+            act(P("rl", 2 * k, PAIRS, 2), P(bk, 0, PAIRS, 2), bias=-2049.0, func=F.Relu)
+        act(P("rl", 4), P("b6", 2), bias=-2049.0 - BIG, func=F.Relu)
         act(P("ty"), P("rl", 4), func=F.Sign)
 
     def new_places(t):
         gg = "g%d" % (t % 2)
         psum("b2", 0, [("id4096", "nm", 0, "f"), ("idm", gg, 1, ""), ("idn4096", "op", 1, "")])
         psum("b2", 1, [("idm", "nx", 0, ""), ("id4096", "u", 0, "")])
-        psum("b1", 2, [("idm", gg, 0, ""), ("idn4096", "op", 0, ""), ("idn4096", "u", 0, "")])
+        psum("b3", 2, [("idm", gg, 0, ""), ("idn4096", "op", 0, ""), ("idn4096", "u", 0, "")])
         act(P("rl", 5, PAIRS, 2), P("b2", 0, PAIRS, 2), bias=-2049.0, func=F.Relu)
-        act(P("rl", 7), P("b1", 2), bias=2047.0, func=F.Relu)
-        ty_, tx_, tb_ = (("0", "N", ""), ("P0", "", "P"), ("", "", "P"))[t]
-        psum("b6", 0, [("id2047", "ones", 0, "f")] + [("idm", "rl", k, ty_) for k in (1, 2, 4, 5)])
+        act(P("rl", 7), P("b3", 2), bias=2047.0, func=F.Relu)
+        tx_, tb_ = (("N", ""), ("", "P"), ("", "P"))[t]
+        psum("b6", 0, [("id1", "rl", k, "") for k in (1, 2, 4, 5)])
         psum("b1", 0, [("id2047", "ones", 0, ""), ("idm", "rl", 3, tb_)] + [("idm", "rl", k, tx_) for k in (0, 6, 7)])
 
     def memories(t):
         gg = "g%d" % (t % 2)
         psum("b4", 2, [("id2047", "op", 0, ""), ("id2047", "op", 1, "P"), ("id2047", "u", 0, "")])
-        psum("b4", 0, [("id4096", "nm", 0, "f"), ("id1", gg, 0, "")])
-        psum("b4", 1, [("id4096", "nm", 0, "f"), ("id1", gg, 1, "")])
-        psum("b2", 2, [("idn2047", "nm", 0, "f"), ("id2047", "op", 0, ""), ("id2047", "op", 1, ""), ("id2047", "ones", 0, ""),
+        for k in range(2):
+            psum("b4", k, [("id4096", "nm", 0, "f"), ("id1", gg, k, "")])
+        psum("b2", 2, [("idn2047", "nm", 0, "f"), ("id2047", "ones", 0, ""), ("id2047", "op", 0, ""), ("id2047", "op", 1, ""),
                        ("id2047", "ty", 0, "")])
         for k, m in enumerate("ab"):
-            old, new = memory(t, m), memory(t + 1, m)
-            tt(P("ab2", k), P("b4", 2), P(old), A.max)
+            tt(P("ab2", k), P("b4", 2), P(*memory(t, m, 0)), A.max)
             for a, b in TURNS[("", "P", "")[t]]:
-                tt(P(new, 0, a) if t < 2 else B("w" + m, U, 2 * U), P("b2", 2, b), P(old, 1, b), A.max)
+                tt(P(*memory(t + 1, m, 0), a) if t < 2 else X("wm", k, slice(U, 2 * U)), P("b2", 2, b),
+                   P(*memory(t, m, 1), b), A.max)
             for a, b in TURNS[("N", "", "")[t]]:
-                tt(P(new, 1, a) if t < 2 else B("w" + m), P("b4", k, b), P("ab2", k, b), A.min)
+                tt(P(*memory(t + 1, m, 1), a) if t < 2 else X("wm", k, slice(0, U)), P("b4", k, b), P("ab2", k, b), A.min)
 
-    def gather(t, l):
-        for c0, c1 in zip(CUTS[l], CUTS[l][1:]):
-            (cp if (l, c0) in ON_VECTOR[t] else act)(B("xg", 16 * (U * l + c0), 16 * (U * l + c1)),
-                                                     ind(B("tab%d" % t, 0, 2048), B(("offx", "offy", "offn")[l], c0, c1)))
-        gathered.append(len(ops) - 1)
-        for o in range(0, 16 * U, 64):
-            a, c = 16 * U * l + o, o // 256
-            tt(B("mx", a, a + 64), B("xg", a, a + 64), B("b0", 64 * c, 64 * c + 64), A.max)
+    def gather(t, l, p):
+        fused[l, p] = None
+        for c0, c1 in zip(CUTS[l, p], CUTS[l, p][1:]):
+            lo, hi = 16 * (U * l + c0), 16 * (U * l + c1)
+            x = ind(B("tab%d" % t, 0, 2048), B(("offx", "offy", "offn")[l], c0, c1))
+            if (l, c0) in ON_VECTOR[t] and t and c0 >= FUSE:
+                tt(B("xg", lo, hi), x, B("vx", 16 * (c0 - FUSE), 16 * (c1 - FUSE)), A.subtract)
+                ts(B("mx", lo, hi), B("xg", lo, hi), 0.0, A.max)
+                fused[l, p] = (c0 // 16, c1 // 16)
+                continue
+            (cp if (l, c0) in ON_VECTOR[t] else act)(B("xg", lo, hi), x)
+            gathered.append(len(ops) - 1)
+            for a in range(lo, hi, 64):
+                tt(B("mx", a, a + 64), B("xg", a, a + 64), X("b0", a // 256 % 8, ALL), A.max)
 
-    def sums_of(l, c0, c1):
-        o, a, b = X("b%d" % (l + 1), slice(c0, c1), PAIRS), 256 * (8 * l + c0), 256 * (8 * l + c1)
-        return [(o, B(z, 15 - r, 143 - r), ST(x, a + r, b, 16)) for z, x in (("zm", "xg"), ("z2", "mx")) for r in range(16)]
+    def sums_of(t, l, p):
+        c0, c1 = PARTS[p]
+        bk = "b%d" % (l + 1)
+        o, a, b = X(bk, slice(c0, c1), PAIRS), 256 * (8 * l + c0), 256 * (8 * l + c1)
+        z = [[(o, B(z, 15 - r, 143 - r), ST(x, a + r, b, 16)) for r in range(16)] for z, x in (("zm", "xg"), ("z2", "mx"))]
+        more = terms(bk, 0, [("idm", "spr", t, ""), ("id2047", "ones", 0, "")], fused[l, p]) if fused[l, p] else []
+        return z[:1] + more + z[1:]
 
-    def scatter(tab, msg, behind):
+    def scatter(tab, msg, o, p, t, behind):
         w = B(tab, 0, WT)
-        note("V", [w], [B(msg, 0, M)], lambda q: q.tensor_copy(out=w[0].indirect(T[msg][:, 128:M]), in_=T[msg][:, 0:128]),
-             CYC * (60 + 3.8 * 128), behind=behind)
+        if OPT["split"][t]:
+            a = o + (M if msg == "mo" or o == landing("e0", 0) else GAP) * p
+            b = a + 64
+        else:
+            a, b = o + 16 * PARTS[p][0], o + U + PARTS[p][0]
+        note("V", [w], [B(msg, a, a + 64), B(msg, b, b + 4)],
+             lambda q: q.tensor_copy(out=w[0].indirect(T[msg][:, b:b + 4]), in_=T[msg][:, a:a + 64]),
+             (60, 64, "s"), behind=behind, firm=True)
+
+    def landing(slot, p):
+        return 2 * GAP * SLOTS.index(slot) + (M if slot == "e0" else GAP) * p
 
     peer = {d: T.cores[(rank + d) % n] for d in (1, 2, -1, -2)}
     sent, last = [0], [None]
 
-    def send(d, slot, msg):
-        dst = peer[d]
+    def send(d, slot, p, o, w=M, later=True):
+        dst, a, sem = peer[d], landing(slot, p), slot + "ab"[p]
         rid, pid = topo.addr(dst, core)
-        k = remote([B(msg, 0, M)], lambda q: q.remote_dma(out_ap=T[slot][:, :], in_ap=T[msg][:, :], remote_sem=T.sem[slot + "_"],
-                                                          local_sem=T.sem.ls, pid=pid, routing_id=rid,
-                                                          dma_engine_mask=topo.mask(core, dst)))
+        k = remote([B("mo", o, o + w)], lambda q: q.remote_dma(out_ap=T.mi[:, a:a + w], in_ap=T.mo[:, o:o + w],
+                                                               remote_sem=T.sem[sem], local_sem=T.sem.ls, pid=pid, routing_id=rid,
+                                                               dma_engine_mask=topo.mask(core, dst)), last[:1] * (w > M and later))
         sent[0] += len(topo.engines(core, dst))
         last[0] = k
-        arrives([B(slot, 0, M)], [], slot + "_", len(topo.engines(peer[-d], core)), k, WAY)
+        arrives([B("mi", a, a + w)], [], sem, len(topo.engines(peer[-d], core)), k, ("way", 1.0))
 
     def send_table(d):
         cs, he = carriers(rank, T, topo), hand_engines(rank, T, topo)
@@ -469,101 +639,160 @@ def rank_program(g, core, T, topo):
         pieces = [tr(peer[-d], 0, "t%d" % d, "tab%d" % d)] + [tr(cs[k], k, "h%d" % d, "hand%d" % d) for k in range(1, len(cs))]
         tab = B("tab0", 0, 2048)
         k = remote([tab], lambda q: q.remote_dma_fused(pieces, local_sem=T.sem.tl))
-        arrives([], [tab], "tl", d * sum(h[1] for h in he), k, COPY / 2)
+        arrives([], [tab], "tl", d * sum(h[1] for h in he), k, ("copy", 0.5))
         far = [len(topo.engines(c, core)) for c in carriers((rank + d) % n, T, topo)[1:]]
-        arrives([B("tab%d" % d, 0, WT)], [], "t%d" % d, hand_engines((rank + d) % n, T, topo)[0][1] + sum(far), k, COPY)
+        arrives([B("tab%d" % d, 0, WT)], [], "t%d" % d, hand_engines((rank + d) % n, T, topo)[0][1] + sum(far), k, ("copy", 1.0))
         return k
 
-    turn_in("ing", "gli")
+    cp(B("ing", 0, 256), ind(B("gli", 0, 256), B("pin", 0, 16)))
     cp(B("offx"), B("ing"))
     hold.append(len(ops) - 1)
     cp(P("g0", 0, PAIRS, 2), B("ing", 0, 256))
     hold.pop()
     cp(P("g0", 0, 0), ST("ing", 15, U, 16))
+    for k, cols in ((1, PAIRS), (0, WHOLE)):
+        none(OPT["f0"], P("em", k, cols), P("g0", k, cols))
     lists(0, B("ing"), P("g0", 1))
     sums = X("b4", slice(0, 24), 0)
-    group([(sums, B("zm", 15 - r, 143 - r), ST("yvs", r, 384, 16)) for r in range(16)])
-    act(B("tex", 0, 8), X("b4", slice(0, 8), 0), scale=-1.0, bias=BIG)
-    act(B("tex", 8, 24), X("b4", slice(8, 24), 0), scale=-1.0, bias=BIG + 128.0)
+    group([[(sums, B("zm", 15 - r, 143 - r), ST("yvs", r, 384, 16)) for r in range(16)]])
+    act(B("tex", 0, 24), sums, bias=MID)
+    for lo, hi in ((0, 8), (8, 24)):
+        act(B("spr", 16 * lo, 16 * hi), ind(B("tex", 0, 24), B("seg", lo, hi)))
     views(0)
-    iota(B("iw", 0, WT), [[1, WT]], 0, 0, [send_table(1)])
-    turn_in("th2", "thi")
-    cp(P("tha", 0, PAIRS, 2), B("th2", 0, 256))
-    turn_in("ina", "ali")
+    iota(B("iw", EARLY, WT), [[1, WT - EARLY]], EARLY, 0, [send_table(1)])
+    {"V": cp, "S": act}[OPT["ina"]](B("ina", 0, 256), ind(B("ali", 0, 256), B("pin", 0, 16)))
+
+    def put_back(t, parts):
+        return [(P("b7", 2, h=h), B("id1"), P("yvs", t, h=h)) for h in [fused[l, p] for l in range(2) for p in parts] if h]
+
+    def writes(t, p):
+        h = c0, c1 = PARTS[p]
+        o = M * (2 * t + p)
+        scan(B("s2", S * c0, S * c1), P("nm", h=h), B("ky", S * c0, S * c1), A.mult, A.max)
+        scan(B("s3", S * c0, S * c1), P("nm", h=h), B("b5", S * c0, S * c1), A.mult, A.max)
+        if OPT["soff"][p] == "V":
+            ts(B("soff", c0, c1), ST("s2", S * c0 + 16, S * c1, S), -1.0, A.mult, 2048.0 - 256 * c0, A.add)
+        else:
+            act(B("soff", c0, c1), ST("s2", S * c0 + 16, S * c1, S), scale=-1.0, bias=2048.0 - 256 * c0, func=F.Relu)
+        ts(B("gi", c0, c1), ST("s3", S * c0 + 16, S * c1, S), 4095, A.bitwise_and)
+        cp(B("goff", c0, c1), B("gi", c0, c1))
+        cp(B("gf", c0, c1), B("gi", c0, c1))
+        halves = P("b7", 2, h=h)
+        for k in range(2):
+            act(B("xv", 32 * c0 + 64 * k, 32 * c0 + 64 * k + 64),
+                ind(B("xg", 256 * (8 * k + c0), 256 * (8 * k + c1)), B("soff", c0, c1)))
+        group([(halves, B("id1"), B("xv", a, a + 64)) for a in (32 * c0, 32 * c0 + 64)] + put_back(t, [p]))
+        act(B("mo", o, o + 64), halves, scale=0.5, bias=-0.25)
+        {"V": cp, "S": act}[OPT["bf"][p]](B("bf", 16 * c0, 16 * c1), ind(B("iw", 0, WT), B("goff", c0, c1)))
+        cp(ST("eq", L * c0 + 64, L * c1, L), B("gi", c0, c1))
+        for c in range(c0, c1):
+            ts(B("eq", L * c, L * c + 64), B("bf", 16 * c0, 16 * c1), B("gf", c, c + 1), A.is_equal, 0.25, A.mult)
+        scan(B("sc", L * c0, L * c1), B("w", L * c0, L * c1), B("eq", L * c0, L * c1), A.mult, A.max)
+        {"V": cp, "S": act}[OPT["mo"][p]](B("mo", o + 64, o + 68), ST("sc", L * c0 + 64, L * c1, L))
+        send(*((-1, "a1"), (-1, "e2"), (2, "c0"))[t], p, o)
+        if (t, p) == (1, 1):
+            send(1, "e0", 0, o - M, 2 * M)
+
+    def writes_whole(t):
+        o = 2 * M * t
+        scan(X("s2"), X("nm"), X("ky"), A.mult, A.max)
+        scan(X("s3"), X("nm"), B("b5", 0, 8 * S), A.mult, A.max)
+        ts(B("soff", 0, 8), ST("s2", 16, 8 * S, S), -1.0, A.mult, 2048.0, A.add)
+        ts(B("gi", 0, 8), ST("s3", 16, 8 * S, S), 4095, A.bitwise_and)
+        cp(B("goff", 0, 8), B("gi", 0, 8))
+        cp(B("gf", 0, 8), B("gi", 0, 8))
+        for k in range(2):
+            act(B("xv", U * k, U * k + U), ind(B("xg", 2048 * k, 2048 * k + 2048), B("soff", 0, 8)))
+        group([(P("b7", 2), B("id1"), B("xv", a, a + U)) for a in (0, U)] + put_back(t, [0, 1]))
+        act(B("mo", o, o + U), P("b7", 2), scale=0.5, bias=-0.25)
+        cp(B("bf"), ind(B("iw", 0, WT), B("goff", 0, 8)))
+        cp(ST("eq", 64, 8 * L, L), B("gi", 0, 8))
+        for c in range(8):
+            ts(B("eq", L * c, L * c + 64), B("bf", 64 * (c // 4), 64 * (c // 4) + 64), B("gf", c, c + 1), A.is_equal, 0.25, A.mult)
+        scan(X("sc"), X("w"), X("eq"), A.mult, A.max)
+        cp(B("mo", o + U, o + U + 8), ST("sc", 64, 8 * L, L))
+        send(*((-1, "a1"), (-1, "e2"), (2, "c0"))[t], 0, o, 2 * M, False)
+        if t == 1:
+            send(1, "e0", 0, o, 2 * M)
 
     def visit(t):
         s = t % 2
-        gg, tab, msg = "g%d" % s, "tab%d" % t, "m%d" % t
+        gg = "g%d" % s
         thresholds(t)
-        keys = [B("b5", 8 * S * k, 8 * S * (k + 1)) for k in range(3)]
-        for o, src in zip(keys, (X("nx"), P(gg, 0, WHOLE), P(gg, 1, WHOLE))):
-            group([(o, B("id2048"), X("jc")), (o, B("id1"), src)])
-        psum("b1", 1, [("idbig", "ones", 0, ""), ("id4096", "f8", 0, "")])
-        gather(t, 0)
-        for c in (0, 4):
-            group(sums_of(0, c, c + 4))
-        cp(P("sgx"), P("b1"))
+        group([(B("b5", 256, 384), B("idbig"), P("em")), (B("b5", 0, 8 * S), B("id32"), X("jc")),
+               (B("b5", 0, 8 * S), B("id1"), X("nx"))])
+        if not OPT["split"][t]:
+            for l in range(2):
+                for p, h in enumerate(PARTS):
+                    gather(t, l, p)
+                    group(sums_of(t, l, p))
+            cp(P("sgx"), P("b1"))
+            tt(P("op", 1), P("b2"), P("thr", 1), A.is_gt)
+            tt(P("mnu"), P("b2"), P("sgx"), A.min)
+            tt(P("oyf"), P("op", 1), P("b5", 2), A.is_gt)
+            tt(P("mnm"), P("mnu"), P("b5", 2), A.subtract)
+            for p in range(2):
+                gather(t, 2, p)
+            z = [sums_of(t, 2, p) for p in range(2)]
+            group(terms("b3", 0, [("idbig", "em", 1, "f")]) + z[0] + z[1][:1]
+                  + terms("b3", 0, [("idbig", "op", 1, "P"), ("idbig", "oyf", 0, "")]) + z[1][1:])
+            tt(P("nm"), P("b3", 0, WHOLE), P("mnm", 0, WHOLE), A.is_ge)
+            writes_whole(t)
+        for p, h in enumerate(PARTS if OPT["split"][t] else ()):
+            gather(t, 0, p)
+            group(sums_of(t, 0, p))
+            cp(P("sgx", h=h), P("b1", h=h))
+            gather(t, 1, p)
+            group(sums_of(t, 1, p))
+            tt(P("op", 1, h=h), P("b2", h=h), P("thr", 1, h=h), A.is_gt)
+            tt(P("mnu", h=h), P("b2", h=h), P("sgx", h=h), A.min)
+            tt(P("oyf", h=h), P("op", 1, h=h), P("b5", 2, h=h), A.is_gt)
+            tt(P("mnm", h=h), P("mnu", h=h), P("b5", 2, h=h), A.subtract)
+            gather(t, 2, p)
+            z = sums_of(t, 2, p)
+            group(terms("b3", 0, [("idbig", "em", 1, "f")], h) + z[:1]
+                  + terms("b3", 0, [("idbig", "op", 1, "P"), ("idbig", "oyf", 0, "")], h) + z[1:])
+            tt(P("nm", h=h), P("b3", 0, WHOLE, h=h), P("mnm", 0, WHOLE, h=h), A.is_ge)
+            writes(t, p)
+        if t == 0:
+            hold.append(gathered[-1])
+            {"V": cp, "S": act}[OPT["inb"]](B("inb", 0, 256), ind(B("bli", 0, 256), B("pin", 0, 16)))
+            hold.pop()
         cp(P("sgx", 0, 0), P("b1", 0, 16))
         tt(P("op"), P("b1"), P("thr"), A.is_gt)
-        gather(t, 1)
-        for c in (0, 4):
-            group(sums_of(1, c, c + 4))
-        tt(P("op", 1), P("b2"), P("thr", 1), A.is_gt)
-        tt(B("mnu"), P("b2"), P("sgx"), A.min)
         tt(P("near"), P("b2"), P("sgx", 0, slice(0, 16)), A.is_lt)
-        tt(P("oyf"), P("op", 1), P("b1", 1), A.is_gt)
-        tt(P("mnm"), B("mnu"), P("b1", 1), A.subtract)
-        gather(t, 2)
-        if t == 0:
-            hold.append(len(ops) - 1)
-            turn_in("inb", "bli")
-            weights()
-            hold.pop()
+        tt(P("u"), P("b3"), P("mnu"), A.is_lt)
         sources_early(t)
-        group(terms("b3", 0, [("idbig", "ones", 0, "f"), ("id4096", "f8", 1, "")]) + sums_of(2, 0, 4)
-              + terms("b3", 0, [("idbig", "op", 1, "P"), ("idbig", "oyf", 0, "")]) + sums_of(2, 4, 8))
-        tt(X("nm"), P("b3", 0, WHOLE), X("mnm"), A.is_ge)
-        tt(P("u"), P("b3"), B("mnu"), A.is_lt)
-        for k in range(3):
-            scan(B("s3", 8 * S * k, 8 * S * (k + 1)), X("nm"), keys[k], A.mult, A.max)
-        for lo, hi in ((0, 8), (8, 24)):
-            ts(B("gi", lo, hi), ST("s3", S * lo + 16, S * hi, S), 4095, A.bitwise_and)
-            cp(B("goff", lo, hi), B("gi", lo, hi))
-        cp(B("gf", 0, 8), B("gi", 0, 8))
-        halves = P("b3", 2)
-        act(B("xv", 0, 256), ind(B(tab, 0, 2048), B("goff", 8, 24)))
-        group([(halves, B("zh"), B("xv", o, o + 128)) for o in (0, 128)])
-        act(B(msg), halves, bias=-0.25)
-        first.append(len(ops) - 1)
-        cp(B("bf", 0, 128), ind(B("iw", 0, WT), B("goff", 0, 8)))
-        cp(ST("eq", 16, 503, 162), B("gi", 0, 4))
-        cp(ST("eq", 583, 144, -146), B("gi", 4, 8))
-        for c in range(8):
-            o = start_of(c)
-            ts(B("eq", o, o + 16 * c + 16), B("bf", 0, 16 * c + 16), B("gf", c, c + 1), A.is_equal, 0.25, A.mult)
-        scan(B("sc", 0, EQ), B("w", 0, EQ), B("eq", 0, EQ), A.mult, A.max)
-        cp(B(msg, 128, 132), ST("sc", 16, 503, 162))
-        cp(B(msg, 132, 136), ST("sc", 583, 144, -146))
-        slots = ((("a1", -1),), (("e2", -1), ("e0", 1)), (("c0", 2),))[t]
-        for slot, d in slots:
-            send(d, slot, msg)
         new_places(t)
         memories(t)
         if t < 2:
             hh = "g%d" % (1 - s)
             if t == 0:
-                act(P("thb"), P("th2", 1), behind=gathered[-1:])
-                for a, b in TURNS["N"]:
-                    act(P("thb", 1, a), P("tha", 0, b), behind=gathered[-1:])
+                act(X("tht", ALL, 0), X("tht", ALL, 32), behind=gathered[-1:])
             views(t + 1)
+            if FUSE < U:
+                for c in range(FUSE // 16, 8):
+                    o = 256 * c - 16 * FUSE
+                    act(B("vx", o, o + 64), X("b0", c, ALL))
+                    for w in (64, 128):
+                        act(B("vx", o + w, o + 2 * w), B("vx", o, o + w))
             count(t + 1)
-            act(P(hh, 0, WHOLE), P("b6", 0, WHOLE))
+            (a, b), (c, d) = TURNS[("0", "P0")[t]]
+            less("S", P(hh, 0, a), P("b6", 0, b))
+            if OPT["pad"] == "S":
+                less("S", P(hh, 0, c), P("b6", 0, d))
+            else:
+                cp(P(hh, 0, c), P(hh, 0, 16 - c))
             act(P(hh, 1), P("b1"))
+            none(OPT["fl"][0], P("em", 0, WHOLE), P(hh, 0, WHOLE))
+            none(OPT["fl"][1], P("em", 1), P("b1") if OPT["fl"][1] == "S" else P(hh, 1))
             lists(t + 1, P(hh), P("b1"))
         if t == 2:
             cp(B("tab0", NONE, NONE + 1), B("xsav", 1, 2))
-        for into, m in ((("tab0", "m0"), ("tab1", "a1")), (("tab2", "e2"),), ())[t]:
-            scatter(into, m, [last[0]])
+        todo = [("tab0", "mo", 0, p) for p in range(2)] * (t == 0)
+        todo += [("tab%d" % (t + 1), "mi", landing(SLOTS[t], 0), p) for p in range(2)] * (t < 2)
+        for into, m, o, p in todo:
+            scatter(into, m, o, p, t, [last[0]] + made * (into == "tab1"))
             last[0] = len(ops) - 1
         if t == 0:
             send_table(2)
@@ -571,14 +800,16 @@ def rank_program(g, core, T, topo):
     for t in range(3):
         visit(t)
     act(B("wg"), P("b1"))
-    act(B("wg", U, 2 * U), P("b6"))
-    for w, b, q, sm in (("wg", "ogs", T.og, "sog"), ("wa", "oas", T.oa, "soa"), ("wb", "obs", T.ob, "sob")):
-        (act if w == "wg" else cp)(B(b, 0, 256), ind(B(w, 0, 256), B("pout", 0, 16)))
-        k = len(ops) - 1
-        dma("S" if w == "wg" else "Y", sm, [], [B(b, 0, 256)], q[:, :], T[b][:, :], STORE)
-    for m in ("e0", "c0"):
-        scatter("tab0", m, [k])
-    dma("Y", "sox", [], [B("tab0", 0, 2048)], T.ox[:, :], T.tab0[:, 0:2048], STORE)
+    less("S", B("wg", U, 2 * U), P("b6"))
+    act(B("ogs", 0, 256), ind(B("wg", 0, 256), B("pout", 0, 16)))
+    {"V": cp, "S": act}[OPT["oas"]](B("oas", 0, 256), ind(X("wm", 0, ALL), B("pout", 0, 16)))
+    {"V": cp, "S": act}[OPT["obs"]](B("obs", 0, 256), ind(X("wm", 1, ALL), B("pout", 0, 16)))
+    for b, q, sm in (("ogs", T.og, "sog"), ("oas", T.oa, "soa"), ("obs", T.ob, "sob")):
+        dma("Y", sm, [], [B(b, 0, 256)], q[:, :], T[b][:, :], ("", STORE - 0.8))
+    for t, m in ((1, "e0"), (2, "c0")):
+        for p in range(2):
+            scatter("tab0", "mi", landing(m, 0), p, t, [])
+    dma("Y", "sox", [], [B("tab0", 0, 2048)], T.ox[:, :], T.tab0[:, 0:2048], ("", STORE))
 
     cnt = issue()
     for sm in ("sog", "soa", "sob", "sox"):

@@ -5,31 +5,41 @@ from concourse.mybir import AluOpType as A
 from concourse.mybir import ActivationFunctionType as F
 
 U = 128
-S = 17
-PARTS = ((4, 8), (0, 4))
-M = 68
-GAP = 72
-L = 65
+M = 136
+FIRST = [146 * c if c < 4 else 162 * (7 - c) + 17 for c in range(8)]
+L = 4 * 146
 NONE = 2047
 WT = 2048 + 256
 BIG = 32768.0
-FUSE = 128
-MID = 2047.0
+MID = 2040.0
 FAR = 1024.0
-CUTS = {(0, 0): (64, 96, 128), (1, 0): (64, 112, 128), (2, 0): (64, 128), (0, 1): (0, 48, 64), (1, 1): (0, 48, 64),
-        (2, 1): (0, 32, 64)}
-ON_VECTOR = (((0, 96), (1, 112), (1, 48)), ((0, 96), (1, 112), (0, 48), (1, 48)), ((0, 96), (1, 112), (0, 48), (1, 48)))
-IDS = {"id1184": 1184.0, "id32": 32.0, "id65": 65.0, "idf": -1.0 / 32, "id217": 217.0,
-       "idbig": BIG, "idm": -1.0, "idnbig": -BIG, "id4096": 4096.0, "idn4096": -4096.0, "id2047": 2047.0, "idn2047": -2047.0}
-ON_SCALAR = ("id4096", "idn4096", "idn2047", "id2047", "idm")
-OPT = {"split": (1, 1, 1), "offx": "S", "off": ("VV", "SS", "SS"), "bf": "SV", "mo": "SV", "soff": "SV", "oas": "V", "pad": "V", "an": "VSS", "fl": "SS", "obs": "S", "inb": "S", "ina": "V", "f0": "V"}
-SLOTS = ("a1", "e2", "e0", "c0")
-EARLY = 512
+CUTS = ["SX3 VX9 SX16 SY8 SY16 SN6 SN12 SN16"] * 3
+
+
+def pieces(t):
+    at, out = {}, []
+    for p in CUTS[t].split():
+        out.append(("XYN".index(p[1]), at.get(p[1], 0), int(p[2:]), p[0]))
+        at[p[1]] = int(p[2:])
+    return out
+
+
+WHOLE = ((0, 0, 16), (1, 0, 16))
+SUMS = (WHOLE, WHOLE, WHOLE)
+WIDTH = 2
+FIFO = 1
+IDS = {"id1184": 1184.0, "id32": 32.0, "id65": 65.0, "idf": -1.0 / 32, "id217": 217.0, "idbig": BIG, "idm": -1.0,
+       "idnbig": -BIG, "id4096": 4096.0, "idn4096": -4096.0, "id2047": 2047.0}
+ON_SCALAR = ("id4096", "idn4096", "id2047", "idm")
+OPT = {"offx": "S", "off": ("VV", "SS", "SS"), "bf": ((0, 4, 8), "VS"), "mo": "VS", "eq": "VV", "an": "VSS", "em": "S",
+       "sg": "VV", "cnt": "S", "cast": "GVG", "op": "VVV", "er": "VVV", "xfirst": False, "late": 2,
+       "qn": ("VV", "VV", "VV"), "pad": "V", "out": "VVV", "tkb": "S"}
+OPT.update(off=("VV",) * 3, em="V", an="VVV", thpad="V", pack="S")
+EARLY = 1152
 CYC, ISSUE, STORE = 0.00083, 0.3, 3.0
-CLOCKS = ((1.0, 1.56, 3.8, 0.000525, 0.11, 1.9, 3.2, 8.0, 1.5), (1.35, 1.15, 3.0, 0.000525, 0.18, 2.0, 2.8, 8.0, 1.0),
-          (1.1, 1.95, 5.0, 0.000525, 0.15, 1.5, 3.2, 10.0, 1.5), (1.05, 1.25, 2.5, 0.000525, 0.06, 2.4, 3.6, 11.0, 2.0))
-PLANS = [(1.0, g, 3.8, 0.000525, wake, way, 2.8, 8.0, 1.0) for g in (1.4, 1.7) for wake in (0.08, 0.13, 0.18)
-         for way in (1.4, 1.9, 2.4)]
+CLOCKS = ((1.0, 1.56, 3.8, 0.000525, 0.1, 1.9, 3.9, 8.0, 1.5), (1.3, 1.3, 3.0, 0.000525, 0.15, 2.0, 3.2, 8.0, 1.0),
+          (1.0, 1.9, 5.0, 0.00042, 0.12, 1.5, 3.5, 10.0, 1.5), (1.1, 1.2, 2.5, 0.00047, 0.17, 2.4, 3.6, 11.0, 2.0))
+PLANS = list(CLOCKS) + [(1.0, g, 3.8, 0.000525, wake, 1.9, 3.6, 8.0, 1.0) for g in (1.4, 1.7) for wake in (0.08, 0.15)]
 
 SCRATCH = {}
 
@@ -39,60 +49,32 @@ def _add(where, dtype, **kw):
         SCRATCH[k] = (where, [128] + (v if isinstance(v, list) else [v]), dtype)
 
 
-L1, L2 = [8, S], [16, S]
-_add("sbuf", "bfloat16", tab0=WT, tab1=WT, tab2=WT, hand1=512, hand2=512, xsav=16, yvs=384, id1=128, idn18=128, z2=144, zm=144,
-     one=128, cb=128, jc=L1, kb=8 * S, xv=256, vx=1024, xg=48 * U, mx=48 * U)
-_add("sbuf", "int32", gli=256, ali=256, bli=256, thi=256, pidx=8, p15=8, p4=8, nxi=U, nxj=U, qyi=U, qyj=U, gi=8, s3=8 * S)
-_add("sbuf", "uint16", offx=U, offy=U, offn=U, goff=8, soff=8, same=8, pin=16, pout=16, seg=24, mo=6 * M, mi=8 * GAP)
-_add("sbuf", "float16", g0=L2, g1=L2, mem0=[32, S], mem1=[32, S], ab2=L2, em=L2, an=L2, qy=L1, nx=L1, ones=L1,
-     kq=U, op=L2, ty=L1, u=L1, oyf=L1, near=L1, nm=8 * S, cnt=8 * S, cnb=8 * S, rs=8 * S, rm=128, rl=[64, S], ing=256, ina=256,
-     inb=256, ids=128 * len(IDS), bf=128, eq=8 * L, w=8 * L, sc=8 * L, spr=3 * U, ky=8 * S, s2=8 * S)
-_add("sbuf", "float32", c16=24, c32=8, cn=16, col=16, dum=8, sp4=8, iw=WT, sgx=L1, mnu=U, mnm=L1, tex=24,
-     thr=2 * U, tht=[8, 34], pp=U, gf=8, wg=256, wm=[2, 256], ogs=256, oas=256, obs=256)
-_add("psum", "float32", b0=[8, 64], b5=512, **{"b%d" % k: [30, S] for k in (1, 2, 3, 4, 6, 7)})
-SEMAPHORES = ["pv", "pa", "pt", "pg", "dg", "dy", "dx", "ds", "da", "db", "dt", "sog", "soa", "sob", "sox", "tl", "ls", "h1",
-              "h2", "t1", "t2"] + [s + h for s in SLOTS for h in "ab" if s + h != "e0b"]
+RING, HALVES, PADDED = [32, 8], 2 * U, [2, U + 8]
+_add("sbuf", "bfloat16", tab=WT, xsav=16, yvs=384, ii=256, idn18=128, zs=16, one=256, cb=128, c8=128, xv=256, xg=48 * U,
+     mx=48 * U, vx0=512, vx1=512, vx2=512)
+_add("sbuf", "int32", gli=RING, pidx=8, pin=8, nxi=U, nxj=U, qyi=U, qyj=U,
+     **{b: RING if e != "S" else 256 for b, e in zip(("ali", "thi", "bli"), OPT["cast"])})
+_add("sbuf", "uint16", offx=U, offy=U, offn=U, goff=8, soff=8, same=8, apart=16, mo=M)
+_add("sbuf", "float16", em=PADDED, an=PADDED, er=HALVES, pack=784, pk1=528, pk2=528, fog=RING, foa=RING, fob=RING, fig=256,
+     fia=256, fib=256, qy=U, nx=U, kq=U, ones=256, sev=U, cm=U, cmid=U, nblk=U, sgx=U, sgy=U, mnu=U, opx=U, opy=U, ty=U, mg=U,
+     tk=U, rp=U, ff=U, nrm=U, blk=U, blk4=U, tri0=U, tri=U, shb=U, w2=8, rob2=U, sum0=U, ids=128 * len(IDS), bf=128, eq=L,
+     w=L, sc=L, rl=[64, 8], **{b % t: k for t in range(3) for b, k in (("g%d", 256), ("go%d", 256), ("m%d", 640), ("mo%d", 640))})
+_add("sbuf", "float32", c16=24, col=16, sp4=8, iw=WT, pp=U, tkb=U, gf=8, ogs=256, oas=256, obs=256)
+_add("psum", "float32", b0=512, **{"b%d" % k: [64, 8] for k in range(1, 8)})
+SEMAPHORES = ["pv", "pa", "pt", "pg", "dg", "dy", "dx", "ds", "da", "db", "dt", "sog", "soa", "sob", "sox", "ls", "pk1", "pk2",
+              "gx1", "gy1", "ma1", "mb1", "gx2", "gy2", "ma2", "mb2", "fig", "fia", "fib"]
 PART = {k: ("ids", 128 * j) for j, k in enumerate(IDS)}
-PART.update(id1=("id1", 0), idn18=("idn18", 0))
+PART.update(id1=("ii", 0), up=("ii", 8), idn18=("idn18", 0), th0=("pack", 256), th1=("pk1", 256), th2=("pk2", 0), v0=("yvs", 0),
+            v1=("pk1", U), v2=("pk2", 272), out1=("pack", 0), out2=("pack", 656), sum1=("pk1", 0), sum2=("pk2", 400))
+for _t in range(3):
+    PART.update({"ma%d" % _t: ("m%d" % _t, 256), "mb%d" % _t: ("m%d" % _t, 0), "cnt%d" % _t: ("m%d" % _t, 512),
+                 "ao%d" % _t: ("mo%d" % _t, 256), "bo%d" % _t: ("mo%d" % _t, 0), "co%d" % _t: ("mo%d" % _t, 512)})
 COLS = {k: np.arange(int(np.prod(v[1][1:]))).reshape(v[1][1:]) for k, v in SCRATCH.items()}
 WIDE = {k: v[2] in ("float32", "int32") for k, v in SCRATCH.items()}
 COUNTER = {"V": "pv", "S": "pa", "P": "pt", "G": "pg"}
-ROUNDS, MOVES, SLACK, SEED = 3, 40000, 0.001, 1
+LOOK, MOVES, SLACK, SEED, ROUNDS, RELAX = 0.5, 40000, 0.001, 1, 4, 0.0
+SOONER = {"opx": 2.0, "opy": 1.0, "em": 2.0}
 ORDER = []
-PAIRS, WHOLE = slice(1, S), slice(0, S)
-TURNS = {"": [(PAIRS, PAIRS)], "f": [(WHOLE, WHOLE)], "n": [(PAIRS, slice(0, 16))], "N": [(slice(2, S), slice(1, 16)), (1, 16)],
-         "P": [(slice(1, 16), slice(2, S)), (16, 1)], "P0": [(slice(0, 16), PAIRS), (16, 1)], "0": [(PAIRS, PAIRS), (0, 16)]}
-
-
-def carriers(rank, T, topo):
-    n, own = len(T.cores), T.cores[rank]
-    to = [T.cores[(rank - d) % n] for d in (1, 2)]
-    return [own] + [c for c in topo.cores_of(own) if c != own and all(topo.may_write(c, d) for d in to)]
-
-
-def hand_engines(rank, T, topo):
-    own, cs = T.cores[rank], carriers(rank, T, topo)
-    out = topo.engines(own, T.cores[(rank - 1) % len(T.cores)])
-    e = out + [x for x in topo.engines(own, cs[1]) if x not in out]
-    h = len(e) // len(cs)
-    return [(sum(1 << x for x in e[k * h:k * h + h]), h) for k in range(len(cs))]
-
-
-def helper_program(g, core, T, topo):
-    n = len(T.cores)
-    for rank in range(n):
-        cs = carriers(rank, T, topo)
-        if core in cs[1:]:
-            k, w = cs.index(core), 2048 // len(cs)
-            sent = 0
-            for d in (1, 2):
-                dst = T.cores[(rank - d) % n]
-                rid, pid = topo.addr(dst, core)
-                g.wait_ge(T.sem["h%d" % d], hand_engines(rank, T, topo)[k][1])
-                g.remote_dma(out_ap=T["tab%d" % d][:, k * w:k * w + w], in_ap=T["hand%d" % d][:, 0:w], remote_sem=T.sem["t%d" % d],
-                             local_sem=T.sem.ls, pid=pid, routing_id=rid, dma_engine_mask=topo.mask(core, dst))
-                sent += len(topo.engines(core, dst))
-            g.wait_ge(T.sem.ls, sent)
 
 
 def timing(ops, clock):
@@ -167,7 +149,8 @@ def issue_order(ops):
         above.append(far | sum(1 << d for d in o["deps"]))
     ops = [dict(o, deps=d) for o, d in zip(ops, near)]
     clocks = [timing(ops, c) for c in CLOCKS]
-    order = min((list_schedule(ops, timing(ops, c)) for c in PLANS), key=lambda o: sum(replay(o, queue, c)[0] for c in clocks))
+    order = min((o for c in PLANS for o in list_schedule(ops, timing(ops, c))),
+                key=lambda o: sum(replay(o, queue, c)[0] for c in clocks))
     deps = [set(o["deps"]) | {d for d in o["behind"] if o["firm"]} for o in ops]
     state = [replay(order, queue, c) for c in clocks]
     scale = [len(clocks) * s[0] for s in state]
@@ -222,57 +205,69 @@ def issue_order(ops):
 
 def list_schedule(ops, times):
     cost, tails, lags = times
+    n = len(ops)
     lag = [dict([(d, 0.0) for d in o["behind"]] + l) for o, l in zip(ops, lags)]
-    back = [{} for _ in ops]
+    after = [[] for _ in ops]
     for k, l in enumerate(lag):
         for d, x in l.items():
-            back[d][k] = x
-
-    def place(before, after, key, first):
-        left, at, start = [len(b) for b in before], list(first), [0.0] * len(ops)
-        busy = {e: [] for e in "VSPGY"}
-        ready = sorted((key[k], k) for k in range(len(ops)) if not left[k])
-        while ready:
-            k = ready.pop(0)[1]
-            t0, c = at[k], cost[k]
-            if ops[k]["e"] != "D":
-                q = busy[ops[k]["e"]]
-                i = len(q)
-                while i and q[i - 1][1] > t0:
-                    i -= 1
-                while i < len(q) and q[i][0] < t0 + c - 1e-9:
-                    t0 = max(t0, q[i][1])
-                    i += 1
-                q.insert(i, (t0, t0 + c))
-            start[k] = t0
-            for x, l in after[k].items():
-                at[x] = max(at[x], t0 + c + l)
-                left[x] -= 1
-                if not left[x]:
-                    ready.append((key[x], x))
-            ready.sort()
-        return start
-
-    key, best = [-k for k in range(len(ops))], None
+            after[d].append((k, x))
+    key = [0.0] * n
+    for k in range(n - 1, -1, -1):
+        key[k] = cost[k] + max([tails[k]] + [x + key[j] for j, x in after[k]]) + SOONER.get(ops[k]["name"], 0.0)
+    out = []
     for _ in range(ROUNDS):
-        rev = place(back, lag, key, tails)
-        fwd = place(lag, back, [-rev[k] - cost[k] for k in range(len(ops))], [0.0] * len(ops))
-        end = max(fwd[k] + cost[k] + tails[k] for k in range(len(ops)))
-        if best is None or end < best[0]:
-            best = (end, fwd)
-        key = [-fwd[k] - cost[k] for k in range(len(ops))]
-    return sorted(range(len(ops)), key=lambda k: (best[1][k], k))
+        out.append(dispatch(ops, cost, lag, after, key))
+        way, nxt = [0.0] * n, {}
+        for k in out[-1][::-1]:
+            e = ops[k]["e"]
+            way[k] = cost[k] + max([tails[k], nxt.get(e, 0.0) - RELAX] + [x + way[j] for j, x in after[k]])
+            if e != "D":
+                nxt[e] = way[k]
+        key = [(a + b) / 2 for a, b in zip(key, way)]
+    return out
+
+
+def dispatch(ops, cost, lag, after, key):
+    n = len(ops)
+    left, at = [len(l) for l in lag], [0.0] * n
+    pool, free, order = {e: [] for e in "DVSPGY"}, {e: 0.0 for e in "DVSPGY"}, []
+    for k in range(n):
+        if not left[k]:
+            pool[ops[k]["e"]].append(k)
+    while len(order) < n:
+        best = None
+        for e, p in pool.items():
+            if not p:
+                continue
+            t = max(free[e], min(at[x] for x in p))
+            k = max((x for x in p if at[x] <= t + 1e-9), key=lambda x: key[x])
+            soon = [x for x in p if t < at[x] < t + LOOK * cost[k] and key[x] > key[k] + 0.3]
+            if soon:
+                k = max(soon, key=lambda x: key[x])
+            if best is None or (max(t, at[k]), k) < best:
+                best = (max(t, at[k]), k)
+        t, k = best
+        e = ops[k]["e"]
+        pool[e].remove(k)
+        if e != "D":
+            free[e] = t + cost[k]
+        order.append(k)
+        for j, x in after[k]:
+            at[j] = max(at[j], t + cost[k] + x)
+            left[j] -= 1
+            if not left[j]:
+                pool[ops[j]["e"]].append(j)
+    return order
 
 
 def rank_program(g, core, T, topo):
     rank = T.rank_of(core)
     if rank is None:
-        helper_program(g, core, T, topo)
         return
     n = len(T.cores)
     Q = {"V": g.vector, "S": g.scalar, "P": g.tensor, "G": g, "Y": g.sync}
 
-    ops, writer, readers, bank, gathered, hold, made, fused = [], {}, {}, {}, [], [], [], {}
+    ops, writer, readers, bank, gathered, hold, made, adds, ends = [], {}, {}, {}, [], [], [], [], {}
 
     def note(e, outs, ins, call, cost, tail=("", 0.0), sem=None, deps=(), behind=(), firm=False):
         k, deps = len(ops), set(deps)
@@ -292,7 +287,7 @@ def rank_program(g, core, T, topo):
                 w[cols] = k
         for ap, parts in ins:
             for b, cols in parts:
-                if b not in ("ids", "zm", "z2"):
+                if b not in ("ids", "ii", "zs"):
                     readers.setdefault(b, {}).setdefault(k, np.zeros(COLS[b].size, bool))[cols] = True
         for b in {b for ap, parts in list(ins) + list(outs) for b, cols in parts if SCRATCH[b][0] == "psum"}:
             rec = bank.setdefault(b, [e, [], []])
@@ -333,28 +328,34 @@ def rank_program(g, core, T, topo):
 
     ALL = slice(None)
 
-    def X(b, *ix):
+    def X(b, *ix, rows=ALL):
         ix = ix or (ALL,) * COLS[b].ndim
-        return (T[b][(ALL,) + ix], [(b, COLS[b][ix].reshape(-1))])
+        return (T[b][(rows,) + ix], [(b, COLS[b][ix].reshape(-1))])
 
-    def B(b, lo=0, hi=U):
+    def B(b, lo=0, hi=U, rows=ALL):
         if b in PART:
             b, o = PART[b]
-            lo, hi = o, o + 128
-        return X(b, slice(lo, hi))
+            lo, hi = o + lo, o + hi
+        return X(b, slice(lo, hi), rows=rows)
 
     def ST(b, lo, hi, step):
         return X(b, slice(lo, hi, step))
 
-    def P(b, k=0, cols=PAIRS, lists=1, h=(0, 8)):
-        if b == "nm":
-            return B(b, S * h[0], S * h[1])
-        if COLS[b].ndim == 1:
-            return B(b, U * k + 16 * h[0], U * (k + lists - 1) + 16 * h[1])
-        return X(b, slice(8 * k + h[0], 8 * (k + lists - 1) + h[1]), cols)
+    def R(b, lo=0, hi=32):
+        return X(b, slice(lo, hi), ALL)
 
-    def memory(t, m, k):
-        return ("in" + m, k) if t == 0 else ("mem%d" % (t % 2), {"b0": 0, "a0": 1, "a1": 2, "b1": 3}[m + str(k)])
+    def E(b, lo, k=16, base=0):
+        if b in PART or COLS[b].ndim == 1:
+            half = U + 8 * (b in ("th0", "th1", "th2"))
+            return B(b, half * (lo % 2) + 8 * (lo // 2), half * (lo % 2) + 8 * (lo // 2 + k))
+        if len(COLS[b]) == 2:
+            return X(b, lo % 2, slice(8 * (lo // 2), 8 * (lo // 2 + k)))
+        if SCRATCH[b][0] == "psum":
+            return R(b, base + 16 * (lo % 2) + lo // 2, base + 16 * (lo % 2) + lo // 2 + k)
+        return X(b, slice(lo, lo + 2 * k - 1, 2), ALL)
+
+    def H(b, lo=0, hi=U):
+        return B(b, 0, 2 * U) if b in PART or COLS[b].ndim == 1 else X(b, ALL, slice(lo, hi))
 
     def ind(w, o):
         return (w[0].indirect(o[0]), w[1] + o[1])
@@ -395,28 +396,18 @@ def rank_program(g, core, T, topo):
         note("S", [o], [a] + cols, lambda q: q.activation(out=o[0], in_=a[0], func=func, bias=y, scale=x),
              (80, k, "g") if len(a[1]) > 1 else (80 + max(64, k), 0, "c"), behind=behind)
 
-    def matmul(o, l, r, start, stop):
-        note("P", [o], [l, r], lambda q: q.matmul(out=o[0], lhsT=l[0], rhs=r[0], start=start, stop=stop),
-             (0.0, max(64, len(o[1][0][1])), "p"))
+    def block(out, mats, each, start=False):
+        end, bk = [len(mats) - 1], out[1][0][0]
+        if not start:
+            ends[bk][0] = -1
+        ends[bk] = end
+        note("P", [out], [x for o, l, r in mats for x in (l, r)],
+             lambda q: [q.matmul(out=o[0], lhsT=l[0], rhs=r[0], start=start and k == 0, stop=k == end[0])
+                        for k, (o, l, r) in enumerate(mats)], (0.0, each * len(mats), "p"))
 
-    def block(mats, start, stop):
-        last = len(mats) - 1
-        note("P", [mats[0][0]], [x for o, l, r in mats for x in (l, r)],
-             lambda q: [q.matmul(out=o[0], lhsT=l[0], rhs=r[0], start=start and k == 0, stop=stop and k == last)
-                        for k, (o, l, r) in enumerate(mats)], (0.0, 64 * len(mats), "p"))
-
-    def group(mats, start=True):
-        for k, m in enumerate(mats):
-            if isinstance(m, list):
-                block(m, start and k == 0, k == len(mats) - 1)
-            else:
-                matmul(*m, start and k == 0, k == len(mats) - 1)
-
-    def terms(bk, k, ts_, h=(0, 8)):
-        return [(P(bk, k, a, h=h), B(l), P(buf, c, b, h=h)) for l, buf, c, turn in ts_ for a, b in TURNS[turn]]
-
-    def psum(bk, k, ts_):
-        group(terms(bk, k, ts_))
+    def group(mats, start=False):
+        for k, (o, l, r) in enumerate(mats):
+            block(o, [(o, l, r)], max(64, len(o[1][0][1])), start and k == 0)
 
     def dma(q, sem, outs, ins, out, in_, time, behind=()):
         return note(q, outs, ins, lambda e: e.dma_start(out=out, in_=in_), (0.05, 0, "r"), time, (sem, 16), behind=behind)
@@ -426,6 +417,10 @@ def rank_program(g, core, T, topo):
         return note("G", [o], [], lambda q: q.iota(o[0], pattern, base, cm, **more), (0.13, 2 * len(o[1][0][1]), "c"),
                     behind=behind)
 
+    def pick(o, a, pattern, op, other, cm, behind=()):
+        return note("G", [o], [a], lambda q: q.affine_select(o[0], a[0], pattern, op, other, 0, cm),
+                    (0.17, 2 * len(o[1][0][1]), "c"), behind=behind)
+
     def remote(ins, call, behind=()):
         def run(q):
             call(q)
@@ -434,65 +429,61 @@ def rank_program(g, core, T, topo):
     def arrives(outs, ins, sem, val, since, time):
         note("D", outs, ins, None, (0.0, 0, "r"), time, (sem, val), [since])
 
-    fill(B("tab0", 2032, 2048), FAR)
+    fill(B("tab", 2032, 2048), FAR)
     k = dma("Y", "dy", [B("yvs", 0, 384)], [], T.yvs[:, :], T.yv[:, :], ("load", 0.55))
-    k = dma("Y", "dg", [B("gli", 0, 256)], [], T.gli[:, :], T.gl[:, :], ("load", 0.65), [k])
-    k = dma("Y", "dx", [B("tab0", 0, 2048)], [], T.tab0[:, 0:NONE], T.xt[:, 0:NONE], ("load", 1.0), [k])
+    k = dma("Y", "dg", [X("gli")], [], T.gli[:, :, :], T.gl[:, :], ("load", 0.65), [k])
+    k = dma("Y", "dx", [B("tab", 0, 2048)], [], T.tab[:, 0:NONE], T.xt[:, 0:NONE], ("load", 1.0), [k])
     for j, (sem, b, src) in enumerate((("da", "ali", T.al), ("dt", "thi", T.th), ("db", "bli", T.bl))):
-        k = dma("Y", sem, [B(b, 0, 256)], [], T[b][:, :], src[:, :], ("load", 1.12 + 0.1 * j), [k])
+        k = dma("Y", sem, [X(b)], [], X(b)[0], src[:, :], ("load", 1.12 + 0.1 * j), [k])
     dma("Y", "ds", [B("xsav", 0, 2)], [], T.xsav[:, 0:2], T.xt[:, NONE - 1:NONE + 1], ("load", 1.4), [k])
 
     def C(k):
         return B("col", k, k + 1)
 
     iota(B("pidx", 0, 2), [[0, 2]], 0, 1)
-    fill(B("one"), 1.0)
-    note("G", [B("id1")], [B("one")], lambda q: q.affine_select(T.id1[:, :], T.one[:, :], [[-1, 128]], A.is_equal, 0.0, 0, 1),
-         (0.17, 256, "c"))
-    iota(B("c16", 0, 24), [[1, 24]], 240, 0)
-    iota(B("c32", 0, 8), [[32, 8]], 2048, 0)
-    iota(B("cb", 0, 128), [[0, 8], [1, 16]], 0, 0)
-    iota(X("jc"), [[0, 8], [-128, S]], 2048, 0)
-    iota(B("kb", 0, 8 * S), [[-256, 8], [-16, S]], 2064, 0)
-    k = iota(B("cn", 0, 16), [[-1, 16]], 15, 0)
-    iota(B("iw", 0, EARLY), [[1, EARLY]], 0, 0, [k])
-    fill(X("ones"), 1.0)
-    fill(X("kq"), 1801.0 / 64)
-    fill(P("mnm", 0, 0), 4 * BIG)
-    fill(P("em", 1, 0), 0.0)
-    ts(B("p15", 0, 1), B("pidx", 0, 1), 15, A.bitwise_and)
-    ts(B("p4", 0, 1), B("pidx", 0, 1), 4, A.arith_shift_right)
-    ts(C(0), B("p15", 0, 1), 16.0, A.mult)
-    cp(C(2), B("p15", 0, 1))
-    ts(C(3), B("p4", 0, 1), 32.0, A.mult, 2048.0, A.add)
-    ts(B("pin", 0, 16), B("c16", 0, 16), C(0), A.subtract)
-    ts(B("pout", 0, 16), B("cn", 0, 16), C(0), A.add)
-    ts(B("rm", 0, 128), B("cb", 0, 128), C(2), A.is_equal)
+    fill(B("one", 0, 256), 1.0)
+    pick(B("ii", 0, 256), B("one", 0, 256), [[0, 2], [-1, 128]], A.is_equal, 0.0, 1)
+    iota(B("c16", 0, 16), [[8, 2], [32, 8]], 0, 0)
+    iota(B("cb"), [[0, 8], [1, 16]], 0, 0)
+    k = iota(B("c8"), [[0, 16], [1, 8]], 0, 0)
+    for a in range(0, EARLY, 576):
+        k = iota(B("iw", a, a + 576), [[1, 576]], a, 0, [k])
+    fill(B("ones", 0, 256), 1.0)
+    fill(B("kq"), 1801.0 / 64)
+    fill(B("sev"), 7.0)
+    fill(B("cm"), -2046.0)
+    for j, (x, op) in enumerate(((15, A.bitwise_and), (4, A.arith_shift_right), (7, A.bitwise_and), (3, A.arith_shift_right))):
+        ts(B("pin", j, j + 1), B("pidx", 0, 1), x, op)
+    cp(B("col", 0, 4), B("pin", 0, 4))
+    ts(C(4), C(3), 256.0, A.mult)
+    ts(C(5), C(0), 2.0, A.mult)
+    ts(B("nrm"), B("cb"), C(0), A.is_equal, -1.0, A.mult)
+    ts(B("blk"), B("c8"), C(2), A.is_equal)
+    ts(B("blk4"), B("c8"), C(2), A.is_equal, 4096.0, A.mult)
+    if any("C" in c for c in CUTS):
+        fill(B("cmid"), MID)
+        ts(B("nblk"), B("c8"), C(2), A.is_equal, -1.0, A.mult)
+    ts(B("w2", 0, 8), B("blk", 0, 8), C(4), A.mult)
+    for j, x in enumerate((-1.0, 2.0, -1.0)[:2]):
+        ts(B("zs", 8 * j, 8 * j + 8), B("c8", 0, 8), C(1), A.is_equal, x, A.mult)
+    ts(B("rob2"), B("c8"), 32.0, A.mult, C(5), A.add)
     for b in IDS:
         if b in ON_SCALAR:
             act(B(b), B("id1"), scale=IDS[b])
         else:
             ts(B(b), B("id1"), IDS[b], A.mult)
     ts(B("idn18"), B("id1"), -8 * BIG, A.mult)
-    fill(X("cnb"), 16.0)
-    ts(B("seg", 0, 24), B("c16", 0, 24), 240.0, A.subtract)
-    ts(X("rs"), X("jc"), 2048.0, A.not_equal)
-    ts(X("ky"), X("kb"), C(2), A.subtract)
-    fill(B("zm", 0, 144), 0.0)
-    ts(ST("zm", 15, 143, 16), B("c32", 0, 8), C(3), A.is_equal, -1.0, A.mult)
-    ts(B("z2", 0, 144), B("zm", 0, 144), -2.0, A.mult)
-    ts(B("dum", 0, 8), B("c32", 0, 8), C(2), A.add, C(2), A.add)
-    cp(P("nx", 0, 0), B("dum", 0, 8))
-    ts(B("same", 0, 8), B("dum", 0, 8), 0.5, A.mult, -1024.0, A.add)
-    ts(B("sp4", 0, 8), B("dum", 0, 8), 4.0, A.mult, -1.0, A.add)
-    fill(B("w", 0, 8 * L), 1.0)
+    ts(B("shb"), B("ii", 120, 248), BIG, A.mult)
+    ts(B("same", 0, 8), B("rob2", 0, 8), 0.5, A.mult)
+    ts(C(6), C(5), C(2), A.subtract)
+    ts(B("apart", 0, 16), B("c16", 0, 16), C(6), A.add)
+    ts(B("sp4", 0, 8), B("rob2", 0, 8), -4.0, A.mult, -8191.0, A.add)
+    fill(B("w", 0, L), 1.0)
     for c in range(8):
-        o = L * c + 16 * (c % 4)
-        act(B("w", o, o + 16), B("rm", 0, 16), scale=B("sp4", c, c + 1), bias=1.0, func=F.Identity)
-    fill(ST("w", 0, 8 * L, L), 0.0)
-
-    def less(e, o, a):
-        act(o, a, scale=-1.0, bias=2047.0)
+        o = FIRST[c] + 16 * c
+        act(B("w", o, o + 16), B("nrm", 0, 16), scale=B("sp4", c, c + 1), bias=1.0, func=F.Identity)
+    fill(ST("w", 0, L, 146), 0.0)
+    fill(ST("w", 17, L, 162), 0.0)
 
     def none(e, o, a):
         if e == "V":
@@ -500,316 +491,316 @@ def rank_program(g, core, T, topo):
         else:
             act(o, a, bias=-2046.0, func=F.Relu)
 
-    def views(t):
-        group([(X("b0", ALL, slice(k, k + 16)), B("id1"), B("yvs", t * 128, t * 128 + 128)) for k in range(0, 64, 16)])
+    def cast(e, o, b):
+        if e == "V":
+            cp(o, B(b))
+        else:
+            act(o, ind(B(b), B("same", 0, 8)))
 
-    def lists(t, xsrc, ysrc):
-        gg = "g%d" % (t % 2)
+    def split(e, o, b, bias=0.0):
+        if e != "S":
+            for k in range(2):
+                if e == "V":
+                    ts(E(o, k), E(b, k), bias, A.add)
+                else:
+                    pick(E(o, k), E(b, k), [[0, U]], A.is_equal, 0.0, 0)
+        else:
+            act(H(o), ind(X(b), B("apart", 0, 16)), bias=bias)
+
+    def views(t):
+        group([(B("b0", k, k + U), B("id1"), B("v%d" % t)) for k in range(0, U * WIDTH, U)], True)
+
+    few = slice(0, 8)
+
+    def view_sums(t):
+        bk = "b%d" % (5 + t)
+        block(R(bk, 0, 16), [(X(bk, slice(r // 8, 16, 2), r % 8, rows=few), ST("yvs", U * t + r, U * t + U, 16), B("zs", 0, 8))
+                             for r in range(16)], 8, True)
+        act(B(("sum0", "out1", "out2")[t], rows=few), X(bk, slice(0, 16), ALL, rows=few), bias=MID)
+
+    def wrapped(lo):
+        k = min(16, (33 - lo) // 2)
+        return ((0, k, lo), (k, 16, lo + 2 * k - 32))[:1 + (k < 16)]
+
+    def turned(o, terms):
+        return [(o, a, B(l)) for a, l in terms]
+
+    def kept(o, terms):
+        return [(o, B(l), a) for a, l in terms]
+
+    def to_rows(bk, base, lo, terms, turn=True):
+        out = []
+        for a, l in terms:
+            for j0, j1, r0 in wrapped(lo):
+                o = E(bk, r0, j1 - j0, base)
+                out.append((o, B(a), B(l, 8 * j0, 8 * j1)) if turn else (o, B(l), B(a, 8 * j0, 8 * j1)))
+        return out
+
+    def lists(t):
+        s, gg = t % 2, "g%d" % t
         if t:
-            {"V": cp, "S": act}[OPT["offx"]](B("offx"), xsrc)
-        tt(B("pp"), P(gg), ysrc, A.mult)
-        psum("b3", 1, [("id217", "kq", 0, ""), ("id65", gg, 0, "n"), ("idf", gg, 0, "n"), ("idn18", "em", 1, "")])
-        psum("b3", 0, [("id1184", gg, 0, ""), ("id32", gg, 1, "")])
-        tt(B("qyi"), P("b3", 1), P(gg, 1), A.min)
-        tt(B("nxi"), P("b3"), B("pp"), A.add)
+            {"V": cp, "S": act}[OPT["offx"]](B("offx"), E(gg, s))
+
+        def rows(bk, base, lo, l):
+            return [(R(bk, base + j0, base + j1), B(l), E(gg, r0, j1 - j0)) for j0, j1, r0 in wrapped(lo)]
+
+        group(kept(R("b2", 0, 16), [(B("cm"), "idn18")]) + rows("b2", 0, s + 1, "idn18") + kept(R("b2", 0, 16), [(B("kq"), "id217")])
+              + rows("b2", 0, s + 2, "id65") + rows("b2", 0, s + 2, "idf"), True)
+        group(rows("b3", 0, s, "id1184") + rows("b3", 32, s + 1, "id1") + rows("b3", 0, s + 1, "id32"), True)
+        tt(B("pp"), R("b3", 32, 48), E(gg, s), A.mult)
+        for o, l, a in rows("b2", 0, s + 1, "id1"):
+            j = o[1][0][1]
+            tt(B("qyi", int(j[0]), int(j[-1]) + 1), o, a, A.min)
+        tt(B("nxi"), R("b3", 0, 16), B("pp"), A.add)
         ts(B("qyj"), B("qyi"), 2047, A.bitwise_and)
         ts(B("nxj"), B("nxi"), 5, A.arith_shift_right, 2047, A.bitwise_and)
         for k, (o, a) in enumerate((("offy", "qyj"), ("offn", "nxj"))):
-            if OPT["off"][t][k] == "V":
-                cp(B(o), B(a))
-            else:
-                act(B(o), ind(B(a), B("same", 0, 8)))
-        made[:] = [len(ops) - 2, len(ops) - 1]
-        cp(P("qy"), B("offy"))
-        cp(P("nx"), B("offn"))
+            cast(OPT["off"][t][k], B(o), a)
+        for k, (o, a, b) in enumerate((("qy", "qyj", "offy"), ("nx", "nxj", "offn"))):
+            e = OPT["qn"][t][k]
+            {"V": cp, "v": cp, "S": act}[e](B(o), B(a if e == "v" else b))
+        none(OPT["em"], H("em"), H(gg))
+        {"V": cp, "S": act}[OPT["pad"]](H("em", U, U + 8), H("em", 0, 8))
 
-    def count(t):
-        back = slice(8 * S - 1, None, -1)
-        scan(X("cnt"), X("rs"), X("nm"), A.mult, A.add)
-        scan(X("cnb", back), X("rs"), X("cnt", back), A.mult, A.max)
+    DX, DY, DN = R("b1", 48, 64), R("b2", 48, 64), R("b3", 48, 64)
+    OX, OY, OT, TK = R("b7", 0, 16), R("b4", 0, 16), R("b7", 16, 32), R("b6", 0, 16)
 
-    def thresholds(t):
-        if t == 0:
-            for c in range(8):
-                ts(X("tht", c, slice(1, 33)), X("thi", slice(248 + c, None, -8)), BIG + MID + 128.0, A.add)
-        none(OPT["an"][t], P("an", 0, PAIRS, 2), P(*memory(t, "a", 0), PAIRS, 2))
-        for k in (1, 0):
-            group([(P("b7", k, WHOLE), B("rm"), X("cnb"))]
-                  + terms("b7", k, [("id1", "spr", t, ""), ("idnbig", "em", k, ""), ("idbig", "em", 1 - k, ("", "n")[k]),
-                                    ("idnbig", "an", k, "")]))
-        for k in (1, 0):
-            a = ((2, 1), (1, 0))[t % 2][k]
-            tt(P("thr", k), X("tht", ALL, slice(a, a + 31, 2)), P("b7", k), A.subtract)
+    def before(t):
+        s = t % 2
+        ex, ey, en = E("em", s), E("em", s + 1), E("em", s + 2)
+        none(OPT["an"][t], H("an"), H("ma%d" % t))
+        if s:
+            none(OPT["an"][t], E("an", 32, 1), E("ma1", 0, 1))
+        for l, d in enumerate((DX, DY, DN)):
+            fused = [j for k, j0, j1, e in pieces(t) if e == "C" and k == l for j in range(j0, j1)]
+            more = slice(0, 16)
+            group([(d, B("blk", rows=more), B("sum%d" % t, rows=more))], True)
+            for j0 in range(0, 16, 4):
+                if j0 in fused:
+                    o = X("b%d" % (l + 1), slice(48, 64), ALL, rows=slice(8 * j0, 8 * j0 + 32))
+                    group([(o, B("nblk", 8 * j0, 8 * j0 + 32, few), B("sum%d" % t, rows=few)), (o, B("id1", 0, 32), B("cmid"))])
+        group(turned(DN, [(ey, "idbig"), (ex, "idbig")]))
+        count = [(B("cnt%d" % t), "nrm")] * (t > 0)
+        group(turned(OX, [(E("th%d" % t, s), "idm"), (ex, "idnbig"), (ey, "idbig"), (E("an", s), "idnbig")] + count), True)
+        group(turned(OY, [(E("th%d" % t, s + 1), "idm"), (ey, "idnbig"), (en, "idbig"), (E("an", s + 1), "idnbig")] + count), True)
+        group(turned(R("b5", 0, 16), [(B("rob2"), "idm"), (B("nx"), "id1")]), True)
 
-    def sources_early(t):
-        for k, (bk, m) in enumerate((("b4", "a"), ("b6", "b"))):
-            group([(P(bk, l), B("idm"), P(*memory(t, m, l))) for l in range(2)]
-                  + [(P(bk, 0, PAIRS, 2), B("id4096"), P("op", 0, PAIRS, 2))])
-        psum("b6", 2, [("idm", "qy", 0, ""), ("idbig", "em", 1, ""), ("idnbig", "em", 0, "n"), ("idn4096", "op", 0, ""),
-                       ("id4096", "near", 0, "")])
-        for k, bk in enumerate(("b4", "b6")):
-            act(P("rl", 2 * k, PAIRS, 2), P(bk, 0, PAIRS, 2), bias=-2049.0, func=F.Relu)
-        act(P("rl", 4), P("b6", 2), bias=-2049.0 - BIG, func=F.Relu)
-        act(P("ty"), P("rl", 4), func=F.Sign)
+    def sums(l, k, j0=0, j1=16):
+        bk, a = "b%d" % (l + 1), 2048 * l
+        rows = slice(8 * j0, 8 * j1)
+        block(R(bk, 48, 64), [(X(bk, slice(48 + r // 8, 64, 2), r % 8, rows=rows),
+                               ST(("xg", "mx")[k], a + U * j0 + r, a + U * j1, 16), B("zs", 8 * k, 8 * k + 8)) for r in range(16)],
+              min(64, 8 * (j1 - j0)))
 
-    def new_places(t):
-        gg = "g%d" % (t % 2)
-        psum("b2", 0, [("id4096", "nm", 0, "f"), ("idm", gg, 1, ""), ("idn4096", "op", 1, "")])
-        psum("b2", 1, [("idm", "nx", 0, ""), ("id4096", "u", 0, "")])
-        psum("b3", 2, [("idm", gg, 0, ""), ("idn4096", "op", 0, ""), ("idn4096", "u", 0, "")])
-        act(P("rl", 5, PAIRS, 2), P("b2", 0, PAIRS, 2), bias=-2049.0, func=F.Relu)
-        act(P("rl", 7), P("b3", 2), bias=2047.0, func=F.Relu)
-        tx_, tb_ = (("N", ""), ("", "P"), ("", "P"))[t]
-        psum("b6", 0, [("id1", "rl", k, "") for k in (1, 2, 4, 5)])
-        psum("b1", 0, [("id2047", "ones", 0, ""), ("idm", "rl", 3, tb_)] + [("idm", "rl", k, tx_) for k in (0, 6, 7)])
+    def distances(t):
+        prev = {}
+        for l, j0, j1, e in pieces(t):
+            gather(t, l, j0, j1, e, prev)
+            q = "S" if e == "S" else "V"
+            first = [prev[q]] if q in prev else made["VS".index(q)] * (t == 0)
+            ops[prev["now"]].update(behind=ops[prev["now"]]["behind"] + first, firm=True)
+            prev[q] = prev["now"]
 
-    def memories(t):
-        gg = "g%d" % (t % 2)
-        psum("b4", 2, [("id2047", "op", 0, ""), ("id2047", "op", 1, "P"), ("id2047", "u", 0, "")])
-        for k in range(2):
-            psum("b4", k, [("id4096", "nm", 0, "f"), ("id1", gg, k, "")])
-        psum("b2", 2, [("idn2047", "nm", 0, "f"), ("id2047", "ones", 0, ""), ("id2047", "op", 0, ""), ("id2047", "op", 1, ""),
-                       ("id2047", "ty", 0, "")])
-        for k, m in enumerate("ab"):
-            tt(P("ab2", k), P("b4", 2), P(*memory(t, m, 0)), A.max)
-            for a, b in TURNS[("", "P", "")[t]]:
-                tt(P(*memory(t + 1, m, 0), a) if t < 2 else X("wm", k, slice(U, 2 * U)), P("b2", 2, b),
-                   P(*memory(t, m, 1), b), A.max)
-            for a, b in TURNS[("N", "", "")[t]]:
-                tt(P(*memory(t + 1, m, 1), a) if t < 2 else X("wm", k, slice(0, U)), P("b4", k, b), P("ab2", k, b), A.min)
-
-    def gather(t, l, p):
-        fused[l, p] = None
-        for c0, c1 in zip(CUTS[l, p], CUTS[l, p][1:]):
-            lo, hi = 16 * (U * l + c0), 16 * (U * l + c1)
-            x = ind(B("tab%d" % t, 0, 2048), B(("offx", "offy", "offn")[l], c0, c1))
-            if (l, c0) in ON_VECTOR[t] and t and c0 >= FUSE:
-                tt(B("xg", lo, hi), x, B("vx", 16 * (c0 - FUSE), 16 * (c1 - FUSE)), A.subtract)
+    def gather(t, l, j0, j1, e, prev):
+        for _ in range(1):
+            lo, hi = 2048 * l + U * j0, 2048 * l + U * j1
+            prev["now"] = len(ops)
+            x = ind(B("tab", 0, 2048), B(("offx", "offy", "offn")[l], 8 * j0, 8 * j1))
+            if e == "C":
+                tt(B("xg", lo, hi), x, B("vx%d" % t, 0, hi - lo), A.subtract)
                 ts(B("mx", lo, hi), B("xg", lo, hi), 0.0, A.max)
-                fused[l, p] = (c0 // 16, c1 // 16)
                 continue
-            (cp if (l, c0) in ON_VECTOR[t] else act)(B("xg", lo, hi), x)
+            {"V": cp, "S": act}[e](B("xg", lo, hi), x)
             gathered.append(len(ops) - 1)
-            for a in range(lo, hi, 64):
-                tt(B("mx", a, a + 64), B("xg", a, a + 64), X("b0", a // 256 % 8, ALL), A.max)
+            for a in range(lo, hi, U * WIDTH):
+                b = min(hi, a + U * WIDTH)
+                k = tt(B("mx", a, b), B("xg", a, b), B("b0", 0, b - a), A.max, [prev.get("max")] * (FIFO and "max" in prev))
+                ops[k]["firm"] = True
+                prev["max"] = k
 
-    def sums_of(t, l, p):
-        c0, c1 = PARTS[p]
-        bk = "b%d" % (l + 1)
-        o, a, b = X(bk, slice(c0, c1), PAIRS), 256 * (8 * l + c0), 256 * (8 * l + c1)
-        z = [[(o, B(z, 15 - r, 143 - r), ST(x, a + r, b, 16)) for r in range(16)] for z, x in (("zm", "xg"), ("z2", "mx"))]
-        more = terms(bk, 0, [("idm", "spr", t, ""), ("id2047", "ones", 0, "")], fused[l, p]) if fused[l, p] else []
-        return z[:1] + more + z[1:]
+    def pass_on(o, a):
+        pick(o, a, [[0, len(o[1][0][1])]], A.is_equal, 0.0, 0)
 
-    def scatter(tab, msg, o, p, t, behind):
-        w = B(tab, 0, WT)
-        if OPT["split"][t]:
-            a = o + (M if msg == "mo" or o == landing("e0", 0) else GAP) * p
-            b = a + 64
+    def repeat(t):
+        if any(p[3] == "C" for p in pieces(t)):
+            b = "vx%d" % t
+            for lo, hi, a in ((0, U, B("v%d" % t)), (U, 2 * U, B("v%d" % t)), (2 * U, 4 * U, B(b, 0, 2 * U))):
+                pass_on(B(b, lo, hi), a)
+
+    def all_sums(l, hi=None, lo=None):
+        for k, j0, j1 in SUMS[l][lo:hi]:
+            sums(l, k, j0, j1)
+
+    def above(e, o, a):
+        if e == "V":
+            ts(o, a, BIG, A.is_gt)
         else:
-            a, b = o + 16 * PARTS[p][0], o + U + PARTS[p][0]
-        note("V", [w], [B(msg, a, a + 64), B(msg, b, b + 4)],
-             lambda q: q.tensor_copy(out=w[0].indirect(T[msg][:, b:b + 4]), in_=T[msg][:, a:a + 64]),
-             (60, 64, "s"), behind=behind, firm=True)
-
-    def landing(slot, p):
-        return 2 * GAP * SLOTS.index(slot) + (M if slot == "e0" else GAP) * p
+            act(o, a, bias=-BIG - 0.5, func=F.Sign)
 
     peer = {d: T.cores[(rank + d) % n] for d in (1, 2, -1, -2)}
-    sent, last = [0], [None]
+    sent = [0]
 
-    def send(d, slot, p, o, w=M, later=True):
-        dst, a, sem = peer[d], landing(slot, p), slot + "ab"[p]
+    def send(d, sem, o, a):
+        dst = peer[d]
         rid, pid = topo.addr(dst, core)
-        k = remote([B("mo", o, o + w)], lambda q: q.remote_dma(out_ap=T.mi[:, a:a + w], in_ap=T.mo[:, o:o + w],
-                                                               remote_sem=T.sem[sem], local_sem=T.sem.ls, pid=pid, routing_id=rid,
-                                                               dma_engine_mask=topo.mask(core, dst)), last[:1] * (w > M and later))
+        k = remote([a], lambda q: q.remote_dma(out_ap=o[0], in_ap=a[0], remote_sem=T.sem[sem], local_sem=T.sem.ls, pid=pid,
+                                               routing_id=rid, dma_engine_mask=topo.mask(core, dst)))
         sent[0] += len(topo.engines(core, dst))
-        last[0] = k
-        arrives([B("mi", a, a + w)], [], sem, len(topo.engines(peer[-d], core)), k, ("way", 1.0))
-
-    def send_table(d):
-        cs, he = carriers(rank, T, topo), hand_engines(rank, T, topo)
-        w = 2048 // len(cs)
-
-        def tr(dst, k, sem, dbuf):
-            return RemoteDMATransfer(dst_ids=[DstId(rid=topo.addr(dst, core)[0], pnc=topo.addr(dst, core)[1])],
-                                     dma_engine_mask=he[k][0], remote_sem=T.sem[sem], src=T.tab0[:, k * w:k * w + w],
-                                     dst=T[dbuf][:, 0:w])
-        pieces = [tr(peer[-d], 0, "t%d" % d, "tab%d" % d)] + [tr(cs[k], k, "h%d" % d, "hand%d" % d) for k in range(1, len(cs))]
-        tab = B("tab0", 0, 2048)
-        k = remote([tab], lambda q: q.remote_dma_fused(pieces, local_sem=T.sem.tl))
-        arrives([], [tab], "tl", d * sum(h[1] for h in he), k, ("copy", 0.5))
-        far = [len(topo.engines(c, core)) for c in carriers((rank + d) % n, T, topo)[1:]]
-        arrives([B("tab%d" % d, 0, WT)], [], "t%d" % d, hand_engines((rank + d) % n, T, topo)[0][1] + sum(far), k, ("copy", 1.0))
+        arrives([o], [], sem, len(topo.engines(peer[-d], core)), k, ("way", 0.85 + len(o[1][0][1]) / 660))
         return k
 
-    cp(B("ing", 0, 256), ind(B("gli", 0, 256), B("pin", 0, 16)))
-    cp(B("offx"), B("ing"))
+    made[:] = [[k for k, o in enumerate(ops) if o["e"] == e] for e in "VS"]
+    cp(B("offx"), E("gli", 0))
     hold.append(len(ops) - 1)
-    cp(P("g0", 0, PAIRS, 2), B("ing", 0, 256))
+    split("V", "g0", "gli")
     hold.pop()
-    cp(P("g0", 0, 0), ST("ing", 15, U, 16))
-    for k, cols in ((1, PAIRS), (0, WHOLE)):
-        none(OPT["f0"], P("em", k, cols), P("g0", k, cols))
-    lists(0, B("ing"), P("g0", 1))
-    sums = X("b4", slice(0, 24), 0)
-    group([[(sums, B("zm", 15 - r, 143 - r), ST("yvs", r, 384, 16)) for r in range(16)]])
-    act(B("tex", 0, 24), sums, bias=MID)
-    for lo, hi in ((0, 8), (8, 24)):
-        act(B("spr", 16 * lo, 16 * hi), ind(B("tex", 0, 24), B("seg", lo, hi)))
+    lists(0)
+    for t in range(3):
+        fill(B(("sum0", "out1", "out2")[t]), -2 * MID)
+        made[0].append(len(ops) - 1)
+        view_sums(t)
+        made[1].append(len(ops) - 1)
     views(0)
-    iota(B("iw", EARLY, WT), [[1, WT - EARLY]], EARLY, 0, [send_table(1)])
-    {"V": cp, "S": act}[OPT["ina"]](B("ina", 0, 256), ind(B("ali", 0, 256), B("pin", 0, 16)))
+    repeat(0)
+    pick(B("tri0"), B("blk4"), [[1, U]], A.is_ge, 0.0, -1)
+    pick(B("tri"), B("tri0"), [[1, U]], A.not_equal, -4096.0, -1)
+    split(OPT["cast"][0], "ma0", "ali")
+    split(OPT["cast"][1], "th0", "thi", -MID)
+    either = {"V": cp, "S": act, "G": pass_on}
+    fill(E("th0", 33, 1), 0.0)
+    either[OPT["thpad"]](E("th0", 32, 1), E("th0", 0, 1))
+    for o, a in ((U, U), (528, 2 * U)):
+        either[OPT["pack"]](B("pack", o, o + U), B("yvs", a, a + U))
+        made["VS".index(OPT["pack"])].append(len(ops) - 1)
+    for d in (1, 2):
+        k = send(d, "pk%d" % d, X("pk%d" % d), B("pack", 256 * d - 256, 256 * d + 272))
+        repeat(d)
+    for a in range(EARLY, WT, 576):
+        k = iota(B("iw", a, a + 576), [[1, 576]], a, 0, [k])
 
-    def put_back(t, parts):
-        return [(P("b7", 2, h=h), B("id1"), P("yvs", t, h=h)) for h in [fused[l, p] for l in range(2) for p in parts] if h]
-
-    def writes(t, p):
-        h = c0, c1 = PARTS[p]
-        o = M * (2 * t + p)
-        scan(B("s2", S * c0, S * c1), P("nm", h=h), B("ky", S * c0, S * c1), A.mult, A.max)
-        scan(B("s3", S * c0, S * c1), P("nm", h=h), B("b5", S * c0, S * c1), A.mult, A.max)
-        if OPT["soff"][p] == "V":
-            ts(B("soff", c0, c1), ST("s2", S * c0 + 16, S * c1, S), -1.0, A.mult, 2048.0 - 256 * c0, A.add)
-        else:
-            act(B("soff", c0, c1), ST("s2", S * c0 + 16, S * c1, S), scale=-1.0, bias=2048.0 - 256 * c0, func=F.Relu)
-        ts(B("gi", c0, c1), ST("s3", S * c0 + 16, S * c1, S), 4095, A.bitwise_and)
-        cp(B("goff", c0, c1), B("gi", c0, c1))
-        cp(B("gf", c0, c1), B("gi", c0, c1))
-        halves = P("b7", 2, h=h)
-        for k in range(2):
-            act(B("xv", 32 * c0 + 64 * k, 32 * c0 + 64 * k + 64),
-                ind(B("xg", 256 * (8 * k + c0), 256 * (8 * k + c1)), B("soff", c0, c1)))
-        group([(halves, B("id1"), B("xv", a, a + 64)) for a in (32 * c0, 32 * c0 + 64)] + put_back(t, [p]))
-        act(B("mo", o, o + 64), halves, scale=0.5, bias=-0.25)
-        {"V": cp, "S": act}[OPT["bf"][p]](B("bf", 16 * c0, 16 * c1), ind(B("iw", 0, WT), B("goff", c0, c1)))
-        cp(ST("eq", L * c0 + 64, L * c1, L), B("gi", c0, c1))
-        for c in range(c0, c1):
-            ts(B("eq", L * c, L * c + 64), B("bf", 16 * c0, 16 * c1), B("gf", c, c + 1), A.is_equal, 0.25, A.mult)
-        scan(B("sc", L * c0, L * c1), B("w", L * c0, L * c1), B("eq", L * c0, L * c1), A.mult, A.max)
-        {"V": cp, "S": act}[OPT["mo"][p]](B("mo", o + 64, o + 68), ST("sc", L * c0 + 64, L * c1, L))
-        send(*((-1, "a1"), (-1, "e2"), (2, "c0"))[t], p, o)
-        if (t, p) == (1, 1):
-            send(1, "e0", 0, o - M, 2 * M)
-
-    def writes_whole(t):
-        o = 2 * M * t
-        scan(X("s2"), X("nm"), X("ky"), A.mult, A.max)
-        scan(X("s3"), X("nm"), B("b5", 0, 8 * S), A.mult, A.max)
-        ts(B("soff", 0, 8), ST("s2", 16, 8 * S, S), -1.0, A.mult, 2048.0, A.add)
-        ts(B("gi", 0, 8), ST("s3", 16, 8 * S, S), 4095, A.bitwise_and)
-        cp(B("goff", 0, 8), B("gi", 0, 8))
-        cp(B("gf", 0, 8), B("gi", 0, 8))
+    def writes(t):
+        group(kept(R("b5", 0, 16), [(B("mg"), "tri")]))
+        group(kept(R("b6", 0, 16), [(B("mg"), "tri")]), True)
+        ts(B("rp"), R("b5", 0, 16), -2048.0, A.min, 3199.0, A.add)
+        act(B("ff"), R("b6", 0, 16), scale=-1.0 / 4096, func=F.Relu)
+        for bk, l, r in (("b5", "rp", "blk"), ("b6", "ff", "w2")):
+            o = R(bk, 16, 17)
+            block(o, [(o, B(l), B(r, 0, 8)), (o, B("id1"), B("rob2", 0, 8))], 64, True)
+        act(B("soff", 0, 8), R("b6", 16, 17), scale=0.5)
+        for o in (B("goff", 0, 8), B("gf", 0, 8)):
+            ts(o, R("b5", 16, 17), 2048.0 - 16 * 1151, A.add)
+        o, either = 0, {"V": cp, "S": act, "G": pass_on}
         for k in range(2):
             act(B("xv", U * k, U * k + U), ind(B("xg", 2048 * k, 2048 * k + 2048), B("soff", 0, 8)))
-        group([(P("b7", 2), B("id1"), B("xv", a, a + U)) for a in (0, U)] + put_back(t, [0, 1]))
-        act(B("mo", o, o + U), P("b7", 2), scale=0.5, bias=-0.25)
-        cp(B("bf"), ind(B("iw", 0, WT), B("goff", 0, 8)))
-        cp(ST("eq", 64, 8 * L, L), B("gi", 0, 8))
+        group(kept(R("b6", 32, 48), [(B("xv", U * k, U * k + U), "id1") for k in range(2)]), True)
+        act(B("mo", o, o + U), R("b6", 32, 48), scale=0.5, bias=-0.25)
+        cut = OPT["bf"]
+        for c0, c1, e in zip(cut[0], cut[0][1:], cut[1]):
+            either[e](B("bf", 16 * c0, 16 * c1), ind(B("iw", 0, WT), B("goff", c0, c1)))
+        either[OPT["eq"][0]](ST("eq", 16, L, 162), B("gf", 0, 4))
+        either[OPT["eq"][1]](ST("eq", 145, L, 146), ST("gf", 7, 3, -1))
         for c in range(8):
-            ts(B("eq", L * c, L * c + 64), B("bf", 64 * (c // 4), 64 * (c // 4) + 64), B("gf", c, c + 1), A.is_equal, 0.25, A.mult)
-        scan(X("sc"), X("w"), X("eq"), A.mult, A.max)
-        cp(B("mo", o + U, o + U + 8), ST("sc", 64, 8 * L, L))
-        send(*((-1, "a1"), (-1, "e2"), (2, "c0"))[t], 0, o, 2 * M, False)
-        if t == 1:
-            send(1, "e0", 0, o, 2 * M)
+            ts(B("eq", FIRST[c], FIRST[c] + 16 * c + 16), B("bf", 0, 16 * c + 16), B("gf", c, c + 1), A.is_equal, 0.25, A.mult)
+        scan(B("sc", 0, L), B("w", 0, L), B("eq", 0, L), A.mult, A.max)
+        either[OPT["mo"][0]](B("mo", o + U, o + U + 4), ST("sc", 16, L, 162))
+        either[OPT["mo"][1]](ST("mo", o + U + 7, o + U + 3, -1), ST("sc", 145, L, 146))
+        if t == 2:
+            cp(B("tab", NONE, NONE + 1), B("xsav", 1, 2))
+        w = B("tab", 0, WT)
+        note("V", [w], [X("mo")], lambda q: q.tensor_copy(out=w[0].indirect(T.mo[:, U:M]), in_=T.mo[:, 0:U]), (60, U, "s"))
+
+    def new_rows(t):
+        s = t % 2
+        gg, ma, mb = "g%d" % t, "ma%d" % t, "mb%d" % t
+        go, ao, bo = ("go%d" % t, "ao%d" % t, "bo%d" % t) if t < 2 else ("fog", "foa", "fob")
+        on_s = OPT["er"][t] == "S"
+        group(kept(R("b1"), [(H(ma), "id1")]) + kept(R("b1", 32, 64), [(B("ones", 0, 256), "id4096")] * (not on_s))
+              + [(E("b1", a, k, 32), B("id1"), E(mb, b, k)) for a, b, k in ((1, 0, 16), (2, 1, 15), (0, 31, 1))]
+              + to_rows("b1", 0, s, [("opx", "idn4096")]) + to_rows("b1", 32, s + 1, [("opx", "idn4096")])
+              + to_rows("b1", 0, s + 1, [("opy", "idn4096")]) + to_rows("b1", 32, s + 2, [("opy", "idn4096")]), True)
+        if on_s:
+            act(X("rl"), X("b1"), scale=-1.0, bias=-2049.0, func=F.Relu)
+            group(kept(R("b1"), [(R("rl", 32 * k, 32 * k + 32), "id1") for k in range(2)]), True)
+            act(H("er"), R("b1"), scale=-1.0, bias=2047.0)
+        else:
+            ts(H("er"), R("b1"), 4096.0, A.add, 2047.0, A.min)
+            tt(H("er"), R("b1", 32, 64), H("er"), A.min)
+        tt(E(go, 1 - s), E("b2", 1 - s), E("er", 1 - s), A.min)
+        if t < 2:
+            send(1, "gx%d" % (t + 1), E("g%d" % (t + 1), 1 - s), E(go, 1 - s))
+        stay, new = R("b3", 0, 16), R("b3", 16, 32)
+        group(kept(stay, [(E(gg, s), "id1")]) + kept(new, [(B("nx"), "id1"), (B("ones"), "id4096")]) + turned(stay, [(B("opx"), "id4096")])
+              + [x for m in ("mg", "tk") for x in turned(stay, [(B(m), "id4096")]) + turned(new, [(B(m), "idn4096")])], True)
+        tt(E("er", s), stay, E("er", s), A.min)
+        tt(E(go, s), new, E("er", s), A.min)
+        if t < 2:
+            send(1, "gy%d" % (t + 1), E("g%d" % (t + 1), s), E(go, s))
+        else:
+            send(-2, "fig", X("fig"), X("fog"))
+        group(to_rows("b7", 16, s, [("opx", "id2047")]) + to_rows("b7", 16, s + 2, [("opy", "id2047")])
+              + to_rows("b7", 16, s + 1, [(m, "id2047") for m in ("opx", "opy", "ty", "mg")])
+              + to_rows("b7", 16, s, [(m, "id2047") for m in ("mg", "tk")]), True)
+        merged = R("b4", 0, 16), R("b4", 16, 32)
+        group(kept(R("b4"), [(B("ones", 0, 256), "id4096")]) + kept(merged[0], [(E(gg, s), "id1")])
+              + [(R("b4", 16 + j0, 16 + j1), B("id1"), E(gg, r0, j1 - j0)) for j0, j1, r0 in wrapped(s + 1)]
+              + [x for o in merged for x in turned(o, [(B("mg"), "idn4096")])], True)
+        for o, old, new in zip(merged, (ma, mb), (ao, bo)):
+            for h in range(2):
+                tt(E(new, h), E("b7", h, 16, 16), E(old, h), A.max)
+            tt(E(new, s), o, E(new, s), A.min)
+            if t == 2:
+                send(-2, "fi" + new[2], X("fi" + new[2]), X(new))
+        if t < 2:
+            group([(R("b5", 0, 16), B("mg"), B("blk"))], True)
+            {"V": cp, "S": act}[OPT["cnt"]](B("co%d" % t), R("b5", 0, 16))
+            for m, lo, hi in (("ma", 256, 640), ("mb", 0, 256)):
+                send(1, m + str(t + 1), B("m%d" % (t + 1), lo, hi), B("mo%d" % t, lo, hi))
 
     def visit(t):
         s = t % 2
-        gg = "g%d" % s
-        thresholds(t)
-        group([(B("b5", 256, 384), B("idbig"), P("em")), (B("b5", 0, 8 * S), B("id32"), X("jc")),
-               (B("b5", 0, 8 * S), B("id1"), X("nx"))])
-        if not OPT["split"][t]:
-            for l in range(2):
-                for p, h in enumerate(PARTS):
-                    gather(t, l, p)
-                    group(sums_of(t, l, p))
-            cp(P("sgx"), P("b1"))
-            tt(P("op", 1), P("b2"), P("thr", 1), A.is_gt)
-            tt(P("mnu"), P("b2"), P("sgx"), A.min)
-            tt(P("oyf"), P("op", 1), P("b5", 2), A.is_gt)
-            tt(P("mnm"), P("mnu"), P("b5", 2), A.subtract)
-            for p in range(2):
-                gather(t, 2, p)
-            z = [sums_of(t, 2, p) for p in range(2)]
-            group(terms("b3", 0, [("idbig", "em", 1, "f")]) + z[0] + z[1][:1]
-                  + terms("b3", 0, [("idbig", "op", 1, "P"), ("idbig", "oyf", 0, "")]) + z[1][1:])
-            tt(P("nm"), P("b3", 0, WHOLE), P("mnm", 0, WHOLE), A.is_ge)
-            writes_whole(t)
-        for p, h in enumerate(PARTS if OPT["split"][t] else ()):
-            gather(t, 0, p)
-            group(sums_of(t, 0, p))
-            cp(P("sgx", h=h), P("b1", h=h))
-            gather(t, 1, p)
-            group(sums_of(t, 1, p))
-            tt(P("op", 1, h=h), P("b2", h=h), P("thr", 1, h=h), A.is_gt)
-            tt(P("mnu", h=h), P("b2", h=h), P("sgx", h=h), A.min)
-            tt(P("oyf", h=h), P("op", 1, h=h), P("b5", 2, h=h), A.is_gt)
-            tt(P("mnm", h=h), P("mnu", h=h), P("b5", 2, h=h), A.subtract)
-            gather(t, 2, p)
-            z = sums_of(t, 2, p)
-            group(terms("b3", 0, [("idbig", "em", 1, "f")], h) + z[:1]
-                  + terms("b3", 0, [("idbig", "op", 1, "P"), ("idbig", "oyf", 0, "")], h) + z[1:])
-            tt(P("nm", h=h), P("b3", 0, WHOLE, h=h), P("mnm", 0, WHOLE, h=h), A.is_ge)
-            writes(t, p)
+        before(t)
+        evac = {"V": cp, "S": act}
+        distances(t)
+        all_sums(0)
+        all_sums(1)
+        evac[OPT["sg"][0]](B("sgx"), DX)
+        group(kept(OX, [(B("sgx"), "id1")]))
+        above(OPT["op"][0], B("opx"), OX)
+        evac[OPT["sg"][1]](B("sgy"), DY)
+        tt(B("mnu"), DY, B("sgx"), A.min)
+        group(kept(OY, [(B("sgy"), "id1")]))
+        above(OPT["op"][1], B("opy"), OY)
+        group(turned(TK, [(E("em", s), "idn18")]) + kept(TK, [(B("sev"), "idbig"), (B("sgy"), "idm"), (B("opy"), "idnbig")]), True)
+        if OPT["tkb"] == "S":
+            act(B("tkb"), TK, scale=-1.0)
+        else:
+            ts(B("tkb"), TK, -1.0, A.mult)
+        group(turned(OT, [(E("em", s + 1), "idbig"), (E("em", s + 2), "idnbig")])
+              + kept(OT, [(B("sgx"), "up"), (B("opx"), "idnbig"), (B("sgy"), "idm")]), True)
+        above(OPT["op"][2], B("ty"), OT)
+        all_sums(2, -OPT["late"])
+        whole = SUMS[2][-1][1:] == (0, 16)
+        group(kept(DN, [(B("opy"), "shb")] + [(B("opy"), "idbig")] * whole))
+        all_sums(2, None, -OPT["late"])
+        group(kept(DN, [(B("opy"), "idbig")] * (not whole)))
+        tt(B("mg"), DN, B("mnu"), A.is_lt)
+        tt(B("tk"), DN, B("tkb"), A.is_lt)
+        writes(t)
+        group(to_rows("b2", 0, s + 1, [("qy", "id1")], False) + [(E("b2", 1 - s), B("id4096"), E("em", 1 - s))]
+              + to_rows("b2", 0, s + 1, [("opy", "id4096"), ("ty", "idn4096"), ("mg", "id4096")]), True)
         if t == 0:
-            hold.append(gathered[-1])
-            {"V": cp, "S": act}[OPT["inb"]](B("inb", 0, 256), ind(B("bli", 0, 256), B("pin", 0, 16)))
-            hold.pop()
-        cp(P("sgx", 0, 0), P("b1", 0, 16))
-        tt(P("op"), P("b1"), P("thr"), A.is_gt)
-        tt(P("near"), P("b2"), P("sgx", 0, slice(0, 16)), A.is_lt)
-        tt(P("u"), P("b3"), P("mnu"), A.is_lt)
-        sources_early(t)
-        new_places(t)
-        memories(t)
+            split(OPT["cast"][2], "mb0", "bli")
+        new_rows(t)
         if t < 2:
-            hh = "g%d" % (1 - s)
-            if t == 0:
-                act(X("tht", ALL, 0), X("tht", ALL, 32), behind=gathered[-1:])
             views(t + 1)
-            if FUSE < U:
-                for c in range(FUSE // 16, 8):
-                    o = 256 * c - 16 * FUSE
-                    act(B("vx", o, o + 64), X("b0", c, ALL))
-                    for w in (64, 128):
-                        act(B("vx", o + w, o + 2 * w), B("vx", o, o + w))
-            count(t + 1)
-            (a, b), (c, d) = TURNS[("0", "P0")[t]]
-            less("S", P(hh, 0, a), P("b6", 0, b))
-            if OPT["pad"] == "S":
-                less("S", P(hh, 0, c), P("b6", 0, d))
-            else:
-                cp(P(hh, 0, c), P(hh, 0, 16 - c))
-            act(P(hh, 1), P("b1"))
-            none(OPT["fl"][0], P("em", 0, WHOLE), P(hh, 0, WHOLE))
-            none(OPT["fl"][1], P("em", 1), P("b1") if OPT["fl"][1] == "S" else P(hh, 1))
-            lists(t + 1, P(hh), P("b1"))
-        if t == 2:
-            cp(B("tab0", NONE, NONE + 1), B("xsav", 1, 2))
-        todo = [("tab0", "mo", 0, p) for p in range(2)] * (t == 0)
-        todo += [("tab%d" % (t + 1), "mi", landing(SLOTS[t], 0), p) for p in range(2)] * (t < 2)
-        for into, m, o, p in todo:
-            scatter(into, m, o, p, t, [last[0]] + made * (into == "tab1"))
-            last[0] = len(ops) - 1
-        if t == 0:
-            send_table(2)
+            lists(t + 1)
 
     for t in range(3):
         visit(t)
-    act(B("wg"), P("b1"))
-    less("S", B("wg", U, 2 * U), P("b6"))
-    act(B("ogs", 0, 256), ind(B("wg", 0, 256), B("pout", 0, 16)))
-    {"V": cp, "S": act}[OPT["oas"]](B("oas", 0, 256), ind(X("wm", 0, ALL), B("pout", 0, 16)))
-    {"V": cp, "S": act}[OPT["obs"]](B("obs", 0, 256), ind(X("wm", 1, ALL), B("pout", 0, 16)))
-    for b, q, sm in (("ogs", T.og, "sog"), ("oas", T.oa, "soa"), ("obs", T.ob, "sob")):
-        dma("Y", sm, [], [B(b, 0, 256)], q[:, :], T[b][:, :], ("", STORE - 0.8))
-    for t, m in ((1, "e0"), (2, "c0")):
-        for p in range(2):
-            scatter("tab0", "mi", landing(m, 0), p, t, [])
-    dma("Y", "sox", [], [B("tab0", 0, 2048)], T.ox[:, :], T.tab0[:, 0:2048], ("", STORE))
+    dma("Y", "sox", [], [B("tab", 0, 2048)], T.ox[:, :], T.tab[:, 0:2048], ("", STORE))
+    for k, (m, q) in enumerate((("g", T.og), ("a", T.oa), ("b", T.ob))):
+        {"V": cp, "S": act}[OPT["out"][k]](X("o%ss" % m), X("fi" + m))
+        dma("Y", "so" + m, [], [X("o%ss" % m)], q[:, :], T["o%ss" % m][:, :], ("", STORE - 0.8))
 
     cnt = issue()
     for sm in ("sog", "soa", "sob", "sox"):

@@ -13,7 +13,7 @@ WT = 2048 + 256
 BIG = 32768.0
 MID = 2040.0
 FAR = 1024.0
-CUTS = ["SX3 VX9 SX16 SY8 SY16 SN6 SN12 SN16"] * 3
+CUTS = ["SX3 VX10 SX16 SY8 SY16 SN8 SN14 SN16"] + ["SX3 VX7 SX16 SY8 SY16 VN3 SN9 SN14 SN16"] * 2
 
 
 def pieces(t):
@@ -28,18 +28,23 @@ WHOLE = ((0, 0, 16), (1, 0, 16))
 SUMS = (WHOLE, WHOLE, WHOLE)
 WIDTH = 2
 FIFO = 1
+LOADS = "gxyatbs"
 IDS = {"id1184": 1184.0, "id32": 32.0, "id65": 65.0, "idf": -1.0 / 32, "id217": 217.0, "idbig": BIG, "idm": -1.0,
        "idnbig": -BIG, "id4096": 4096.0, "idn4096": -4096.0, "id2047": 2047.0}
 ON_SCALAR = ("id4096", "idn4096", "id2047", "idm")
 OPT = {"offx": "S", "off": ("VV", "SS", "SS"), "bf": ((0, 4, 8), "VS"), "mo": "VS", "eq": "VV", "an": "VSS", "em": "S",
        "sg": "VV", "cnt": "S", "cast": "GVG", "op": "VVV", "er": "VVV", "xfirst": False, "late": 2,
        "qn": ("VV", "VV", "VV"), "pad": "V", "out": "VVV", "tkb": "S"}
-OPT.update(off=("VV",) * 3, em="V", an="VVV", thpad="V", pack="S")
+OPT.update(off=("VV",) * 3, em="V", an="VVV", thpad="V", pack="S", home=((0, 3), (3, 5)), anpad="G",
+           qn=("GG",) * 3, pad="G", shipem=1, shipan=0, w=0)
+OPT.update(home=((0, 2), (2, 4), (4, 5)), early=1, sums="VSS", thpad="G", pre=1, offx="s", shipem=0,
+           bf=[((0, 4, 8), "VS")] * 3, mo=("VS",) * 3, xv=("SS",) * 3, shifted=1, xp="G")
+OPT.update(off=("VG",) * 3, shipan=1, shipem=1)
 EARLY = 1152
-CYC, ISSUE, STORE = 0.00083, 0.3, 3.0
-CLOCKS = ((1.0, 1.56, 3.8, 0.000525, 0.1, 1.9, 3.9, 8.0, 1.5), (1.3, 1.3, 3.0, 0.000525, 0.15, 2.0, 3.2, 8.0, 1.0),
-          (1.0, 1.9, 5.0, 0.00042, 0.12, 1.5, 3.5, 10.0, 1.5), (1.1, 1.2, 2.5, 0.00047, 0.17, 2.4, 3.6, 11.0, 2.0))
-PLANS = list(CLOCKS) + [(1.0, g, 3.8, 0.000525, wake, 1.9, 3.6, 8.0, 1.0) for g in (1.4, 1.7) for wake in (0.08, 0.15)]
+CYC, ISSUE, STORE = 0.00083, 0.3, 1.5
+CLOCKS = ((1.0, 1.56, 3.8, 0.000525, 0.1, 1.9, 3.9, 0.0025, 1.5, 0.3), (1.3, 1.3, 3.0, 0.000525, 0.15, 1.6, 3.2, 0.002, 1.0, 0.7),
+          (1.2, 1.9, 5.0, 0.00042, 0.12, 1.5, 3.5, 0.004, 1.5, 0.4), (1.1, 1.2, 2.5, 0.00047, 0.17, 2.4, 3.6, 0.002, 2.0, 0.2))
+PLANS = list(CLOCKS) + [(1.0, g, 3.8, 0.000525, wake, 1.9, 3.6, 0.003, 1.0, 0.3) for g in (1.4, 1.7) for wake in (0.08, 0.15)]
 
 SCRATCH = {}
 
@@ -50,57 +55,62 @@ def _add(where, dtype, **kw):
 
 
 RING, HALVES, PADDED = [32, 8], 2 * U, [2, U + 8]
-_add("sbuf", "bfloat16", tab=WT, xsav=16, yvs=384, ii=256, idn18=128, zs=16, one=256, cb=128, c8=128, xv=256, xg=48 * U,
+_add("sbuf", "bfloat16", tab=WT, xsav=16, yvs=384, v1=U, v2=U, ii=256, idn18=128, zs=16, one=256, cb=128, c8=128, xv=256, xg=48 * U,
      mx=48 * U, vx0=512, vx1=512, vx2=512)
 _add("sbuf", "int32", gli=RING, pidx=8, pin=8, nxi=U, nxj=U, qyi=U, qyj=U,
      **{b: RING if e != "S" else 256 for b, e in zip(("ali", "thi", "bli"), OPT["cast"])})
-_add("sbuf", "uint16", offx=U, offy=U, offn=U, goff=8, soff=8, same=8, apart=16, mo=M)
-_add("sbuf", "float16", em=PADDED, an=PADDED, er=HALVES, pack=784, pk1=528, pk2=528, fog=RING, foa=RING, fob=RING, fig=256,
-     fia=256, fib=256, qy=U, nx=U, kq=U, ones=256, sev=U, cm=U, cmid=U, nblk=U, sgx=U, sgy=U, mnu=U, opx=U, opy=U, ty=U, mg=U,
-     tk=U, rp=U, ff=U, nrm=U, blk=U, blk4=U, tri0=U, tri=U, shb=U, w2=8, rob2=U, sum0=U, ids=128 * len(IDS), bf=128, eq=L,
-     w=L, sc=L, rl=[64, 8], **{b % t: k for t in range(3) for b, k in (("g%d", 256), ("go%d", 256), ("m%d", 640), ("mo%d", 640))})
-_add("sbuf", "float32", c16=24, col=16, sp4=8, iw=WT, pp=U, tkb=U, gf=8, ogs=256, oas=256, obs=256)
-_add("psum", "float32", b0=512, **{"b%d" % k: [64, 8] for k in range(1, 8)})
-SEMAPHORES = ["pv", "pa", "pt", "pg", "dg", "dy", "dx", "ds", "da", "db", "dt", "sog", "soa", "sob", "sox", "ls", "pk1", "pk2",
-              "gx1", "gy1", "ma1", "mb1", "gx2", "gy2", "ma2", "mb2", "fig", "fia", "fib"]
+_add("sbuf", "uint16", offx0=U, offx1=U, offx2=U, oxo0=U, oxo1=U, offy=U, offn=U, goff=8, soff=8, same=8, apart=16, mo=M)
+_add("sbuf", "float16", em0=PADDED, em1=PADDED, em2=PADDED, eo0=PADDED, eo1=PADDED, er=HALVES,
+     ac0=[3, U + 8], ac1=[3, U + 8], ac2=[3, U + 8], an0=[3, U + 8], an1=[3, U + 8], th0=PADDED, th1=PADDED, th2=PADDED, hs=768, hq=256, hk=640, hem=U, xp=U, sid4096=U, sidn4096=U, sid2047=U,
+     nq=256, mk=640, kq=U, ones=256, sev=U, cm=U, cmid=U, nblk=U, sgx=U, sgy=U, mnu=U, rp=U, ff=U, nrm=U, blk=U, blk4=U, tri0=U, tri=U, shb=U, w2=8, rob2=U, sums=U, ids=128 * len(IDS), bf=128, eq=L,
+     w=L, sc=L, rl=[64, 8], st0=896, st1=896, st2=896, so0=896, so1=896)
+_add("sbuf", "float32", c16=24, col=16, sp4=8, iw=WT, pp=U, tkb=U, gf=8, ogs=RING, oas=RING, obs=RING)
+_add("psum", "float32", **{"b%d" % k: [64, 8] for k in range(8)})
+SEMAPHORES = ["pv", "pa", "pt", "pg", "dg", "dy", "dx", "ds", "da", "db", "dt", "sog", "soa", "sob", "sox", "ls", "pv1", "pv2", "pt1", "pt2",
+              "gx1", "gy1", "ma1", "mb1", "gx2", "gy2", "ma2", "em1", "em2", "gt1", "gt2", "hs", "hq", "hk0", "hk1", "hk2", "hk3"]
 PART = {k: ("ids", 128 * j) for j, k in enumerate(IDS)}
-PART.update(id1=("ii", 0), up=("ii", 8), idn18=("idn18", 0), th0=("pack", 256), th1=("pk1", 256), th2=("pk2", 0), v0=("yvs", 0),
-            v1=("pk1", U), v2=("pk2", 272), out1=("pack", 0), out2=("pack", 656), sum1=("pk1", 0), sum2=("pk2", 400))
+PART.update(id1=("ii", 0), up=("ii", 8), idn18=("idn18", 0), v0=("yvs", 0))
 for _t in range(3):
-    PART.update({"ma%d" % _t: ("m%d" % _t, 256), "mb%d" % _t: ("m%d" % _t, 0), "cnt%d" % _t: ("m%d" % _t, 512),
-                 "ao%d" % _t: ("mo%d" % _t, 256), "bo%d" % _t: ("mo%d" % _t, 0), "co%d" % _t: ("mo%d" % _t, 512)})
+    for _k, (_a, _b) in enumerate((("g", "go"), ("mb", "bo"), ("ma", "ao"), ("cnt", "co"))):
+        PART.update({_a + str(_t): ("st%d" % _t, 256 * _k), _b + str(_t): ("so%d" % _t, 256 * _k)})
+for _k, _a in enumerate(("opx", "opy", "ty", "mg", "tk")):
+    PART.update({_a: ("mk", U * _k), "h" + _a: ("hk", U * _k)})
+PART.update(nx=("nq", 0), qy=("nq", U), hnx=("hq", 0), hqy=("hq", U), hg=("hs", 0), hb=("hs", 256), ha=("hs", 512))
+NAME = {v: k for k, v in PART.items()}
 COLS = {k: np.arange(int(np.prod(v[1][1:]))).reshape(v[1][1:]) for k, v in SCRATCH.items()}
 WIDE = {k: v[2] in ("float32", "int32") for k, v in SCRATCH.items()}
 COUNTER = {"V": "pv", "S": "pa", "P": "pt", "G": "pg"}
-LOOK, MOVES, SLACK, SEED, ROUNDS, RELAX = 0.5, 40000, 0.001, 1, 4, 0.0
-SOONER = {"opx": 2.0, "opy": 1.0, "em": 2.0}
+LOOK, MOVES, SLACK, SEED, ROUNDS, RELAX = 0.5, 60000, 0.0003, 1, 4, 0.0
+SOONER = {"opx": 2.0, "opy": 1.0, "em0": 2.0, "em1": 2.0, "em2": 2.0, "mnu": 2.0, "mb0": 3.0, "st0": 3.0, "st1": 2.0,
+          "ac0": 2.0, "ac1": 2.0, "ac2": 2.0, "nx": 2.0, "qy": 2.0, "nxi": 1.5, "th1": 5.0, "th2": 5.0, "v1": 6.0, "v2": 6.0}
+PROMPT, ANY = 1.0, 0.4
 ORDER = []
 
 
 def timing(ops, clock):
-    f, gather, scatter, tensor, wake, way, load, copy, first = clock
+    f, gather, scatter, tensor, wake, way, load, copy, first, call = clock
     cost, tail = [], []
     for o in ops:
         fix, more, kind = o["cost"]
-        per = {"g": gather * CYC * f, "s": scatter * CYC * f, "p": tensor * f, "c": CYC * f, "r": 0.0}[kind]
+        per = {"g": gather * CYC * f, "s": scatter * CYC * f, "p": tensor * f, "c": CYC * f, "r": 0.0, "l": copy}[kind]
         cost.append((fix * CYC * f if o["e"] in "VS" else fix) + more * per)
         if kind == "r" and more:
-            cost[-1], first = cost[-1] + first, 0.0
+            cost[-1], first = call + first, 0.0
         what, share = o["tail"]
         tail.append({"": 1.0, "way": way, "load": load, "copy": copy}[what] * share)
-    lags = [[(d, tail[d] + (0.0 if ops[d]["e"] == o["e"] in "PY" or o["e"] == "D" else wake)) for d in o["deps"]] for o in ops]
+    lags = [[(d, tail[d] + (0.0 if ops[d]["e"] == o["e"] in "PY" or o["e"] in "DL" else wake)) for d in o["deps"]] for o in ops]
     return cost, tail, lags
 
 
 def replay(order, queue, times, lo=0, hi=0, old=None, reach=None):
     cost, tail, lags = times
     b = lo >> 5
-    done, marks = (old[1][:], old[2][:b + 1]) if old else ([0.0] * len(order), [(0.0,) * 7])
+    done, marks = (old[1][:], old[2][:b + 1]) if old else ([0.0] * len(order), [(0.0,) * 8])
     free = list(marks[b])
     for i in range(b << 5, len(order)):
         if not i & 31 and i >> 5 > b:
-            if old and i > hi and old[2][i >> 5][:6] == tuple(free[:6]):
-                return max(old[0], free[6]), done, marks + old[2][i >> 5:]
+            if old and i > hi and old[2][i >> 5][:7] == tuple(free[:7]):
+                return max(old[0], free[7]), done, marks + old[2][i >> 5:]
             marks.append(tuple(free))
         k = order[i]
         e = queue[k]
@@ -114,9 +124,9 @@ def replay(order, queue, times, lo=0, hi=0, old=None, reach=None):
         done[k] = t
         if e:
             free[e] = t
-        if t + tail[k] > free[6]:
-            free[6] = t + tail[k]
-    return free[6], done, marks
+        if t + tail[k] > free[7]:
+            free[7] = t + tail[k]
+    return free[7], done, marks
 
 
 def runs(order, before, times, done):
@@ -139,7 +149,7 @@ def runs(order, before, times, done):
 
 
 def issue_order(ops):
-    queue = ["DVSPGY".index(o["e"]) for o in ops]
+    queue = ["DVSPGYL".index(o["e"]) for o in ops]
     above, near = [], []
     for o in ops:
         far = 0
@@ -162,7 +172,7 @@ def issue_order(ops):
 
     for step in range(MOVES):
         if found is None:
-            place, before, reach, last = [0] * len(ops), [-1] * len(ops), [0] * len(ops), [-1] * 6
+            place, before, reach, last = [0] * len(ops), [-1] * len(ops), [0] * len(ops), [-1] * 7
             for i, k in enumerate(order):
                 place[k] = i
                 if queue[k]:
@@ -174,6 +184,12 @@ def issue_order(ops):
         i = int(draw() * (len(run) - 1))
         j = len(run) - 1 if m < 0.25 else min(len(run) - 1, i + (1, 1, 2, 3, 5, 8, 16, 40)[int(draw() * 8)])
         u, v = run[0 if m > 0.85 else i], run[j]
+        if draw() < ANY:
+            u = v = int(draw() * len(ops))
+            for _ in range((1, 1, 2, 3, 5, 8)[int(draw() * 6)]):
+                u = before[u] if before[u] >= 0 else u
+            if u == v:
+                continue
         part = order[place[u]:place[v] + 1]
         if draw() < 0.5:
             moved, need = {v}, set(deps[v])
@@ -193,7 +209,7 @@ def issue_order(ops):
         limit, tried, change = -SLACK * (1 - step / MOVES) * math.log(draw() + 1e-12), [], 0.0
         for c, s, z in zip(clocks, state, scale):
             tried.append(replay(new, queue, c, place[u], place[v], s, reach))
-            change += (tried[-1][0] - s[0]) / z
+            change += (tried[-1][0] - s[0] + PROMPT * (sum(tried[-1][1]) - sum(s[1])) / len(ops)) / z
             if change > limit + 0.002:
                 break
         if change <= limit:
@@ -230,7 +246,7 @@ def list_schedule(ops, times):
 def dispatch(ops, cost, lag, after, key):
     n = len(ops)
     left, at = [len(l) for l in lag], [0.0] * n
-    pool, free, order = {e: [] for e in "DVSPGY"}, {e: 0.0 for e in "DVSPGY"}, []
+    pool, free, order = {e: [] for e in "DVSPGYL"}, {e: 0.0 for e in "DVSPGYL"}, []
     for k in range(n):
         if not left[k]:
             pool[ops[k]["e"]].append(k)
@@ -267,7 +283,7 @@ def rank_program(g, core, T, topo):
     n = len(T.cores)
     Q = {"V": g.vector, "S": g.scalar, "P": g.tensor, "G": g, "Y": g.sync}
 
-    ops, writer, readers, bank, gathered, hold, made, adds, ends = [], {}, {}, {}, [], [], [], [], {}
+    ops, writer, readers, bank, gathered, hold, made, placed, ends = [], {}, {}, {}, [], [], [], [], {}
 
     def note(e, outs, ins, call, cost, tail=("", 0.0), sem=None, deps=(), behind=(), firm=False):
         k, deps = len(ops), set(deps)
@@ -296,7 +312,7 @@ def rank_program(g, core, T, topo):
             deps.update(rec[2] + (rec[1][-1:] if e == "P" else []))
             rec[1].append(k)
         ops.append({"e": e, "deps": sorted(deps - {-1, k}), "call": call, "cost": cost, "tail": tail, "sem": sem,
-                    "behind": list(behind) + hold, "firm": firm or e in "GY", "name": outs[0][1][0][0] if outs else ""})
+                    "behind": list(behind) + hold, "firm": firm or e in "GY", "name": NAME.get((outs[0][1][0][0], int(outs[0][1][0][1][0])), outs[0][1][0][0]) if outs else ""})
         return k
 
     def issue():
@@ -306,8 +322,9 @@ def rank_program(g, core, T, topo):
         for k in ORDER:
             o = ops[k]
             e = o["e"]
-            if e == "D":
-                token[k] = o["sem"] + ({},)
+            if e in "DL":
+                if e == "D":
+                    token[k] = o["sem"] + ({},)
                 continue
             toks = [token[d] for d in o["deps"] if d in token and not ops[d]["e"] == e == "P"]
             for sem, val, snap in sorted(toks, key=lambda x: -x[1]):
@@ -346,9 +363,8 @@ def rank_program(g, core, T, topo):
 
     def E(b, lo, k=16, base=0):
         if b in PART or COLS[b].ndim == 1:
-            half = U + 8 * (b in ("th0", "th1", "th2"))
-            return B(b, half * (lo % 2) + 8 * (lo // 2), half * (lo % 2) + 8 * (lo // 2 + k))
-        if len(COLS[b]) == 2:
+            return B(b, U * (lo % 2) + 8 * (lo // 2), U * (lo % 2) + 8 * (lo // 2 + k))
+        if len(COLS[b]) < 4:
             return X(b, lo % 2, slice(8 * (lo // 2), 8 * (lo // 2 + k)))
         if SCRATCH[b][0] == "psum":
             return R(b, base + 16 * (lo % 2) + lo // 2, base + 16 * (lo % 2) + lo // 2 + k)
@@ -430,12 +446,15 @@ def rank_program(g, core, T, topo):
         note("D", outs, ins, None, (0.0, 0, "r"), time, (sem, val), [since])
 
     fill(B("tab", 2032, 2048), FAR)
-    k = dma("Y", "dy", [B("yvs", 0, 384)], [], T.yvs[:, :], T.yv[:, :], ("load", 0.55))
-    k = dma("Y", "dg", [X("gli")], [], T.gli[:, :, :], T.gl[:, :], ("load", 0.65), [k])
-    k = dma("Y", "dx", [B("tab", 0, 2048)], [], T.tab[:, 0:NONE], T.xt[:, 0:NONE], ("load", 1.0), [k])
-    for j, (sem, b, src) in enumerate((("da", "ali", T.al), ("dt", "thi", T.th), ("db", "bli", T.bl))):
-        k = dma("Y", sem, [X(b)], [], X(b)[0], src[:, :], ("load", 1.12 + 0.1 * j), [k])
-    dma("Y", "ds", [B("xsav", 0, 2)], [], T.xsav[:, 0:2], T.xt[:, NONE - 1:NONE + 1], ("load", 1.4), [k])
+    loads = {"y": ("yvs", X("yvs")[0], T.yv[:, :], 0.08), "g": ("gli", X("gli")[0], T.gl[:, :], 0.12),
+             "x": ("tab", T.tab[:, 0:NONE], T.xt[:, 0:NONE], 0.4), "a": ("ali", X("ali")[0], T.al[:, :], 0.12),
+             "t": ("thi", X("thi")[0], T.th[:, :], 0.12), "b": ("bli", X("bli")[0], T.bl[:, :], 0.12),
+             "s": ("xsav", T.xsav[:, 0:2], T.xt[:, NONE - 1:NONE + 1], 0.03)}
+    k, at = [], 0.4
+    for m in LOADS:
+        b, o, src, time = loads[m]
+        at += time
+        k = [dma("Y", "d" + m, [B(b, 0, 2048) if m == "x" else X(b)], [], o, src, ("load", at), k)]
 
     def C(k):
         return B("col", k, k + 1)
@@ -450,7 +469,8 @@ def rank_program(g, core, T, topo):
         k = iota(B("iw", a, a + 576), [[1, 576]], a, 0, [k])
     fill(B("ones", 0, 256), 1.0)
     fill(B("kq"), 1801.0 / 64)
-    fill(B("sev"), 7.0)
+    for b in ("an0", "an1") * OPT["shipan"]:
+        fill(X(b, ALL, slice(U, U + 8)), 0.0)
     fill(B("cm"), -2046.0)
     for j, (x, op) in enumerate(((15, A.bitwise_and), (4, A.arith_shift_right), (7, A.bitwise_and), (3, A.arith_shift_right))):
         ts(B("pin", j, j + 1), B("pidx", 0, 1), x, op)
@@ -474,6 +494,8 @@ def rank_program(g, core, T, topo):
             ts(B(b), B("id1"), IDS[b], A.mult)
     ts(B("idn18"), B("id1"), -8 * BIG, A.mult)
     ts(B("shb"), B("ii", 120, 248), BIG, A.mult)
+    for b in ("id4096", "idn4096", "id2047") * OPT["shifted"]:
+        act(B("s" + b), B("ii", 120, 248), scale=IDS[b])
     ts(B("same", 0, 8), B("rob2", 0, 8), 0.5, A.mult)
     ts(C(6), C(5), C(2), A.subtract)
     ts(B("apart", 0, 16), B("c16", 0, 16), C(6), A.add)
@@ -494,6 +516,8 @@ def rank_program(g, core, T, topo):
     def cast(e, o, b):
         if e == "V":
             cp(o, B(b))
+        elif e == "G":
+            pass_on(o, B(b))
         else:
             act(o, ind(B(b), B("same", 0, 8)))
 
@@ -508,15 +532,17 @@ def rank_program(g, core, T, topo):
             act(H(o), ind(X(b), B("apart", 0, 16)), bias=bias)
 
     def views(t):
-        group([(B("b0", k, k + U), B("id1"), B("v%d" % t)) for k in range(0, U * WIDTH, U)], True)
+        v = ("yvs", "v1", "v2")[t]
+        bk = "b0" if t else "b6"
+        block(R(bk, 48, 64), [(X(bk, slice(48 + r // 8, 64, 2), r % 8, rows=few), ST(v, r, U, 16), B("zs", 0, 8))
+                              for r in range(16)], 8, True)
+        if OPT["sums"][t] == "S":
+            act(B("sums", rows=few), X(bk, slice(48, 64), ALL, rows=few), bias=MID)
+        else:
+            ts(B("sums", rows=few), X(bk, slice(48, 64), ALL, rows=few), MID, A.add)
+        group([(R("b0", k, k + 16), B("id1"), B(v)) for k in (0, 16)], True)
 
     few = slice(0, 8)
-
-    def view_sums(t):
-        bk = "b%d" % (5 + t)
-        block(R(bk, 0, 16), [(X(bk, slice(r // 8, 16, 2), r % 8, rows=few), ST("yvs", U * t + r, U * t + U, 16), B("zs", 0, 8))
-                             for r in range(16)], 8, True)
-        act(B(("sum0", "out1", "out2")[t], rows=few), X(bk, slice(0, 16), ALL, rows=few), bias=MID)
 
     def wrapped(lo):
         k = min(16, (33 - lo) // 2)
@@ -531,6 +557,9 @@ def rank_program(g, core, T, topo):
     def to_rows(bk, base, lo, terms, turn=True):
         out = []
         for a, l in terms:
+            if turn and lo > 1 and OPT["shifted"]:
+                out.append((E(bk, lo - 2, 16, base), B(a), B("s" + l)))
+                continue
             for j0, j1, r0 in wrapped(lo):
                 o = E(bk, r0, j1 - j0, base)
                 out.append((o, B(a), B(l, 8 * j0, 8 * j1)) if turn else (o, B(l), B(a, 8 * j0, 8 * j1)))
@@ -538,14 +567,18 @@ def rank_program(g, core, T, topo):
 
     def lists(t):
         s, gg = t % 2, "g%d" % t
-        if t:
-            {"V": cp, "S": act}[OPT["offx"]](B("offx"), E(gg, s))
+        if t and OPT["offx"] in "VS":
+            {"V": cp, "S": act}[OPT["offx"]](B("offx%d" % t), E(gg, s))
+        elif t and OPT["pre"] != 2:
+            {"V": cp, "G": pass_on}[OPT["xp"]](B("xp") if OPT["pre"] else E(gg, s), B("offx%d" % t))
 
         def rows(bk, base, lo, l):
             return [(R(bk, base + j0, base + j1), B(l), E(gg, r0, j1 - j0)) for j0, j1, r0 in wrapped(lo)]
 
         group(kept(R("b2", 0, 16), [(B("cm"), "idn18")]) + rows("b2", 0, s + 1, "idn18") + kept(R("b2", 0, 16), [(B("kq"), "id217")])
-              + rows("b2", 0, s + 2, "id65") + rows("b2", 0, s + 2, "idf"), True)
+              + (rows("b2", 0, s + 2, "id65") + rows("b2", 0, s + 2, "idf") if not (t and OPT["pre"] == 1) else
+                 [(R("b2", a, b), B(l), B("xp", 8 * c, 8 * (c + b - a))) for l in ("id65", "idf") for a, b, c in ((0, 15, 1), (15, 16, 0))]),
+              True)
         group(rows("b3", 0, s, "id1184") + rows("b3", 32, s + 1, "id1") + rows("b3", 0, s + 1, "id32"), True)
         tt(B("pp"), R("b3", 32, 48), E(gg, s), A.mult)
         for o, l, a in rows("b2", 0, s + 1, "id1"):
@@ -558,31 +591,34 @@ def rank_program(g, core, T, topo):
             cast(OPT["off"][t][k], B(o), a)
         for k, (o, a, b) in enumerate((("qy", "qyj", "offy"), ("nx", "nxj", "offn"))):
             e = OPT["qn"][t][k]
-            {"V": cp, "v": cp, "S": act}[e](B(o), B(a if e == "v" else b))
-        none(OPT["em"], H("em"), H(gg))
-        {"V": cp, "S": act}[OPT["pad"]](H("em", U, U + 8), H("em", 0, 8))
+            {"V": cp, "v": cp, "S": act, "G": pass_on}[e](B(o), B(a if e in "vG" else b))
+        if not (t and OPT["shipem"]):
+            none(OPT["em"], H("em%d" % t), H(gg))
+            {"V": cp, "S": act, "G": pass_on}[OPT["pad"]](H("em%d" % t, U, U + 8), H("em%d" % t, 0, 8))
 
     DX, DY, DN = R("b1", 48, 64), R("b2", 48, 64), R("b3", 48, 64)
     OX, OY, OT, TK = R("b7", 0, 16), R("b4", 0, 16), R("b7", 16, 32), R("b6", 0, 16)
 
     def before(t):
         s = t % 2
-        ex, ey, en = E("em", s), E("em", s + 1), E("em", s + 2)
-        none(OPT["an"][t], H("an"), H("ma%d" % t))
-        if s:
-            none(OPT["an"][t], E("an", 32, 1), E("ma1", 0, 1))
+        em, an = "em%d" % t, "ac%d" % t
+        ex, ey, en = E(em, s), E(em, s + 1), E(em, s + 2)
+        if not (t and OPT["shipan"]):
+            none(OPT["an"][t], X(an, slice(0, 2), slice(0, U)), H("ma%d" % t))
+            if s:
+                {"V": cp, "S": act, "G": pass_on}[OPT["anpad"]](E(an, 32, 1), E(an, 0, 1))
         for l, d in enumerate((DX, DY, DN)):
             fused = [j for k, j0, j1, e in pieces(t) if e == "C" and k == l for j in range(j0, j1)]
             more = slice(0, 16)
-            group([(d, B("blk", rows=more), B("sum%d" % t, rows=more))], True)
+            group([(d, B("blk", rows=more), B("sums", rows=more))], True)
             for j0 in range(0, 16, 4):
                 if j0 in fused:
                     o = X("b%d" % (l + 1), slice(48, 64), ALL, rows=slice(8 * j0, 8 * j0 + 32))
-                    group([(o, B("nblk", 8 * j0, 8 * j0 + 32, few), B("sum%d" % t, rows=few)), (o, B("id1", 0, 32), B("cmid"))])
+                    group([(o, B("nblk", 8 * j0, 8 * j0 + 32, few), B("sums", rows=few)), (o, B("id1", 0, 32), B("cmid"))])
         group(turned(DN, [(ey, "idbig"), (ex, "idbig")]))
-        count = [(B("cnt%d" % t), "nrm")] * (t > 0)
-        group(turned(OX, [(E("th%d" % t, s), "idm"), (ex, "idnbig"), (ey, "idbig"), (E("an", s), "idnbig")] + count), True)
-        group(turned(OY, [(E("th%d" % t, s + 1), "idm"), (ey, "idnbig"), (en, "idbig"), (E("an", s + 1), "idnbig")] + count), True)
+        count = [(X(an, 2, slice(0, U)) if OPT["shipan"] else B("cnt%d" % t), "nrm")] * (t > 0)
+        group(turned(OX, [(E("th%d" % t, s), "idm"), (ex, "idnbig"), (ey, "idbig"), (E(an, s), "idnbig")] + count), True)
+        group(turned(OY, [(E("th%d" % t, s + 1), "idm"), (ey, "idnbig"), (en, "idbig"), (E(an, s + 1), "idnbig")] + count), True)
         group(turned(R("b5", 0, 16), [(B("rob2"), "idm"), (B("nx"), "id1")]), True)
 
     def sums(l, k, j0=0, j1=16):
@@ -605,7 +641,7 @@ def rank_program(g, core, T, topo):
         for _ in range(1):
             lo, hi = 2048 * l + U * j0, 2048 * l + U * j1
             prev["now"] = len(ops)
-            x = ind(B("tab", 0, 2048), B(("offx", "offy", "offn")[l], 8 * j0, 8 * j1))
+            x = ind(B("tab", 0, 2048), B(("offx%d" % t, "offy", "offn")[l], 8 * j0, 8 * j1))
             if e == "C":
                 tt(B("xg", lo, hi), x, B("vx%d" % t, 0, hi - lo), A.subtract)
                 ts(B("mx", lo, hi), B("xg", lo, hi), 0.0, A.max)
@@ -614,7 +650,7 @@ def rank_program(g, core, T, topo):
             gathered.append(len(ops) - 1)
             for a in range(lo, hi, U * WIDTH):
                 b = min(hi, a + U * WIDTH)
-                k = tt(B("mx", a, b), B("xg", a, b), B("b0", 0, b - a), A.max, [prev.get("max")] * (FIFO and "max" in prev))
+                k = tt(B("mx", a, b), B("xg", a, b), R("b0", 0, (b - a) // 8), A.max, [prev.get("max")] * (FIFO and "max" in prev))
                 ops[k]["firm"] = True
                 prev["max"] = k
 
@@ -646,37 +682,45 @@ def rank_program(g, core, T, topo):
         k = remote([a], lambda q: q.remote_dma(out_ap=o[0], in_ap=a[0], remote_sem=T.sem[sem], local_sem=T.sem.ls, pid=pid,
                                                routing_id=rid, dma_engine_mask=topo.mask(core, dst)))
         sent[0] += len(topo.engines(core, dst))
-        arrives([o], [], sem, len(topo.engines(peer[-d], core)), k, ("way", 0.85 + len(o[1][0][1]) / 660))
+        link = note("L", [], [], None, (0.0, len(o[1][0][1]), "l"), deps=[k])
+        arrives([o], [], sem, len(topo.engines(peer[-d], core)), link, ("way", 0.85))
         return k
 
-    made[:] = [[k for k, o in enumerate(ops) if o["e"] == e] for e in "VS"]
-    cp(B("offx"), E("gli", 0))
+    def ahead(sem, outs, ins):
+        def half(src, d):
+            e = topo.engines(src, T.cores[(T.rank_of(src) + d) % n])
+            return e[len(e) // 2 * (d - 1):len(e) // 2 * d]
+
+        both = [RemoteDMATransfer(dst_ids=[DstId(rid=topo.addr(peer[d], core)[0], pnc=topo.addr(peer[d], core)[1])],
+                                  dma_engine_mask=sum(1 << x for x in half(core, d)), remote_sem=T.sem[sem + "%d" % d],
+                                  src=ins[d - 1][0], dst=outs[d - 1][0]) for d in (1, 2)]
+        k = remote(ins, lambda q: q.remote_dma_fused(both, local_sem=T.sem.ls))
+        link = note("L", [], [], None, (0.0, 2 * len(outs[0][1][0][1]), "l"), deps=[k])
+        for d in (1, 2):
+            sent[0] += len(half(core, d))
+            arrives([outs[d - 1]], [], sem + "%d" % d, len(half(peer[-d], d)), link, ("way", 0.85))
+
+    fill(B("sums"), -2 * MID)
+    made[:] = [[k for k, o in enumerate(ops) if o["e"] == e and (o["name"] != "w" or e == "V" or OPT["w"])] for e in "VS"]
+    cp(B("offx0"), E("gli", 0))
     hold.append(len(ops) - 1)
     split("V", "g0", "gli")
     hold.pop()
     lists(0)
-    for t in range(3):
-        fill(B(("sum0", "out1", "out2")[t]), -2 * MID)
-        made[0].append(len(ops) - 1)
-        view_sums(t)
-        made[1].append(len(ops) - 1)
     views(0)
     repeat(0)
+    ahead("pv", [B("v%d" % d) for d in (1, 2)], [B("yvs", U * d, U * d + U) for d in (1, 2)])
     pick(B("tri0"), B("blk4"), [[1, U]], A.is_ge, 0.0, -1)
     pick(B("tri"), B("tri0"), [[1, U]], A.not_equal, -4096.0, -1)
     split(OPT["cast"][0], "ma0", "ali")
     split(OPT["cast"][1], "th0", "thi", -MID)
     either = {"V": cp, "S": act, "G": pass_on}
-    fill(E("th0", 33, 1), 0.0)
-    either[OPT["thpad"]](E("th0", 32, 1), E("th0", 0, 1))
-    for o, a in ((U, U), (528, 2 * U)):
-        either[OPT["pack"]](B("pack", o, o + U), B("yvs", a, a + U))
-        made["VS".index(OPT["pack"])].append(len(ops) - 1)
+    either[OPT["thpad"]](H("th0", U, U + 8), H("th0", 0, 8))
+    ahead("pt", [X("th1"), X("th2")], [X("th0")] * 2)
     for d in (1, 2):
-        k = send(d, "pk%d" % d, X("pk%d" % d), B("pack", 256 * d - 256, 256 * d + 272))
         repeat(d)
     for a in range(EARLY, WT, 576):
-        k = iota(B("iw", a, a + 576), [[1, 576]], a, 0, [k])
+        iota(B("iw", a, a + 576), [[1, 576]], a, 0)
 
     def writes(t):
         group(kept(R("b5", 0, 16), [(B("mg"), "tri")]))
@@ -686,15 +730,16 @@ def rank_program(g, core, T, topo):
         for bk, l, r in (("b5", "rp", "blk"), ("b6", "ff", "w2")):
             o = R(bk, 16, 17)
             block(o, [(o, B(l), B(r, 0, 8)), (o, B("id1"), B("rob2", 0, 8))], 64, True)
+            placed[:] = placed[-1:] + [len(ops) - 1]
         act(B("soff", 0, 8), R("b6", 16, 17), scale=0.5)
         for o in (B("goff", 0, 8), B("gf", 0, 8)):
             ts(o, R("b5", 16, 17), 2048.0 - 16 * 1151, A.add)
         o, either = 0, {"V": cp, "S": act, "G": pass_on}
         for k in range(2):
-            act(B("xv", U * k, U * k + U), ind(B("xg", 2048 * k, 2048 * k + 2048), B("soff", 0, 8)))
+            either[OPT["xv"][t][k]](B("xv", U * k, U * k + U), ind(B("xg", 2048 * k, 2048 * k + 2048), B("soff", 0, 8)))
         group(kept(R("b6", 32, 48), [(B("xv", U * k, U * k + U), "id1") for k in range(2)]), True)
         act(B("mo", o, o + U), R("b6", 32, 48), scale=0.5, bias=-0.25)
-        cut = OPT["bf"]
+        cut = OPT["bf"][t]
         for c0, c1, e in zip(cut[0], cut[0][1:], cut[1]):
             either[e](B("bf", 16 * c0, 16 * c1), ind(B("iw", 0, WT), B("goff", c0, c1)))
         either[OPT["eq"][0]](ST("eq", 16, L, 162), B("gf", 0, 4))
@@ -702,22 +747,34 @@ def rank_program(g, core, T, topo):
         for c in range(8):
             ts(B("eq", FIRST[c], FIRST[c] + 16 * c + 16), B("bf", 0, 16 * c + 16), B("gf", c, c + 1), A.is_equal, 0.25, A.mult)
         scan(B("sc", 0, L), B("w", 0, L), B("eq", 0, L), A.mult, A.max)
-        either[OPT["mo"][0]](B("mo", o + U, o + U + 4), ST("sc", 16, L, 162))
-        either[OPT["mo"][1]](ST("mo", o + U + 7, o + U + 3, -1), ST("sc", 145, L, 146))
+        either[OPT["mo"][t][0]](B("mo", o + U, o + U + 4), ST("sc", 16, L, 162))
+        either[OPT["mo"][t][1]](ST("mo", o + U + 7, o + U + 3, -1), ST("sc", 145, L, 146))
         if t == 2:
             cp(B("tab", NONE, NONE + 1), B("xsav", 1, 2))
         w = B("tab", 0, WT)
         note("V", [w], [X("mo")], lambda q: q.tensor_copy(out=w[0].indirect(T.mo[:, U:M]), in_=T.mo[:, 0:U]), (60, U, "s"))
 
+    def y_rows(t, qy, opy, empty):
+        s = t % 2
+        group(to_rows("b2", 0, s + 1, [(qy, "id1")], False) + [(E("b2", 1 - s), B("id4096"), empty)]
+              + to_rows("b2", 0, s + 1, [(opy, "id4096")]), True)
+
     def new_rows(t):
         s = t % 2
-        gg, ma, mb = "g%d" % t, "ma%d" % t, "mb%d" % t
-        go, ao, bo = ("go%d" % t, "ao%d" % t, "bo%d" % t) if t < 2 else ("fog", "foa", "fob")
+        gg, ma, mb = ("g%d" % t, "ma%d" % t, "mb%d" % t) if t < 2 else ("hg", "ha", "hb")
+        go, ao, bo = ("go%d" % t, "ao%d" % t, "bo%d" % t) if t < 2 else ("ogs", "oas", "obs")
+        opx, opy, ty, mg, tk, nx, qy = [("h" if t == 2 else "") + m for m in ("opx", "opy", "ty", "mg", "tk", "nx", "qy")]
+        if t == 2:
+            none("V", B("hem"), E(gg, 1))
+        if t == 2:
+            y_rows(t, qy, opy, B("hem"))
+        pre = t < 2 and OPT["pre"]
+        group(to_rows("b2", 0, s + 1, [(ty, "idn4096"), (mg, "id4096")][:2 - pre]))
         on_s = OPT["er"][t] == "S"
         group(kept(R("b1"), [(H(ma), "id1")]) + kept(R("b1", 32, 64), [(B("ones", 0, 256), "id4096")] * (not on_s))
               + [(E("b1", a, k, 32), B("id1"), E(mb, b, k)) for a, b, k in ((1, 0, 16), (2, 1, 15), (0, 31, 1))]
-              + to_rows("b1", 0, s, [("opx", "idn4096")]) + to_rows("b1", 32, s + 1, [("opx", "idn4096")])
-              + to_rows("b1", 0, s + 1, [("opy", "idn4096")]) + to_rows("b1", 32, s + 2, [("opy", "idn4096")]), True)
+              + to_rows("b1", 0, s, [(opx, "idn4096")]) + to_rows("b1", 32, s + 1, [(opx, "idn4096")])
+              + to_rows("b1", 0, s + 1, [(opy, "idn4096")]) + to_rows("b1", 32, s + 2, [(opy, "idn4096")]), True)
         if on_s:
             act(X("rl"), X("b1"), scale=-1.0, bias=-2049.0, func=F.Relu)
             group(kept(R("b1"), [(R("rl", 32 * k, 32 * k + 32), "id1") for k in range(2)]), True)
@@ -725,36 +782,64 @@ def rank_program(g, core, T, topo):
         else:
             ts(H("er"), R("b1"), 4096.0, A.add, 2047.0, A.min)
             tt(H("er"), R("b1", 32, 64), H("er"), A.min)
-        tt(E(go, 1 - s), E("b2", 1 - s), E("er", 1 - s), A.min)
-        if t < 2:
-            send(1, "gx%d" % (t + 1), E("g%d" % (t + 1), 1 - s), E(go, 1 - s))
-        stay, new = R("b3", 0, 16), R("b3", 16, 32)
-        group(kept(stay, [(E(gg, s), "id1")]) + kept(new, [(B("nx"), "id1"), (B("ones"), "id4096")]) + turned(stay, [(B("opx"), "id4096")])
-              + [x for m in ("mg", "tk") for x in turned(stay, [(B(m), "id4096")]) + turned(new, [(B(m), "idn4096")])], True)
+        tt(E("er" if pre else go, 1 - s), E("b2", 1 - s), E("er", 1 - s), A.min)
+        if pre:
+            {"v": cp, "s": act}[OPT["offx"]](B("oxo%d" % t), E("er", 1 - s))
+            send(1, "gx%d" % (t + 1), B("offx%d" % (t + 1)), B("oxo%d" % t))
+            group(to_rows("b2", 0, s + 1, [(mg, "id2047")]), True)
+            tt(E(go, 1 - s), E("b2", 1 - s), E("er", 1 - s), A.max)
+            if OPT["pre"] == 1:
+                send(1, "gt%d" % (t + 1), E("g%d" % (t + 1), 1 - s), E(go, 1 - s))
+        elif t < 2:
+            if OPT["offx"] in "VS":
+                send(1, "gx%d" % (t + 1), E("g%d" % (t + 1), 1 - s), E(go, 1 - s))
+            else:
+                {"v": cp, "s": act}[OPT["offx"]](B("oxo%d" % t), E(go, 1 - s))
+                send(1, "gx%d" % (t + 1), B("offx%d" % (t + 1)), B("oxo%d" % t))
+        stay, new = R("b4", 0, 16), R("b4", 16, 32)
+        group(kept(stay, [(E(gg, s), "id1")]) + kept(new, [(B(nx), "id1"), (B("ones"), "id4096")]) + turned(stay, [(B(opx), "id4096")])
+              + [x for m in (mg, tk) for x in turned(stay, [(B(m), "id4096")]) + turned(new, [(B(m), "idn4096")])], True)
         tt(E("er", s), stay, E("er", s), A.min)
         tt(E(go, s), new, E("er", s), A.min)
         if t < 2:
-            send(1, "gy%d" % (t + 1), E("g%d" % (t + 1), s), E(go, s))
-        else:
-            send(-2, "fig", X("fig"), X("fog"))
-        group(to_rows("b7", 16, s, [("opx", "id2047")]) + to_rows("b7", 16, s + 2, [("opy", "id2047")])
-              + to_rows("b7", 16, s + 1, [(m, "id2047") for m in ("opx", "opy", "ty", "mg")])
-              + to_rows("b7", 16, s, [(m, "id2047") for m in ("mg", "tk")]), True)
-        merged = R("b4", 0, 16), R("b4", 16, 32)
-        group(kept(R("b4"), [(B("ones", 0, 256), "id4096")]) + kept(merged[0], [(E(gg, s), "id1")])
-              + [(R("b4", 16 + j0, 16 + j1), B("id1"), E(gg, r0, j1 - j0)) for j0, j1, r0 in wrapped(s + 1)]
-              + [x for o in merged for x in turned(o, [(B("mg"), "idn4096")])], True)
+            if OPT["pre"] == 2:
+                send(1, "gy%d" % (t + 1), H("g%d" % (t + 1)), H(go))
+            else:
+                send(1, "gy%d" % (t + 1), E("g%d" % (t + 1), s), E(go, s))
+            if OPT["shipem"]:
+                em = "eo%d" % t
+                none("S", H(em), H(go))
+                pass_on(H(em, U, U + 8), H(em, 0, 8))
+                send(1, "em%d" % (t + 1), X("em%d" % (t + 1)), X(em))
+        group(to_rows("b7", 16, s, [(opx, "id2047")]) + to_rows("b7", 16, s + 2, [(opy, "id2047")])
+              + to_rows("b7", 16, s + 1, [(m, "id2047") for m in (opx, opy, ty, mg)])
+              + to_rows("b7", 16, s, [(m, "id2047") for m in (mg, tk)]), True)
+        bk = "b1" if t < 2 else "b3"
+        merged = R(bk, 0, 16), R(bk, 16, 32)
+        group(kept(R(bk), [(B("ones", 0, 256), "id4096")]) + kept(merged[0], [(E(gg, s), "id1")])
+              + [(R(bk, 16 + j0, 16 + j1), B("id1"), E(gg, r0, j1 - j0)) for j0, j1, r0 in wrapped(s + 1)]
+              + [x for o in merged for x in turned(o, [(B(mg), "idn4096")])], True)
         for o, old, new in zip(merged, (ma, mb), (ao, bo)):
             for h in range(2):
                 tt(E(new, h), E("b7", h, 16, 16), E(old, h), A.max)
             tt(E(new, s), o, E(new, s), A.min)
-            if t == 2:
-                send(-2, "fi" + new[2], X("fi" + new[2]), X(new))
         if t < 2:
             group([(R("b5", 0, 16), B("mg"), B("blk"))], True)
-            {"V": cp, "S": act}[OPT["cnt"]](B("co%d" % t), R("b5", 0, 16))
-            for m, lo, hi in (("ma", 256, 640), ("mb", 0, 256)):
-                send(1, m + str(t + 1), B("m%d" % (t + 1), lo, hi), B("mo%d" % t, lo, hi))
+            if OPT["shipan"]:
+                an = "an%d" % t
+                {"V": cp, "S": act}[OPT["cnt"]](X(an, 2, slice(0, U)), R("b5", 0, 16))
+                none("S", X(an, slice(0, 2), slice(0, U)), H(ao))
+                if t == 0:
+                    pass_on(E(an, 32, 1), E(an, 0, 1))
+                send(1, "ma%d" % (t + 1), X("ac%d" % (t + 1)), X(an))
+            else:
+                {"V": cp, "S": act}[OPT["cnt"]](B("co%d" % t), R("b5", 0, 16))
+                send(1, "ma%d" % (t + 1), B("st%d" % (t + 1), 512, 896), B("so%d" % t, 512, 896))
+        if t == 0:
+            w = 768 if OPT["shipan"] else 512
+            send(1, "mb1", B("st1", 256, w), B("so0", 256, w))
+        if t == 1:
+            send(-1, "hs", X("hs"), B("so1", 0, 768))
 
     def visit(t):
         s = t % 2
@@ -770,37 +855,48 @@ def rank_program(g, core, T, topo):
         tt(B("mnu"), DY, B("sgx"), A.min)
         group(kept(OY, [(B("sgy"), "id1")]))
         above(OPT["op"][1], B("opy"), OY)
-        group(turned(TK, [(E("em", s), "idn18")]) + kept(TK, [(B("sev"), "idbig"), (B("sgy"), "idm"), (B("opy"), "idnbig")]), True)
-        if OPT["tkb"] == "S":
-            act(B("tkb"), TK, scale=-1.0)
-        else:
-            ts(B("tkb"), TK, -1.0, A.mult)
-        group(turned(OT, [(E("em", s + 1), "idbig"), (E("em", s + 2), "idnbig")])
+        group(turned(TK, [(E("em%d" % t, s), "idn18")]) + kept(TK, [(B("sgy"), "idm"), (B("opy"), "idnbig")]), True)
+        act(B("tkb"), TK, scale=-1.0, bias=-7 * BIG)
+        group(turned(OT, [(E("em%d" % t, s + 1), "idbig"), (E("em%d" % t, s + 2), "idnbig")])
               + kept(OT, [(B("sgx"), "up"), (B("opx"), "idnbig"), (B("sgy"), "idm")]), True)
         above(OPT["op"][2], B("ty"), OT)
+        if t < 2:
+            y_rows(t, "qy", "opy", E("em%d" % t, 1 - s))
+        early = [len(ops) - 1] * (OPT["early"] and t < 2)
         all_sums(2, -OPT["late"])
+        hold.extend(early)
+        first = len(ops)
         whole = SUMS[2][-1][1:] == (0, 16)
         group(kept(DN, [(B("opy"), "shb")] + [(B("opy"), "idbig")] * whole))
         all_sums(2, None, -OPT["late"])
         group(kept(DN, [(B("opy"), "idbig")] * (not whole)))
+        hold[:] = []
+        for o in ops[first:]:
+            o["firm"] = True
         tt(B("mg"), DN, B("mnu"), A.is_lt)
         tt(B("tk"), DN, B("tkb"), A.is_lt)
+        if t == 2:
+            send(-2, "hq", X("hq"), X("nq"))
+            for k, (lo, hi) in enumerate(OPT["home"]):
+                send(-2, "hk%d" % k, B("hk", U * lo, U * hi), B("mk", U * lo, U * hi))
         writes(t)
-        group(to_rows("b2", 0, s + 1, [("qy", "id1")], False) + [(E("b2", 1 - s), B("id4096"), E("em", 1 - s))]
-              + to_rows("b2", 0, s + 1, [("opy", "id4096"), ("ty", "idn4096"), ("mg", "id4096")]), True)
         if t == 0:
             split(OPT["cast"][2], "mb0", "bli")
+        first = len(ops)
         new_rows(t)
+        for o in ops[first:] * (t == 2):
+            if o["e"] == "P":
+                o.update(behind=o["behind"] + placed, firm=True)
         if t < 2:
             views(t + 1)
             lists(t + 1)
 
     for t in range(3):
         visit(t)
-    dma("Y", "sox", [], [B("tab", 0, 2048)], T.ox[:, :], T.tab[:, 0:2048], ("", STORE))
-    for k, (m, q) in enumerate((("g", T.og), ("a", T.oa), ("b", T.ob))):
-        {"V": cp, "S": act}[OPT["out"][k]](X("o%ss" % m), X("fi" + m))
-        dma("Y", "so" + m, [], [X("o%ss" % m)], q[:, :], T["o%ss" % m][:, :], ("", STORE - 0.8))
+    for m, q, a, time in (("x", T.ox, B("tab", 0, 2048), 1.5), ("g", T.og, X("ogs"), 0.4), ("a", T.oa, X("oas"), 0.4),
+                          ("b", T.ob, X("obs"), 0.4)):
+        k = dma("Y", "so" + m, [], [a], q[:, :], a[0], ("", STORE))
+        note("L", [], [], None, (time, 0, "l"), deps=[k])
 
     cnt = issue()
     for sm in ("sog", "soa", "sob", "sox"):

import math
import numpy as np
from concourse.bass import DstId, RemoteDMATransfer
from concourse.mybir import AluOpType as A
from concourse.mybir import ActivationFunctionType as F

U = 128
M = 136
FIRST = [146 * c if c < 4 else 162 * (7 - c) + 17 for c in range(8)]
L = 4 * 146
NONE = 2047
WT = 2048 + 256
BIG = 32768.0
MID = 2040.0
FAR = 1024.0
CUTS = ["SX3 VX10 SX16 SY8 SY16 SN8 SN14 SN16"] + ["SX3 VX7 SX16 SY8 SY16 VN3 SN9 SN14 SN16"] * 2


def pieces(t):
    at, out = {}, []
    for p in CUTS[t].split():
        out.append(("XYN".index(p[1]), at.get(p[1], 0), int(p[2:]), p[0]))
        at[p[1]] = int(p[2:])
    return out


WHOLE = ((0, 0, 16), (1, 0, 16))
SUMS = (WHOLE, WHOLE, WHOLE)
WIDTH = 2
FIFO = 1
LOADS = "gxyatbs"
IDS = {"id1184": 1184.0, "id32": 32.0, "id65": 65.0, "idf": -1.0 / 32, "id217": 217.0, "idbig": BIG, "idm": -1.0,
       "idnbig": -BIG, "id4096": 4096.0, "idn4096": -4096.0, "id2047": 2047.0}
ON_SCALAR = ("id4096", "idn4096", "id2047", "idm")
OPT = {"offx": "S", "off": ("VV", "SS", "SS"), "bf": ((0, 4, 8), "VS"), "mo": "VS", "eq": "VV", "an": "VSS", "em": "S",
       "sg": "VV", "cnt": "S", "cast": "GVG", "op": "VVV", "er": "VVV", "xfirst": False, "late": 2,
       "qn": ("VV", "VV", "VV"), "pad": "V", "out": "VVV", "tkb": "S"}
OPT.update(off=("VV",) * 3, em="V", an="VVV", thpad="V", pack="S", home=((0, 3), (3, 5)), anpad="G",
           qn=("GG",) * 3, pad="G", shipem=1, shipan=0, w=0)
OPT.update(home=((0, 2), (2, 4), (4, 5)), early=1, sums="VSS", thpad="G", pre=1, offx="s", shipem=0,
           bf=[((0, 4, 8), "VS")] * 3, mo=("VS",) * 3, xv=("SS",) * 3, shifted=1, xp="G")
OPT.update(off=("VG",) * 3, shipan=1, shipem=1)
EARLY = 1152
CYC, ISSUE, STORE = 0.00083, 0.3, 1.5
CLOCKS = ((1.0, 1.56, 3.8, 0.000525, 0.1, 1.9, 3.9, 0.0025, 1.5, 0.3), (1.3, 1.3, 3.0, 0.000525, 0.15, 1.6, 3.2, 0.002, 1.0, 0.7),
          (1.2, 1.9, 5.0, 0.00042, 0.12, 1.5, 3.5, 0.004, 1.5, 0.4), (1.1, 1.2, 2.5, 0.00047, 0.17, 2.4, 3.6, 0.002, 2.0, 0.2))
PLANS = list(CLOCKS) + [(1.0, g, 3.8, 0.000525, wake, 1.9, 3.6, 0.003, 1.0, 0.3) for g in (1.4, 1.7) for wake in (0.08, 0.15)]

SCRATCH = {}


def _add(where, dtype, **kw):
    for k, v in kw.items():
        SCRATCH[k] = (where, [128] + (v if isinstance(v, list) else [v]), dtype)


RING, HALVES, PADDED = [32, 8], 2 * U, [2, U + 8]
_add("sbuf", "bfloat16", tab=WT, xsav=16, yvs=384, v1=U, v2=U, ii=256, idn18=128, zs=16, one=256, cb=128, c8=128, xv=256, xg=48 * U,
     mx=48 * U, vx0=512, vx1=512, vx2=512)
_add("sbuf", "int32", gli=RING, pidx=8, pin=8, nxi=U, nxj=U, qyi=U, qyj=U,
     **{b: RING if e != "S" else 256 for b, e in zip(("ali", "thi", "bli"), OPT["cast"])})
_add("sbuf", "uint16", offx0=U, offx1=U, offx2=U, oxo0=U, oxo1=U, offy=U, offn=U, goff=8, soff=8, same=8, apart=16, mo=M)
_add("sbuf", "float16", em0=PADDED, em1=PADDED, em2=PADDED, eo0=PADDED, eo1=PADDED, er=HALVES,
     ac0=[3, U + 8], ac1=[3, U + 8], ac2=[3, U + 8], an0=[3, U + 8], an1=[3, U + 8], th0=PADDED, th1=PADDED, th2=PADDED, hs=768, hq=256, hk=640, hem=U, xp=U, sid4096=U, sidn4096=U, sid2047=U,
     nq=256, mk=640, kq=U, ones=256, sev=U, cm=U, cmid=U, nblk=U, sgx=U, sgy=U, mnu=U, rp=U, ff=U, nrm=U, blk=U, blk4=U, tri0=U, tri=U, shb=U, w2=8, rob2=U, sums=U, ids=128 * len(IDS), bf=128, eq=L,
     w=L, sc=L, rl=[64, 8], st0=896, st1=896, st2=896, so0=896, so1=896)
_add("sbuf", "float32", c16=24, col=16, sp4=8, iw=WT, pp=U, tkb=U, gf=8, ogs=RING, oas=RING, obs=RING)
_add("psum", "float32", **{"b%d" % k: [64, 8] for k in range(8)})
SEMAPHORES = ["pv", "pa", "pt", "pg", "dg", "dy", "dx", "ds", "da", "db", "dt", "sog", "soa", "sob", "sox", "ls", "pv1", "pv2", "pt1", "pt2",
              "gx1", "gy1", "ma1", "mb1", "gx2", "gy2", "ma2", "em1", "em2", "gt1", "gt2", "hs", "hq", "hk0", "hk1", "hk2", "hk3"]
PART = {k: ("ids", 128 * j) for j, k in enumerate(IDS)}
PART.update(id1=("ii", 0), up=("ii", 8), idn18=("idn18", 0), v0=("yvs", 0))
for _t in range(3):
    for _k, (_a, _b) in enumerate((("g", "go"), ("mb", "bo"), ("ma", "ao"), ("cnt", "co"))):
        PART.update({_a + str(_t): ("st%d" % _t, 256 * _k), _b + str(_t): ("so%d" % _t, 256 * _k)})
for _k, _a in enumerate(("opx", "opy", "ty", "mg", "tk")):
    PART.update({_a: ("mk", U * _k), "h" + _a: ("hk", U * _k)})
PART.update(nx=("nq", 0), qy=("nq", U), hnx=("hq", 0), hqy=("hq", U), hg=("hs", 0), hb=("hs", 256), ha=("hs", 512))
NAME = {v: k for k, v in PART.items()}
COLS = {k: np.arange(int(np.prod(v[1][1:]))).reshape(v[1][1:]) for k, v in SCRATCH.items()}
WIDE = {k: v[2] in ("float32", "int32") for k, v in SCRATCH.items()}
COUNTER = {"V": "pv", "S": "pa", "P": "pt", "G": "pg"}
LOOK, MOVES, SLACK, SEED, ROUNDS, RELAX = 0.5, 60000, 0.0003, 1, 4, 0.0
SOONER = {"opx": 2.0, "opy": 1.0, "em0": 2.0, "em1": 2.0, "em2": 2.0, "mnu": 2.0, "mb0": 3.0, "st0": 3.0, "st1": 2.0,
          "ac0": 2.0, "ac1": 2.0, "ac2": 2.0, "nx": 2.0, "qy": 2.0, "nxi": 1.5, "th1": 5.0, "th2": 5.0, "v1": 6.0, "v2": 6.0}
PROMPT, ANY = 1.0, 0.4
ORDER = []


def timing(ops, clock):
    f, gather, scatter, tensor, wake, way, load, copy, first, call = clock
    cost, tail = [], []
    for o in ops:
        fix, more, kind = o["cost"]
        per = {"g": gather * CYC * f, "s": scatter * CYC * f, "p": tensor * f, "c": CYC * f, "r": 0.0, "l": copy}[kind]
        cost.append((fix * CYC * f if o["e"] in "VS" else fix) + more * per)
        if kind == "r" and more:
            cost[-1], first = call + first, 0.0
        what, share = o["tail"]
        tail.append({"": 1.0, "way": way, "load": load, "copy": copy}[what] * share)
    lags = [[(d, tail[d] + (0.0 if ops[d]["e"] == o["e"] in "PY" or o["e"] in "DL" else wake)) for d in o["deps"]] for o in ops]
    return cost, tail, lags


def replay(order, queue, times, lo=0, hi=0, old=None, reach=None):
    cost, tail, lags = times
    b = lo >> 5
    done, marks = (old[1][:], old[2][:b + 1]) if old else ([0.0] * len(order), [(0.0,) * 8])
    free = list(marks[b])
    for i in range(b << 5, len(order)):
        if not i & 31 and i >> 5 > b:
            if old and i > hi and old[2][i >> 5][:7] == tuple(free[:7]):
                return max(old[0], free[7]), done, marks + old[2][i >> 5:]
            marks.append(tuple(free))
        k = order[i]
        e = queue[k]
        t = free[e]
        for d, l in lags[k]:
            if done[d] + l > t:
                t = done[d] + l
        t += cost[k]
        if old and t != done[k] and reach[k] > hi:
            hi = reach[k]
        done[k] = t
        if e:
            free[e] = t
        if t + tail[k] > free[7]:
            free[7] = t + tail[k]
    return free[7], done, marks


def runs(order, before, times, done):
    cost, tail, lags = times
    k = max(order[-32:], key=lambda x: done[x] + tail[x])
    out, run = [], [k]
    while True:
        start, q = done[k] - cost[k], before[k]
        if q >= 0 and abs(done[q] - start) < 1e-9:
            k = q
            run.append(k)
            continue
        if len(run) > 1:
            out.append(run[::-1])
        by = [d for d, l in lags[k] if abs(done[d] + l - start) < 1e-9]
        if not by:
            return out
        k = by[0]
        run = [k]


def issue_order(ops):
    queue = ["DVSPGYL".index(o["e"]) for o in ops]
    above, near = [], []
    for o in ops:
        far = 0
        for d in o["deps"]:
            far |= above[d]
        near.append([d for d in o["deps"] if not far >> d & 1])
        above.append(far | sum(1 << d for d in o["deps"]))
    ops = [dict(o, deps=d) for o, d in zip(ops, near)]
    clocks = [timing(ops, c) for c in CLOCKS]
    order = min((o for c in PLANS for o in list_schedule(ops, timing(ops, c))),
                key=lambda o: sum(replay(o, queue, c)[0] for c in clocks))
    deps = [set(o["deps"]) | {d for d in o["behind"] if o["firm"]} for o in ops]
    state = [replay(order, queue, c) for c in clocks]
    scale = [len(clocks) * s[0] for s in state]
    now, best, found, seed = 0.0, (0.0, order), None, [SEED]

    def draw():
        seed[0] = (seed[0] * 6364136223846793005 + 1442695040888963407) % 2 ** 64
        return (seed[0] >> 11) / 2.0 ** 53

    for step in range(MOVES):
        if found is None:
            place, before, reach, last = [0] * len(ops), [-1] * len(ops), [0] * len(ops), [-1] * 7
            for i, k in enumerate(order):
                place[k] = i
                if queue[k]:
                    before[k], last[queue[k]] = last[queue[k]], k
                for d in near[k]:
                    reach[d] = i
            found = [r for c, s in zip(clocks, state) for r in runs(order, before, c, s[1]) for _ in range(int(len(r) ** 0.5))]
        run, m = found[int(draw() * len(found))], draw()
        i = int(draw() * (len(run) - 1))
        j = len(run) - 1 if m < 0.25 else min(len(run) - 1, i + (1, 1, 2, 3, 5, 8, 16, 40)[int(draw() * 8)])
        u, v = run[0 if m > 0.85 else i], run[j]
        if draw() < ANY:
            u = v = int(draw() * len(ops))
            for _ in range((1, 1, 2, 3, 5, 8)[int(draw() * 6)]):
                u = before[u] if before[u] >= 0 else u
            if u == v:
                continue
        part = order[place[u]:place[v] + 1]
        if draw() < 0.5:
            moved, need = {v}, set(deps[v])
            for x in part[-2::-1]:
                if x in need:
                    moved.add(x)
                    need |= deps[x]
        else:
            stay = {u}
            for x in part[1:]:
                if deps[x] & stay:
                    stay.add(x)
            moved = set(part) - stay
        if u in moved or v not in moved:
            continue
        new = order[:place[u]] + [x for x in part if x in moved] + [x for x in part if x not in moved] + order[place[v] + 1:]
        limit, tried, change = -SLACK * (1 - step / MOVES) * math.log(draw() + 1e-12), [], 0.0
        for c, s, z in zip(clocks, state, scale):
            tried.append(replay(new, queue, c, place[u], place[v], s, reach))
            change += (tried[-1][0] - s[0] + PROMPT * (sum(tried[-1][1]) - sum(s[1])) / len(ops)) / z
            if change > limit + 0.002:
                break
        if change <= limit:
            order, state, now, found = new, tried, now + change, None
            if now < best[0]:
                best = (now, order)
    return best[1]


def list_schedule(ops, times):
    cost, tails, lags = times
    n = len(ops)
    lag = [dict([(d, 0.0) for d in o["behind"]] + l) for o, l in zip(ops, lags)]
    after = [[] for _ in ops]
    for k, l in enumerate(lag):
        for d, x in l.items():
            after[d].append((k, x))
    key = [0.0] * n
    for k in range(n - 1, -1, -1):
        key[k] = cost[k] + max([tails[k]] + [x + key[j] for j, x in after[k]]) + SOONER.get(ops[k]["name"], 0.0)
    out = []
    for _ in range(ROUNDS):
        out.append(dispatch(ops, cost, lag, after, key))
        way, nxt = [0.0] * n, {}
        for k in out[-1][::-1]:
            e = ops[k]["e"]
            way[k] = cost[k] + max([tails[k], nxt.get(e, 0.0) - RELAX] + [x + way[j] for j, x in after[k]])
            if e != "D":
                nxt[e] = way[k]
        key = [(a + b) / 2 for a, b in zip(key, way)]
    return out


def dispatch(ops, cost, lag, after, key):
    n = len(ops)
    left, at = [len(l) for l in lag], [0.0] * n
    pool, free, order = {e: [] for e in "DVSPGYL"}, {e: 0.0 for e in "DVSPGYL"}, []
    for k in range(n):
        if not left[k]:
            pool[ops[k]["e"]].append(k)
    while len(order) < n:
        best = None
        for e, p in pool.items():
            if not p:
                continue
            t = max(free[e], min(at[x] for x in p))
            k = max((x for x in p if at[x] <= t + 1e-9), key=lambda x: key[x])
            soon = [x for x in p if t < at[x] < t + LOOK * cost[k] and key[x] > key[k] + 0.3]
            if soon:
                k = max(soon, key=lambda x: key[x])
            if best is None or (max(t, at[k]), k) < best:
                best = (max(t, at[k]), k)
        t, k = best
        e = ops[k]["e"]
        pool[e].remove(k)
        if e != "D":
            free[e] = t + cost[k]
        order.append(k)
        for j, x in after[k]:
            at[j] = max(at[j], t + cost[k] + x)
            left[j] -= 1
            if not left[j]:
                pool[ops[j]["e"]].append(j)
    return order


def rank_program(g, core, T, topo):
    rank = T.rank_of(core)
    if rank is None:
        return
    n = len(T.cores)
    Q = {"V": g.vector, "S": g.scalar, "P": g.tensor, "G": g, "Y": g.sync}

    ops, writer, readers, bank, gathered, hold, made, placed, ends = [], {}, {}, {}, [], [], [], [], {}

    def note(e, outs, ins, call, cost, tail=("", 0.0), sem=None, deps=(), behind=(), firm=False):
        k, deps = len(ops), set(deps)
        for ap, parts in ins:
            for b, cols in parts:
                deps.update(np.unique(writer[b][cols]).tolist() if b in writer else [])
        for ap, parts in outs:
            for b, cols in parts:
                w = writer.setdefault(b, np.full(COLS[b].size, -1))
                deps.update(np.unique(w[cols]).tolist())
                for r, m in list(readers.get(b, {}).items()):
                    if m[cols].any():
                        deps.add(r)
                        m[cols] = False
                        if not m.any():
                            del readers[b][r]
                w[cols] = k
        for ap, parts in ins:
            for b, cols in parts:
                if b not in ("ids", "ii", "zs"):
                    readers.setdefault(b, {}).setdefault(k, np.zeros(COLS[b].size, bool))[cols] = True
        for b in {b for ap, parts in list(ins) + list(outs) for b, cols in parts if SCRATCH[b][0] == "psum"}:
            rec = bank.setdefault(b, [e, [], []])
            if rec[0] != e:
                rec[:] = [e, [], rec[1]]
            deps.update(rec[2] + (rec[1][-1:] if e == "P" else []))
            rec[1].append(k)
        ops.append({"e": e, "deps": sorted(deps - {-1, k}), "call": call, "cost": cost, "tail": tail, "sem": sem,
                    "behind": list(behind) + hold, "firm": firm or e in "GY", "name": NAME.get((outs[0][1][0][0], int(outs[0][1][0][1][0])), outs[0][1][0][0]) if outs else ""})
        return k

    def issue():
        if not ORDER:
            ORDER.extend(issue_order(ops))
        cnt, known, token = {e: 0 for e in COUNTER}, {e: {} for e in Q}, {}
        for k in ORDER:
            o = ops[k]
            e = o["e"]
            if e in "DL":
                if e == "D":
                    token[k] = o["sem"] + ({},)
                continue
            toks = [token[d] for d in o["deps"] if d in token and not ops[d]["e"] == e == "P"]
            for sem, val, snap in sorted(toks, key=lambda x: -x[1]):
                if known[e].get(sem, 0) < val:
                    Q[e].wait_ge(T.sem[sem], val)
                    for s, v in list(snap.items()) + [(sem, val)]:
                        known[e][s] = max(known[e].get(s, 0), v)
            i = o["call"](Q[e])
            if o["sem"]:
                i.then_inc(T.sem[o["sem"][0]], 16)
                token[k] = o["sem"] + (dict(known[e]),)
            elif i is not None:
                for j in i if isinstance(i, list) else [i]:
                    cnt[e] += 1
                    j.then_inc(T.sem[COUNTER[e]], 1)
                token[k] = (COUNTER[e], cnt[e], dict(known[e]))
        return cnt

    ALL = slice(None)

    def X(b, *ix, rows=ALL):
        ix = ix or (ALL,) * COLS[b].ndim
        return (T[b][(rows,) + ix], [(b, COLS[b][ix].reshape(-1))])

    def B(b, lo=0, hi=U, rows=ALL):
        if b in PART:
            b, o = PART[b]
            lo, hi = o + lo, o + hi
        return X(b, slice(lo, hi), rows=rows)

    def ST(b, lo, hi, step):
        return X(b, slice(lo, hi, step))

    def R(b, lo=0, hi=32):
        return X(b, slice(lo, hi), ALL)

    def E(b, lo, k=16, base=0):
        if b in PART or COLS[b].ndim == 1:
            return B(b, U * (lo % 2) + 8 * (lo // 2), U * (lo % 2) + 8 * (lo // 2 + k))
        if len(COLS[b]) < 4:
            return X(b, lo % 2, slice(8 * (lo // 2), 8 * (lo // 2 + k)))
        if SCRATCH[b][0] == "psum":
            return R(b, base + 16 * (lo % 2) + lo // 2, base + 16 * (lo % 2) + lo // 2 + k)
        return X(b, slice(lo, lo + 2 * k - 1, 2), ALL)

    def H(b, lo=0, hi=U):
        return B(b, 0, 2 * U) if b in PART or COLS[b].ndim == 1 else X(b, ALL, slice(lo, hi))

    def ind(w, o):
        return (w[0].indirect(o[0]), w[1] + o[1])

    def cycles(o, ins, two=False):
        k = len(o[1][0][1])
        if len(ins[0][1]) > 1:
            return (60, k, "g")
        if two:
            return (max(64, k * (1 if any(SCRATCH[v[1][0][0]][0] == "psum" for v in ins) else 2)), 0, "c")
        return (max(64, k * (1 if any(WIDE[v[1][0][0]] for v in [o] + ins) else 0.5)), 0, "c")

    def tt(o, a, b, op, behind=()):
        return note("V", [o], [a, b], lambda q: q.tensor_tensor(out=o[0], in0=a[0], in1=b[0], op=op),
                    cycles(o, [a, b], True), behind=behind)

    def ts(o, a, s1, op0, s2=None, op1=None):
        cols = [s for s in (s1, s2) if isinstance(s, tuple)]
        x, y = [s[0] if isinstance(s, tuple) else s for s in (s1, s2)]
        more = {} if op1 is None else {"op1": op1}
        note("V", [o], [a] + cols, lambda q: q.tensor_scalar(out=o[0], in0=a[0], scalar1=x, scalar2=y, op0=op0, **more),
             cycles(o, [a]))

    def cp(o, a):
        note("V", [o], [a], lambda q: q.tensor_copy(out=o[0], in_=a[0]), cycles(o, [a]))

    def fill(o, x):
        note("V", [o], [], lambda q: q.memset(o[0], x), cycles(o, [o]))

    def scan(o, d0, d1, op0, op1):
        note("V", [o], [d0, d1], lambda q: q.tensor_tensor_scan(out=o[0], data0=d0[0], data1=d1[0], initial=0.0, op0=op0, op1=op1),
             cycles(o, [d0, d1]))

    def act(o, a, scale=1.0, bias=0.0, func=F.Copy, behind=()):
        cols = [s for s in (scale, bias) if isinstance(s, tuple)]
        x, y = [s[0] if isinstance(s, tuple) else s for s in (scale, bias)]
        k = len(o[1][0][1])
        note("S", [o], [a] + cols, lambda q: q.activation(out=o[0], in_=a[0], func=func, bias=y, scale=x),
             (80, k, "g") if len(a[1]) > 1 else (80 + max(64, k), 0, "c"), behind=behind)

    def block(out, mats, each, start=False):
        end, bk = [len(mats) - 1], out[1][0][0]
        if not start:
            ends[bk][0] = -1
        ends[bk] = end
        note("P", [out], [x for o, l, r in mats for x in (l, r)],
             lambda q: [q.matmul(out=o[0], lhsT=l[0], rhs=r[0], start=start and k == 0, stop=k == end[0])
                        for k, (o, l, r) in enumerate(mats)], (0.0, each * len(mats), "p"))

    def group(mats, start=False):
        for k, (o, l, r) in enumerate(mats):
            block(o, [(o, l, r)], max(64, len(o[1][0][1])), start and k == 0)

    def dma(q, sem, outs, ins, out, in_, time, behind=()):
        return note(q, outs, ins, lambda e: e.dma_start(out=out, in_=in_), (0.05, 0, "r"), time, (sem, 16), behind=behind)

    def iota(o, pattern, base, cm, behind=()):
        more = {"allow_small_or_imprecise_dtypes": True} if SCRATCH[o[1][0][0]][2] != "int32" else {}
        return note("G", [o], [], lambda q: q.iota(o[0], pattern, base, cm, **more), (0.13, 2 * len(o[1][0][1]), "c"),
                    behind=behind)

    def pick(o, a, pattern, op, other, cm, behind=()):
        return note("G", [o], [a], lambda q: q.affine_select(o[0], a[0], pattern, op, other, 0, cm),
                    (0.17, 2 * len(o[1][0][1]), "c"), behind=behind)

    def remote(ins, call, behind=()):
        def run(q):
            call(q)
        return note("G", [], ins, run, (ISSUE, 1, "r"), behind=behind)

    def arrives(outs, ins, sem, val, since, time):
        note("D", outs, ins, None, (0.0, 0, "r"), time, (sem, val), [since])

    fill(B("tab", 2032, 2048), FAR)
    loads = {"y": ("yvs", X("yvs")[0], T.yv[:, :], 0.08), "g": ("gli", X("gli")[0], T.gl[:, :], 0.12),
             "x": ("tab", T.tab[:, 0:NONE], T.xt[:, 0:NONE], 0.4), "a": ("ali", X("ali")[0], T.al[:, :], 0.12),
             "t": ("thi", X("thi")[0], T.th[:, :], 0.12), "b": ("bli", X("bli")[0], T.bl[:, :], 0.12),
             "s": ("xsav", T.xsav[:, 0:2], T.xt[:, NONE - 1:NONE + 1], 0.03)}
    k, at = [], 0.4
    for m in LOADS:
        b, o, src, time = loads[m]
        at += time
        k = [dma("Y", "d" + m, [B(b, 0, 2048) if m == "x" else X(b)], [], o, src, ("load", at), k)]

    def C(k):
        return B("col", k, k + 1)

    iota(B("pidx", 0, 2), [[0, 2]], 0, 1)
    fill(B("one", 0, 256), 1.0)
    pick(B("ii", 0, 256), B("one", 0, 256), [[0, 2], [-1, 128]], A.is_equal, 0.0, 1)
    iota(B("c16", 0, 16), [[8, 2], [32, 8]], 0, 0)
    iota(B("cb"), [[0, 8], [1, 16]], 0, 0)
    k = iota(B("c8"), [[0, 16], [1, 8]], 0, 0)
    for a in range(0, EARLY, 576):
        k = iota(B("iw", a, a + 576), [[1, 576]], a, 0, [k])
    fill(B("ones", 0, 256), 1.0)
    fill(B("kq"), 1801.0 / 64)
    for b in ("an0", "an1") * OPT["shipan"]:
        fill(X(b, ALL, slice(U, U + 8)), 0.0)
    fill(B("cm"), -2046.0)
    for j, (x, op) in enumerate(((15, A.bitwise_and), (4, A.arith_shift_right), (7, A.bitwise_and), (3, A.arith_shift_right))):
        ts(B("pin", j, j + 1), B("pidx", 0, 1), x, op)
    cp(B("col", 0, 4), B("pin", 0, 4))
    ts(C(4), C(3), 256.0, A.mult)
    ts(C(5), C(0), 2.0, A.mult)
    ts(B("nrm"), B("cb"), C(0), A.is_equal, -1.0, A.mult)
    ts(B("blk"), B("c8"), C(2), A.is_equal)
    ts(B("blk4"), B("c8"), C(2), A.is_equal, 4096.0, A.mult)
    if any("C" in c for c in CUTS):
        fill(B("cmid"), MID)
        ts(B("nblk"), B("c8"), C(2), A.is_equal, -1.0, A.mult)
    ts(B("w2", 0, 8), B("blk", 0, 8), C(4), A.mult)
    for j, x in enumerate((-1.0, 2.0, -1.0)[:2]):
        ts(B("zs", 8 * j, 8 * j + 8), B("c8", 0, 8), C(1), A.is_equal, x, A.mult)
    ts(B("rob2"), B("c8"), 32.0, A.mult, C(5), A.add)
    for b in IDS:
        if b in ON_SCALAR:
            act(B(b), B("id1"), scale=IDS[b])
        else:
            ts(B(b), B("id1"), IDS[b], A.mult)
    ts(B("idn18"), B("id1"), -8 * BIG, A.mult)
    ts(B("shb"), B("ii", 120, 248), BIG, A.mult)
    for b in ("id4096", "idn4096", "id2047") * OPT["shifted"]:
        act(B("s" + b), B("ii", 120, 248), scale=IDS[b])
    ts(B("same", 0, 8), B("rob2", 0, 8), 0.5, A.mult)
    ts(C(6), C(5), C(2), A.subtract)
    ts(B("apart", 0, 16), B("c16", 0, 16), C(6), A.add)
    ts(B("sp4", 0, 8), B("rob2", 0, 8), -4.0, A.mult, -8191.0, A.add)
    fill(B("w", 0, L), 1.0)
    for c in range(8):
        o = FIRST[c] + 16 * c
        act(B("w", o, o + 16), B("nrm", 0, 16), scale=B("sp4", c, c + 1), bias=1.0, func=F.Identity)
    fill(ST("w", 0, L, 146), 0.0)
    fill(ST("w", 17, L, 162), 0.0)

    def none(e, o, a):
        if e == "V":
            ts(o, a, 2047.0, A.is_equal)
        else:
            act(o, a, bias=-2046.0, func=F.Relu)

    def cast(e, o, b):
        if e == "V":
            cp(o, B(b))
        elif e == "G":
            pass_on(o, B(b))
        else:
            act(o, ind(B(b), B("same", 0, 8)))

    def split(e, o, b, bias=0.0):
        if e != "S":
            for k in range(2):
                if e == "V":
                    ts(E(o, k), E(b, k), bias, A.add)
                else:
                    pick(E(o, k), E(b, k), [[0, U]], A.is_equal, 0.0, 0)
        else:
            act(H(o), ind(X(b), B("apart", 0, 16)), bias=bias)

    def views(t):
        v = ("yvs", "v1", "v2")[t]
        bk = "b0" if t else "b6"
        block(R(bk, 48, 64), [(X(bk, slice(48 + r // 8, 64, 2), r % 8, rows=few), ST(v, r, U, 16), B("zs", 0, 8))
                              for r in range(16)], 8, True)
        if OPT["sums"][t] == "S":
            act(B("sums", rows=few), X(bk, slice(48, 64), ALL, rows=few), bias=MID)
        else:
            ts(B("sums", rows=few), X(bk, slice(48, 64), ALL, rows=few), MID, A.add)
        group([(R("b0", k, k + 16), B("id1"), B(v)) for k in (0, 16)], True)

    few = slice(0, 8)

    def wrapped(lo):
        k = min(16, (33 - lo) // 2)
        return ((0, k, lo), (k, 16, lo + 2 * k - 32))[:1 + (k < 16)]

    def turned(o, terms):
        return [(o, a, B(l)) for a, l in terms]

    def kept(o, terms):
        return [(o, B(l), a) for a, l in terms]

    def to_rows(bk, base, lo, terms, turn=True):
        out = []
        for a, l in terms:
            if turn and lo > 1 and OPT["shifted"]:
                out.append((E(bk, lo - 2, 16, base), B(a), B("s" + l)))
                continue
            for j0, j1, r0 in wrapped(lo):
                o = E(bk, r0, j1 - j0, base)
                out.append((o, B(a), B(l, 8 * j0, 8 * j1)) if turn else (o, B(l), B(a, 8 * j0, 8 * j1)))
        return out

    def lists(t):
        s, gg = t % 2, "g%d" % t
        if t and OPT["offx"] in "VS":
            {"V": cp, "S": act}[OPT["offx"]](B("offx%d" % t), E(gg, s))
        elif t and OPT["pre"] != 2:
            {"V": cp, "G": pass_on}[OPT["xp"]](B("xp") if OPT["pre"] else E(gg, s), B("offx%d" % t))

        def rows(bk, base, lo, l):
            return [(R(bk, base + j0, base + j1), B(l), E(gg, r0, j1 - j0)) for j0, j1, r0 in wrapped(lo)]

        group(kept(R("b2", 0, 16), [(B("cm"), "idn18")]) + rows("b2", 0, s + 1, "idn18") + kept(R("b2", 0, 16), [(B("kq"), "id217")])
              + (rows("b2", 0, s + 2, "id65") + rows("b2", 0, s + 2, "idf") if not (t and OPT["pre"] == 1) else
                 [(R("b2", a, b), B(l), B("xp", 8 * c, 8 * (c + b - a))) for l in ("id65", "idf") for a, b, c in ((0, 15, 1), (15, 16, 0))]),
              True)
        group(rows("b3", 0, s, "id1184") + rows("b3", 32, s + 1, "id1") + rows("b3", 0, s + 1, "id32"), True)
        tt(B("pp"), R("b3", 32, 48), E(gg, s), A.mult)
        for o, l, a in rows("b2", 0, s + 1, "id1"):
            j = o[1][0][1]
            tt(B("qyi", int(j[0]), int(j[-1]) + 1), o, a, A.min)
        tt(B("nxi"), R("b3", 0, 16), B("pp"), A.add)
        ts(B("qyj"), B("qyi"), 2047, A.bitwise_and)
        ts(B("nxj"), B("nxi"), 5, A.arith_shift_right, 2047, A.bitwise_and)
        for k, (o, a) in enumerate((("offy", "qyj"), ("offn", "nxj"))):
            cast(OPT["off"][t][k], B(o), a)
        for k, (o, a, b) in enumerate((("qy", "qyj", "offy"), ("nx", "nxj", "offn"))):
            e = OPT["qn"][t][k]
            {"V": cp, "v": cp, "S": act, "G": pass_on}[e](B(o), B(a if e in "vG" else b))
        if not (t and OPT["shipem"]):
            none(OPT["em"], H("em%d" % t), H(gg))
            {"V": cp, "S": act, "G": pass_on}[OPT["pad"]](H("em%d" % t, U, U + 8), H("em%d" % t, 0, 8))

    DX, DY, DN = R("b1", 48, 64), R("b2", 48, 64), R("b3", 48, 64)
    OX, OY, OT, TK = R("b7", 0, 16), R("b4", 0, 16), R("b7", 16, 32), R("b6", 0, 16)

    def before(t):
        s = t % 2
        em, an = "em%d" % t, "ac%d" % t
        ex, ey, en = E(em, s), E(em, s + 1), E(em, s + 2)
        if not (t and OPT["shipan"]):
            none(OPT["an"][t], X(an, slice(0, 2), slice(0, U)), H("ma%d" % t))
            if s:
                {"V": cp, "S": act, "G": pass_on}[OPT["anpad"]](E(an, 32, 1), E(an, 0, 1))
        for l, d in enumerate((DX, DY, DN)):
            fused = [j for k, j0, j1, e in pieces(t) if e == "C" and k == l for j in range(j0, j1)]
            more = slice(0, 16)
            group([(d, B("blk", rows=more), B("sums", rows=more))], True)
            for j0 in range(0, 16, 4):
                if j0 in fused:
                    o = X("b%d" % (l + 1), slice(48, 64), ALL, rows=slice(8 * j0, 8 * j0 + 32))
                    group([(o, B("nblk", 8 * j0, 8 * j0 + 32, few), B("sums", rows=few)), (o, B("id1", 0, 32), B("cmid"))])
        group(turned(DN, [(ey, "idbig"), (ex, "idbig")]))
        count = [(X(an, 2, slice(0, U)) if OPT["shipan"] else B("cnt%d" % t), "nrm")] * (t > 0)
        group(turned(OX, [(E("th%d" % t, s), "idm"), (ex, "idnbig"), (ey, "idbig"), (E(an, s), "idnbig")] + count), True)
        group(turned(OY, [(E("th%d" % t, s + 1), "idm"), (ey, "idnbig"), (en, "idbig"), (E(an, s + 1), "idnbig")] + count), True)
        group(turned(R("b5", 0, 16), [(B("rob2"), "idm"), (B("nx"), "id1")]), True)

    def sums(l, k, j0=0, j1=16):
        bk, a = "b%d" % (l + 1), 2048 * l
        rows = slice(8 * j0, 8 * j1)
        block(R(bk, 48, 64), [(X(bk, slice(48 + r // 8, 64, 2), r % 8, rows=rows),
                               ST(("xg", "mx")[k], a + U * j0 + r, a + U * j1, 16), B("zs", 8 * k, 8 * k + 8)) for r in range(16)],
              min(64, 8 * (j1 - j0)))

    def distances(t):
        prev = {}
        for l, j0, j1, e in pieces(t):
            gather(t, l, j0, j1, e, prev)
            q = "S" if e == "S" else "V"
            first = [prev[q]] if q in prev else made["VS".index(q)] * (t == 0)
            ops[prev["now"]].update(behind=ops[prev["now"]]["behind"] + first, firm=True)
            prev[q] = prev["now"]

    def gather(t, l, j0, j1, e, prev):
        for _ in range(1):
            lo, hi = 2048 * l + U * j0, 2048 * l + U * j1
            prev["now"] = len(ops)
            x = ind(B("tab", 0, 2048), B(("offx%d" % t, "offy", "offn")[l], 8 * j0, 8 * j1))
            if e == "C":
                tt(B("xg", lo, hi), x, B("vx%d" % t, 0, hi - lo), A.subtract)
                ts(B("mx", lo, hi), B("xg", lo, hi), 0.0, A.max)
                continue
            {"V": cp, "S": act}[e](B("xg", lo, hi), x)
            gathered.append(len(ops) - 1)
            for a in range(lo, hi, U * WIDTH):
                b = min(hi, a + U * WIDTH)
                k = tt(B("mx", a, b), B("xg", a, b), R("b0", 0, (b - a) // 8), A.max, [prev.get("max")] * (FIFO and "max" in prev))
                ops[k]["firm"] = True
                prev["max"] = k

    def pass_on(o, a):
        pick(o, a, [[0, len(o[1][0][1])]], A.is_equal, 0.0, 0)

    def repeat(t):
        if any(p[3] == "C" for p in pieces(t)):
            b = "vx%d" % t
            for lo, hi, a in ((0, U, B("v%d" % t)), (U, 2 * U, B("v%d" % t)), (2 * U, 4 * U, B(b, 0, 2 * U))):
                pass_on(B(b, lo, hi), a)

    def all_sums(l, hi=None, lo=None):
        for k, j0, j1 in SUMS[l][lo:hi]:
            sums(l, k, j0, j1)

    def above(e, o, a):
        if e == "V":
            ts(o, a, BIG, A.is_gt)
        else:
            act(o, a, bias=-BIG - 0.5, func=F.Sign)

    peer = {d: T.cores[(rank + d) % n] for d in (1, 2, -1, -2)}
    sent = [0]

    def send(d, sem, o, a):
        dst = peer[d]
        rid, pid = topo.addr(dst, core)
        k = remote([a], lambda q: q.remote_dma(out_ap=o[0], in_ap=a[0], remote_sem=T.sem[sem], local_sem=T.sem.ls, pid=pid,
                                               routing_id=rid, dma_engine_mask=topo.mask(core, dst)))
        sent[0] += len(topo.engines(core, dst))
        link = note("L", [], [], None, (0.0, len(o[1][0][1]), "l"), deps=[k])
        arrives([o], [], sem, len(topo.engines(peer[-d], core)), link, ("way", 0.85))
        return k

    def ahead(sem, outs, ins):
        def half(src, d):
            e = topo.engines(src, T.cores[(T.rank_of(src) + d) % n])
            return e[len(e) // 2 * (d - 1):len(e) // 2 * d]

        both = [RemoteDMATransfer(dst_ids=[DstId(rid=topo.addr(peer[d], core)[0], pnc=topo.addr(peer[d], core)[1])],
                                  dma_engine_mask=sum(1 << x for x in half(core, d)), remote_sem=T.sem[sem + "%d" % d],
                                  src=ins[d - 1][0], dst=outs[d - 1][0]) for d in (1, 2)]
        k = remote(ins, lambda q: q.remote_dma_fused(both, local_sem=T.sem.ls))
        link = note("L", [], [], None, (0.0, 2 * len(outs[0][1][0][1]), "l"), deps=[k])
        for d in (1, 2):
            sent[0] += len(half(core, d))
            arrives([outs[d - 1]], [], sem + "%d" % d, len(half(peer[-d], d)), link, ("way", 0.85))

    fill(B("sums"), -2 * MID)
    made[:] = [[k for k, o in enumerate(ops) if o["e"] == e and (o["name"] != "w" or e == "V" or OPT["w"])] for e in "VS"]
    cp(B("offx0"), E("gli", 0))
    hold.append(len(ops) - 1)
    split("V", "g0", "gli")
    hold.pop()
    lists(0)
    views(0)
    repeat(0)
    ahead("pv", [B("v%d" % d) for d in (1, 2)], [B("yvs", U * d, U * d + U) for d in (1, 2)])
    pick(B("tri0"), B("blk4"), [[1, U]], A.is_ge, 0.0, -1)
    pick(B("tri"), B("tri0"), [[1, U]], A.not_equal, -4096.0, -1)
    split(OPT["cast"][0], "ma0", "ali")
    split(OPT["cast"][1], "th0", "thi", -MID)
    either = {"V": cp, "S": act, "G": pass_on}
    either[OPT["thpad"]](H("th0", U, U + 8), H("th0", 0, 8))
    ahead("pt", [X("th1"), X("th2")], [X("th0")] * 2)
    for d in (1, 2):
        repeat(d)
    for a in range(EARLY, WT, 576):
        iota(B("iw", a, a + 576), [[1, 576]], a, 0)

    def writes(t):
        group(kept(R("b5", 0, 16), [(B("mg"), "tri")]))
        group(kept(R("b6", 0, 16), [(B("mg"), "tri")]), True)
        ts(B("rp"), R("b5", 0, 16), -2048.0, A.min, 3199.0, A.add)
        act(B("ff"), R("b6", 0, 16), scale=-1.0 / 4096, func=F.Relu)
        for bk, l, r in (("b5", "rp", "blk"), ("b6", "ff", "w2")):
            o = R(bk, 16, 17)
            block(o, [(o, B(l), B(r, 0, 8)), (o, B("id1"), B("rob2", 0, 8))], 64, True)
            placed[:] = placed[-1:] + [len(ops) - 1]
        act(B("soff", 0, 8), R("b6", 16, 17), scale=0.5)
        for o in (B("goff", 0, 8), B("gf", 0, 8)):
            ts(o, R("b5", 16, 17), 2048.0 - 16 * 1151, A.add)
        o, either = 0, {"V": cp, "S": act, "G": pass_on}
        for k in range(2):
            either[OPT["xv"][t][k]](B("xv", U * k, U * k + U), ind(B("xg", 2048 * k, 2048 * k + 2048), B("soff", 0, 8)))
        group(kept(R("b6", 32, 48), [(B("xv", U * k, U * k + U), "id1") for k in range(2)]), True)
        act(B("mo", o, o + U), R("b6", 32, 48), scale=0.5, bias=-0.25)
        cut = OPT["bf"][t]
        for c0, c1, e in zip(cut[0], cut[0][1:], cut[1]):
            either[e](B("bf", 16 * c0, 16 * c1), ind(B("iw", 0, WT), B("goff", c0, c1)))
        either[OPT["eq"][0]](ST("eq", 16, L, 162), B("gf", 0, 4))
        either[OPT["eq"][1]](ST("eq", 145, L, 146), ST("gf", 7, 3, -1))
        for c in range(8):
            ts(B("eq", FIRST[c], FIRST[c] + 16 * c + 16), B("bf", 0, 16 * c + 16), B("gf", c, c + 1), A.is_equal, 0.25, A.mult)
        scan(B("sc", 0, L), B("w", 0, L), B("eq", 0, L), A.mult, A.max)
        either[OPT["mo"][t][0]](B("mo", o + U, o + U + 4), ST("sc", 16, L, 162))
        either[OPT["mo"][t][1]](ST("mo", o + U + 7, o + U + 3, -1), ST("sc", 145, L, 146))
        if t == 2:
            cp(B("tab", NONE, NONE + 1), B("xsav", 1, 2))
        w = B("tab", 0, WT)
        note("V", [w], [X("mo")], lambda q: q.tensor_copy(out=w[0].indirect(T.mo[:, U:M]), in_=T.mo[:, 0:U]), (60, U, "s"))

    def y_rows(t, qy, opy, empty):
        s = t % 2
        group(to_rows("b2", 0, s + 1, [(qy, "id1")], False) + [(E("b2", 1 - s), B("id4096"), empty)]
              + to_rows("b2", 0, s + 1, [(opy, "id4096")]), True)

    def new_rows(t):
        s = t % 2
        gg, ma, mb = ("g%d" % t, "ma%d" % t, "mb%d" % t) if t < 2 else ("hg", "ha", "hb")
        go, ao, bo = ("go%d" % t, "ao%d" % t, "bo%d" % t) if t < 2 else ("ogs", "oas", "obs")
        opx, opy, ty, mg, tk, nx, qy = [("h" if t == 2 else "") + m for m in ("opx", "opy", "ty", "mg", "tk", "nx", "qy")]
        if t == 2:
            none("V", B("hem"), E(gg, 1))
        if t == 2:
            y_rows(t, qy, opy, B("hem"))
        pre = t < 2 and OPT["pre"]
        group(to_rows("b2", 0, s + 1, [(ty, "idn4096"), (mg, "id4096")][:2 - pre]))
        on_s = OPT["er"][t] == "S"
        group(kept(R("b1"), [(H(ma), "id1")]) + kept(R("b1", 32, 64), [(B("ones", 0, 256), "id4096")] * (not on_s))
              + [(E("b1", a, k, 32), B("id1"), E(mb, b, k)) for a, b, k in ((1, 0, 16), (2, 1, 15), (0, 31, 1))]
              + to_rows("b1", 0, s, [(opx, "idn4096")]) + to_rows("b1", 32, s + 1, [(opx, "idn4096")])
              + to_rows("b1", 0, s + 1, [(opy, "idn4096")]) + to_rows("b1", 32, s + 2, [(opy, "idn4096")]), True)
        if on_s:
            act(X("rl"), X("b1"), scale=-1.0, bias=-2049.0, func=F.Relu)
            group(kept(R("b1"), [(R("rl", 32 * k, 32 * k + 32), "id1") for k in range(2)]), True)
            act(H("er"), R("b1"), scale=-1.0, bias=2047.0)
        else:
            ts(H("er"), R("b1"), 4096.0, A.add, 2047.0, A.min)
            tt(H("er"), R("b1", 32, 64), H("er"), A.min)
        tt(E("er" if pre else go, 1 - s), E("b2", 1 - s), E("er", 1 - s), A.min)
        if pre:
            {"v": cp, "s": act}[OPT["offx"]](B("oxo%d" % t), E("er", 1 - s))
            send(1, "gx%d" % (t + 1), B("offx%d" % (t + 1)), B("oxo%d" % t))
            group(to_rows("b2", 0, s + 1, [(mg, "id2047")]), True)
            tt(E(go, 1 - s), E("b2", 1 - s), E("er", 1 - s), A.max)
            if OPT["pre"] == 1:
                send(1, "gt%d" % (t + 1), E("g%d" % (t + 1), 1 - s), E(go, 1 - s))
        elif t < 2:
            if OPT["offx"] in "VS":
                send(1, "gx%d" % (t + 1), E("g%d" % (t + 1), 1 - s), E(go, 1 - s))
            else:
                {"v": cp, "s": act}[OPT["offx"]](B("oxo%d" % t), E(go, 1 - s))
                send(1, "gx%d" % (t + 1), B("offx%d" % (t + 1)), B("oxo%d" % t))
        stay, new = R("b4", 0, 16), R("b4", 16, 32)
        group(kept(stay, [(E(gg, s), "id1")]) + kept(new, [(B(nx), "id1"), (B("ones"), "id4096")]) + turned(stay, [(B(opx), "id4096")])
              + [x for m in (mg, tk) for x in turned(stay, [(B(m), "id4096")]) + turned(new, [(B(m), "idn4096")])], True)
        tt(E("er", s), stay, E("er", s), A.min)
        tt(E(go, s), new, E("er", s), A.min)
        if t < 2:
            if OPT["pre"] == 2:
                send(1, "gy%d" % (t + 1), H("g%d" % (t + 1)), H(go))
            else:
                send(1, "gy%d" % (t + 1), E("g%d" % (t + 1), s), E(go, s))
            if OPT["shipem"]:
                em = "eo%d" % t
                none("S", H(em), H(go))
                pass_on(H(em, U, U + 8), H(em, 0, 8))
                send(1, "em%d" % (t + 1), X("em%d" % (t + 1)), X(em))
        group(to_rows("b7", 16, s, [(opx, "id2047")]) + to_rows("b7", 16, s + 2, [(opy, "id2047")])
              + to_rows("b7", 16, s + 1, [(m, "id2047") for m in (opx, opy, ty, mg)])
              + to_rows("b7", 16, s, [(m, "id2047") for m in (mg, tk)]), True)
        bk = "b1" if t < 2 else "b3"
        merged = R(bk, 0, 16), R(bk, 16, 32)
        group(kept(R(bk), [(B("ones", 0, 256), "id4096")]) + kept(merged[0], [(E(gg, s), "id1")])
              + [(R(bk, 16 + j0, 16 + j1), B("id1"), E(gg, r0, j1 - j0)) for j0, j1, r0 in wrapped(s + 1)]
              + [x for o in merged for x in turned(o, [(B(mg), "idn4096")])], True)
        for o, old, new in zip(merged, (ma, mb), (ao, bo)):
            for h in range(2):
                tt(E(new, h), E("b7", h, 16, 16), E(old, h), A.max)
            tt(E(new, s), o, E(new, s), A.min)
        if t < 2:
            group([(R("b5", 0, 16), B("mg"), B("blk"))], True)
            if OPT["shipan"]:
                an = "an%d" % t
                {"V": cp, "S": act}[OPT["cnt"]](X(an, 2, slice(0, U)), R("b5", 0, 16))
                none("S", X(an, slice(0, 2), slice(0, U)), H(ao))
                if t == 0:
                    pass_on(E(an, 32, 1), E(an, 0, 1))
                send(1, "ma%d" % (t + 1), X("ac%d" % (t + 1)), X(an))
            else:
                {"V": cp, "S": act}[OPT["cnt"]](B("co%d" % t), R("b5", 0, 16))
                send(1, "ma%d" % (t + 1), B("st%d" % (t + 1), 512, 896), B("so%d" % t, 512, 896))
        if t == 0:
            w = 768 if OPT["shipan"] else 512
            send(1, "mb1", B("st1", 256, w), B("so0", 256, w))
        if t == 1:
            send(-1, "hs", X("hs"), B("so1", 0, 768))

    def visit(t):
        s = t % 2
        before(t)
        evac = {"V": cp, "S": act}
        distances(t)
        all_sums(0)
        all_sums(1)
        evac[OPT["sg"][0]](B("sgx"), DX)
        group(kept(OX, [(B("sgx"), "id1")]))
        above(OPT["op"][0], B("opx"), OX)
        evac[OPT["sg"][1]](B("sgy"), DY)
        tt(B("mnu"), DY, B("sgx"), A.min)
        group(kept(OY, [(B("sgy"), "id1")]))
        above(OPT["op"][1], B("opy"), OY)
        group(turned(TK, [(E("em%d" % t, s), "idn18")]) + kept(TK, [(B("sgy"), "idm"), (B("opy"), "idnbig")]), True)
        act(B("tkb"), TK, scale=-1.0, bias=-7 * BIG)
        group(turned(OT, [(E("em%d" % t, s + 1), "idbig"), (E("em%d" % t, s + 2), "idnbig")])
              + kept(OT, [(B("sgx"), "up"), (B("opx"), "idnbig"), (B("sgy"), "idm")]), True)
        above(OPT["op"][2], B("ty"), OT)
        if t < 2:
            y_rows(t, "qy", "opy", E("em%d" % t, 1 - s))
        early = [len(ops) - 1] * (OPT["early"] and t < 2)
        all_sums(2, -OPT["late"])
        hold.extend(early)
        first = len(ops)
        whole = SUMS[2][-1][1:] == (0, 16)
        group(kept(DN, [(B("opy"), "shb")] + [(B("opy"), "idbig")] * whole))
        all_sums(2, None, -OPT["late"])
        group(kept(DN, [(B("opy"), "idbig")] * (not whole)))
        hold[:] = []
        for o in ops[first:]:
            o["firm"] = True
        tt(B("mg"), DN, B("mnu"), A.is_lt)
        tt(B("tk"), DN, B("tkb"), A.is_lt)
        if t == 2:
            send(-2, "hq", X("hq"), X("nq"))
            for k, (lo, hi) in enumerate(OPT["home"]):
                send(-2, "hk%d" % k, B("hk", U * lo, U * hi), B("mk", U * lo, U * hi))
        writes(t)
        if t == 0:
            split(OPT["cast"][2], "mb0", "bli")
        first = len(ops)
        new_rows(t)
        for o in ops[first:] * (t == 2):
            if o["e"] == "P":
                o.update(behind=o["behind"] + placed, firm=True)
        if t < 2:
            views(t + 1)
            lists(t + 1)

    for t in range(3):
        visit(t)
    for m, q, a, time in (("x", T.ox, B("tab", 0, 2048), 1.5), ("g", T.og, X("ogs"), 0.4), ("a", T.oa, X("oas"), 0.4),
                          ("b", T.ob, X("obs"), 0.4)):
        k = dma("Y", "so" + m, [], [a], q[:, :], a[0], ("", STORE))
        note("L", [], [], None, (time, 0, "l"), deps=[k])

    cnt = issue()
    for sm in ("sog", "soa", "sob", "sox"):
        g.sync.wait_ge(T.sem[sm], 16)
    for e in COUNTER:
        g.wait_ge(T.sem[COUNTER[e]], cnt[e])
    g.wait_ge(T.sem.ls, sent[0])
